import numpy as np, ml_dtypes
CORES = [13,21,141,149]
N = 4
BF = ml_dtypes.bfloat16
def gentries(a):
    return np.ascontiguousarray(a.reshape(8, 16, -1).transpose(0, 2, 1)).reshape(8, -1)
def gtable(e):
    e = np.asarray(e); return np.ascontiguousarray(e.reshape(8, -1, 16).transpose(0, 2, 1)).reshape(128, -1).astype(np.int32)
W, NW, P, RO, F = 4096, 128, 32, 3, 2
S = W // NW
def parts(rng):
    x = rng.integers(0, 16, (N, 8, 16, W)); l = rng.integers(0, W, (N, 8, NW, P))
    n = np.where(rng.random((N, 8, NW)) < 0.12, rng.integers(0, P + 1, (N, 8, NW)), rng.integers(P // 2, P + 1, (N, 8, NW)))
    return x, l, n, rng.integers(0, 256, (N, 8, 16)), rng.integers(68, 100, (N, 8))
def pack(x, l, n, w, t):
    return {"xv": np.ascontiguousarray(x.reshape(N, 128, W)).astype(np.float32).astype(BF), "wl": np.stack([gtable(a.reshape(8, NW * P)) for a in l]),
            "wn": np.ascontiguousarray(n).astype(np.int32), "wt": np.ascontiguousarray(w.reshape(N, 128, 1)).astype(np.int32), "th": np.ascontiguousarray(t.reshape(N, 8, 1)).astype(np.int32)}
def setup_inputs(rng):
    return pack(*parts(rng))
def setup_inputs_alike(rng):
    x, l, n, w, t = parts(rng)
    l[:, ::2] = rng.choice(np.array([0, W - 1, W // 2, 3]), (N, 4, NW, P))
    l[:, 1] = l[:, 1, :, :1]; x[:, 3] = x[:, 3, :, :1]; w[:, 5] = 0; n[:, 6] = P; t[:, 7] = 0
    return pack(x, l, n, w, t)
def setup_inputs_corners(rng):
    x, l, n, w, t = parts(rng); k = np.arange(P)
    x = rng.integers(0, 4, (N, 8, 16, W)) + 12 * (np.arange(W) & 1); t = rng.integers(48, 144, (N, 8)); t[:, 0] = 48; t[:, 7] = 143
    w = np.where(rng.random((N, 8, 1)) < 0.3, 255 * rng.integers(0, 2, (N, 8, 1)), w)
    n = rng.choice(np.array([0, 1, 2, P - 1, P, P, P, P]), (N, 8, NW)); m = np.minimum(n, rng.choice(np.array([1, 2, P // 2, P // 2 + 1, P - 1, P]), (N, 8, NW)))
    pick = rng.random((8, NW)) < 0.4; a = rng.integers(P // 2, P + 1, (8, NW)); a[:, 0] = P // 2 + 1; a[:, NW - 1] = P; pick[:, 0] = True; pick[:, NW - 1] = True
    for q in range(0, N - 1, 2):
        m[q] = np.where(pick, a, m[q]); n[q] = np.where(pick, np.maximum(a, rng.integers(0, P + 1, (8, NW))), n[q])
        m[q + 1] = np.where(pick, P - a, m[q + 1]); n[q + 1] = np.where(pick, np.where(a == P, 0, np.maximum(P - a, rng.integers(1, P + 1, (8, NW)))), n[q + 1])
    m[0, 5] = P; n[0, 5] = P; m[1, 4] = 0; n[1, 4] = 0
    m[N - 2] = P; n[N - 2] = P; m[N - 1] = 0; n[N - 1] = 0
    for q in (0, 1):
        fr = np.where(pick, 0, m[q]); fr[5] = 0; fr = fr.reshape(-1); o = rng.permutation(8 * NW); b = fr[o]; cut = np.zeros_like(b)
        cut[o] = np.clip((int(np.sum(m[q])) - 256) % 512 - (np.add.accumulate(b) - b), 0, b)
        m[q] = m[q] - cut.reshape(8, NW); n[q] = np.where(m[q] == 0, 0, n[q])
    sc = np.where((k == 0) | (k >= n[..., None]), 2.0, rng.random((N, 8, NW, P)))
    brk = np.argsort(np.argsort(sc, axis=-1), axis=-1) < (m - 1)[..., None]
    cl = (rng.integers(0, 2, (N, 8, NW, 1)) + np.add.accumulate(brk.astype(np.int64), axis=-1)) & 1
    l = np.where(rng.random((N, 8, NW, P)) < 0.1, cl * (W - 1), 2 * rng.integers(0, W // 2, (N, 8, NW, P)) + cl)
    return pack(x, l, n, w, t)
def setup_inputs_ends(rng):
    kind = rng.integers(0, 3, (N, 8, 1, W)); k = np.arange(P); c = np.arange(1, P + 1)
    x = np.where(kind == 0, 0, np.where(kind == 1, 15, 15 * rng.integers(0, 2, (N, 8, 16, W))))
    for u, v in ((0, 15), ((240 * 255) & (W - 1), 0)):
        hh = ((u * u >> 5) + 37 * u + 611 * c) & (W - 1)
        for g in (0, 7): x[:, g][..., hh] = v
    x[..., 0] = 0; x[..., W - 1] = 15
    w = 255 * rng.integers(0, 2, (N, 8, 16)); w[:, 0] = 255; w[:, 7] = 255; w[:, 3, 0] = 0; w[:, 4] = 0
    t = 239 * rng.integers(0, 2, (N, 8)); t[:, 0] = 0; t[:, 1] = 239; t[:, 7] = 239
    kd = rng.integers(0, 4, (N, 8, NW, 1)); s = rng.integers(0, 2, (N, 8, NW, 1)); em = np.where(np.arange(N) == N - 1, 0.05, 0.25).reshape(N, 1, 1)
    kd[N - 1] = np.where(rng.random((8, NW, 1)) < 0.9, 1, kd[N - 1]); kd[:, :, 0] = 1; kd[:, 7, NW - 1] = 1; kd[:, 7, NW - 2] = 0; s[:, 7, NW - 2] = 1
    b = np.where(kd == 0, s, np.where(kd == 1, (k + s) & 1, rng.integers(0, 2, (N, 8, NW, P))))
    n = P * (rng.random((N, 8, NW)) > em).astype(np.int64); n[:, :, 0] = P; n[:, :, 1] = 0; n[:, :, NW - 2] = P; n[:, :, NW - 1] = P
    return pack(x, (W - 1) * b, n, w, t)
def setup_inputs_spread(rng):
    x, l, n, w, t = parts(rng)
    x = (rng.random((N, 8, 16, W)) * np.exp2(rng.integers(0, 5, (N, 8, 1, W)))).astype(np.int64)
    l = np.minimum((W * rng.random((N, 8, NW, P)) ** rng.choice(np.array([0.3, 1.0, 3.0]), (N, 8, 1, 1))).astype(np.int64), W - 1)
    n = rng.integers(0, P + 1, (N, 8, NW)); w = (256 * rng.random((N, 8, 16)) ** 2).astype(np.int64)
    t = np.exp2(7.9 * rng.random((N, 8))).astype(np.int64) - 1
    return pack(x, l, n, w, t)
def setup_inputs_ties(rng):
    x, l, n, w, t = parts(rng)
    lane = np.argsort(rng.random((N, 8, 16)), axis=-1); pm = np.argsort(rng.random((N, 8, W)), axis=-1)
    lev = np.zeros((N, 8, W), np.int64); np.put_along_axis(lev, pm, np.broadcast_to(np.arange(W) % 241, (N, 8, W)), 2)
    x = np.clip(lev[:, :, None, :] - 15 * lane[..., None], 0, 15)
    t = rng.choice(np.array([0, 1, 15, 16, 47, 80, 100]), (N, 8)); s = rng.integers(0, 241, (N, 8, NW))
    for k in range(P):
        l[..., k] = np.take_along_axis(pm, s + 241 * rng.integers(0, W // 241, (N, 8, NW)), 2)
        st = np.abs(t[:, :, None] + rng.integers(-1, 2, (N, 8, NW))); up = ((rng.random((N, 8, NW)) < 0.5) & (s + st <= 240)) | (s - st < 0)
        s = np.where(up, s + st, s - st)
    t[:, 7] = 239
    hl = 239 * ((np.arange(P) + rng.integers(0, 2, (N, NW, 1))) & 1) + rng.integers(0, 2, (N, NW, P)) + 241 * rng.integers(0, W // 241, (N, NW, P))
    l[:, 7] = np.take_along_axis(pm[:, 7], hl.reshape(N, NW * P), 1).reshape(N, NW, P)
    return pack(x, l, n, w, t)
def check_inputs(d):
    bad = []
    for k, lo, hi in (("xv", 0, 15), ("wl", 0, W - 1), ("wn", 0, P), ("wt", 0, 255), ("th", 0, 239)):
        v = np.asarray(d[k]).astype(np.float64)
        if not (np.min(v) >= lo and np.max(v) <= hi): bad.append("range of " + k)
        elif np.any(v != np.floor(v)): bad.append("whole numbers of " + k)
    return bad
def reference(xv, wl, wn, wt, th):
    x = xv.astype(np.int32).reshape(N, 8, 16, W); w = wt.astype(np.int32).reshape(N, 8, 16, 1, 1); lim = th.astype(np.int64).reshape(N, 8, 1, 1)
    l = np.stack([gentries(a) for a in wl]).astype(np.int64).reshape(N, 8, NW, P); n = wn.astype(np.int64)
    last = np.zeros((N, 1, 1, 1), np.int64); k = np.arange(P); M = W - 1
    for t in range(RO):
        if t > 0:
            l = np.roll(l, (1, 1), axis=(0, 1)); n = np.roll(n, (1, 1), axis=(0, 1))
        live = k < n[..., None]
        v = np.take_along_axis(x, l.reshape(N, 8, 1, NW * P), 3).reshape(N, 8, 16, NW, P)
        dist = np.add.reduce(np.abs(v[..., 1:] - v[..., :-1]), axis=2)
        start = live.copy(); start[..., 1:] &= dist > lim
        end = live.copy(); end[..., :-1] &= start[..., 1:] | ~live[..., 1:]
        num = np.add.accumulate(start.astype(np.int64), axis=-1) - 1; m = np.add.reduce(start.astype(np.int64), axis=-1)
        z = v.copy(); c = np.ones((N, 8, NW, P), np.int64); f = l.copy()
        for j in range(1, P):
            s = start[..., j]
            z[..., j] = np.where(s[:, :, None], v[..., j], np.maximum(z[..., j - 1], v[..., j]))
            c[..., j] = np.where(s, 1, c[..., j - 1] + 1); f[..., j] = np.where(s, l[..., j], f[..., j - 1])
        u = np.add.reduce(w * z, axis=2).astype(np.int64) & M
        h = ((u * u >> 5) + 37 * u + 611 * c) & M
        xh = np.take_along_axis(x, h.reshape(N, 8, 1, NW * P), 3).reshape(N, 8, 16, NW, P)
        dd = np.add.reduce(np.abs(xh - z), axis=2).astype(np.int64)
        y = np.zeros((N, 8, NW, 2 * P + 2), np.int64)
        np.put_along_axis(y, np.where(end, 2 * num, 2 * P), ((f * (2 * c + 1) >> 2) + last) & M, 3)
        np.put_along_axis(y, np.where(end, 2 * num + 1, 2 * P + 1), (h + dd * (2 * c + 1)) & M, 3)
        own = np.minimum(2 * m, P); over = np.roll(2 * m - own, 1, axis=0); oy = np.roll(y[..., P:2 * P], 1, axis=0)
        n = np.minimum(own + over, P); o = own[..., None]
        l = np.where(k < o, y[..., :P], np.where(k < n[..., None], np.take_along_axis(oy, np.clip(k - o, 0, P - 1), 3), 0))
        e = np.argmax(end, axis=-1)[..., None]; e5 = e[:, :, None]
        val = ((np.take_along_axis(z, e5, 4) + np.take_along_axis(xh, e5, 4)) >> 1)[..., 0]
        at = (S * np.arange(NW) + (np.take_along_axis(u, e, 3)[..., 0] & (S - 1)))[:, :, None]
        np.put_along_axis(x, at, np.where((m > 0)[:, :, None], val, np.take_along_axis(x, at, 3)), 3)
        last = np.add.reduce(m.reshape(N, 8 * NW), axis=1).reshape(N, 1, 1, 1) & 255
    return {"yx": np.add.reduce(x.reshape(N, 128, W // F, F), axis=3).astype(np.float32).astype(BF), "yl": np.stack([gtable(a.reshape(8, NW * P)) for a in l]).astype(np.float32), "yn": n.astype(np.float32)}

@@ -1,0 +1,694 @@
+import numpy as np
+from concourse.bass import DstId, RemoteDMATransfer
+from concourse.mybir import dt, AluOpType, AxisListType, ActivationFunctionType
+
+NW, P, RO = 128, 32, 3
+NB = 64
+NBK = NW // NB
+W = 4096
+DEAD = 4096
+ROWS = P * NB
+CH = 512
+AF = ActivationFunctionType
+OP = AluOpType
+
+SCRATCH = {}
+for _i in range(8):
+    SCRATCH["ps%d" % _i] = ("psum", [128, 512], "float32")
+
+
+SIZE, PLACE, FILL = {}, {}, {"float32": 0, "int32": 0, "uint16": 0, "bfloat16": 0}
+OWN = ("DG", "HT", "XT0", "XT1", "XT2", "wli", "wni", "thi", "wti", "YX", "snd", "rcv", "mos", "mor", "yl3", "yno")
+
+
+def _sb(name, n, dtype):
+    SIZE[name] = (n, dtype)
+    if name[:3] in OWN or name in OWN:
+        SCRATCH[name] = ("sbuf", [128, n], dtype)
+        PLACE[name] = (name, 0)
+    else:
+        PLACE[name] = ("all_" + dtype, FILL[dtype])
+        FILL[dtype] += -(-n // 16) * 16
+
+
+for _i in range(RO):
+    _sb("XT%d" % _i, W + 16 + 128, "bfloat16")
+_sb("DG", W + 16, "bfloat16"); _sb("LUT", 1552, "bfloat16"); _sb("QW", 4096, "bfloat16")
+_sb("wli", 2 * NW, "int32"); _sb("wni", NW, "int32"); _sb("thi", 1, "int32"); _sb("wti", 1, "int32")
+_sb("wnf", NW + 1, "float32"); _sb("E8", 128, "float32"); _sb("nr0", NW + 1, "float32")
+_sb("pint", 1, "int32"); _sb("lani", 1, "int32"); _sb("grpi", 1, "int32"); _sb("roti", 1, "int32"); _sb("rotj", 1, "int32")
+_sb("cols", 40, "float32")
+_sb("XR", 144, "float32"); _sb("GR", 128, "float32"); _sb("YI", 52, "float32"); _sb("IO", NB, "bfloat16")
+_sb("E1", 144, "bfloat16"); _sb("E2", 144, "bfloat16"); _sb("E3", 144, "bfloat16"); _sb("OB", 128, "bfloat16"); _sb("OF", 128, "float32"); _sb("L0B", 1, "bfloat16")
+_sb("SC", 1, "float32"); _sb("mA", NW, "float32")
+_sb("WI", 8, "float32"); _sb("WI1", 8, "float32"); _sb("WI2", 8, "float32")
+_sb("HT", W, "bfloat16"); _sb("VY", 52, "bfloat16")
+_sb("ID", 128, "bfloat16"); _sb("NEG", 128, "bfloat16"); _sb("BLK", 128, "bfloat16"); _sb("BLK2", 128, "bfloat16"); _sb("BL16", 128, "bfloat16")
+_sb("EW", 144, "bfloat16"); _sb("WW", 144, "bfloat16"); _sb("DW", 144, "bfloat16"); _sb("L0W", 144, "bfloat16")
+for _i in range(4):
+    _sb("SE%d" % _i, 144, "bfloat16"); _sb("PM%d" % _i, 128, "float32")
+_sb("GT", 1024, "bfloat16"); _sb("TBf", 128, "float32"); _sb("AS", 128, "float32"); _sb("ROT", 128, "float32"); _sb("ROT4", 128, "bfloat16")
+_sb("IDF", 128, "float32"); _sb("IDF4", 128, "bfloat16"); _sb("BIG", 128, "bfloat16"); _sb("ONE", CH // P, "bfloat16"); _sb("P8", 8, "float32")
+_sb("NLi", 2 * NW, "float32"); _sb("NLf", 2 * NW, "float32"); _sb("NL", 2 * NW, "uint16")
+_sb("MS", NBK, "float32"); _sb("AT", 1, "float32"); _sb("ATi", 1, "int32"); _sb("ATj", 1, "int32"); _sb("AC", 4, "float32")
+_sb("ZF", NW, "bfloat16"); _sb("VAL", NW, "bfloat16")
+for _n, _d in (("wa", "int32"), ("wb", "int32"), ("wc", "float32"), ("wd", "float32"), ("we", "float32"), ("wf", "float32")):
+    _sb(_n, 8, _d)
+_sb("WL", 8, "uint16"); _sb("YX", 2048, "bfloat16")
+for _b in range(NBK):
+    _s = str(_b)
+    _sb("V" + _s, ROWS + 16, "bfloat16"); _sb("B" + _s, ROWS + 16, "bfloat16"); _sb("D" + _s, ROWS, "bfloat16")
+    _sb("C" + _s, ROWS, "bfloat16"); _sb("Z" + _s, ROWS, "bfloat16")
+    _sb("n" + _s, NB, "float32"); _sb("nI" + _s, NB, "float32"); _sb("K3" + _s, NB, "float32"); _sb("IB" + _s, NB, "float32")
+    _sb("mg" + _s, 2 * NB, "float32"); _sb("nm" + _s, 2 * NB, "uint16"); _sb("pv" + _s, NB, "bfloat16")
+    _sb("e2" + _s, NB, "int32"); _sb("io" + _s, NB, "float32")
+    _sb("yl1" + _s, 2 * NB, "float32"); _sb("yl2" + _s, 2 * NB, "float32"); _sb("yl3" + _s, 2 * NB, "float32"); _sb("yno" + _s, NB, "float32")
+    for _t in range(RO):
+        _sb("mos%d%d" % (_t, _b), NB, "bfloat16"); _sb("mor%d%d" % (_t, _b), NB, "bfloat16")
+        for _h in (0, 1):
+            _sb("snd%d%d%d" % (_t, _b, _h), 2 * NB, "float32"); _sb("rcv%d%d%d" % (_t, _b, _h), 2 * NB, "float32")
+    for _h in (0, 1):
+        _s = "%d%d" % (_b, _h)
+        for _n, _k, _d in (("ix", NB, "uint16"), ("G", 16 * NB, "bfloat16"), ("ao", NB, "uint16"), ("zo", NB, "uint16"), ("iv", NB, "bfloat16"),
+                           ("iw", NB, "bfloat16"), ("c2", NB, "float32"), ("c6", NB, "float32"), ("Zc", 16 * NB, "bfloat16"),
+                           ("Ac", 16 * NB, "bfloat16"), ("t1", NB, "float32"), ("t2", NB, "float32"), ("ui", NB, "int32"), ("um", NB, "int32"),
+                           ("sq", NB, "int32"), ("qq", NB, "int32"), ("hh", NB, "int32"), ("hm", NB, "int32"), ("hu", NB, "uint16"),
+                           ("D2", 16 * NB, "bfloat16"), ("AD", 16 * NB, "bfloat16"), ("na", NB, "float32"), ("nc", NB, "float32"),
+                           ("NN", 2 * NB, "int32"), ("NM", 2 * NB, "int32"), ("NF", 2 * NB, "float32")):
+            _sb(_n + _s, _k, _d)
+for _i in range(8):
+    SIZE["ps%d" % _i] = (512, "float32"); PLACE["ps%d" % _i] = ("ps%d" % _i, 0)
+for _d in FILL:
+    SCRATCH["all_" + _d] = ("sbuf", [128, FILL[_d]], _d)
+
+SEMAPHORES = ["sv", "sa", "st", "sg", "loc"]
+SEMAPHORES += ["d%d" % i for i in range(6 + RO + 2 * NBK)]
+for _t in range(RO):
+    for _b in range(NBK):
+        SEMAPHORES += ["mo%d%d" % (_t, _b), "nm%d%d0" % (_t, _b), "nm%d%d1" % (_t, _b)]
+
+CY = 0.00083
+HOP1, HOP2 = 3.5, 6.5
+LINK = 0.06
+NOISE, SEED = 0.0, 1
+FIRST = 8.0
+GP2 = 2
+VPEN = 0.2
+
+
+def messages(q, n):
+    out = []
+    for t in range(RO):
+        for b in range(NBK):
+            out.append(("mo", t, b, (q - 1) % n))
+            if t < RO - 1:
+                out.append(("own", t, b, (q + 1) % n))
+                out.append(("over", t, b, (q + 2) % n))
+            else:
+                out.append(("over", t, b, (q + 1) % n))
+    return out
+
+
+def names_of(kind, t, b):
+    if kind == "mo":
+        return "mos%d%d" % (t, b), "mor%d%d" % (t, b), "mo%d%d" % (t, b)
+    h = 1 if kind == "over" else 0
+    return "snd%d%d%d" % (t, b, h), "rcv%d%d%d" % (t, b, h), "nm%d%d%d" % (t, b, h)
+
+
+def relay_of(topo, src, dst, kind):
+    if topo.may_write(src, dst):
+        return None
+    c = [x for x in topo.cores_of(src) if x != src and topo.die(x) == topo.die(src) and topo.may_write(x, dst)]
+    return c[0] if kind != "mo" else c[-1]
+
+
+def emask(topo, src, dst, n=8):
+    m = 0
+    for e in topo.engines(src, dst)[:n]:
+        m |= 1 << e
+    return m, len(topo.engines(src, dst)[:n])
+
+
+def send(g, T, topo, core, dst, sbuf, dbuf, sem):
+    m, k = emask(topo, core, dst)
+    rid, pid = topo.addr(dst, core)
+    g.remote_dma(T[dbuf][:, :], T[sbuf][:, :], T.sem[sem], T.sem["loc"], pid, rid, m)
+    return k
+
+
+def relay_program(g, core, T, topo):
+    todo = []
+    n = len(T.cores)
+    for q in range(n):
+        for kind, t, b, d in messages(q, n):
+            dst = T.cores[d]
+            if relay_of(topo, T.cores[q], dst, kind) == core:
+                todo.append((t, kind == "over", b, kind, T.cores[q], dst))
+    tot = 0
+    for t, _, b, kind, src, dst in sorted(todo):
+        sb, lb, sem = names_of(kind, t, b)
+        g.wait_ge(T.sem[sem], emask(topo, src, core)[1])
+        tot += send(g, T, topo, core, dst, lb, lb, sem)
+    if tot:
+        g.wait_ge(T.sem["loc"], tot)
+
+
+def clash(a, b):
+    if a[0] != b[0]:
+        return False
+    if a[0][:2] == "ps":
+        return True
+    if a[2] <= b[1] or b[2] <= a[1]:
+        return False
+    if a[3] == b[3] and a[3] > 1 and (a[1] - b[1]) % a[3]:
+        return False
+    return True
+
+
+def rank_program(g, core, T, topo):
+    rank = T.rank_of(core)
+    if rank is None:
+        return relay_program(g, core, T, topo)
+    nr = len(T.cores)
+    nodes = []
+    cur = {"plus": 0.0}
+    hist = {}
+    eng = {"v": g.vector, "a": g.scalar, "p": g.tensor, "g": g, "s": g.sync}
+    esem = {"v": "sv", "a": "sa", "p": "st", "g": "sg"}
+
+    def add(e, dur, w, r, fn, sem=None, inc=1, after=(), lat=0.0):
+        i = len(nodes)
+        deps = {}
+        for x in r:
+            ps = x[0][:2] == "ps"
+            for (j, y, k) in hist.get(x[0], ()):
+                if (k or ps) and clash(x, y):
+                    deps[j] = 1
+        for x in w:
+            for (j, y, k) in hist.get(x[0], ()):
+                if clash(x, y):
+                    deps[j] = 1
+        for j in after:
+            deps[j] = 1
+        for x in w:
+            h = hist.setdefault(x[0], [])
+            h[:] = [z for z in h if not (x[3] == 1 and x[1] <= z[1][1] and z[1][2] <= x[2])] if x[0][:2] != "ps" else []
+            h.append((i, x, 1))
+        for x in r:
+            hist.setdefault(x[0], []).append((i, x, 1 if x[0][:2] == "ps" else 0))
+        banks = []
+        for x in list(w) + list(r):
+            if x[0][:2] == "ps" and x[0] not in banks:
+                banks.append(x[0])
+        if not isinstance(dur, dict):
+            dur, f1 = {e: dur}, fn
+            fn = lambda e: f1()
+        nodes.append({"e": e, "d": dur, "plus": cur["plus"], "banks": banks, "w": w, "deps": sorted(deps), "fn": fn, "sem": sem, "inc": inc, "lat": lat})
+        return i
+
+    def A(r, rows=None):
+        n, o = ("ps%d" % phys[r[0]], 0) if r[0][:3] == "ps@" else PLACE[r[0]]
+        p = slice(None) if rows is None else slice(0, rows)
+        return T[n][p, o + r[1]:o + r[2]:r[3]] if r[3] > 1 else T[n][p, o + r[1]:o + r[2]]
+
+    def R(name, lo=0, hi=None, step=1):
+        return (name, lo, SIZE[name][0] if hi is None else hi, step)
+
+    def num(r):
+        return -(-(r[2] - r[1]) // r[3])
+
+    def two(r):
+        return r[0][:2] != "ps" and SIZE[r[0]][1] in ("bfloat16", "uint16")
+
+    def copy(o, i, e="v"):
+        dv, da = 0.07 + num(o) * CY * (0.5 if two(o) and two(i) else 1), 0.2 + num(o) * CY
+        return add(e, {"v": dv, "a": da}, [o], [i], lambda e: g.vector.tensor_copy(A(o), A(i)) if e == "v" else
+                   g.scalar.activation(A(o), A(i), AF.Copy))
+
+    def scaled(o, i, k):
+        return add("va", {"v": 0.07 + num(o) * CY, "a": 0.2 + num(o) * CY}, [o], [i],
+                   lambda e: g.vector.tensor_scalar(A(o), A(i), k, None, OP.mult) if e == "v" else
+                   g.scalar.activation(A(o), A(i), AF.Copy, scale=k))
+
+    def ts(o, i, s1, op0, s2=None, op1=None):
+        rd = [i] + [s for s in (s1, s2) if isinstance(s, tuple)]
+        f = lambda s: A(s) if isinstance(s, tuple) else s
+
+        def fn():
+            if op1 is None:
+                return g.vector.tensor_scalar(A(o), A(i), f(s1), None, op0)
+            return g.vector.tensor_scalar(A(o), A(i), f(s1), f(s2), op0, op1)
+        return add("v", 0.07 + num(o) * CY * (0.5 if two(o) and two(i) else 1), [o], rd, fn)
+
+    def tt(o, i, j, op):
+        k = 1 if "ps" in (i[0][:2], j[0][:2]) else 2
+        return add("v", 0.07 + k * num(o) * CY, [o], [i, j], lambda: g.vector.tensor_tensor(A(o), A(i), A(j), op))
+
+    def act(o, i, func, bias=None, scale=1.0):
+        if bias is None:
+            return add("a", 0.2 + num(o) * CY, [o], [i], lambda: g.scalar.activation(A(o), A(i), func, scale=scale))
+        return add("a", 0.2 + num(o) * CY, [o], [i, bias], lambda: g.scalar.activation(A(o), A(i), func, bias=A(bias), scale=scale))
+
+    def mset(o, c):
+        return add("v", 0.07 + num(o) * CY, [o], [], lambda: g.vector.memset(A(o), c))
+
+    def gather(e, o, win, off):
+        f = lambda: A(win).indirect(A(off))
+        d = 0.07 + num(o) * CY * 1.5
+        return add(e, {"v": d, "a": d + 0.1}, [o], [win, off], lambda e: g.vector.tensor_copy(A(o), f()) if e == "v" else
+                   g.scalar.activation(A(o), f(), AF.Copy))
+
+    def mms(lst):
+        w, r, d = [], [], 0.05
+        for o, l, x, s, p in lst:
+            if o not in w:
+                w.append(o)
+            for y in (l, x):
+                if y not in r:
+                    r.append(y)
+            d += max(64, num(x)) * 0.00071 * (4 if not two(x) else 1)
+
+        def fn():
+            z = None
+            for o, l, x, s, p in lst:
+                z = g.tensor.matmul(A(o), A(l), A(x), s, p)
+            return z
+        return add("p", d, w, r, fn)
+
+    def acc(o, pairs):
+        n = len(pairs)
+        return mms([(o, l, x, i == 0, i == n - 1) for i, (l, x) in enumerate(pairs)])
+
+    phys, nbank = {}, [0]
+
+    def bank(kind, n):
+        nbank[0] += 1
+        return ("ps@%d" % nbank[0], 0, n, 1)
+
+    ndma = [0]
+
+    def dma(e, w, r, out, in_, dur=2.0):
+        s = "d%d" % ndma[0]; ndma[0] += 1
+        return add(e, 0.1, w, r, lambda: eng[e].dma_start(out, in_), sem=s, inc=16, lat=dur)
+
+    def iota(o, pattern, base, cm, ints=False):
+        return add("g", 0.15 + num(o) * 2 * CY, [o], [], (lambda: g.iota(A(o), pattern, base, cm)) if ints else
+                   (lambda: g.iota(A(o), pattern, base, cm, allow_small_or_imprecise_dtypes=True)))
+
+    dma("s", [R("XT0", 0, W)], [], T.XT0[:, 0:W], T.xv[:, :], 6.0)
+    dma("a", [R("wli")], [], T.wli[:, :], T.wl[:, :], 2.5)
+    dma("s", [R("wni")], [], T.wni[0:8, :], T.wn[:, :])
+    dma("a", [R("thi")], [], T.thi[0:8, :], T.th[:, :])
+    dma("s", [R("wti")], [], T.wti[:, :], T.wt[:, :])
+    for x in range(1, RO):
+        dma("s", [R("XT%d" % x, 0, W)], [R("XT0", 0, W)], T["XT%d" % x][:, 0:W], T.XT0[:, 0:W], 6.0)
+    col = lambda i: R("cols", i, i + 1)
+    PC, LA, GP, G15, K0, L1P, KA, KB, TH, WC, NLA, L0, L1, L2, DWC, RC = [col(i) for i in range(16)]
+    iota(R("pint"), [[0, 1]], 0, 1, True); iota(R("XR"), [[1, 144]], 0, 0); iota(R("GR"), [[1, 8], [0, 16]], 0, 0)
+    iota(R("WI"), [[16, 8]], 0, 0); iota(R("YI"), [[1, 52]], -17, 0); iota(R("IO"), [[32, NB]], 0, 0)
+    iota(R("DG", 0, W), [[0, 256], [1, 16]], 0, 0); iota(R("HT"), [[1, 256], [0, 16]], 0, 0)
+    copy(PC, R("pint")); ts(R("lani"), R("pint"), 15, OP.bitwise_and); ts(R("grpi"), R("pint"), 4, OP.arith_shift_right)
+    copy(LA, R("lani")); copy(GP, R("grpi")); ts(G15, GP, 16.0, OP.mult, 15.0, OP.add)
+    add("v", 0.2, [R("E8")], [R("GR"), PC], lambda: g.vector.tensor_scalar(A(R("E8"), 8), A(R("GR"), 8), A(PC, 8), None, OP.is_equal))
+    add("v", 0.2, [R("wnf", 0, NW)], [R("wni")], lambda: g.vector.tensor_copy(A(R("wnf", 0, NW), 8), A(R("wni"), 8)))
+    add("v", 0.1, [R("wnf", NW, NW + 1)], [R("thi")], lambda: g.vector.tensor_copy(A(R("wnf", NW, NW + 1), 8), A(R("thi"), 8)))
+    bn = bank("n", NW + 1); b0 = bn
+    add("p", 0.4, [b0], [R("E8"), R("wnf")], lambda: g.tensor.matmul(A(bn), A(R("E8"), 8), A(R("wnf"), 8), True, True))
+    copy(R("nr0"), b0)
+    ts(TH, R("nr0", NW, NW + 1), 0.5, OP.add, 200.0, OP.mult)
+    THR = R("nr0", NW, NW + 1)
+    for h in (0, 1):
+        k = col(20 + h)
+        ts(k, LA, float(16 * h), OP.add)
+        ts(R("NLi", h, 2 * NW, 2), R("nr0", 0, NW), k, OP.is_le, float(DEAD), OP.mult)
+    tt(R("NLf"), R("NLi"), R("wli"), OP.max)
+    copy(R("NL"), R("NLf"))
+    for x in range(RO):
+        mset(R("XT%d" % x, W, W + 16), 255.0)
+    ts(R("ID"), R("XR", 0, 128), PC, OP.is_equal); ts(R("NEG"), R("XR", 0, 128), PC, OP.is_equal, -1.0, OP.mult)
+    ts(R("BLK"), R("GR"), GP, OP.is_equal); ts(R("BL16"), R("GR"), GP, OP.is_equal, 0.0625, OP.mult)
+    ts(R("BIG"), R("XR", 0, 128), PC, OP.is_equal, 1024.0, OP.mult); mset(R("ONE"), 1.0)
+    for b in range(NBK):
+        mset(R("V%d" % b, 0, 16), 0.0); mset(R("B%d" % b, ROWS, ROWS + 16), 0.0)
+    dma("s", [R("DG", 0, W)], [R("HT"), R("DG", 0, W)], T.DG[1::16, 0:W], T.HT[1::16, :], 3.0)
+    for x, v in ((L0, 0.0), (L1, 1.0)):
+        ts(x, LA, v, OP.is_equal)
+    mset(R("DG", W, W + 16), 0.0)
+    ts(R("E1"), R("XR"), G15, OP.is_equal); ts(col(24), G15, 8.0, OP.add); ts(R("E2"), R("XR"), col(24), OP.is_equal)
+    tt(R("E3"), R("E1"), R("E2"), OP.add)
+    for i in range(4):
+        ts(R("SE%d" % i), R("E3"), 3.0 * 2 ** i, OP.mult)
+    for c in range(8):
+        o = R("GT", 128 * c, 128 * c + 128)
+        add("g", 0.4, [o], [R("BL16")], lambda o=o, c=c: g.affine_select(A(o), A(R("BL16")), [[0, 16], [1, 8]], OP.is_gt, 0.0, -c, 0))
+    for c in range(8):
+        b0 = bank("n", 512); l = []
+        for i in range(4):
+            o = R(b0[0], 128 * i, 128 * i + 128)
+            l += [(o, R("ID"), R("GT", 128 * c, 128 * c + 128), True, False), (o, R("ID"), R("SE%d" % i, 15 - c, 143 - c), False, True)]
+        mms(l)
+        copy(R("QW", 512 * c, 512 * c + 512), b0, "va")
+    ts(K0, LA, 8.0, OP.is_ge, 736.0, OP.mult)
+    ts(col(22), LA, 4.0, OP.mult, 737.0, OP.add); tt(KA, col(22), K0, OP.add); ts(KB, KA, 16.0, OP.add)
+    ts(R("VY"), R("YI"), LA, OP.is_le)
+    for part in range(2):
+        b0 = bank("n", 384); l = []
+        for j in range(8):
+            nib = 8 * part + j; c = 0
+            for p in range(4):
+                c += nib >> p & 1
+                l.append((R(b0[0], 48 * j, 48 * j + 48), R("ID"), R("VY", c, c + 48), p == 0, p == 3))
+        mms(l)
+        copy(R("LUT", 16 + 384 * part, 400 + 384 * part), b0, "va")
+    mset(R("LUT", 0, 16), 0.0)
+    for part in range(2):
+        b0 = bank("n", 384); x = 16 + 384 * part
+        acc(b0, [(R("ID"), R("LUT", x - 1, x + 383)), (R("NEG"), R("LUT", x, x + 384))])
+        copy(R("LUT", 768 + x, 1152 + x), b0, "va")
+    mset(R("OB"), 1.0 / 128); mset(R("OF"), 1.0); copy(R("L0B", 0, 1), L0); ts(NLA, LA, -1.0, OP.mult)
+    copy(WC, R("wti")); ts(R("EW"), R("XR"), G15, OP.is_equal); ts(R("WW"), R("XR"), G15, OP.is_equal, WC, OP.mult)
+    ts(col(25), L1, 16.0, OP.mult); tt(DWC, L0, col(25), OP.add)
+    ts(R("DW"), R("XR"), G15, OP.is_equal, DWC, OP.mult); ts(R("L0W"), R("XR"), G15, OP.is_equal, L0, OP.mult)
+    ts(R("roti"), R("pint"), 16.0, OP.add); ts(R("rotj"), R("roti"), 127, OP.bitwise_and); copy(RC, R("rotj"))
+    ts(R("ROT"), R("XR", 0, 128), RC, OP.is_equal); ts(R("ROT4"), R("XR", 0, 128), RC, OP.is_equal, float(DEAD), OP.mult)
+    ts(R("IDF"), R("XR", 0, 128), PC, OP.is_equal); ts(R("IDF4"), R("XR", 0, 128), PC, OP.is_equal, float(DEAD), OP.mult); ts(R("BLK2"), R("GR"), GP, OP.is_equal, 2.0, OP.mult)
+    ts(R("WI1"), R("WI"), LA, OP.add, 31.0, OP.mult); ts(R("WI2"), R("WI"), LA, OP.add, float(W + 16), OP.add)
+    ts(R("wf"), R("WI1"), float(-W - 16), OP.add); copy(R("WI1"), R("wf"))
+    mset(R("AC", 0, 1), -0.375)
+    nloc = [0]
+    win = lambda name, r: R(name, 15 - r, 143 - r)
+    chunks = ROWS // CH
+
+    def transmit(kind, t, b):
+        d = [x[3] for x in messages(rank, nr) if x[:3] == (kind, t, b)][0]
+        sb, lb, sem = names_of(kind, t, b)
+        dst = T.cores[d]; via = relay_of(topo, core, dst, kind)
+        to = dst if via is None else via
+        nloc[0] += emask(topo, core, to)[1]
+        s = add("g", 1.0, [], [R(sb)], lambda: send(g, T, topo, core, to, sb, lb, sem), sem="loc", inc=0)
+        n = [x for q in range(nr) for x in messages(q, nr) if x == (kind, t, b, rank)]
+        src = [q for q in range(nr) if (kind, t, b, rank) in messages(q, nr)][0]
+        v2 = relay_of(topo, T.cores[src], T.cores[rank], kind)
+        k = emask(topo, T.cores[src] if v2 is None else v2, core)[1]
+        add(None, 0.0, [R(lb)], [], None, sem=sem, inc=k, after=[s], lat=HOP1 if via is None else HOP2)
+
+    def merge(b, own, over):
+        tt(R("mg%d" % b), own, over, OP.min)
+        ts(R("pv%d" % b), R("mg%d" % b, 0, NB), float(DEAD), OP.is_lt)
+        b0 = bank("n", 2 * NB)
+        mms([(R(b0[0], 0, NB), R("BLK2"), R("pv%d" % b), True, True), (R(b0[0], NB, 2 * NB), R("BLK2"), R("pv%d" % b), True, False),
+             (R(b0[0], NB, 2 * NB), R("OB"), R("IO"), False, True)])
+        copy(R("n%d" % b), R(b0[0], 0, NB), "va")
+        copy(R("nI%d" % b), R(b0[0], NB, 2 * NB), "va")
+
+    for t in range(RO):
+        XT = "XT%d" % t
+        for b in range(NBK):
+            s = str(b)
+            cur["plus"] = FIRST if b == 0 else 0.0
+            V, B, D, C, Z = "V" + s, "B" + s, "D" + s, "C" + s, "Z" + s
+            if t == 0:
+                for q in range(chunks):
+                    n = 2 * NB // chunks
+                    off = R("NL", 2 * NB * b + n * q, 2 * NB * b + n * q + n)
+                    gather("va", R(V, 16 + CH * q, 16 + CH * q + CH), R(XT, 0, W + 16), off)
+                    gather("va", R(B, CH * q, CH * q + CH), R("DG"), off)
+                copy(R("n" + s), R("nr0", NB * b, NB * b + NB), "va")
+                tt(R("nI" + s), R("nr0", NB * b, NB * b + NB), R("IO"), OP.add)
+            else:
+                merge(b, R("rcv%d%d0" % (t - 1, b)), R("rcv%d%d1" % (t - 1, b)))
+                ts(R("nm" + s), R("mg" + s), float(DEAD), OP.min)
+                n = NB // GP2
+                for q in range(GP2):
+                    for e in (0, 1):
+                        off = R("nm" + s, NB * e + n * q, NB * e + n * q + n)
+                        gather("va", R(V, 16 + P * n * q + e, 16 + P * n * (q + 1), 2), R(XT, 0, W + 16), off)
+                for e in (0, 1):
+                    gather("va", R(B, e, ROWS, 2), R("DG"), R("nm" + s, NB * e, NB * e + NB))
+            ts(R("K3" + s), R("n" + s), float(P), OP.is_ge, float(P - 1), OP.add)
+            for q in range(chunks):
+                x = CH * q
+                f = bank("f", CH)
+                mms([(f, R("ID"), R(V, 16 + x, 16 + x + CH), True, False), (R(f[0], 0, CH, P), R("BIG"), R("ONE"), False, False),
+                     (f, R("NEG"), R(V, 15 + x, 15 + x + CH), False, True)])
+                act(R(D, x, x + CH), f, AF.Abs)
+                f = bank("s", CH)
+                acc(f, [(R("BLK"), R(D, x, x + CH))])
+                o = R(C, x, x + CH)
+                add("va", {"v": 0.07 + CH * CY, "a": 0.2 + CH * CY}, [o], [f, TH, THR],
+                    lambda e, o=o, f=f: g.vector.tensor_scalar(A(o), A(f), A(THR), None, OP.is_le) if e == "v" else
+                    g.scalar.activation(A(o), A(f), AF.Sigmoid, bias=A(TH), scale=-200.0))
+                add("v", 0.07 + CH * CY / 2, [R(Z, x, x + CH)], [R(C, x, x + CH), R(V, 16 + x, 16 + x + CH)],
+                    lambda x=x, C=C, V=V, Z=Z: g.vector.tensor_tensor_scan(A(R(Z, x, x + CH)), A(R(C, x, x + CH)), A(R(V, 16 + x, 16 + x + CH)),
+                                                                           0.0, OP.mult, OP.max))
+            f = bank("n", NB)
+            acc(f, [(R("BL16"), R(C, k, ROWS, P)) for k in range(1, P)])
+            mA = R("mA", NB * b, NB * b + NB)
+            tt(mA, R("K3" + s), f, OP.subtract)
+            ts(R("mos%d%d" % (t, b)), mA, 16.0, OP.min)
+            transmit("mo", t, b)
+            f = bank("n", NB)
+            acc(f, [(R("QW", 128 * k, 128 * k + 128), R(C, k, ROWS, P)) for k in range(1, P)])
+            ts(R("IB" + s), f, -1.0, OP.mult, KA, OP.add)
+            ts(R("ix%d0" % b), f, -1.0, OP.mult, KB, OP.add)
+        if t < RO - 1:
+            f = bank("n", 1)
+            acc(f, [(R("mA"), L0)])
+            copy(R("SC"), f, "va")
+            f = bank("n", 1)
+            acc(f, [(R("OF"), R("SC"))])
+            copy(R("ATi"), f)
+            ts(R("ATj"), R("ATi"), 255, OP.bitwise_and); ts(R("AC", t + 1, t + 2), R("ATj"), -0.375, OP.add)
+        for h in (0, 1):
+            for b in range(NBK):
+                cur["plus"] = FIRST if b == 0 else 0.0
+                s = str(b); u = "%d%d" % (b, h)
+                r = lambda n, lo=0, hi=None, step=1: R(n + u, lo, hi, step)
+                if h == 1:
+                    mr = R("mor%d%d" % (t, b))
+                    f = bank("n", NB)
+                    acc(f, [(R("IDF"), R("IB" + s)), (R("ID"), mr)])
+                    copy(r("ix"), f)
+                gather("va", r("G"), R("LUT"), r("ix"))
+                f = bank("n", 3 * NB)
+                fs, fe, fc = R(f[0], 0, NB), R(f[0], NB, 2 * NB), R(f[0], 2 * NB, 3 * NB)
+                bias = [(R("OB"), R("IO"))]
+                ps = [(R("ID"), r("G", c, None, 16)) for c in range(16)]
+                l = []
+                for o, x in ((fe, ps + bias), (fs, ps[:8] + bias), (fc, ps[8:])):
+                    l += [(o, y, z, i == 0, i == len(x) - 1) for i, (y, z) in enumerate(x)]
+                mms(l)
+                ts(r("zo"), fe, -1.0, OP.add)
+                bad = r("iv")
+                tt(bad, fs, R("nI" + s), OP.is_ge)
+                copy(r("ao"), fs)
+                scaled(r("c6"), fc, 611.0)
+                add("va", {"v": 0.07 + NB * CY, "a": 0.2 + NB * CY}, [r("c2")], [fc],
+                    lambda e, o=r("c2"), f=fc: g.vector.tensor_scalar(A(o), A(f), 2.0, 1.0, OP.mult, OP.add) if e == "v" else
+                    g.scalar.activation(A(o), A(f), AF.Copy, bias=1.0, scale=2.0))
+                if h == 1:
+                    act(r("iw"), mr, AF.Relu, NLA)
+                gather("va", r("Zc"), R("Z" + s), r("zo"))
+                gather("va", r("Ac"), R("B" + s), r("ao"))
+                f = bank("n", NB)
+                acc(f, [(win("WW", x), r("Zc", x, None, 16)) for x in range(16)])
+                copy(r("ui"), f)
+                scaled(r("t1"), f, 37.0)
+                ts(r("um"), r("ui"), W - 1, OP.bitwise_and)
+                tt(r("t2"), r("t1"), r("c6"), OP.add)
+                tt(r("sq"), r("um"), r("um"), OP.mult)
+                ts(r("qq"), r("sq"), 5, OP.arith_shift_right)
+                tt(r("hh"), r("qq"), r("t2"), OP.add)
+                ts(r("hm"), r("hh"), W - 1, OP.bitwise_and)
+                copy(r("hu"), r("hm"))
+                add("v", 0.07 + 16 * NB * CY * 1.5, [r("D2")], [R(XT, 0, W), r("hu"), r("Zc")],
+                    lambda u=u, XT=XT: g.vector.tensor_tensor(A(R("D2" + u)), A(R(XT, 0, W)).indirect(A(R("hu" + u))), A(R("Zc" + u)), OP.subtract))
+                act(r("AD"), r("D2"), AF.Abs)
+                f = bank("n", NB)
+                acc(f, [(win("DW", x), r("Ac", x, None, 16)) for x in range(16)])
+                tt(r("na"), f, r("c2"), OP.mult)
+                ts(r("NN", 0, NB), r("na"), 0.25, OP.mult, R("AC", t, t + 1), OP.add)
+                f = bank("n", NB)
+                acc(f, [(win("EW", x), r("AD", x, None, 16)) for x in range(16)])
+                tt(r("nc"), f, r("c2"), OP.mult)
+                tt(r("NN", NB, 2 * NB), r("nc"), r("hh"), OP.add)
+                ts(r("NM"), r("NN"), W - 1, OP.bitwise_and)
+                sd = R("snd%d%d%d" % (t, b, h))
+                copy(r("NF"), r("NM"))
+                f = bank("n", 2 * NB); l = []
+                x = ("ROT", "ROT4") if t < RO - 1 else ("IDF", "IDF4")
+                for e in (0, 1):
+                    o = R(f[0], NB * e, NB * e + NB)
+                    l += [(o, R(x[0]), r("NF", NB * e, NB * e + NB), True, False), (o, R(x[1]), bad, False, h == 0)]
+                    if h == 1:
+                        l.append((o, R(x[1]), r("iw"), False, True))
+                mms(l)
+                copy(sd, f, "va")
+                if t < RO - 1 or h == 1:
+                    transmit("over" if h else "own", t, b)
+                if h == 0:
+                    z0 = R("ZF", NB * b, NB * b + NB)
+                    copy(z0, r("Zc", 0, None, 16), "va")
+                    ts(R("e2" + s), r("D2", 0, None, 16), 0.5, OP.mult, -0.25, OP.add)
+                    tt(R("VAL", NB * b, NB * b + NB), z0, R("e2" + s), OP.add)
+        cur["plus"] = 0.0
+        f = bank("n", 16)
+        fu, fz = R(f[0], 0, 8), R(f[0], 8, 16)
+        mms([(fu, win("WW", x), R("ZF", x, None, 16), x == 0, x == 15) for x in range(16)] +
+            [(fz, win("L0W", x), R("ZF", x, None, 16), x == 0, x == 15) for x in range(16)])
+        copy(R("wa"), fu); ts(R("wc"), fz, 16.0, OP.is_lt)
+        ts(R("wb"), R("wa"), 31, OP.bitwise_and)
+        tt(R("wd"), R("wb"), R("WI1"), OP.add); tt(R("we"), R("wd"), R("wc"), OP.mult); tt(R("wf"), R("we"), R("WI2"), OP.add)
+        copy(R("WL"), R("wf"))
+        for x in range(t + 1, RO) if t < RO - 1 else (RO - 1,):
+            o = R("XT%d" % x)
+            add("v", 0.07 + NW * CY * 3, [o], [R("VAL"), R("WL")],
+                lambda o=o: g.vector.tensor_copy(A(o).indirect(A(R("WL"))), A(R("VAL"))))
+    for q in range(4):
+        f = bank("f", 512)
+        acc(f, [(R("ID"), R("XT%d" % (RO - 1), 1024 * q + e, 1024 * q + 1024, 2)) for e in (0, 1)])
+        copy(R("YX", 512 * q, 512 * q + 512), f, "a")
+    outs = [dma("s", [("yx", 0, 1, 1)], [R("YX")], T.yx[:, :], T.YX[:, :])]
+    for h in (0, 1):
+        for e in (0, 1):
+            v, x, y, z = [col(28 + i) for i in range(4)]
+            ts(v, LA, 2.0, OP.mult, float(e - 16 * h), OP.add)
+            ts(x, v, 0.0, OP.is_ge); ts(y, v, 15.0, OP.is_le); tt(z, x, y, OP.mult)
+            ts(x, v, G15, OP.add, -14.0, OP.add); tt(y, x, z, OP.mult); ts(v, y, -1.0, OP.add)
+            ts(R("PM%d" % (2 * h + e)), R("XR", 0, 128), v, OP.is_equal)
+    ts(R("P8"), R("XR", 0, 8), GP, OP.is_equal, L0, OP.mult)
+    for b in range(NBK):
+        s = str(b)
+        merge(b, R("snd%d%d0" % (RO - 1, b)), R("rcv%d%d1" % (RO - 1, b)))
+        ts(R("yl1" + s), R("mg" + s), float(DEAD), OP.is_lt); tt(R("yl2" + s), R("yl1" + s), R("mg" + s), OP.mult)
+        f = bank("n", 2 * NB)
+        l = []
+        for h in (0, 1):
+            for e in (0, 1):
+                l.append((R(f[0], h, 2 * NB, 2), R("PM%d" % (2 * h + e)), R("yl2" + s, NB * e, NB * e + NB), e == 0, e == 1))
+        mms(l)
+        copy(R("yl3" + s), f)
+        outs.append(dma("s", [("yl", b, b + 1, 1)], [R("yl3" + s)], T.yl[:, 2 * NB * b:2 * NB * b + 2 * NB], T["yl3" + s][:, :]))
+        f = bank("n", NB)
+        add("p", 0.3, [f], [R("P8"), R("n" + s)], lambda f=f, s=s: g.tensor.matmul(A(f, 8), A(R("P8")), A(R("n" + s)), True, True))
+        add("v", 0.1, [R("yno" + s)], [f], lambda f=f, s=s: g.vector.tensor_copy(A(R("yno" + s), 8), A(f, 8)))
+        outs.append(dma("s", [("yn", b, b + 1, 1)], [R("yno" + s)], T.yn[:, NB * b:NB * b + NB], T["yno" + s][0:8, :]))
+
+    n = len(nodes)
+    users = [[] for _ in range(n)]
+    for i, x in enumerate(nodes):
+        for j in x["deps"]:
+            users[j].append(i)
+    prio = [0.0] * n
+    for i in range(n - 1, -1, -1):
+        x = nodes[i]
+        prio[i] = (min(x["d"].values()) if x["e"] == "va" else x["d"][x["e"]] if x["e"] else 0.0) + x["lat"] + LINK + max([prio[k] for k in users[i]] + [0.0])
+    for i in range(n):
+        prio[i] += nodes[i]["plus"] + NOISE * ((i * SEED) % 997) / 997.0
+    left = [len(x["deps"]) for x in nodes]
+    ready_at = [0.0] * n
+    free = {"v": 0.0, "a": 0.0, "p": 0.0, "g": 0.0, "s": 0.0}
+    ready = {k: [] for k in free}
+    order = []
+    busy = {k: 0.0 for k in free}
+    bfree = [0.0] * 8
+    blast = [[] for _ in range(8)]
+    buse = {}
+    for i, x in enumerate(nodes):
+        for k in x["banks"]:
+            buse.setdefault(k, []).append(i)
+    bleft = {k: len(v) for k, v in buse.items()}
+
+    def done(i, at):
+        for k in users[i]:
+            ready_at[k] = max(ready_at[k], at)
+            left[k] -= 1
+            if left[k] == 0:
+                release(k)
+
+    def release(k):
+        x = nodes[k]
+        if x["e"] is None:
+            x["t"] = ready_at[k]
+            done(k, ready_at[k] + x["lat"])
+        else:
+            for e in x["e"]:
+                ready[e].append(k)
+
+    for i in range(n):
+        if left[i] == 0 and not nodes[i]["deps"]:
+            release(i)
+    while any(ready.values()):
+        best = None
+        for e in free:
+            for k in ready[e]:
+                st = max(free[e], ready_at[k])
+                x = nodes[k]
+                new = [y for y in x["banks"] if y not in phys]
+                if new:
+                    fr = [z for z in bfree if z is not None]
+                    if not fr:
+                        continue
+                    st = max(st, min(fr))
+                key = (st + (VPEN if len(x["e"]) > 1 and e == "v" else 0.0), -prio[k])
+                if best is None or key < best[0]:
+                    best = (key, e, k, st)
+        _, e, k, st = best
+        x = nodes[k]
+        for y in x["e"]:
+            ready[y].remove(k)
+        x["e"] = e
+        x["t"] = st
+        fin = st + x["d"][e]
+        for y in x["banks"]:
+            if y not in phys:
+                z = min([z for z in range(8) if bfree[z] is not None], key=lambda z: bfree[z])
+                phys[y] = z
+                bfree[z] = None
+                x["deps"] = sorted(set(x["deps"] + blast[z]))
+                blast[z] = []
+            bleft[y] -= 1
+            blast[phys[y]].append(k)
+            if bleft[y] == 0:
+                bfree[phys[y]] = fin + LINK
+        free[e] = fin
+        busy[e] += x["d"][e]
+        order.append(k)
+        done(k, fin + x["lat"] + LINK)
+    if "want_est" in T.tables:
+        T.tables["want_est"].append((max(free.values()), busy, n, [(x["e"], x.get("t", 0), x["d"].get(x["e"], 0), x) for x in nodes]))
+    cnt = {"v": 0, "a": 0, "p": 0, "g": 0}
+    for k in order:
+        x = nodes[k]
+        if x["sem"] is None:
+            cnt[x["e"]] += 1
+            x["at"] = (esem[x["e"]], cnt[x["e"]])
+        else:
+            x["at"] = (x["sem"], x["inc"])
+    for x in nodes:
+        if x["e"] is None:
+            x["at"] = (x["sem"], x["inc"])
+    known = {k: {} for k in free}
+    for k in order:
+        x = nodes[k]
+        q = eng[x["e"]]
+        need = {}
+        for j in x["deps"]:
+            sm, v = nodes[j]["at"]
+            if sm != "loc":
+                need[sm] = max(need.get(sm, 0), v)
+        for sm in sorted(need):
+            if known[x["e"]].get(sm, 0) < need[sm]:
+                q.wait_ge(T.sem[sm], need[sm])
+                known[x["e"]][sm] = need[sm]
+        z = x["fn"](x["e"])
+        if x["sem"] is None:
+            z.then_inc(T.sem[esem[x["e"]]], 1)
+        elif x["sem"] != "loc":
+            z.then_inc(T.sem[x["sem"]], x["inc"])
+    for e in ("v", "a", "p", "g"):
+        g.wait_ge(T.sem[esem[e]], cnt[e])
+    for i in range(ndma[0]):
+        g.wait_ge(T.sem["d%d" % i], 16)
+    g.wait_ge(T.sem["loc"], nloc[0])

@@ -5,151 +5,132 @@ from concourse.mybir import dt, AluOpType, AxisListType, ActivationFunctionType
 NW, P, RO = 128, 32, 3
 NB = 64
 NBK = NW // NB
+NX = NB // 16
+L = P * NX
+ROWS = 16 * L
 W = 4096
 DEAD = 4096
-ROWS = P * NB
+HALF = 2048
+CELL = 34
+REG = CELL * NX
+LS = 49
 CH = 512
+MAGIC = 12582912.0
 AF = ActivationFunctionType
 OP = AluOpType
 
-SCRATCH = {}
-for _i in range(8):
+DIFF = (0, 0)
+USC = 1
+
+SCRATCH = {"psz": ("psum", [128, 16, 32], "float32")}
+NPS = 7
+for _i in range(NPS):
     SCRATCH["ps%d" % _i] = ("psum", [128, 512], "float32")
 
-
-SIZE, PLACE, FILL = {}, {}, {"float32": 0, "int32": 0, "uint16": 0, "bfloat16": 0}
-OWN = ("DG", "HT", "XT0", "XT1", "XT2", "wli", "wni", "thi", "wti", "YX", "snd", "rcv", "mos", "mor", "yl3", "yno")
+SIZE, PLACE, FILL = {"psz": (512, "float32")}, {}, {"float32": 0, "int32": 0, "uint16": 0, "bfloat16": 0, "float16": 0}
 
 
-def _sb(name, n, dtype):
-    SIZE[name] = (n, dtype)
-    if name[:3] in OWN or name in OWN:
-        SCRATCH[name] = ("sbuf", [128, n], dtype)
+def _sb(name, n, dtype, own=False):
+    if own or not isinstance(n, int):
+        shape = [n] if isinstance(n, int) else list(n)
+        SIZE[name] = (int(np.prod(shape)), dtype)
+        SCRATCH[name] = ("sbuf", [128] + shape, dtype)
         PLACE[name] = (name, 0)
     else:
+        SIZE[name] = (n, dtype)
         PLACE[name] = ("all_" + dtype, FILL[dtype])
         FILL[dtype] += -(-n // 16) * 16
 
 
-for _i in range(RO):
-    _sb("XT%d" % _i, W + 16 + 128, "bfloat16")
-_sb("DG", W + 16, "bfloat16"); _sb("LUT", 1552, "bfloat16"); _sb("QW", 4096, "bfloat16")
-_sb("wli", 2 * NW, "int32"); _sb("wni", NW, "int32"); _sb("thi", 1, "int32"); _sb("wti", 1, "int32")
-_sb("wnf", NW + 1, "float32"); _sb("E8", 128, "float32"); _sb("nr0", NW + 1, "float32")
-_sb("pint", 1, "int32"); _sb("lani", 1, "int32"); _sb("grpi", 1, "int32"); _sb("roti", 1, "int32"); _sb("rotj", 1, "int32")
-_sb("cols", 40, "float32")
-_sb("XR", 144, "float32"); _sb("GR", 128, "float32"); _sb("YI", 52, "float32"); _sb("IO", NB, "bfloat16")
-_sb("E1", 144, "bfloat16"); _sb("E2", 144, "bfloat16"); _sb("E3", 144, "bfloat16"); _sb("OB", 128, "bfloat16"); _sb("OF", 128, "float32"); _sb("L0B", 1, "bfloat16")
-_sb("SC", 1, "float32"); _sb("mA", NW, "float32")
-_sb("WI", 8, "float32"); _sb("WI1", 8, "float32"); _sb("WI2", 8, "float32")
-_sb("HT", W, "bfloat16"); _sb("VY", 52, "bfloat16")
-_sb("ID", 128, "bfloat16"); _sb("NEG", 128, "bfloat16"); _sb("BLK", 128, "bfloat16"); _sb("BLK2", 128, "bfloat16"); _sb("BL16", 128, "bfloat16")
-_sb("EW", 144, "bfloat16"); _sb("WW", 144, "bfloat16"); _sb("DW", 144, "bfloat16"); _sb("L0W", 144, "bfloat16")
+_sb("XT", 2 * W + 16, "bfloat16", True); _sb("YX", 2048, "bfloat16", True)
+_sb("wli", 2 * NW, "int32", True); _sb("wni", NW, "int32", True); _sb("thi", 1, "int32", True); _sb("wti", 1, "int32", True)
+_sb("SN", (RO * NBK * 2 * NX, CELL), "int32"); _sb("OT", (8, P), "float16"); _sb("yno", NW, "float32", True)
+for _n, _k in (("wnf", NW + 1), ("E8", 128), ("cols", 40), ("XR", 144), ("GR", 128), ("YI", 56), ("RA", L), ("W5", 8), ("LM", 16),
+               ("NLi", 2 * NW), ("NLf", 2 * NW), ("AC", 4), ("W32", 8), ("iv", 8), ("bs", 8), ("wf", 8)):
+    _sb(_n, _k, "float32")
+for _n, _k in (("PI", 2), ("ci", 16), ("ATi", 1), ("ATj", 1), ("wa", 8), ("wb", 8)):
+    _sb(_n, _k, "int32")
+for _n, _k in (("ID", 128), ("NEG", 128), ("N8", 128), ("N15", 128), ("JM", 128), ("W0", 128), ("W1", 128), ("W2", 128), ("W3", 128),
+               ("ONE", 128), ("EW", 144), ("WW", 144), ("SEL", 2048), ("LUT", 16 * LS), ("VY", 56), ("K0", L), ("PAT", L), ("TWO", L),
+               ("MQ", 128), ("CK", L), ("VP", 8 * NX), ("M16", 8 * NX), ("B34", NB), ("ZF", NW), ("e2", NW), ("n1", 8), ("n2", 8), ("n3", 8)):
+    _sb(_n, _k, "bfloat16")
+for _n, _k in (("I16", 128), ("ROT", 128), ("DR", 2048), ("RAMP", L), ("IN", 2 * NW), ("NF", 2 * NW)):
+    _sb(_n, _k, "float16")
 for _i in range(4):
-    _sb("SE%d" % _i, 144, "bfloat16"); _sb("PM%d" % _i, 128, "float32")
-_sb("GT", 1024, "bfloat16"); _sb("TBf", 128, "float32"); _sb("AS", 128, "float32"); _sb("ROT", 128, "float32"); _sb("ROT4", 128, "bfloat16")
-_sb("IDF", 128, "float32"); _sb("IDF4", 128, "bfloat16"); _sb("BIG", 128, "bfloat16"); _sb("ONE", CH // P, "bfloat16"); _sb("P8", 8, "float32")
-_sb("NLi", 2 * NW, "float32"); _sb("NLf", 2 * NW, "float32"); _sb("NL", 2 * NW, "uint16")
-_sb("MS", NBK, "float32"); _sb("AT", 1, "float32"); _sb("ATi", 1, "int32"); _sb("ATj", 1, "int32"); _sb("AC", 4, "float32")
-_sb("ZF", NW, "bfloat16"); _sb("VAL", NW, "bfloat16")
-for _n, _d in (("wa", "int32"), ("wb", "int32"), ("wc", "float32"), ("wd", "float32"), ("we", "float32"), ("wf", "float32")):
-    _sb(_n, 8, _d)
-_sb("WL", 8, "uint16"); _sb("YX", 2048, "bfloat16")
+    _sb("PM%d" % _i, 128, "float16"); _sb("QM%d" % _i, 128, "float16")
+_sb("nm", 2 * NW, "uint16"); _sb("WL", 8, "uint16")
 for _b in range(NBK):
     _s = str(_b)
-    _sb("V" + _s, ROWS + 16, "bfloat16"); _sb("B" + _s, ROWS + 16, "bfloat16"); _sb("D" + _s, ROWS, "bfloat16")
-    _sb("C" + _s, ROWS, "bfloat16"); _sb("Z" + _s, ROWS, "bfloat16")
-    _sb("n" + _s, NB, "float32"); _sb("nI" + _s, NB, "float32"); _sb("K3" + _s, NB, "float32"); _sb("IB" + _s, NB, "float32")
-    _sb("mg" + _s, 2 * NB, "float32"); _sb("nm" + _s, 2 * NB, "uint16"); _sb("pv" + _s, NB, "bfloat16")
-    _sb("e2" + _s, NB, "int32"); _sb("io" + _s, NB, "float32")
-    _sb("yl1" + _s, 2 * NB, "float32"); _sb("yl2" + _s, 2 * NB, "float32"); _sb("yl3" + _s, 2 * NB, "float32"); _sb("yno" + _s, NB, "float32")
+    for _n, _k, _d in (("V", ROWS + 16, "bfloat16"), ("M", ROWS, "bfloat16"), ("Z", ROWS, "bfloat16"), ("D2", ROWS, "bfloat16"),
+                       ("AD", ROWS, "bfloat16"), ("S", L + 16, "bfloat16"), ("C", L, "bfloat16"), ("E", L, "bfloat16"),
+                       ("cm", L, "bfloat16"), ("c2", L, "bfloat16"), ("a", L, "float32"), ("na", L, "float32"), ("ni", L, "int32"),
+                       ("y", L, "float32"), ("zo", NX, "uint16"), ("ui", L, "int32"), ("um", L, "int32"), ("q", L, "float32"),
+                       ("r", L, "float32"), ("v", L, "float32"), ("sq", L, "float32"), ("si", L, "int32"), ("hm", L, "int32"),
+                       ("hu", L, "uint16"), ("nc", L, "float32"), ("nj", L, "int32"), ("of", NB, "uint16")):
+        _sb(_n + _s, _k, _d)
+    _sb("G" + _s, (NX, 192), "bfloat16"); _sb("IX" + _s, (NX, 16), "uint16"); _sb("NB" + _s, (NX, P), "float16")
+    _sb("N0" + _s, (NX, 256), "float16"); _sb("N1" + _s, (NX, 256), "float16"); _sb("yl" + _s, L, "float32", True)
     for _t in range(RO):
-        _sb("mos%d%d" % (_t, _b), NB, "bfloat16"); _sb("mor%d%d" % (_t, _b), NB, "bfloat16")
-        for _h in (0, 1):
-            _sb("snd%d%d%d" % (_t, _b, _h), 2 * NB, "float32"); _sb("rcv%d%d%d" % (_t, _b, _h), 2 * NB, "float32")
-    for _h in (0, 1):
-        _s = "%d%d" % (_b, _h)
-        for _n, _k, _d in (("ix", NB, "uint16"), ("G", 16 * NB, "bfloat16"), ("ao", NB, "uint16"), ("zo", NB, "uint16"), ("iv", NB, "bfloat16"),
-                           ("iw", NB, "bfloat16"), ("c2", NB, "float32"), ("c6", NB, "float32"), ("Zc", 16 * NB, "bfloat16"),
-                           ("Ac", 16 * NB, "bfloat16"), ("t1", NB, "float32"), ("t2", NB, "float32"), ("ui", NB, "int32"), ("um", NB, "int32"),
-                           ("sq", NB, "int32"), ("qq", NB, "int32"), ("hh", NB, "int32"), ("hm", NB, "int32"), ("hu", NB, "uint16"),
-                           ("D2", 16 * NB, "bfloat16"), ("AD", 16 * NB, "bfloat16"), ("na", NB, "float32"), ("nc", NB, "float32"),
-                           ("NN", 2 * NB, "int32"), ("NM", 2 * NB, "int32"), ("NF", 2 * NB, "float32")):
-            _sb(_n + _s, _k, _d)
-for _i in range(8):
-    SIZE["ps%d" % _i] = (512, "float32"); PLACE["ps%d" % _i] = ("ps%d" % _i, 0)
+        _s = "%d%d" % (_t, _b)
+        for _n in ("cs", "ct", "cr0", "cr1"):
+            _sb(_n + _s, L, "bfloat16", True)
+        _sb("WN0" + _s, 2 * REG, "int32", True); _sb("WN1" + _s, 2 * REG, "int32", True)
 for _d in FILL:
     SCRATCH["all_" + _d] = ("sbuf", [128, FILL[_d]], _d)
 
-SEMAPHORES = ["sv", "sa", "st", "sg", "loc"]
-SEMAPHORES += ["d%d" % i for i in range(6 + RO + 2 * NBK)]
-for _t in range(RO):
-    for _b in range(NBK):
-        SEMAPHORES += ["mo%d%d" % (_t, _b), "nm%d%d0" % (_t, _b), "nm%d%d1" % (_t, _b)]
+SEMAPHORES = ["sv", "sa", "st", "sg", "loc"] + ["d%d" % i for i in range(7 + 3 * NBK)]
+SEMAPHORES += ["m%d%d%d%d" % (k, t, b, h) for k in range(3) for t in range(RO) for b in range(NBK) for h in (0, 1)]
 
 CY = 0.00083
+PE = 0.00071
 HOP1, HOP2 = 3.5, 6.5
 LINK = 0.06
-NOISE, SEED = 0.0, 1
-FIRST = 8.0
-GP2 = 2
+FIRST = 4.0
 VPEN = 0.2
 
 
-def messages(q, n):
-    out = []
-    for t in range(RO):
-        for b in range(NBK):
-            out.append(("mo", t, b, (q - 1) % n))
-            if t < RO - 1:
-                out.append(("own", t, b, (q + 1) % n))
-                out.append(("over", t, b, (q + 2) % n))
-            else:
-                out.append(("over", t, b, (q + 1) % n))
-    return out
+def target(q, n, t, h):
+    return (q + h + (1 if t < RO - 1 else 0)) % n
 
 
-def names_of(kind, t, b):
-    if kind == "mo":
-        return "mos%d%d" % (t, b), "mor%d%d" % (t, b), "mo%d%d" % (t, b)
-    h = 1 if kind == "over" else 0
-    return "snd%d%d%d" % (t, b, h), "rcv%d%d%d" % (t, b, h), "nm%d%d%d" % (t, b, h)
+def landing(T, k, t, b, h):
+    if k == 0:
+        return T["cr%d%d%d" % (h, t, b)][:, :]
+    return T["WN%d%d%d" % (k - 1, t, b)][:, REG * h:REG * h + REG]
 
 
-def relay_of(topo, src, dst, kind):
+def relay_of(topo, src, dst, b):
     if topo.may_write(src, dst):
         return None
     c = [x for x in topo.cores_of(src) if x != src and topo.die(x) == topo.die(src) and topo.may_write(x, dst)]
-    return c[0] if kind != "mo" else c[-1]
+    return c[b % len(c)]
 
 
-def emask(topo, src, dst, n=8):
-    m = 0
-    for e in topo.engines(src, dst)[:n]:
-        m |= 1 << e
-    return m, len(topo.engines(src, dst)[:n])
+def engines(topo, src, dst):
+    return topo.engines(src, dst)[-8:]
 
 
-def send(g, T, topo, core, dst, sbuf, dbuf, sem):
-    m, k = emask(topo, core, dst)
+def transfer(T, topo, core, dst, src_ap, dst_ap, sem):
     rid, pid = topo.addr(dst, core)
-    g.remote_dma(T[dbuf][:, :], T[sbuf][:, :], T.sem[sem], T.sem["loc"], pid, rid, m)
-    return k
+    return RemoteDMATransfer(dst_ids=[DstId(rid=rid, pnc=pid)], dma_engine_mask=sum(1 << e for e in engines(topo, core, dst)),
+                             remote_sem=T.sem[sem], src=src_ap, dst=dst_ap)
 
 
 def relay_program(g, core, T, topo):
-    todo = []
     n = len(T.cores)
-    for q in range(n):
-        for kind, t, b, d in messages(q, n):
-            dst = T.cores[d]
-            if relay_of(topo, T.cores[q], dst, kind) == core:
-                todo.append((t, kind == "over", b, kind, T.cores[q], dst))
     tot = 0
-    for t, _, b, kind, src, dst in sorted(todo):
-        sb, lb, sem = names_of(kind, t, b)
-        g.wait_ge(T.sem[sem], emask(topo, src, core)[1])
-        tot += send(g, T, topo, core, dst, lb, lb, sem)
+    for t in range(RO):
+        for b in range(NBK):
+            for k in range(3):
+                for h in (0, 1):
+                    for q in range(n):
+                        d = target(q, n, t, h)
+                        if d != q and relay_of(topo, T.cores[q], T.cores[d], b) == core:
+                            sem = "m%d%d%d%d" % (k, t, b, h)
+                            g.wait_ge(T.sem[sem], len(engines(topo, T.cores[q], core)))
+                            x = landing(T, k, t, b, h)
+                            g.remote_dma_fused([transfer(T, topo, core, T.cores[d], x, x, sem)], local_sem=T.sem["loc"])
+                            tot += len(engines(topo, core, T.cores[d]))
     if tot:
         g.wait_ge(T.sem["loc"], tot)
 
@@ -184,30 +165,33 @@ def rank_program(g, core, T, topo):
             ps = x[0][:2] == "ps"
             for (j, y, k) in hist.get(x[0], ()):
                 if (k or ps) and clash(x, y):
-                    deps[j] = 1
+                    deps[j] = min(deps.get(j, 2), 1 if k else 2)
         for x in w:
             for (j, y, k) in hist.get(x[0], ()):
                 if clash(x, y):
-                    deps[j] = 1
+                    deps[j] = min(deps.get(j, 2), 2 if e == "p" and nodes[j]["e"] == "p" else 1)
         for j in after:
             deps[j] = 1
         for x in w:
             h = hist.setdefault(x[0], [])
-            h[:] = [z for z in h if not (x[3] == 1 and x[1] <= z[1][1] and z[1][2] <= x[2])] if x[0][:2] != "ps" else []
+            h[:] = [z for z in h if not (x[3] == 1 and len(x) == 4 and x[1] <= z[1][1] and z[1][2] <= x[2])] if x[0][:2] != "ps" else []
             h.append((i, x, 1))
         for x in r:
-            hist.setdefault(x[0], []).append((i, x, 1 if x[0][:2] == "ps" else 0))
+            hist.setdefault(x[0], []).append((i, x, 0))
         banks = []
         for x in list(w) + list(r):
-            if x[0][:2] == "ps" and x[0] not in banks:
+            if x[0][:3] == "ps@" and x[0] not in banks:
                 banks.append(x[0])
         if not isinstance(dur, dict):
             dur, f1 = {e: dur}, fn
             fn = lambda e: f1()
-        nodes.append({"e": e, "d": dur, "plus": cur["plus"], "banks": banks, "w": w, "deps": sorted(deps), "fn": fn, "sem": sem, "inc": inc, "lat": lat})
+        nodes.append({"e": e, "d": dur, "plus": cur["plus"], "banks": banks, "w": w, "deps": sorted(deps), "fn": fn, "sem": sem, "inc": inc,
+                      "lat": lat, "soft": [j for j in deps if deps[j] == 2]})
         return i
 
     def A(r, rows=None):
+        if len(r) > 4:
+            return T[r[0]][r[4]]
         n, o = ("ps%d" % phys[r[0]], 0) if r[0][:3] == "ps@" else PLACE[r[0]]
         p = slice(None) if rows is None else slice(0, rows)
         return T[n][p, o + r[1]:o + r[2]:r[3]] if r[3] > 1 else T[n][p, o + r[1]:o + r[2]]
@@ -215,49 +199,65 @@ def rank_program(g, core, T, topo):
     def R(name, lo=0, hi=None, step=1):
         return (name, lo, SIZE[name][0] if hi is None else hi, step)
 
+    def R3(name, w0, w1, lo, hi):
+        k = SCRATCH[name][1][2]
+        if w1 is None:
+            return (name, k * w0 + lo, k * w0 + hi, 1, (slice(None), w0, slice(lo, hi)), hi - lo)
+        return (name, k * w0 + lo, k * (w1 - 1) + hi, 1, (slice(None), slice(w0, w1), slice(lo, hi)), (w1 - w0) * (hi - lo))
+
     def num(r):
-        return -(-(r[2] - r[1]) // r[3])
+        return r[5] if len(r) > 4 else -(-(r[2] - r[1]) // r[3])
 
     def two(r):
-        return r[0][:2] != "ps" and SIZE[r[0]][1] in ("bfloat16", "uint16")
+        return r[0][:2] != "ps" and SIZE[r[0]][1] in ("bfloat16", "uint16", "float16")
+
+    def dv(o, *i):
+        return 0.07 + num(o) * CY * (0.5 if two(o) and all(two(x) for x in i) else 1)
+
+    def da(o):
+        return 0.2 + num(o) * CY
+
+    val = lambda s: A(s) if isinstance(s, tuple) else s
 
     def copy(o, i, e="v"):
-        dv, da = 0.07 + num(o) * CY * (0.5 if two(o) and two(i) else 1), 0.2 + num(o) * CY
-        return add(e, {"v": dv, "a": da}, [o], [i], lambda e: g.vector.tensor_copy(A(o), A(i)) if e == "v" else
+        return add(e, {"v": dv(o, i), "a": da(o)}, [o], [i], lambda e: g.vector.tensor_copy(A(o), A(i)) if e == "v" else
                    g.scalar.activation(A(o), A(i), AF.Copy))
 
-    def scaled(o, i, k):
-        return add("va", {"v": 0.07 + num(o) * CY, "a": 0.2 + num(o) * CY}, [o], [i],
-                   lambda e: g.vector.tensor_scalar(A(o), A(i), k, None, OP.mult) if e == "v" else
-                   g.scalar.activation(A(o), A(i), AF.Copy, scale=k))
+    def tsf(o, i, s1, op0, s2, op1):
+        if op1 is None:
+            return g.vector.tensor_scalar(o, i, val(s1), None, op0)
+        return g.vector.tensor_scalar(o, i, val(s1), val(s2), op0, op1)
 
     def ts(o, i, s1, op0, s2=None, op1=None):
-        rd = [i] + [s for s in (s1, s2) if isinstance(s, tuple)]
-        f = lambda s: A(s) if isinstance(s, tuple) else s
+        return add("v", dv(o, i), [o], [i] + [s for s in (s1, s2) if isinstance(s, tuple)], lambda: tsf(A(o), A(i), s1, op0, s2, op1))
 
-        def fn():
-            if op1 is None:
-                return g.vector.tensor_scalar(A(o), A(i), f(s1), None, op0)
-            return g.vector.tensor_scalar(A(o), A(i), f(s1), f(s2), op0, op1)
-        return add("v", 0.07 + num(o) * CY * (0.5 if two(o) and two(i) else 1), [o], rd, fn)
+    def lin(o, i, k, c, e="va"):
+        return add(e, {"v": dv(o, i), "a": da(o)}, [o], [i], lambda e: g.vector.tensor_scalar(A(o), A(i), k, c, OP.mult, OP.add)
+                   if e == "v" else g.scalar.activation(A(o), A(i), AF.Identity, bias=c, scale=k))
 
     def tt(o, i, j, op):
         k = 1 if "ps" in (i[0][:2], j[0][:2]) else 2
         return add("v", 0.07 + k * num(o) * CY, [o], [i, j], lambda: g.vector.tensor_tensor(A(o), A(i), A(j), op))
 
-    def act(o, i, func, bias=None, scale=1.0):
-        if bias is None:
-            return add("a", 0.2 + num(o) * CY, [o], [i], lambda: g.scalar.activation(A(o), A(i), func, scale=scale))
-        return add("a", 0.2 + num(o) * CY, [o], [i, bias], lambda: g.scalar.activation(A(o), A(i), func, bias=A(bias), scale=scale))
+    def act(o, i, func, bias=0.0, scale=1.0):
+        return add("a", da(o), [o], [i] + ([bias] if isinstance(bias, tuple) else []),
+                   lambda: g.scalar.activation(A(o), A(i), func, bias=val(bias), scale=scale))
 
     def mset(o, c):
-        return add("v", 0.07 + num(o) * CY, [o], [], lambda: g.vector.memset(A(o), c))
+        return add("v", dv(o), [o], [], lambda: g.vector.memset(A(o), c))
+
+    def scans(lst, init, op0, op1):
+        return add("v", sum(dv(*x) for x in lst), [x[0] for x in lst], [y for x in lst for y in x[1:]],
+                   lambda: [g.vector.tensor_tensor_scan(A(o), A(i), A(j), init, op0, op1) for o, i, j in lst], inc=len(lst))
 
     def gather(e, o, win, off):
         f = lambda: A(win).indirect(A(off))
-        d = 0.07 + num(o) * CY * 1.5
-        return add(e, {"v": d, "a": d + 0.1}, [o], [win, off], lambda e: g.vector.tensor_copy(A(o), f()) if e == "v" else
+        d = 0.06 + num(o) * CY * 1.5
+        return add(e, {"v": d, "a": d + 0.03}, [o], [win, off], lambda e: g.vector.tensor_copy(A(o), f()) if e == "v" else
                    g.scalar.activation(A(o), f(), AF.Copy))
+
+    def gts(o, win, off, s1, op0, s2=None, op1=None):
+        return add("v", 0.06 + num(o) * CY * 1.5, [o], [win, off], lambda: tsf(A(o), A(win).indirect(A(off)), s1, op0, s2, op1))
 
     def mms(lst):
         w, r, d = [], [], 0.05
@@ -267,7 +267,7 @@ def rank_program(g, core, T, topo):
             for y in (l, x):
                 if y not in r:
                     r.append(y)
-            d += max(64, num(x)) * 0.00071 * (4 if not two(x) else 1)
+            d += max(64, num(x)) * PE * (4 if not two(x) else 1)
 
         def fn():
             z = None
@@ -276,13 +276,13 @@ def rank_program(g, core, T, topo):
             return z
         return add("p", d, w, r, fn)
 
-    def acc(o, pairs):
+    def acc(o, pairs, first=True, last=True):
         n = len(pairs)
-        return mms([(o, l, x, i == 0, i == n - 1) for i, (l, x) in enumerate(pairs)])
+        return mms([(x[2] if len(x) > 2 else o, x[0], x[1], first and i == 0, last and i == n - 1) for i, x in enumerate(pairs)])
 
     phys, nbank = {}, [0]
 
-    def bank(kind, n):
+    def bank(n):
         nbank[0] += 1
         return ("ps@%d" % nbank[0], 0, n, 1)
 
@@ -296,284 +296,259 @@ def rank_program(g, core, T, topo):
         return add("g", 0.15 + num(o) * 2 * CY, [o], [], (lambda: g.iota(A(o), pattern, base, cm)) if ints else
                    (lambda: g.iota(A(o), pattern, base, cm, allow_small_or_imprecise_dtypes=True)))
 
-    dma("s", [R("XT0", 0, W)], [], T.XT0[:, 0:W], T.xv[:, :], 6.0)
-    dma("a", [R("wli")], [], T.wli[:, :], T.wl[:, :], 2.5)
-    dma("s", [R("wni")], [], T.wni[0:8, :], T.wn[:, :])
+    dma("s", [R("XT", 0, W)], [], T.XT[:, 0:W], T.xv[:, :], 6.0)
+    dma("a", [R("wni")], [], T.wni[0:8, :], T.wn[:, :])
     dma("a", [R("thi")], [], T.thi[0:8, :], T.th[:, :])
+    dma("a", [R("wli")], [], T.wli[:, :], T.wl[:, :], 2.5)
     dma("s", [R("wti")], [], T.wti[:, :], T.wt[:, :])
-    for x in range(1, RO):
-        dma("s", [R("XT%d" % x, 0, W)], [R("XT0", 0, W)], T["XT%d" % x][:, 0:W], T.XT0[:, 0:W], 6.0)
     col = lambda i: R("cols", i, i + 1)
-    PC, LA, GP, G15, K0, L1P, KA, KB, TH, WC, NLA, L0, L1, L2, DWC, RC = [col(i) for i in range(16)]
-    iota(R("pint"), [[0, 1]], 0, 1, True); iota(R("XR"), [[1, 144]], 0, 0); iota(R("GR"), [[1, 8], [0, 16]], 0, 0)
-    iota(R("WI"), [[16, 8]], 0, 0); iota(R("YI"), [[1, 52]], -17, 0); iota(R("IO"), [[32, NB]], 0, 0)
-    iota(R("DG", 0, W), [[0, 256], [1, 16]], 0, 0); iota(R("HT"), [[1, 256], [0, 16]], 0, 0)
-    copy(PC, R("pint")); ts(R("lani"), R("pint"), 15, OP.bitwise_and); ts(R("grpi"), R("pint"), 4, OP.arith_shift_right)
-    copy(LA, R("lani")); copy(GP, R("grpi")); ts(G15, GP, 16.0, OP.mult, 15.0, OP.add)
+    ci = lambda i: R("ci", i, i + 1)
+    PC, LA, LB, GP, G15, THR, TH, TN, WC, RC, PB, QA = [col(i) for i in range(12)]
+    PI, PJ = R("PI", 0, 1), R("PI", 1, 2)
+    iota(R("PI"), [[112, 2]], 0, 1, True); iota(R("GR"), [[1, 8], [0, 16]], 0, 0); iota(R("XR"), [[1, 144]], 0, 0)
+    copy(PC, PI); ts(ci(0), PI, 15, OP.bitwise_and); ts(ci(1), PI, 4, OP.arith_shift_right)
+    copy(LA, ci(0)); copy(GP, ci(1)); ts(G15, GP, 16.0, OP.mult, 15.0, OP.add); ts(LB, LA, 16.0, OP.add)
     add("v", 0.2, [R("E8")], [R("GR"), PC], lambda: g.vector.tensor_scalar(A(R("E8"), 8), A(R("GR"), 8), A(PC, 8), None, OP.is_equal))
     add("v", 0.2, [R("wnf", 0, NW)], [R("wni")], lambda: g.vector.tensor_copy(A(R("wnf", 0, NW), 8), A(R("wni"), 8)))
     add("v", 0.1, [R("wnf", NW, NW + 1)], [R("thi")], lambda: g.vector.tensor_copy(A(R("wnf", NW, NW + 1), 8), A(R("thi"), 8)))
-    bn = bank("n", NW + 1); b0 = bn
-    add("p", 0.4, [b0], [R("E8"), R("wnf")], lambda: g.tensor.matmul(A(bn), A(R("E8"), 8), A(R("wnf"), 8), True, True))
-    copy(R("nr0"), b0)
-    ts(TH, R("nr0", NW, NW + 1), 0.5, OP.add, 200.0, OP.mult)
-    THR = R("nr0", NW, NW + 1)
-    for h in (0, 1):
-        k = col(20 + h)
-        ts(k, LA, float(16 * h), OP.add)
-        ts(R("NLi", h, 2 * NW, 2), R("nr0", 0, NW), k, OP.is_le, float(DEAD), OP.mult)
+    bn = bank(NW + 1)
+    add("p", 0.4, [bn], [R("E8"), R("wnf")], lambda: g.tensor.matmul(A(bn), A(R("E8"), 8), A(R("wnf"), 8), True, True))
+    for h, k in ((0, LA), (1, LB)):
+        ts(R("NLi", h, 2 * NW, 2), R(bn[0], 0, NW), k, OP.is_le, float(DEAD), OP.mult)
+    ts(THR, R(bn[0], NW, NW + 1), 0.5, OP.mult)
+    ts(TH, THR, 0.25, OP.add, 400.0, OP.mult); ts(TN, TH, -1.0, OP.mult)
     tt(R("NLf"), R("NLi"), R("wli"), OP.max)
-    copy(R("NL"), R("NLf"))
-    for x in range(RO):
-        mset(R("XT%d" % x, W, W + 16), 255.0)
-    ts(R("ID"), R("XR", 0, 128), PC, OP.is_equal); ts(R("NEG"), R("XR", 0, 128), PC, OP.is_equal, -1.0, OP.mult)
-    ts(R("BLK"), R("GR"), GP, OP.is_equal); ts(R("BL16"), R("GR"), GP, OP.is_equal, 0.0625, OP.mult)
-    ts(R("BIG"), R("XR", 0, 128), PC, OP.is_equal, 1024.0, OP.mult); mset(R("ONE"), 1.0)
+    ts(R("IN"), R("NLf"), float(-HALF), OP.add)
+    add("v", 8 * 0.085, [R("OT")], [R("IN")],
+        lambda: [g.vector.transpose(A(R3("OT", w, None, 0, P)), A(R("IN", P * w, P * w + P))) for w in range(8)], inc=8)
+    ts(ci(2), PI, 31, OP.bitwise_and, 1, OP.arith_shift_right); ts(ci(3), PI, 96, OP.bitwise_and); ts(ci(4), PI, 1, OP.bitwise_and)
+    tt(col(12), ci(2), ci(3), OP.add); ts(col(13), col(12), 16.0, OP.add); copy(col(15), ci(4)); ts(col(14), col(15), -1.0, OP.mult, 1.0, OP.add)
+    for x in range(4):
+        ts(R("PM%d" % x), R("XR", 0, 128), col(12 + x // 2), OP.is_equal, col(14 + x % 2), OP.mult)
+    mms([(R3("psz", 0, 8, 16 * y, 16 * y + 16), R("PM%d" % (2 * x + y)), R3("OT", 0, 8, 16 * x, 16 * x + 16), x == 0, x == 1)
+         for y in (0, 1) for x in (0, 1)])
     for b in range(NBK):
-        mset(R("V%d" % b, 0, 16), 0.0); mset(R("B%d" % b, ROWS, ROWS + 16), 0.0)
-    dma("s", [R("DG", 0, W)], [R("HT"), R("DG", 0, W)], T.DG[1::16, 0:W], T.HT[1::16, :], 3.0)
-    for x, v in ((L0, 0.0), (L1, 1.0)):
-        ts(x, LA, v, OP.is_equal)
-    mset(R("DG", W, W + 16), 0.0)
-    ts(R("E1"), R("XR"), G15, OP.is_equal); ts(col(24), G15, 8.0, OP.add); ts(R("E2"), R("XR"), col(24), OP.is_equal)
-    tt(R("E3"), R("E1"), R("E2"), OP.add)
-    for i in range(4):
-        ts(R("SE%d" % i), R("E3"), 3.0 * 2 ** i, OP.mult)
-    for c in range(8):
-        o = R("GT", 128 * c, 128 * c + 128)
-        add("g", 0.4, [o], [R("BL16")], lambda o=o, c=c: g.affine_select(A(o), A(R("BL16")), [[0, 16], [1, 8]], OP.is_gt, 0.0, -c, 0))
-    for c in range(8):
-        b0 = bank("n", 512); l = []
-        for i in range(4):
-            o = R(b0[0], 128 * i, 128 * i + 128)
-            l += [(o, R("ID"), R("GT", 128 * c, 128 * c + 128), True, False), (o, R("ID"), R("SE%d" % i, 15 - c, 143 - c), False, True)]
-        mms(l)
-        copy(R("QW", 512 * c, 512 * c + 512), b0, "va")
-    ts(K0, LA, 8.0, OP.is_ge, 736.0, OP.mult)
-    ts(col(22), LA, 4.0, OP.mult, 737.0, OP.add); tt(KA, col(22), K0, OP.add); ts(KB, KA, 16.0, OP.add)
+        z = R3("psz", NX * b, NX * b + NX, 0, P)
+        ts(R("nm", L * b, L * b + L), z, float(HALF), OP.add); copy(R("NF", L * b, L * b + L), z)
+    mset(R("XT", W, W + 16), 255.0)
+    eye = lambda n, k: ts(R(n), R("XR", 0, 128), PC, OP.is_equal, float(k), OP.mult)
+    for n, k in (("ID", 1), ("NEG", -1), ("N8", -8192), ("N15", -1584), ("JM", REG - 15), ("W0", 1 - LS), ("W1", -LS),
+                 ("W2", -2 * LS), ("W3", 4 * LS), ("I16", 1)):
+        eye(n, k)
+    copy(WC, R("wti"))
+    ts(R("EW"), R("XR"), G15, OP.is_equal); ts(R("WW"), R("XR"), G15, OP.is_equal, WC, OP.mult)
+    for n, k in (("ONE", 1.0), ("K0", 0.0), ("PAT", 1.0), ("TWO", 2.0), ("MQ", -0.25), ("CK", 167.0 / 32), ("VP", 0.0), ("M16", -16.0)):
+        mset(R(n), k)
+    mset(R("K0", 0, L, P), 16384.0); mset(R("PAT", 0, L, P), 0.0); mset(R("VP", 7, 8 * NX, 8), 8.0 * LS)
+    for b in range(NBK):
+        mset(R("V%d" % b, 0, 16), 0.0); mset(R("S%d" % b, 0, 16), 0.0)
+    k = (RO - 1) * NBK * 2 * NX
+    mset(R3("SN", 0, k, P, CELL), DEAD); mset(R3("SN", k, k + NBK * 2 * NX, P, CELL), 0)
+    mset(R("AC", 0, 1), -0.375)
+    iota(R("SEL"), [[1, 16], [16, 8], [0, 16]], 0, 0); ts(R("SEL"), R("SEL"), PC, OP.is_equal)
+    iota(R("RA"), [[16, L]], 0, 0); ts(R("RAMP"), R("RA"), LA, OP.add)
+    iota(R("B34"), [[CELL, NX], [0, 16]], 0, 0); iota(R("YI"), [[1, 56]], 0, 0); iota(R("W5"), [[512, 8]], 0, 0)
+    ts(col(16), LA, 32.0, OP.mult); ts(R("W32"), R("W5"), col(16), OP.add)
+    ts(ci(5), PI, 16.0, OP.add); ts(ci(6), ci(5), 127, OP.bitwise_and); copy(RC, ci(6))
+    ts(R("LM"), R("XR", 0, 16), LA, OP.is_equal)
+    for x in range(16):
+        ts(R("DR", 128 * x, 128 * x + 128), R("XR", 0, 128), RC, OP.is_equal, R("LM", x, x + 1), OP.mult)
     ts(R("VY"), R("YI"), LA, OP.is_le)
     for part in range(2):
-        b0 = bank("n", 384); l = []
+        b0 = bank(8 * LS); l = []
         for j in range(8):
-            nib = 8 * part + j; c = 0
+            c = 0
             for p in range(4):
-                c += nib >> p & 1
-                l.append((R(b0[0], 48 * j, 48 * j + 48), R("ID"), R("VY", c, c + 48), p == 0, p == 3))
+                c += (j >> (p - 1) & 1) if p else 0
+                l.append((R(b0[0], LS * j, LS * j + LS), R("JM" if part and p == 3 else "ID"), R("VY", c, c + LS), p == 0, p == 3))
         mms(l)
-        copy(R("LUT", 16 + 384 * part, 400 + 384 * part), b0, "va")
-    mset(R("LUT", 0, 16), 0.0)
-    for part in range(2):
-        b0 = bank("n", 384); x = 16 + 384 * part
-        acc(b0, [(R("ID"), R("LUT", x - 1, x + 383)), (R("NEG"), R("LUT", x, x + 384))])
-        copy(R("LUT", 768 + x, 1152 + x), b0, "va")
-    mset(R("OB"), 1.0 / 128); mset(R("OF"), 1.0); copy(R("L0B", 0, 1), L0); ts(NLA, LA, -1.0, OP.mult)
-    copy(WC, R("wti")); ts(R("EW"), R("XR"), G15, OP.is_equal); ts(R("WW"), R("XR"), G15, OP.is_equal, WC, OP.mult)
-    ts(col(25), L1, 16.0, OP.mult); tt(DWC, L0, col(25), OP.add)
-    ts(R("DW"), R("XR"), G15, OP.is_equal, DWC, OP.mult); ts(R("L0W"), R("XR"), G15, OP.is_equal, L0, OP.mult)
-    ts(R("roti"), R("pint"), 16.0, OP.add); ts(R("rotj"), R("roti"), 127, OP.bitwise_and); copy(RC, R("rotj"))
-    ts(R("ROT"), R("XR", 0, 128), RC, OP.is_equal); ts(R("ROT4"), R("XR", 0, 128), RC, OP.is_equal, float(DEAD), OP.mult)
-    ts(R("IDF"), R("XR", 0, 128), PC, OP.is_equal); ts(R("IDF4"), R("XR", 0, 128), PC, OP.is_equal, float(DEAD), OP.mult); ts(R("BLK2"), R("GR"), GP, OP.is_equal, 2.0, OP.mult)
-    ts(R("WI1"), R("WI"), LA, OP.add, 31.0, OP.mult); ts(R("WI2"), R("WI"), LA, OP.add, float(W + 16), OP.add)
-    ts(R("wf"), R("WI1"), float(-W - 16), OP.add); copy(R("WI1"), R("wf"))
-    mset(R("AC", 0, 1), -0.375)
+        copy(R("LUT", 8 * LS * part, 8 * LS * (part + 1)), b0, "va")
     nloc = [0]
     win = lambda name, r: R(name, 15 - r, 143 - r)
-    chunks = ROWS // CH
 
-    def transmit(kind, t, b):
-        d = [x[3] for x in messages(rank, nr) if x[:3] == (kind, t, b)][0]
-        sb, lb, sem = names_of(kind, t, b)
-        dst = T.cores[d]; via = relay_of(topo, core, dst, kind)
-        to = dst if via is None else via
-        nloc[0] += emask(topo, core, to)[1]
-        s = add("g", 1.0, [], [R(sb)], lambda: send(g, T, topo, core, to, sb, lb, sem), sem="loc", inc=0)
-        n = [x for q in range(nr) for x in messages(q, nr) if x == (kind, t, b, rank)]
-        src = [q for q in range(nr) if (kind, t, b, rank) in messages(q, nr)][0]
-        v2 = relay_of(topo, T.cores[src], T.cores[rank], kind)
-        k = emask(topo, T.cores[src] if v2 is None else v2, core)[1]
-        add(None, 0.0, [R(lb)], [], None, sem=sem, inc=k, after=[s], lat=HOP1 if via is None else HOP2)
+    def transmit(k, t, b, srcs):
+        todo = []
+        for h in (0, 1):
+            d = target(rank, nr, t, h)
+            if d != rank:
+                via = relay_of(topo, core, T.cores[d], b)
+                todo.append((h, T.cores[d] if via is None else via, via))
+                nloc[0] += len(engines(topo, core, todo[-1][1]))
+        s = add("g", 1.0, [], [srcs[h] for h, _, _ in todo], lambda: g.remote_dma_fused(
+            [transfer(T, topo, core, to, A(srcs[h]), landing(T, k, t, b, h), "m%d%d%d%d" % (k, t, b, h)) for h, to, _ in todo],
+            local_sem=T.sem["loc"]), sem="loc", inc=0)
+        for h, to, via in todo:
+            src = [q for q in range(nr) if target(q, nr, t, h) == rank][0]
+            v2 = relay_of(topo, T.cores[src], core, b)
+            o = R("cr%d%d%d" % (h, t, b)) if k == 0 else R("WN%d%d%d" % (k - 1, t, b), REG * h, REG * h + REG)
+            add(None, 0.0, [o], [], None, sem="m%d%d%d%d" % (k, t, b, h), inc=len(engines(topo, T.cores[src] if v2 is None else v2, core)),
+                after=[s], lat=HOP1 if via is None else HOP2)
 
-    def merge(b, own, over):
-        tt(R("mg%d" % b), own, over, OP.min)
-        ts(R("pv%d" % b), R("mg%d" % b, 0, NB), float(DEAD), OP.is_lt)
-        b0 = bank("n", 2 * NB)
-        mms([(R(b0[0], 0, NB), R("BLK2"), R("pv%d" % b), True, True), (R(b0[0], NB, 2 * NB), R("BLK2"), R("pv%d" % b), True, False),
-             (R(b0[0], NB, 2 * NB), R("OB"), R("IO"), False, True)])
-        copy(R("n%d" % b), R(b0[0], 0, NB), "va")
-        copy(R("nI%d" % b), R(b0[0], NB, 2 * NB), "va")
+    def send_names(e, t, b, x):
+        k = ((t * NBK + b) * 2 + e) * NX
+        ts(R3("SN", k, k + NX, 0, P), x, W - 1, OP.bitwise_and)
+        src = R3("SN", k, k + NX, 0, CELL)
+        transmit(1 + e, t, b, [src, src])
+        if t == RO - 1:
+            n = "WN%d%d%d" % (e, t, b)
+            dma("s", [R(n, 0, REG)], [src], T[n][:, 0:REG], A(src))
+
+    def join(t, b):
+        s = str(b)
+        own = ("cr0%d%d" if t < RO - 1 else "cs%d%d") % (t, b)
+        over = "cr1%d%d" % (t, b)
+        f = bank(8 * NX)
+        acc(f, [(R("W%d" % i), R(own, i, L, 4)) for i in range(4)] + [(R("ID"), R("VP"))])
+        copy(R3("IX" + s, 0, NX, 8, 16), f)
+        f = bank(8 * NX)
+        acc(f, [(R("W%d" % i), R(over, i, L, 4)) for i in range(4)] +
+            [(R("ID"), R(own, P - 1, L, P), R(f[0], c, 8 * NX, 8)) for c in range(4, 8)] + [(R("ID"), R("M16"))])
+        copy(R3("IX" + s, 0, NX, 0, 8), f)
+        for w in range(NX):
+            gather("va", R3("G" + s, w, None, 0, 192), R("LUT"), R3("IX" + s, w, None, 4, 16))
+        f = bank(NB)
+        acc(f, [(R("ID"), R3("G" + s, 0, NX, 16 * c, 16 * c + 16)) for c in range(12)] + [(R("ID"), R("B34"))])
+        copy(R("of" + s), f)
+        f = bank(L)
+        for e in (0, 1):
+            n = "N%d%s" % (e, s)
+            for w in range(NX):
+                gts(R3(n, w, None, 0, 256), R("WN%d%d%d" % (e, t, b)), R("of" + s, 16 * w, 16 * w + 16), float(-HALF), OP.add)
+            acc(R(f[0], e, L, 2), [(R("DR", 128 * x, 128 * x + 128), R3(n, 0, NX, 16 * x, 16 * x + 16)) for x in range(16)])
+        return f
+
+    def step(o, i, k, more):
+        return add("va", {"v": dv(o, i), "a": da(o)}, [o], [i, TH, TN, THR],
+                   lambda e: g.vector.tensor_scalar(A(o), A(i), k, A(THR), OP.mult, OP.is_gt if more else OP.is_le) if e == "v" else
+                   g.scalar.activation(A(o), A(i), AF.Sigmoid, bias=A(TN if more else TH), scale=(400.0 if more else -400.0) * k))
 
     for t in range(RO):
-        XT = "XT%d" % t
         for b in range(NBK):
             s = str(b)
+            r = lambda n, lo=0, hi=None, step=1: R(n + s, lo, hi, step)
             cur["plus"] = FIRST if b == 0 else 0.0
-            V, B, D, C, Z = "V" + s, "B" + s, "D" + s, "C" + s, "Z" + s
-            if t == 0:
-                for q in range(chunks):
-                    n = 2 * NB // chunks
-                    off = R("NL", 2 * NB * b + n * q, 2 * NB * b + n * q + n)
-                    gather("va", R(V, 16 + CH * q, 16 + CH * q + CH), R(XT, 0, W + 16), off)
-                    gather("va", R(B, CH * q, CH * q + CH), R("DG"), off)
-                copy(R("n" + s), R("nr0", NB * b, NB * b + NB), "va")
-                tt(R("nI" + s), R("nr0", NB * b, NB * b + NB), R("IO"), OP.add)
+            nm, nf = R("nm", L * b, L * b + L), R("NF", L * b, L * b + L)
+            if t:
+                f = join(t - 1, b)
+                ts(nm, f, float(HALF), OP.add); copy(nf, f)
+            for w in range(NX):
+                gather("va", r("V", 16 + CH * w, 16 + CH * w + CH), R("XT", 0, W + 16), R("nm", L * b + P * w, L * b + P * w + P))
+            D = bank(L)
+            if DIFF[b]:
+                for x in range(0, ROWS, CH):
+                    f = bank(CH)
+                    acc(f, [(R("ID"), r("V", 16 + x, 16 + x + CH)), (R("NEG"), r("V", x, x + CH))])
+                    act(r("M", x, x + CH), f, AF.Abs)
+                acc(D, [(win("EW", x), r("M", x, ROWS, 16)) for x in range(16)] + [(R("ID"), R("K0"))])
             else:
-                merge(b, R("rcv%d%d0" % (t - 1, b)), R("rcv%d%d1" % (t - 1, b)))
-                ts(R("nm" + s), R("mg" + s), float(DEAD), OP.min)
-                n = NB // GP2
-                for q in range(GP2):
-                    for e in (0, 1):
-                        off = R("nm" + s, NB * e + n * q, NB * e + n * q + n)
-                        gather("va", R(V, 16 + P * n * q + e, 16 + P * n * (q + 1), 2), R(XT, 0, W + 16), off)
-                for e in (0, 1):
-                    gather("va", R(B, e, ROWS, 2), R("DG"), R("nm" + s, NB * e, NB * e + NB))
-            ts(R("K3" + s), R("n" + s), float(P), OP.is_ge, float(P - 1), OP.add)
-            for q in range(chunks):
-                x = CH * q
-                f = bank("f", CH)
-                mms([(f, R("ID"), R(V, 16 + x, 16 + x + CH), True, False), (R(f[0], 0, CH, P), R("BIG"), R("ONE"), False, False),
-                     (f, R("NEG"), R(V, 15 + x, 15 + x + CH), False, True)])
-                act(R(D, x, x + CH), f, AF.Abs)
-                f = bank("s", CH)
-                acc(f, [(R("BLK"), R(D, x, x + CH))])
-                o = R(C, x, x + CH)
-                add("va", {"v": 0.07 + CH * CY, "a": 0.2 + CH * CY}, [o], [f, TH, THR],
-                    lambda e, o=o, f=f: g.vector.tensor_scalar(A(o), A(f), A(THR), None, OP.is_le) if e == "v" else
-                    g.scalar.activation(A(o), A(f), AF.Sigmoid, bias=A(TH), scale=-200.0))
-                add("v", 0.07 + CH * CY / 2, [R(Z, x, x + CH)], [R(C, x, x + CH), R(V, 16 + x, 16 + x + CH)],
-                    lambda x=x, C=C, V=V, Z=Z: g.vector.tensor_tensor_scan(A(R(Z, x, x + CH)), A(R(C, x, x + CH)), A(R(V, 16 + x, 16 + x + CH)),
-                                                                           0.0, OP.mult, OP.max))
-            f = bank("n", NB)
-            acc(f, [(R("BL16"), R(C, k, ROWS, P)) for k in range(1, P)])
-            mA = R("mA", NB * b, NB * b + NB)
-            tt(mA, R("K3" + s), f, OP.subtract)
-            ts(R("mos%d%d" % (t, b)), mA, 16.0, OP.min)
-            transmit("mo", t, b)
-            f = bank("n", NB)
-            acc(f, [(R("QW", 128 * k, 128 * k + 128), R(C, k, ROWS, P)) for k in range(1, P)])
-            ts(R("IB" + s), f, -1.0, OP.mult, KA, OP.add)
-            ts(R("ix%d0" % b), f, -1.0, OP.mult, KB, OP.add)
+                f = bank(L)
+                acc(f, [(win("EW", x), r("V", 16 + x, 16 + ROWS, 16)) for x in range(16)])
+                lin(r("S", 16, 16 + L), f, 0.5, 0.0)
+                for y in range(0, 16, 4):
+                    scans([(r("M", L * x, L * x + L), r("V", x, ROWS, 16), r("V", 16 + x, 16 + ROWS, 16)) for x in range(y, y + 4)], 256.0, OP.min, OP.max)
+                    acc(D, [(win("EW", x), r("M", L * x, L * x + L)) for x in range(y, y + 4)], y == 0, False)
+                acc(D, [(R("NEG"), r("S", 16, 16 + L)), (R("NEG"), r("S", 15, 15 + L)), (R("ID"), R("K0"))], False)
+            half = 0.5 if DIFF[b] else 1.0
+            step(r("C"), D, half, False)
+            step(r("E", 0, L - 1), R(D[0], 1, L), half, True)
+            ts(r("E", P - 1, L, P), R("nm", L * b + P - 1, L * b + L, P), float(DEAD), OP.is_lt)
+            per = CH // L
+            for y in range(0, 16, per):
+                f = bank(CH)
+                mms([(R(f[0], L * (x - y), L * (x - y + 1)), R("SEL", 128 * x, 128 * x + 128), r("C"), True, True) for x in range(y, y + per)])
+                scans([(r("Z", x, ROWS, 16), R(f[0], L * (x - y), L * (x - y + 1)), r("V", 16 + x, 16 + ROWS, 16)) for x in range(y, y + per)],
+                      0.0, OP.mult, OP.max)
+            cs, ct = R("cs%d%d" % (t, b)), R("ct%d%d" % (t, b))
+            scans([(cs, R("PAT"), r("E"))], 0.0, OP.mult, OP.add)
+            ts(ct, cs, 16.0, OP.max)
+            transmit(0, t, b, [cs, ct])
+            scans([(r("cm"), r("C"), R("TWO"))], 0.0, OP.mult, OP.add)
+            lin(r("c2"), r("cm"), 1.0, 1.0)
+            f = bank(L)
+            acc(f, [(R("I16"), nf), (R("N8"), r("C")), (R("N8"), R("MQ", 0, L))])
+            scans([(r("a"), r("C"), f)], 0.0, OP.mult, OP.max)
+            tt(r("na"), r("a"), r("c2"), OP.mult)
+            ts(r("ni"), r("na"), 0.25, OP.mult, R("AC", t, t + 1), OP.add)
+            send_names(0, t, b, r("ni"))
+            f = bank(L)
+            acc(f, [(R("I16"), R("RAMP")), (R("N8"), r("E"))])
+            scans([(r("y"), R("K0"), f)], 0.0, OP.add, OP.min)
+            ts(r("zo"), r("y", P - 1, L, P), 8192.0, OP.add, float(ROWS - 1), OP.min)
+            ts(R("iv", NX * b, NX * b + NX), r("y", P - 1, L, P), 0.0, OP.is_ge, float(W + 16), OP.mult)
+            gts(R("ZF", NB * b, NB * b + NB), r("Z"), r("zo"), -192.0, OP.add)
+            f = bank(L)
+            acc(f, [(win("WW", x), r("Z", x, ROWS, 16)) for x in range(16)] + ([(R("N8"), R("MQ", 0, L))] if USC else []))
+            if USC:
+                act(r("q"), f, AF.Identity, MAGIC, (1.0 + 2.0 ** -17) / W)
+                act(r("r"), r("q"), AF.Identity, MAGIC * W, float(-W))
+                tt(r("v"), f, r("r"), OP.add)
+                act(r("sq"), r("v"), AF.Square, 592.0 + HALF)
+            else:
+                copy(r("ui"), f)
+                ts(r("um"), r("ui"), W - 1, OP.bitwise_and)
+                ts(r("v"), r("um"), 592.0, OP.add)
+                tt(r("sq"), r("v"), r("v"), OP.mult)
+            f = bank(L)
+            acc(f, [(R("N8"), r("cm")), (R("N15"), r("cm")), (R("N8"), R("CK"))])
+            tt(r("si"), r("sq"), f, OP.subtract)
+            ts(r("hm"), r("si"), 5, OP.arith_shift_right, W - 1, OP.bitwise_and)
+            copy(r("hu"), r("hm"))
+            for w in range(NX):
+                o, off, z = r("D2", CH * w, CH * w + CH), r("hu", P * w, P * w + P), r("Z", CH * w, CH * w + CH)
+                add("v", 0.06 + CH * CY * 1.5, [o], [R("XT", 0, W), off, z],
+                    lambda o=o, off=off, z=z: g.vector.tensor_tensor(A(o), A(R("XT", 0, W)).indirect(A(off)), A(z), OP.subtract))
+                act(r("AD", CH * w, CH * w + CH), o, AF.Abs)
+            gts(R("e2", NB * b, NB * b + NB), r("D2"), r("zo"), 0.5, OP.mult, 191.75, OP.add)
+            f = bank(L)
+            acc(f, [(win("EW", x), r("AD", x, ROWS, 16)) for x in range(16)])
+            tt(r("nc"), f, r("c2"), OP.mult)
+            tt(r("nj"), r("nc"), r("hm"), OP.add)
+            send_names(1, t, b, r("nj"))
+        cur["plus"] = 0.0
         if t < RO - 1:
-            f = bank("n", 1)
-            acc(f, [(R("mA"), L0)])
-            copy(R("SC"), f, "va")
-            f = bank("n", 1)
-            acc(f, [(R("OF"), R("SC"))])
+            f = bank(1)
+            acc(f, [(R("ONE"), R("cs%d%d" % (t, b), x, x + 1)) for b in range(NBK) for x in range(P - 1, L, P)])
             copy(R("ATi"), f)
             ts(R("ATj"), R("ATi"), 255, OP.bitwise_and); ts(R("AC", t + 1, t + 2), R("ATj"), -0.375, OP.add)
-        for h in (0, 1):
-            for b in range(NBK):
-                cur["plus"] = FIRST if b == 0 else 0.0
-                s = str(b); u = "%d%d" % (b, h)
-                r = lambda n, lo=0, hi=None, step=1: R(n + u, lo, hi, step)
-                if h == 1:
-                    mr = R("mor%d%d" % (t, b))
-                    f = bank("n", NB)
-                    acc(f, [(R("IDF"), R("IB" + s)), (R("ID"), mr)])
-                    copy(r("ix"), f)
-                gather("va", r("G"), R("LUT"), r("ix"))
-                f = bank("n", 3 * NB)
-                fs, fe, fc = R(f[0], 0, NB), R(f[0], NB, 2 * NB), R(f[0], 2 * NB, 3 * NB)
-                bias = [(R("OB"), R("IO"))]
-                ps = [(R("ID"), r("G", c, None, 16)) for c in range(16)]
-                l = []
-                for o, x in ((fe, ps + bias), (fs, ps[:8] + bias), (fc, ps[8:])):
-                    l += [(o, y, z, i == 0, i == len(x) - 1) for i, (y, z) in enumerate(x)]
-                mms(l)
-                ts(r("zo"), fe, -1.0, OP.add)
-                bad = r("iv")
-                tt(bad, fs, R("nI" + s), OP.is_ge)
-                copy(r("ao"), fs)
-                scaled(r("c6"), fc, 611.0)
-                add("va", {"v": 0.07 + NB * CY, "a": 0.2 + NB * CY}, [r("c2")], [fc],
-                    lambda e, o=r("c2"), f=fc: g.vector.tensor_scalar(A(o), A(f), 2.0, 1.0, OP.mult, OP.add) if e == "v" else
-                    g.scalar.activation(A(o), A(f), AF.Copy, bias=1.0, scale=2.0))
-                if h == 1:
-                    act(r("iw"), mr, AF.Relu, NLA)
-                gather("va", r("Zc"), R("Z" + s), r("zo"))
-                gather("va", r("Ac"), R("B" + s), r("ao"))
-                f = bank("n", NB)
-                acc(f, [(win("WW", x), r("Zc", x, None, 16)) for x in range(16)])
-                copy(r("ui"), f)
-                scaled(r("t1"), f, 37.0)
-                ts(r("um"), r("ui"), W - 1, OP.bitwise_and)
-                tt(r("t2"), r("t1"), r("c6"), OP.add)
-                tt(r("sq"), r("um"), r("um"), OP.mult)
-                ts(r("qq"), r("sq"), 5, OP.arith_shift_right)
-                tt(r("hh"), r("qq"), r("t2"), OP.add)
-                ts(r("hm"), r("hh"), W - 1, OP.bitwise_and)
-                copy(r("hu"), r("hm"))
-                add("v", 0.07 + 16 * NB * CY * 1.5, [r("D2")], [R(XT, 0, W), r("hu"), r("Zc")],
-                    lambda u=u, XT=XT: g.vector.tensor_tensor(A(R("D2" + u)), A(R(XT, 0, W)).indirect(A(R("hu" + u))), A(R("Zc" + u)), OP.subtract))
-                act(r("AD"), r("D2"), AF.Abs)
-                f = bank("n", NB)
-                acc(f, [(win("DW", x), r("Ac", x, None, 16)) for x in range(16)])
-                tt(r("na"), f, r("c2"), OP.mult)
-                ts(r("NN", 0, NB), r("na"), 0.25, OP.mult, R("AC", t, t + 1), OP.add)
-                f = bank("n", NB)
-                acc(f, [(win("EW", x), r("AD", x, None, 16)) for x in range(16)])
-                tt(r("nc"), f, r("c2"), OP.mult)
-                tt(r("NN", NB, 2 * NB), r("nc"), r("hh"), OP.add)
-                ts(r("NM"), r("NN"), W - 1, OP.bitwise_and)
-                sd = R("snd%d%d%d" % (t, b, h))
-                copy(r("NF"), r("NM"))
-                f = bank("n", 2 * NB); l = []
-                x = ("ROT", "ROT4") if t < RO - 1 else ("IDF", "IDF4")
-                for e in (0, 1):
-                    o = R(f[0], NB * e, NB * e + NB)
-                    l += [(o, R(x[0]), r("NF", NB * e, NB * e + NB), True, False), (o, R(x[1]), bad, False, h == 0)]
-                    if h == 1:
-                        l.append((o, R(x[1]), r("iw"), False, True))
-                mms(l)
-                copy(sd, f, "va")
-                if t < RO - 1 or h == 1:
-                    transmit("over" if h else "own", t, b)
-                if h == 0:
-                    z0 = R("ZF", NB * b, NB * b + NB)
-                    copy(z0, r("Zc", 0, None, 16), "va")
-                    ts(R("e2" + s), r("D2", 0, None, 16), 0.5, OP.mult, -0.25, OP.add)
-                    tt(R("VAL", NB * b, NB * b + NB), z0, R("e2" + s), OP.add)
-        cur["plus"] = 0.0
-        f = bank("n", 16)
-        fu, fz = R(f[0], 0, 8), R(f[0], 8, 16)
-        mms([(fu, win("WW", x), R("ZF", x, None, 16), x == 0, x == 15) for x in range(16)] +
-            [(fz, win("L0W", x), R("ZF", x, None, 16), x == 0, x == 15) for x in range(16)])
-        copy(R("wa"), fu); ts(R("wc"), fz, 16.0, OP.is_lt)
-        ts(R("wb"), R("wa"), 31, OP.bitwise_and)
-        tt(R("wd"), R("wb"), R("WI1"), OP.add); tt(R("we"), R("wd"), R("wc"), OP.mult); tt(R("wf"), R("we"), R("WI2"), OP.add)
-        copy(R("WL"), R("wf"))
-        for x in range(t + 1, RO) if t < RO - 1 else (RO - 1,):
-            o = R("XT%d" % x)
-            add("v", 0.07 + NW * CY * 3, [o], [R("VAL"), R("WL")],
-                lambda o=o: g.vector.tensor_copy(A(o).indirect(A(R("WL"))), A(R("VAL"))))
+        f = bank(8)
+        acc(f, [(win("WW", x), R("ZF", x, NW, 16)) for x in range(16)])
+        copy(R("wa"), f); ts(R("wb"), R("wa"), 31, OP.bitwise_and)
+        tt(R("bs"), R("iv"), R("W32"), OP.add); tt(R("wf"), R("wb"), R("bs"), OP.add); copy(R("WL"), R("wf"))
+        add("v", 0.07 + NW * CY * 3.5, [R("XT")], [R("ZF"), R("e2"), R("WL")],
+            lambda: g.vector.tensor_tensor(A(R("XT")).indirect(A(R("WL"))), A(R("ZF")), A(R("e2")), OP.add))
     for q in range(4):
-        f = bank("f", 512)
-        acc(f, [(R("ID"), R("XT%d" % (RO - 1), 1024 * q + e, 1024 * q + 1024, 2)) for e in (0, 1)])
-        copy(R("YX", 512 * q, 512 * q + 512), f, "a")
-    outs = [dma("s", [("yx", 0, 1, 1)], [R("YX")], T.yx[:, :], T.YX[:, :])]
-    for h in (0, 1):
-        for e in (0, 1):
-            v, x, y, z = [col(28 + i) for i in range(4)]
-            ts(v, LA, 2.0, OP.mult, float(e - 16 * h), OP.add)
-            ts(x, v, 0.0, OP.is_ge); ts(y, v, 15.0, OP.is_le); tt(z, x, y, OP.mult)
-            ts(x, v, G15, OP.add, -14.0, OP.add); tt(y, x, z, OP.mult); ts(v, y, -1.0, OP.add)
-            ts(R("PM%d" % (2 * h + e)), R("XR", 0, 128), v, OP.is_equal)
-    ts(R("P8"), R("XR", 0, 8), GP, OP.is_equal, L0, OP.mult)
+        f = bank(512)
+        acc(f, [(R("ID"), R("XT", 1024 * q + e, 1024 * q + 1024, 2)) for e in (0, 1)])
+        copy(R("YX", 512 * q, 512 * q + 512), f, "va")
+    dma("s", [("yx", 0, 1, 1)], [R("YX")], T.yx[:, :], T.YX[:, :])
+    ts(ci(7), PJ, 96, OP.bitwise_and); ts(ci(8), PJ, 4, OP.arith_shift_right, 1, OP.bitwise_and)
+    ts(col(17), LA, 2.0, OP.mult); tt(col(18), col(17), ci(7), OP.add); ts(col(19), col(18), 1.0, OP.add)
+    copy(col(21), ci(8)); ts(col(20), col(21), -1.0, OP.mult, 1.0, OP.add)
+    for x in range(4):
+        ts(R("QM%d" % x), R("XR", 0, 128), col(18 + x % 2), OP.is_equal, col(20 + x // 2), OP.mult)
+    t = RO - 1
     for b in range(NBK):
         s = str(b)
-        merge(b, R("snd%d%d0" % (RO - 1, b)), R("rcv%d%d1" % (RO - 1, b)))
-        ts(R("yl1" + s), R("mg" + s), float(DEAD), OP.is_lt); tt(R("yl2" + s), R("yl1" + s), R("mg" + s), OP.mult)
-        f = bank("n", 2 * NB)
+        cur["plus"] = FIRST if b == 0 else 0.0
+        tt(R("n1", NX * b, NX * b + NX), R("cs%d%d" % (t, b), P - 1, L, P), R("cr1%d%d" % (t, b), P - 1, L, P), OP.add)
+        f = join(t, b)
+        copy(R3("NB" + s, 0, NX, 0, P), f)
         l = []
-        for h in (0, 1):
-            for e in (0, 1):
-                l.append((R(f[0], h, 2 * NB, 2), R("PM%d" % (2 * h + e)), R("yl2" + s, NB * e, NB * e + NB), e == 0, e == 1))
+        for x in (0, 1):
+            o = R3("psz", NX * b, NX * b + NX, 16 * x, 16 * x + 16)
+            l += [(o, R("QM%d" % (2 * x), 0, 128), R3("NB" + s, 0, NX, 0, 16), True, False), (o, R("N8"), R("MQ", 0, NB), False, False),
+                  (o, R("QM%d" % (2 * x + 1), 0, 128), R3("NB" + s, 0, NX, 16, P), False, True)]
         mms(l)
-        copy(R("yl3" + s), f)
-        outs.append(dma("s", [("yl", b, b + 1, 1)], [R("yl3" + s)], T.yl[:, 2 * NB * b:2 * NB * b + 2 * NB], T["yl3" + s][:, :]))
-        f = bank("n", NB)
-        add("p", 0.3, [f], [R("P8"), R("n" + s)], lambda f=f, s=s: g.tensor.matmul(A(f, 8), A(R("P8")), A(R("n" + s)), True, True))
-        add("v", 0.1, [R("yno" + s)], [f], lambda f=f, s=s: g.vector.tensor_copy(A(R("yno" + s), 8), A(f, 8)))
-        outs.append(dma("s", [("yn", b, b + 1, 1)], [R("yno" + s)], T.yn[:, NB * b:NB * b + NB], T["yno" + s][0:8, :]))
+        add("v", NX * 0.1, [R("yl" + s)], [R("psz")], lambda b=b, s=s: [
+            g.vector.transpose(A(R("yl" + s, P * w, P * w + P)), A(R3("psz", NX * b + w, None, 0, P))) for w in range(NX)], inc=NX)
+        dma("s" if b else "a", [("yl", b, b + 1, 1)], [R("yl" + s)], T.yl[:, L * b:L * b + L], T["yl" + s][:, :])
+    cur["plus"] = 0.0
+    ts(R("n2"), R("n1"), -16.0, OP.add, 16.0, OP.min); ts(R("n3"), R("n2"), 2.0, OP.mult)
+    f = bank(NW)
+    add("p", 0.8, [f], [R("SEL"), R("n3")], lambda f=f: [g.tensor.matmul(A(R(f[0], x, NW, 16), 8), A(R("SEL", 128 * x, 128 * x + 128, 16)),
+                                                                      A(R("n3")), True, True) for x in range(16)][-1])
+    add("v", 0.2, [R("yno")], [f], lambda f=f: g.vector.tensor_copy(A(R("yno"), 8), A(f, 8)))
+    dma("s", [("yn", 0, 1, 1)], [R("yno")], T.yn[:, :], T.yno[0:8, :])
 
     n = len(nodes)
     users = [[] for _ in range(n)]
@@ -585,15 +560,15 @@ def rank_program(g, core, T, topo):
         x = nodes[i]
         prio[i] = (min(x["d"].values()) if x["e"] == "va" else x["d"][x["e"]] if x["e"] else 0.0) + x["lat"] + LINK + max([prio[k] for k in users[i]] + [0.0])
     for i in range(n):
-        prio[i] += nodes[i]["plus"] + NOISE * ((i * SEED) % 997) / 997.0
+        prio[i] += nodes[i]["plus"]
     left = [len(x["deps"]) for x in nodes]
     ready_at = [0.0] * n
     free = {"v": 0.0, "a": 0.0, "p": 0.0, "g": 0.0, "s": 0.0}
     ready = {k: [] for k in free}
     order = []
     busy = {k: 0.0 for k in free}
-    bfree = [0.0] * 8
-    blast = [[] for _ in range(8)]
+    bfree = [0.0] * NPS
+    blast = [[] for _ in range(NPS)]
     buse = {}
     for i, x in enumerate(nodes):
         for k in x["banks"]:
@@ -643,7 +618,7 @@ def rank_program(g, core, T, topo):
         fin = st + x["d"][e]
         for y in x["banks"]:
             if y not in phys:
-                z = min([z for z in range(8) if bfree[z] is not None], key=lambda z: bfree[z])
+                z = min([z for z in range(NPS) if bfree[z] is not None], key=lambda z: bfree[z])
                 phys[y] = z
                 bfree[z] = None
                 x["deps"] = sorted(set(x["deps"] + blast[z]))
@@ -657,12 +632,12 @@ def rank_program(g, core, T, topo):
         order.append(k)
         done(k, fin + x["lat"] + LINK)
     if "want_est" in T.tables:
-        T.tables["want_est"].append((max(free.values()), busy, n, [(x["e"], x.get("t", 0), x["d"].get(x["e"], 0), x) for x in nodes]))
+        T.tables["want_est"].append((max(x["t"] + x["lat"] for x in nodes), busy, n, nodes))
     cnt = {"v": 0, "a": 0, "p": 0, "g": 0}
     for k in order:
         x = nodes[k]
         if x["sem"] is None:
-            cnt[x["e"]] += 1
+            cnt[x["e"]] += x["inc"]
             x["at"] = (esem[x["e"]], cnt[x["e"]])
         else:
             x["at"] = (x["sem"], x["inc"])
@@ -676,7 +651,7 @@ def rank_program(g, core, T, topo):
         need = {}
         for j in x["deps"]:
             sm, v = nodes[j]["at"]
-            if sm != "loc":
+            if sm != "loc" and not (j in x["soft"] and nodes[j]["e"] == x["e"]):
                 need[sm] = max(need.get(sm, 0), v)
         for sm in sorted(need):
             if known[x["e"]].get(sm, 0) < need[sm]:
@@ -684,7 +659,8 @@ def rank_program(g, core, T, topo):
                 known[x["e"]][sm] = need[sm]
         z = x["fn"](x["e"])
         if x["sem"] is None:
-            z.then_inc(T.sem[esem[x["e"]]], 1)
+            for y in (z if isinstance(z, list) else [z]):
+                y.then_inc(T.sem[esem[x["e"]]], 1)
         elif x["sem"] != "loc":
             z.then_inc(T.sem[x["sem"]], x["inc"])
     for e in ("v", "a", "p", "g"):

@@ -11,15 +11,16 @@ ROWS = 16 * L
 W = 4096
 DEAD = 4096
 HALF = 2048
-CELL = 34
-REG = CELL * NX
+REG = 2 * L
 LS = 49
 CH = 512
-MAGIC = 12582912.0
+MAGIC = 786432.0
 AF = ActivationFunctionType
 OP = AluOpType
 
 DIFF = (0, 0)
+XA = (2, 0)
+ZC = (2, 3)
 USC = 1
 
 SCRATCH = {"psz": ("psum", [128, 16, 32], "float32")}
@@ -44,48 +45,55 @@ def _sb(name, n, dtype, own=False):
 
 _sb("XT", 2 * W + 16, "bfloat16", True); _sb("YX", 2048, "bfloat16", True)
 _sb("wli", 2 * NW, "int32", True); _sb("wni", NW, "int32", True); _sb("thi", 1, "int32", True); _sb("wti", 1, "int32", True)
-_sb("SN", (RO * NBK * 2 * NX, CELL), "int32"); _sb("OT", (8, P), "float16"); _sb("yno", NW, "float32", True)
-for _n, _k in (("wnf", NW + 1), ("E8", 128), ("cols", 40), ("XR", 144), ("GR", 128), ("YI", 56), ("RA", L), ("W5", 8), ("LM", 16),
+_sb("MS", RO * NBK * 2 * L, "float16", True); _sb("MR", RO * NBK * 4 * L, "float16", True)
+_sb("OT", (8, P), "float16"); _sb("yno", NW, "float32", True)
+for _n, _k in (("wnf", NW + 1), ("E8", 128), ("cols", 8), ("ZF32", 128), ("YI", 56), ("RA", L), ("W5", 8), ("IDF", 128), ("NF", 2 * NW),
                ("NLi", 2 * NW), ("NLf", 2 * NW), ("AC", 4), ("W32", 8), ("iv", 8), ("bs", 8), ("wf", 8)):
     _sb(_n, _k, "float32")
-for _n, _k in (("PI", 2), ("ci", 16), ("ATi", 1), ("ATj", 1), ("wa", 8), ("wb", 8)):
+for _n, _k in (("ci", 2), ("ATi", 1), ("ATj", 1), ("wa", 8), ("wb", 8)):
     _sb(_n, _k, "int32")
 for _n, _k in (("ID", 128), ("NEG", 128), ("N8", 128), ("N15", 128), ("JM", 128), ("W0", 128), ("W1", 128), ("W2", 128), ("W3", 128),
                ("ONE", 128), ("EW", 144), ("WW", 144), ("SEL", 2048), ("LUT", 16 * LS), ("VY", 56), ("K0", L), ("PAT", L), ("TWO", L),
-               ("MQ", 128), ("CK", L), ("VP", 8 * NX), ("M16", 8 * NX), ("B34", NB), ("ZF", NW), ("e2", NW), ("n1", 8), ("n2", 8), ("n3", 8)):
+               ("MQ", 128), ("CK", L), ("VP", 8 * NX), ("DR", 16 * 144), ("BW", NB), ("ZF", NW), ("e1", NW), ("e2", NW), ("k1", 8), ("k3", 8),
+               ("ZB", 576), ("SH", 128), ("E9", 9)):
     _sb(_n, _k, "bfloat16")
-for _n, _k in (("I16", 128), ("ROT", 128), ("DR", 2048), ("RAMP", L), ("IN", 2 * NW), ("NF", 2 * NW)):
+for _n, _k in (("RAMP", L), ("IN", 2 * NW)):
     _sb(_n, _k, "float16")
 for _i in range(4):
-    _sb("PM%d" % _i, 128, "float16"); _sb("QM%d" % _i, 128, "float16")
+    _sb("PM%d" % _i, 128, "bfloat16"); _sb("QM%d" % _i, 128, "bfloat16"); _sb("XM%d" % _i, 128, "bfloat16")
 _sb("nm", 2 * NW, "uint16"); _sb("WL", 8, "uint16")
 for _b in range(NBK):
     _s = str(_b)
     for _n, _k, _d in (("V", ROWS + 16, "bfloat16"), ("M", ROWS, "bfloat16"), ("Z", ROWS, "bfloat16"), ("D2", ROWS, "bfloat16"),
-                       ("AD", ROWS, "bfloat16"), ("S", L + 16, "bfloat16"), ("C", L, "bfloat16"), ("E", L, "bfloat16"),
+                       ("AD", ROWS, "bfloat16"), ("S", 128, "bfloat16"), ("r", L, "bfloat16"), ("C", L, "bfloat16"), ("E", L, "bfloat16"),
                        ("cm", L, "bfloat16"), ("c2", L, "bfloat16"), ("a", L, "float32"), ("na", L, "float32"), ("ni", L, "int32"),
-                       ("y", L, "float32"), ("zo", NX, "uint16"), ("ui", L, "int32"), ("um", L, "int32"), ("q", L, "float32"),
-                       ("r", L, "float32"), ("v", L, "float32"), ("sq", L, "float32"), ("si", L, "int32"), ("hm", L, "int32"),
-                       ("hu", L, "uint16"), ("nc", L, "float32"), ("nj", L, "int32"), ("of", NB, "uint16")):
+                       ("y", L, "float32"), ("zo", NX, "uint16"), ("ui", L, "int32"), ("um", L, "int32"),
+                       ("v", L, "float32"), ("sq", L, "float32"), ("si", L, "int32"), ("hm", L, "int32"),
+                       ("hu", L, "uint16"), ("nc", L, "float32"), ("nj", L, "int32"), ("of", NB, "uint16"),
+                       ("CR0", CH, "bfloat16"), ("CR1", CH, "bfloat16"), ("CR2", CH, "bfloat16"), ("CR3", CH, "bfloat16"),
+                       ("n0", L, "int32"), ("n1", L, "int32"), ("WN", 3 * REG, "float32")):
         _sb(_n + _s, _k, _d)
     _sb("G" + _s, (NX, 192), "bfloat16"); _sb("IX" + _s, (NX, 16), "uint16"); _sb("NB" + _s, (NX, P), "float16")
-    _sb("N0" + _s, (NX, 256), "float16"); _sb("N1" + _s, (NX, 256), "float16"); _sb("yl" + _s, L, "float32", True)
+    _sb("N" + _s, 16 * NB, "float16"); _sb("yl" + _s, L, "float32", True)
     for _t in range(RO):
         _s = "%d%d" % (_t, _b)
         for _n in ("cs", "ct", "cr0", "cr1"):
             _sb(_n + _s, L, "bfloat16", True)
-        _sb("WN0" + _s, 2 * REG, "int32", True); _sb("WN1" + _s, 2 * REG, "int32", True)
 for _d in FILL:
     SCRATCH["all_" + _d] = ("sbuf", [128, FILL[_d]], _d)
 
-SEMAPHORES = ["sv", "sa", "st", "sg", "loc"] + ["d%d" % i for i in range(7 + 3 * NBK)]
+SEMAPHORES = ["sv", "sa", "st", "sg", "loc"] + ["d%d" % i for i in range(7 + NBK)]
 SEMAPHORES += ["m%d%d%d%d" % (k, t, b, h) for k in range(3) for t in range(RO) for b in range(NBK) for h in (0, 1)]
 
 CY = 0.00083
-PE = 0.00071
+PE = 0.00055
+FV = 0.05
+FA = 0.1
 HOP1, HOP2 = 3.5, 6.5
-LINK = 0.06
-FIRST = 4.0
+LINK = 0.1
+FIRST = 3.0
+URGE = 0.02
+PASSES = 6
 VPEN = 0.2
 
 
@@ -93,10 +101,14 @@ def target(q, n, t, h):
     return (q + h + (1 if t < RO - 1 else 0)) % n
 
 
+def slot(t, b, h):
+    return ((t * NBK + b) * 2 + h) * 2 * L
+
+
 def landing(T, k, t, b, h):
     if k == 0:
         return T["cr%d%d%d" % (h, t, b)][:, :]
-    return T["WN%d%d%d" % (k - 1, t, b)][:, REG * h:REG * h + REG]
+    return T.MR[:, slot(t, b, h) + L * (k - 1):slot(t, b, h) + L * k]
 
 
 def relay_of(topo, src, dst, b):
@@ -106,13 +118,13 @@ def relay_of(topo, src, dst, b):
     return c[b % len(c)]
 
 
-def engines(topo, src, dst):
-    return topo.engines(src, dst)[-8:]
+def engines(topo, src, dst, k):
+    return topo.engines(src, dst)[-8:] if k < 2 else topo.engines(src, dst)
 
 
-def transfer(T, topo, core, dst, src_ap, dst_ap, sem):
+def transfer(T, topo, core, dst, src_ap, dst_ap, k, sem):
     rid, pid = topo.addr(dst, core)
-    return RemoteDMATransfer(dst_ids=[DstId(rid=rid, pnc=pid)], dma_engine_mask=sum(1 << e for e in engines(topo, core, dst)),
+    return RemoteDMATransfer(dst_ids=[DstId(rid=rid, pnc=pid)], dma_engine_mask=sum(1 << e for e in engines(topo, core, dst, k)),
                              remote_sem=T.sem[sem], src=src_ap, dst=dst_ap)
 
 
@@ -127,10 +139,10 @@ def relay_program(g, core, T, topo):
                         d = target(q, n, t, h)
                         if d != q and relay_of(topo, T.cores[q], T.cores[d], b) == core:
                             sem = "m%d%d%d%d" % (k, t, b, h)
-                            g.wait_ge(T.sem[sem], len(engines(topo, T.cores[q], core)))
+                            g.wait_ge(T.sem[sem], len(engines(topo, T.cores[q], core, k)))
                             x = landing(T, k, t, b, h)
-                            g.remote_dma_fused([transfer(T, topo, core, T.cores[d], x, x, sem)], local_sem=T.sem["loc"])
-                            tot += len(engines(topo, core, T.cores[d]))
+                            g.remote_dma_fused([transfer(T, topo, core, T.cores[d], x, x, k, sem)], local_sem=T.sem["loc"])
+                            tot += len(engines(topo, core, T.cores[d], k))
     if tot:
         g.wait_ge(T.sem["loc"], tot)
 
@@ -158,7 +170,7 @@ def rank_program(g, core, T, topo):
     eng = {"v": g.vector, "a": g.scalar, "p": g.tensor, "g": g, "s": g.sync}
     esem = {"v": "sv", "a": "sa", "p": "st", "g": "sg"}
 
-    def add(e, dur, w, r, fn, sem=None, inc=1, after=(), lat=0.0):
+    def add(e, dur, w, r, fn, sem=None, inc=1, after=(), lat=0.0, ga=0):
         i = len(nodes)
         deps = {}
         for x in r:
@@ -186,7 +198,7 @@ def rank_program(g, core, T, topo):
             dur, f1 = {e: dur}, fn
             fn = lambda e: f1()
         nodes.append({"e": e, "d": dur, "plus": cur["plus"], "banks": banks, "w": w, "deps": sorted(deps), "fn": fn, "sem": sem, "inc": inc,
-                      "lat": lat, "soft": [j for j in deps if deps[j] == 2]})
+                      "lat": lat, "ga": ga, "soft": [j for j in deps if deps[j] == 2]})
         return i
 
     def A(r, rows=None):
@@ -212,10 +224,10 @@ def rank_program(g, core, T, topo):
         return r[0][:2] != "ps" and SIZE[r[0]][1] in ("bfloat16", "uint16", "float16")
 
     def dv(o, *i):
-        return 0.07 + num(o) * CY * (0.5 if two(o) and all(two(x) for x in i) else 1)
+        return FV + num(o) * CY * (0.5 if two(o) and all(two(x) for x in i) else 1)
 
     def da(o):
-        return 0.2 + num(o) * CY
+        return FA + num(o) * CY
 
     val = lambda s: A(s) if isinstance(s, tuple) else s
 
@@ -237,7 +249,7 @@ def rank_program(g, core, T, topo):
 
     def tt(o, i, j, op):
         k = 1 if "ps" in (i[0][:2], j[0][:2]) else 2
-        return add("v", 0.07 + k * num(o) * CY, [o], [i, j], lambda: g.vector.tensor_tensor(A(o), A(i), A(j), op))
+        return add("v", FV + k * num(o) * CY, [o], [i, j], lambda: g.vector.tensor_tensor(A(o), A(i), A(j), op))
 
     def act(o, i, func, bias=0.0, scale=1.0):
         return add("a", da(o), [o], [i] + ([bias] if isinstance(bias, tuple) else []),
@@ -254,10 +266,14 @@ def rank_program(g, core, T, topo):
         f = lambda: A(win).indirect(A(off))
         d = 0.06 + num(o) * CY * 1.5
         return add(e, {"v": d, "a": d + 0.03}, [o], [win, off], lambda e: g.vector.tensor_copy(A(o), f()) if e == "v" else
-                   g.scalar.activation(A(o), f(), AF.Copy))
+                   g.scalar.activation(A(o), f(), AF.Copy), ga=num(o))
 
     def gts(o, win, off, s1, op0, s2=None, op1=None):
-        return add("v", 0.06 + num(o) * CY * 1.5, [o], [win, off], lambda: tsf(A(o), A(win).indirect(A(off)), s1, op0, s2, op1))
+        return add("v", 0.06 + num(o) * CY * 1.5, [o], [win, off], lambda: tsf(A(o), A(win).indirect(A(off)), s1, op0, s2, op1), ga=num(o))
+
+    def gtt(o, win, off, j):
+        return add("v", 0.06 + num(o) * CY * 1.5, [o], [win, off, j],
+                   lambda: g.vector.tensor_tensor(A(o), A(win).indirect(A(off)), A(j), OP.subtract), ga=num(o))
 
     def mms(lst):
         w, r, d = [], [], 0.05
@@ -303,12 +319,17 @@ def rank_program(g, core, T, topo):
     dma("s", [R("wti")], [], T.wti[:, :], T.wt[:, :])
     col = lambda i: R("cols", i, i + 1)
     ci = lambda i: R("ci", i, i + 1)
-    PC, LA, LB, GP, G15, THR, TH, TN, WC, RC, PB, QA = [col(i) for i in range(12)]
-    PI, PJ = R("PI", 0, 1), R("PI", 1, 2)
-    iota(R("PI"), [[112, 2]], 0, 1, True); iota(R("GR"), [[1, 8], [0, 16]], 0, 0); iota(R("XR"), [[1, 144]], 0, 0)
-    copy(PC, PI); ts(ci(0), PI, 15, OP.bitwise_and); ts(ci(1), PI, 4, OP.arith_shift_right)
-    copy(LA, ci(0)); copy(GP, ci(1)); ts(G15, GP, 16.0, OP.mult, 15.0, OP.add); ts(LB, LA, 16.0, OP.add)
-    add("v", 0.2, [R("E8")], [R("GR"), PC], lambda: g.vector.tensor_scalar(A(R("E8"), 8), A(R("GR"), 8), A(PC, 8), None, OP.is_equal))
+    LA, LB, THR, TH, TN, WC, L32 = [col(i) for i in range(7)]
+
+    def select(o, i, pattern, op, fill, base, cm=1):
+        return add("g", 0.17 + num(o) * 2 * CY, [o], [i], lambda: g.affine_select(A(o), A(i), pattern, op, float(fill), base, cm))
+
+    def pick(o, pattern, base, k=1.0, zero="ZB"):
+        return select(o, R(zero, 0, num(o)), pattern, OP.not_equal, k, base)
+
+    mset(R("ZF32"), 0.0); mset(R("ZB", 0, 144), 0.0); mset(R("ZB", 144), 0.0)
+    iota(ci(0), [[0, 1]], 0, 1, True); ts(ci(1), ci(0), 15, OP.bitwise_and); copy(LA, ci(1)); ts(LB, LA, 16.0, OP.add)
+    pick(R("E8"), [[-1, 8], [0, 16]], 0, zero="ZF32")
     add("v", 0.2, [R("wnf", 0, NW)], [R("wni")], lambda: g.vector.tensor_copy(A(R("wnf", 0, NW), 8), A(R("wni"), 8)))
     add("v", 0.1, [R("wnf", NW, NW + 1)], [R("thi")], lambda: g.vector.tensor_copy(A(R("wnf", NW, NW + 1), 8), A(R("thi"), 8)))
     bn = bank(NW + 1)
@@ -321,38 +342,39 @@ def rank_program(g, core, T, topo):
     ts(R("IN"), R("NLf"), float(-HALF), OP.add)
     add("v", 8 * 0.085, [R("OT")], [R("IN")],
         lambda: [g.vector.transpose(A(R3("OT", w, None, 0, P)), A(R("IN", P * w, P * w + P))) for w in range(8)], inc=8)
-    ts(ci(2), PI, 31, OP.bitwise_and, 1, OP.arith_shift_right); ts(ci(3), PI, 96, OP.bitwise_and); ts(ci(4), PI, 1, OP.bitwise_and)
-    tt(col(12), ci(2), ci(3), OP.add); ts(col(13), col(12), 16.0, OP.add); copy(col(15), ci(4)); ts(col(14), col(15), -1.0, OP.mult, 1.0, OP.add)
     for x in range(4):
-        ts(R("PM%d" % x), R("XR", 0, 128), col(12 + x // 2), OP.is_equal, col(14 + x % 2), OP.mult)
+        pick(R("PM%d" % x), [[-32, 4], [1000, 2], [-2, 16]], -(x % 2) - 1000 * (x // 2))
     mms([(R3("psz", 0, 8, 16 * y, 16 * y + 16), R("PM%d" % (2 * x + y)), R3("OT", 0, 8, 16 * x, 16 * x + 16), x == 0, x == 1)
          for y in (0, 1) for x in (0, 1)])
     for b in range(NBK):
         z = R3("psz", NX * b, NX * b + NX, 0, P)
-        ts(R("nm", L * b, L * b + L), z, float(HALF), OP.add); copy(R("NF", L * b, L * b + L), z)
+        ts(R("nm", L * b, L * b + L), z, float(HALF), OP.add); lin(R("NF", L * b, L * b + L), z, 1.0, float(HALF))
     mset(R("XT", W, W + 16), 255.0)
-    eye = lambda n, k: ts(R(n), R("XR", 0, 128), PC, OP.is_equal, float(k), OP.mult)
     for n, k in (("ID", 1), ("NEG", -1), ("N8", -8192), ("N15", -1584), ("JM", REG - 15), ("W0", 1 - LS), ("W1", -LS),
-                 ("W2", -2 * LS), ("W3", 4 * LS), ("I16", 1)):
-        eye(n, k)
-    copy(WC, R("wti"))
-    ts(R("EW"), R("XR"), G15, OP.is_equal); ts(R("WW"), R("XR"), G15, OP.is_equal, WC, OP.mult)
-    for n, k in (("ONE", 1.0), ("K0", 0.0), ("PAT", 1.0), ("TWO", 2.0), ("MQ", -0.25), ("CK", 167.0 / 32), ("VP", 0.0), ("M16", -16.0)):
+                 ("W2", -2 * LS), ("W3", 4 * LS)):
+        pick(R(n), [[-1, 128]], 0, k)
+    pick(R("IDF"), [[-1, 128]], 0, zero="ZF32")
+    pick(R("SH"), [[-1, 128]], 0, -0.5); select(R("SH"), R("SH"), [[-1, 128]], OP.not_equal, -0.5, 1)
+    copy(WC, R("wti")); mset(R("EW"), 0.0); mset(R("WW"), 0.0); mset(R("ONE"), 1.0)
+    select(R("E9"), R("ONE", 0, 9), [[-16, 9]], OP.is_ge, 0, 0); select(R("EW", 15, 144, 16), R("E9"), [[16, 9]], OP.is_ge, 0, 15, -1)
+    ts(R("WW", 15, 144, 16), R("EW", 15, 144, 16), WC, OP.mult)
+    for n, k in (("K0", 0.0), ("PAT", 1.0), ("TWO", 2.0), ("MQ", -0.25), ("CK", 167.0 / 32), ("VP", 0.0)):
         mset(R(n), k)
     mset(R("K0", 0, L, P), 16384.0); mset(R("PAT", 0, L, P), 0.0); mset(R("VP", 7, 8 * NX, 8), 8.0 * LS)
     for b in range(NBK):
-        mset(R("V%d" % b, 0, 16), 0.0); mset(R("S%d" % b, 0, 16), 0.0)
-    k = (RO - 1) * NBK * 2 * NX
-    mset(R3("SN", 0, k, P, CELL), DEAD); mset(R3("SN", k, k + NBK * 2 * NX, P, CELL), 0)
+        mset(R("V%d" % b, 0, 16), 0.0)
+        mset(R("WN%d" % b, 2 * REG), float(DEAD - HALF))
     mset(R("AC", 0, 1), -0.375)
-    iota(R("SEL"), [[1, 16], [16, 8], [0, 16]], 0, 0); ts(R("SEL"), R("SEL"), PC, OP.is_equal)
+    for x in range(0, 16, 4):
+        pick(R("SEL", 128 * x, 128 * x + 512), [[-1, 4], [-16, 8], [0, 16]], -x)
     iota(R("RA"), [[16, L]], 0, 0); ts(R("RAMP"), R("RA"), LA, OP.add)
-    iota(R("B34"), [[CELL, NX], [0, 16]], 0, 0); iota(R("YI"), [[1, 56]], 0, 0); iota(R("W5"), [[512, 8]], 0, 0)
-    ts(col(16), LA, 32.0, OP.mult); ts(R("W32"), R("W5"), col(16), OP.add)
-    ts(ci(5), PI, 16.0, OP.add); ts(ci(6), ci(5), 127, OP.bitwise_and); copy(RC, ci(6))
-    ts(R("LM"), R("XR", 0, 16), LA, OP.is_equal)
-    for x in range(16):
-        ts(R("DR", 128 * x, 128 * x + 128), R("XR", 0, 128), RC, OP.is_equal, R("LM", x, x + 1), OP.mult)
+    iota(R("BW"), [[P, NX], [0, 8], [L, 2]], 0, 0); iota(R("YI"), [[1, 56]], 0, 0); iota(R("W5"), [[512, 8]], 0, 0)
+    ts(L32, LA, 32.0, OP.mult); ts(R("W32"), R("W5"), L32, OP.add)
+    for x in range(0, 16, 4):
+        pick(R("DR", 144 * x, 144 * x + 576), [[-1, 4], [-16, 9], [1000, 16]], 16 - x - 15000)
+    select(R("DR", 15, None, 144), R("DR", 15, None, 144), [[-1, 16]], OP.not_equal, 1, -112)
+    for x in range(4):
+        pick(R("XM%d" % x), [[-16, 8], [1000, 2], [-2, 8]], -(x % 2) - 1000 * (x // 2))
     ts(R("VY"), R("YI"), LA, OP.is_le)
     for part in range(2):
         b0 = bank(8 * LS); l = []
@@ -373,25 +395,29 @@ def rank_program(g, core, T, topo):
             if d != rank:
                 via = relay_of(topo, core, T.cores[d], b)
                 todo.append((h, T.cores[d] if via is None else via, via))
-                nloc[0] += len(engines(topo, core, todo[-1][1]))
-        s = add("g", 1.0, [], [srcs[h] for h, _, _ in todo], lambda: g.remote_dma_fused(
-            [transfer(T, topo, core, to, A(srcs[h]), landing(T, k, t, b, h), "m%d%d%d%d" % (k, t, b, h)) for h, to, _ in todo],
-            local_sem=T.sem["loc"]), sem="loc", inc=0)
-        for h, to, via in todo:
-            src = [q for q in range(nr) if target(q, nr, t, h) == rank][0]
-            v2 = relay_of(topo, T.cores[src], core, b)
-            o = R("cr%d%d%d" % (h, t, b)) if k == 0 else R("WN%d%d%d" % (k - 1, t, b), REG * h, REG * h + REG)
-            add(None, 0.0, [o], [], None, sem="m%d%d%d%d" % (k, t, b, h), inc=len(engines(topo, T.cores[src] if v2 is None else v2, core)),
-                after=[s], lat=HOP1 if via is None else HOP2)
+                nloc[0] += len(engines(topo, core, todo[-1][1], k))
+        for part in ([todo] if k < 2 else [[x] for x in todo]):
+            sent[:] = [add("g", 1.0, [], [srcs[h] for h, _, _ in part], lambda part=part: g.remote_dma_fused(
+                [transfer(T, topo, core, to, A(srcs[h]), landing(T, k, t, b, h), k, "m%d%d%d%d" % (k, t, b, h)) for h, to, _ in part],
+                local_sem=T.sem["loc"]), sem="loc", inc=0, after=sent[:1] if k else [])]
+            for h, to, via in part:
+                src = [q for q in range(nr) if target(q, nr, t, h) == rank][0]
+                v2 = relay_of(topo, T.cores[src], core, b)
+                o = R("cr%d%d%d" % (h, t, b)) if k == 0 else names(t, b, k - 1, h)
+                add(None, 0.0, [o], [], None, sem="m%d%d%d%d" % (k, t, b, h), after=sent[:1], lat=HOP1 if via is None else HOP2,
+                    inc=len(engines(topo, T.cores[src] if v2 is None else v2, core, k)))
 
-    def send_names(e, t, b, x):
-        k = ((t * NBK + b) * 2 + e) * NX
-        ts(R3("SN", k, k + NX, 0, P), x, W - 1, OP.bitwise_and)
-        src = R3("SN", k, k + NX, 0, CELL)
-        transmit(1 + e, t, b, [src, src])
-        if t == RO - 1:
-            n = "WN%d%d%d" % (e, t, b)
-            dma("s", [R(n, 0, REG)], [src], T[n][:, 0:REG], A(src))
+    sent = []
+
+    def names(t, b, e, h):
+        n, x = ("MS", slot(t, b, 0) // 2) if target(rank, nr, t, h) == rank else ("MR", slot(t, b, h))
+        return R(n, x + L * e, x + L * e + L)
+
+    def put_names(e, t, b, x):
+        y, k = R("n%d%d" % (e, b)), slot(t, b, 0) // 2 + L * e
+        ts(y, x, W - 1, OP.bitwise_and)
+        ts(R("MS", k, k + L), y, float(-HALF), OP.add)
+        transmit(1 + e, t, b, [R("MS", k, k + L)] * 2)
 
     def join(t, b):
         s = str(b)
@@ -402,19 +428,26 @@ def rank_program(g, core, T, topo):
         copy(R3("IX" + s, 0, NX, 8, 16), f)
         f = bank(8 * NX)
         acc(f, [(R("W%d" % i), R(over, i, L, 4)) for i in range(4)] +
-            [(R("ID"), R(own, P - 1, L, P), R(f[0], c, 8 * NX, 8)) for c in range(4, 8)] + [(R("ID"), R("M16"))])
+            [(R("ID"), R(own, P - 1, L, P), R(f[0], c, 8 * NX, 8)) for c in range(4, 8)] + [(R("ID"), R("VP"))])
         copy(R3("IX" + s, 0, NX, 0, 8), f)
         for w in range(NX):
             gather("va", R3("G" + s, w, None, 0, 192), R("LUT"), R3("IX" + s, w, None, 4, 16))
         f = bank(NB)
-        acc(f, [(R("ID"), R3("G" + s, 0, NX, 16 * c, 16 * c + 16)) for c in range(12)] + [(R("ID"), R("B34"))])
-        copy(R("of" + s), f)
+        acc(f, [(R("ID"), R3("G" + s, 0, NX, 16 * c, 16 * c + 16)) for c in range(12)] + [(R("ID"), R("BW"))])
+        add("v", NX * (FV + 16 * CY), [R("of" + s)], [f], lambda f=f: [
+            g.vector.tensor_copy(A(R("of" + s, w, NB, NX)), A(R(f[0], 16 * w, 16 * w + 16))) for w in range(NX)], inc=NX)
+        if t == RO - 1:
+            mset(R("WN" + s, 2 * REG + 16, 3 * REG, P), float(-HALF))
+        for h in (1, 0):
+            f = bank(REG)
+            mms([(R(f[0], L * y, L * y + L), R("XM%d" % (2 * e + y)), names(t, b, e, h), e == 0, e == 1) for y in (0, 1) for e in (0, 1)])
+            copy(R("WN" + s, REG * h, REG * h + REG), f, "va")
         f = bank(L)
-        for e in (0, 1):
-            n = "N%d%s" % (e, s)
-            for w in range(NX):
-                gts(R3(n, w, None, 0, 256), R("WN%d%d%d" % (e, t, b)), R("of" + s, 16 * w, 16 * w + 16), float(-HALF), OP.add)
-            acc(R(f[0], e, L, 2), [(R("DR", 128 * x, 128 * x + 128), R3(n, 0, NX, 16 * x, 16 * x + 16)) for x in range(16)])
+        for y in range(0, 16, 4):
+            gather("v", R("N" + s, NB * y, NB * y + 4 * NB), R("WN" + s), R("of" + s, NX * y, NX * y + 4 * NX))
+            acc(f, ([(R("N8"), R("MQ", 0, L))] if y == 0 else []) +
+                [(R("DR", 144 * (8 * e + x // 2) + 15 - x, 144 * (8 * e + x // 2) + 143 - x), R("N" + s, NB * x, NB * x + NB), R(f[0], e, L, 2))
+                 for x in range(y, y + 4) for e in (0, 1)], y == 0, y == 12)
         return f
 
     def step(o, i, k, more):
@@ -430,7 +463,7 @@ def rank_program(g, core, T, topo):
             nm, nf = R("nm", L * b, L * b + L), R("NF", L * b, L * b + L)
             if t:
                 f = join(t - 1, b)
-                ts(nm, f, float(HALF), OP.add); copy(nf, f)
+                copy(nm, f); copy(nf, f, "va")
             for w in range(NX):
                 gather("va", r("V", 16 + CH * w, 16 + CH * w + CH), R("XT", 0, W + 16), R("nm", L * b + P * w, L * b + P * w + P))
             D = bank(L)
@@ -439,50 +472,61 @@ def rank_program(g, core, T, topo):
                     f = bank(CH)
                     acc(f, [(R("ID"), r("V", 16 + x, 16 + x + CH)), (R("NEG"), r("V", x, x + CH))])
                     act(r("M", x, x + CH), f, AF.Abs)
-                acc(D, [(win("EW", x), r("M", x, ROWS, 16)) for x in range(16)] + [(R("ID"), R("K0"))])
+                    if x % (2 * CH):
+                        y = (x - CH) // 16
+                        acc(R(D[0], y, y + 64), [(win("EW", z), r("M", 16 * y + z, x + CH, 16)) for z in range(16)] + [(R("ID"), R("K0", 0, 64))])
             else:
-                f = bank(L)
-                acc(f, [(win("EW", x), r("V", 16 + x, 16 + ROWS, 16)) for x in range(16)])
-                lin(r("S", 16, 16 + L), f, 0.5, 0.0)
+                f = bank(128)
+                add("p", 0.05 + 1024 * PE, [f], [r("V"), R("EW")], lambda f=f, s=s: [g.tensor.matmul(
+                    A(R(f[0], x, 128, 16), L), A(R("V" + s, 16 + x, 16 + ROWS, 16)), A(R("EW", 15, 143, 16)), True, True) for x in range(16)][-1])
+                add("va", {"v": dv(f), "a": da(f)}, [r("S")], [f], lambda e, f=f, s=s: g.vector.tensor_copy(A(R("S" + s), L), A(f, L))
+                    if e == "v" else g.scalar.activation(A(R("S" + s), L), A(f, L), AF.Copy))
                 for y in range(0, 16, 4):
                     scans([(r("M", L * x, L * x + L), r("V", x, ROWS, 16), r("V", 16 + x, 16 + ROWS, 16)) for x in range(y, y + 4)], 256.0, OP.min, OP.max)
                     acc(D, [(win("EW", x), r("M", L * x, L * x + L)) for x in range(y, y + 4)], y == 0, False)
-                acc(D, [(R("NEG"), r("S", 16, 16 + L)), (R("NEG"), r("S", 15, 15 + L)), (R("ID"), R("K0"))], False)
+                add("p", 0.05 + 2 * L * PE, [D], [r("S"), R("SH"), R("ID"), R("K0")], lambda D=D, s=s: [
+                    g.tensor.matmul(A(D), A(R("S" + s), L), A(R("SH", 0, L), L), False, False),
+                    g.tensor.matmul(A(D), A(R("ID")), A(R("K0")), False, True)][-1])
             half = 0.5 if DIFF[b] else 1.0
             step(r("C"), D, half, False)
             step(r("E", 0, L - 1), R(D[0], 1, L), half, True)
             ts(r("E", P - 1, L, P), R("nm", L * b + P - 1, L * b + L, P), float(DEAD), OP.is_lt)
             per = CH // L
+            fu = bank(L)
             for y in range(0, 16, per):
                 f = bank(CH)
                 mms([(R(f[0], L * (x - y), L * (x - y + 1)), R("SEL", 128 * x, 128 * x + 128), r("C"), True, True) for x in range(y, y + per)])
-                scans([(r("Z", x, ROWS, 16), R(f[0], L * (x - y), L * (x - y + 1)), r("V", 16 + x, 16 + ROWS, 16)) for x in range(y, y + per)],
+                n = f[0]
+                if y // per in ZC:
+                    n = "CR%d%s" % (y // per, s)
+                    copy(R(n), f, "a")
+                scans([(r("Z", x, ROWS, 16), R(n, L * (x - y), L * (x - y + 1)), r("V", 16 + x, 16 + ROWS, 16)) for x in range(y, y + per)],
                       0.0, OP.mult, OP.max)
+                acc(fu, [(win("WW", x), r("Z", x, ROWS, 16)) for x in range(y, y + per)], y == 0, y + per == 16)
             cs, ct = R("cs%d%d" % (t, b)), R("ct%d%d" % (t, b))
             scans([(cs, R("PAT"), r("E"))], 0.0, OP.mult, OP.add)
-            ts(ct, cs, 16.0, OP.max)
+            add("va", {"v": dv(ct, cs), "a": da(ct)}, [ct], [cs], lambda e, o=ct, i=cs: g.vector.tensor_scalar(A(o), A(i), -16.0, 0.0, OP.add, OP.max)
+                if e == "v" else g.scalar.activation(A(o), A(i), AF.Relu, bias=-16.0))
             transmit(0, t, b, [cs, ct])
             scans([(r("cm"), r("C"), R("TWO"))], 0.0, OP.mult, OP.add)
             lin(r("c2"), r("cm"), 1.0, 1.0)
             f = bank(L)
-            acc(f, [(R("I16"), nf), (R("N8"), r("C")), (R("N8"), R("MQ", 0, L))])
+            acc(f, [(R("IDF"), nf), (R("N8"), r("C"))])
             scans([(r("a"), r("C"), f)], 0.0, OP.mult, OP.max)
             tt(r("na"), r("a"), r("c2"), OP.mult)
             ts(r("ni"), r("na"), 0.25, OP.mult, R("AC", t, t + 1), OP.add)
-            send_names(0, t, b, r("ni"))
+            put_names(0, t, b, r("ni"))
             f = bank(L)
-            acc(f, [(R("I16"), R("RAMP")), (R("N8"), r("E"))])
+            acc(f, [(R("ID"), R("RAMP")), (R("N8"), r("E"))])
             scans([(r("y"), R("K0"), f)], 0.0, OP.add, OP.min)
             ts(r("zo"), r("y", P - 1, L, P), 8192.0, OP.add, float(ROWS - 1), OP.min)
             ts(R("iv", NX * b, NX * b + NX), r("y", P - 1, L, P), 0.0, OP.is_ge, float(W + 16), OP.mult)
             gts(R("ZF", NB * b, NB * b + NB), r("Z"), r("zo"), -192.0, OP.add)
-            f = bank(L)
-            acc(f, [(win("WW", x), r("Z", x, ROWS, 16)) for x in range(16)] + ([(R("N8"), R("MQ", 0, L))] if USC else []))
+            f = fu
             if USC:
-                act(r("q"), f, AF.Identity, MAGIC, (1.0 + 2.0 ** -17) / W)
-                act(r("r"), r("q"), AF.Identity, MAGIC * W, float(-W))
+                lin(r("r"), f, -1.0, HALF - 0.5 - MAGIC)
                 tt(r("v"), f, r("r"), OP.add)
-                act(r("sq"), r("v"), AF.Square, 592.0 + HALF)
+                act(r("sq"), r("v"), AF.Square, 592.0 + MAGIC)
             else:
                 copy(r("ui"), f)
                 ts(r("um"), r("ui"), W - 1, OP.bitwise_and)
@@ -493,17 +537,28 @@ def rank_program(g, core, T, topo):
             tt(r("si"), r("sq"), f, OP.subtract)
             ts(r("hm"), r("si"), 5, OP.arith_shift_right, W - 1, OP.bitwise_and)
             copy(r("hu"), r("hm"))
+            fd = bank(L)
             for w in range(NX):
                 o, off, z = r("D2", CH * w, CH * w + CH), r("hu", P * w, P * w + P), r("Z", CH * w, CH * w + CH)
-                add("v", 0.06 + CH * CY * 1.5, [o], [R("XT", 0, W), off, z],
-                    lambda o=o, off=off, z=z: g.vector.tensor_tensor(A(o), A(R("XT", 0, W)).indirect(A(off)), A(z), OP.subtract))
-                act(r("AD", CH * w, CH * w + CH), o, AF.Abs)
-            gts(R("e2", NB * b, NB * b + NB), r("D2"), r("zo"), 0.5, OP.mult, 191.75, OP.add)
-            f = bank(L)
-            acc(f, [(win("EW", x), r("AD", x, ROWS, 16)) for x in range(16)])
-            tt(r("nc"), f, r("c2"), OP.mult)
+                if w < XA[b]:
+                    gather("a", o, R("XT", 0, W), off)
+                    f = bank(CH)
+                    acc(f, [(R("NEG"), z), (R("ID"), o)])
+                    act(r("AD", CH * w, CH * w + CH), f, AF.Abs)
+                else:
+                    gtt(o, R("XT", 0, W), off, z)
+                    act(r("AD", CH * w, CH * w + CH), o, AF.Abs)
+                if w % 2:
+                    acc(R(fd[0], P * w - P, P * w + P), [(win("EW", x), r("AD", CH * w - CH + x, CH * w + CH, 16)) for x in range(16)])
+            x, y = NB * b, NB * b + 16 * XA[b]
+            if XA[b]:
+                gtt(R("e1", x, y), r("D2"), r("zo", 0, XA[b]), R("ZF", x, y))
+                ts(R("e2", x, y), R("e1", x, y), 0.5, OP.mult, 95.75, OP.add)
+            if XA[b] < NX:
+                gts(R("e2", y, x + NB), r("D2"), r("zo", XA[b]), 0.5, OP.mult, 191.75, OP.add)
+            tt(r("nc"), fd, r("c2"), OP.mult)
             tt(r("nj"), r("nc"), r("hm"), OP.add)
-            send_names(1, t, b, r("nj"))
+            put_names(1, t, b, r("nj"))
         cur["plus"] = 0.0
         if t < RO - 1:
             f = bank(1)
@@ -521,18 +576,18 @@ def rank_program(g, core, T, topo):
         acc(f, [(R("ID"), R("XT", 1024 * q + e, 1024 * q + 1024, 2)) for e in (0, 1)])
         copy(R("YX", 512 * q, 512 * q + 512), f, "va")
     dma("s", [("yx", 0, 1, 1)], [R("YX")], T.yx[:, :], T.YX[:, :])
-    ts(ci(7), PJ, 96, OP.bitwise_and); ts(ci(8), PJ, 4, OP.arith_shift_right, 1, OP.bitwise_and)
-    ts(col(17), LA, 2.0, OP.mult); tt(col(18), col(17), ci(7), OP.add); ts(col(19), col(18), 1.0, OP.add)
-    copy(col(21), ci(8)); ts(col(20), col(21), -1.0, OP.mult, 1.0, OP.add)
     for x in range(4):
-        ts(R("QM%d" % x), R("XR", 0, 128), col(18 + x % 2), OP.is_equal, col(20 + x // 2), OP.mult)
+        pat, base = [[-32, 4], [-1, 16], [1000, 2]], -16 * (x // 2) - 16 - 1000 * (x % 2)
+        pick(R("QM%d" % x), pat, base)
+        if x // 2:
+            select(R("QM%d" % x), R("QM%d" % x), pat, OP.not_equal, 1, base + 128)
     t = RO - 1
     for b in range(NBK):
         s = str(b)
         cur["plus"] = FIRST if b == 0 else 0.0
-        tt(R("n1", NX * b, NX * b + NX), R("cs%d%d" % (t, b), P - 1, L, P), R("cr1%d%d" % (t, b), P - 1, L, P), OP.add)
+        tt(R("k1", NX * b, NX * b + NX), R("cs%d%d" % (t, b), P - 1, L, P), R("cr1%d%d" % (t, b), P - 1, L, P), OP.add)
         f = join(t, b)
-        copy(R3("NB" + s, 0, NX, 0, P), f)
+        ts(R3("NB" + s, 0, NX, 0, P), f, float(-HALF), OP.add)
         l = []
         for x in (0, 1):
             o = R3("psz", NX * b, NX * b + NX, 16 * x, 16 * x + 16)
@@ -543,10 +598,10 @@ def rank_program(g, core, T, topo):
             g.vector.transpose(A(R("yl" + s, P * w, P * w + P)), A(R3("psz", NX * b + w, None, 0, P))) for w in range(NX)], inc=NX)
         dma("s" if b else "a", [("yl", b, b + 1, 1)], [R("yl" + s)], T.yl[:, L * b:L * b + L], T["yl" + s][:, :])
     cur["plus"] = 0.0
-    ts(R("n2"), R("n1"), -16.0, OP.add, 16.0, OP.min); ts(R("n3"), R("n2"), 2.0, OP.mult)
+    ts(R("k3"), R("k1"), 16.0, OP.min, 2.0, OP.mult)
     f = bank(NW)
-    add("p", 0.8, [f], [R("SEL"), R("n3")], lambda f=f: [g.tensor.matmul(A(R(f[0], x, NW, 16), 8), A(R("SEL", 128 * x, 128 * x + 128, 16)),
-                                                                      A(R("n3")), True, True) for x in range(16)][-1])
+    add("p", 0.8, [f], [R("SEL"), R("k3")], lambda f=f: [g.tensor.matmul(A(R(f[0], x, NW, 16), 8), A(R("SEL", 128 * x, 128 * x + 128, 16)),
+                                                                      A(R("k3")), True, True) for x in range(16)][-1])
     add("v", 0.2, [R("yno")], [f], lambda f=f: g.vector.tensor_copy(A(R("yno"), 8), A(f, 8)))
     dma("s", [("yn", 0, 1, 1)], [R("yno")], T.yn[:, :], T.yno[0:8, :])
 
@@ -561,78 +616,84 @@ def rank_program(g, core, T, topo):
         prio[i] = (min(x["d"].values()) if x["e"] == "va" else x["d"][x["e"]] if x["e"] else 0.0) + x["lat"] + LINK + max([prio[k] for k in users[i]] + [0.0])
     for i in range(n):
         prio[i] += nodes[i]["plus"]
-    left = [len(x["deps"]) for x in nodes]
-    ready_at = [0.0] * n
     free = {"v": 0.0, "a": 0.0, "p": 0.0, "g": 0.0, "s": 0.0}
-    ready = {k: [] for k in free}
-    order = []
-    busy = {k: 0.0 for k in free}
-    bfree = [0.0] * NPS
-    blast = [[] for _ in range(NPS)]
-    buse = {}
-    for i, x in enumerate(nodes):
-        for k in x["banks"]:
-            buse.setdefault(k, []).append(i)
-    bleft = {k: len(v) for k, v in buse.items()}
 
-    def done(i, at):
-        for k in users[i]:
-            ready_at[k] = max(ready_at[k], at)
-            left[k] -= 1
-            if left[k] == 0:
-                release(k)
+    def sweep(urgency, back, on):
+        before, after = (users, [x["deps"] for x in nodes]) if back else ([x["deps"] for x in nodes], users)
+        left = [len(x) for x in before]
+        ready_at, at, fin, took, more = [0.0] * n, [0.0] * n, [0.0] * n, [None] * n, [[] for _ in range(n)]
+        busy = dict(free)
+        ready = {k: [] for k in free}
+        order, banks, bleft = [], {}, {}
+        bfree = [0.0] * NPS
+        blast = [[] for _ in range(NPS)]
+        for x in nodes:
+            for k in x["banks"]:
+                bleft[k] = bleft.get(k, 0) + 1
 
-    def release(k):
-        x = nodes[k]
-        if x["e"] is None:
-            x["t"] = ready_at[k]
-            done(k, ready_at[k] + x["lat"])
-        else:
-            for e in x["e"]:
-                ready[e].append(k)
+        def done(i):
+            for k in after[i]:
+                ready_at[k] = max(ready_at[k], fin[i] + (0.0 if on[i] == on[k] == "p" else LINK) + nodes[k if back else i]["lat"])
+                left[k] -= 1
+                if left[k] == 0:
+                    release(k)
 
-    for i in range(n):
-        if left[i] == 0 and not nodes[i]["deps"]:
+        def release(k):
+            if on[k] is None:
+                at[k] = fin[k] = ready_at[k]
+                done(k)
+            else:
+                for e in on[k]:
+                    ready[e].append(k)
+
+        for i in [i for i in range(n) if not before[i]]:
+            ready_at[i] = nodes[i]["lat"] if back else 0.0
             release(i)
-    while any(ready.values()):
-        best = None
-        for e in free:
-            for k in ready[e]:
-                st = max(free[e], ready_at[k])
-                x = nodes[k]
-                new = [y for y in x["banks"] if y not in phys]
-                if new:
-                    fr = [z for z in bfree if z is not None]
-                    if not fr:
-                        continue
-                    st = max(st, min(fr))
-                key = (st + (VPEN if len(x["e"]) > 1 and e == "v" else 0.0), -prio[k])
-                if best is None or key < best[0]:
-                    best = (key, e, k, st)
-        _, e, k, st = best
-        x = nodes[k]
-        for y in x["e"]:
-            ready[y].remove(k)
-        x["e"] = e
-        x["t"] = st
-        fin = st + x["d"][e]
-        for y in x["banks"]:
-            if y not in phys:
-                z = min([z for z in range(NPS) if bfree[z] is not None], key=lambda z: bfree[z])
-                phys[y] = z
-                bfree[z] = None
-                x["deps"] = sorted(set(x["deps"] + blast[z]))
-                blast[z] = []
-            bleft[y] -= 1
-            blast[phys[y]].append(k)
-            if bleft[y] == 0:
-                bfree[phys[y]] = fin + LINK
-        free[e] = fin
-        busy[e] += x["d"][e]
-        order.append(k)
-        done(k, fin + x["lat"] + LINK)
+        while any(ready.values()):
+            best = None
+            fr = [z for z in bfree if z is not None]
+            for e in free:
+                for k in ready[e]:
+                    st = max(busy[e], ready_at[k])
+                    if not back and [y for y in nodes[k]["banks"] if y not in banks]:
+                        if not fr:
+                            continue
+                        st = max(st, min(fr))
+                    key = (st + (VPEN if len(on[k]) > 1 and e == "v" else 0.0) - URGE * urgency[k], -urgency[k])
+                    if best is None or key < best[0]:
+                        best = (key, e, k, st)
+            _, e, k, st = best
+            for y in on[k]:
+                ready[y].remove(k)
+            took[k], at[k], fin[k] = e, st, st + nodes[k]["d"][e]
+            for y in ([] if back else nodes[k]["banks"]):
+                if y not in banks:
+                    z = min([z for z in range(NPS) if bfree[z] is not None], key=lambda z: bfree[z])
+                    banks[y] = z
+                    bfree[z] = None
+                    more[k] += blast[z]
+                    blast[z] = []
+                bleft[y] -= 1
+                blast[banks[y]].append(k)
+                if bleft[y] == 0:
+                    bfree[banks[y]] = fin[k] + LINK
+            busy[e] = fin[k]
+            order.append(k)
+            done(k)
+        return max(fin[i] + nodes[i]["lat"] for i in range(n)), order, took, at, fin, banks, more
+
+    kept = None
+    for _ in range(PASSES):
+        res = sweep(prio, False, [x["e"] for x in nodes])
+        if kept is None or res[0] < kept[0]:
+            kept = res
+        prio = sweep(res[4], True, res[2])[4]
+    end, order, took, at, fin, banks, more = kept
+    phys.update(banks)
+    for i, x in enumerate(nodes):
+        x["e"], x["t"], x["deps"] = took[i], at[i], sorted(set(x["deps"] + more[i]))
     if "want_est" in T.tables:
-        T.tables["want_est"].append((max(x["t"] + x["lat"] for x in nodes), busy, n, nodes))
+        T.tables["want_est"].append((end, {e: sum(x["d"][e] for x in nodes if x["e"] == e) for e in free}, n, nodes))
     cnt = {"v": 0, "a": 0, "p": 0, "g": 0}
     for k in order:
         x = nodes[k]

@@ -11,7 +11,10 @@ ROWS = 16 * L
 W = 4096
 DEAD = 4096
 HALF = 2048
-REG = 2 * L
+REG = L
+MROWS = 20
+S_OVER, S_OWN, S_N, S_UP = 0, 1, 3, 3 + 2 * NX
+R_OWN, R_N, R_OVER, R_UP = 0, 2, 2 + 2 * NX, 4 + 2 * NX
 LS = 49
 CH = 512
 MAGIC = 786432.0
@@ -19,8 +22,10 @@ AF = ActivationFunctionType
 OP = AluOpType
 
 DIFF = (0, 0)
-XA = (2, 0)
-ZC = (2, 3)
+XA = ((2, 0), (2, 0), (2, 2))
+ZC = (3,)
+MT = 0
+YV = (1,)
 USC = 1
 
 SCRATCH = {"psz": ("psum", [128, 16, 32], "float32")}
@@ -45,19 +50,19 @@ def _sb(name, n, dtype, own=False):
 
 _sb("XT", 2 * W + 16, "bfloat16", True); _sb("YX", 2048, "bfloat16", True)
 _sb("wli", 2 * NW, "int32", True); _sb("wni", NW, "int32", True); _sb("thi", 1, "int32", True); _sb("wti", 1, "int32", True)
-_sb("MS", RO * NBK * 2 * L, "float16", True); _sb("MR", RO * NBK * 4 * L, "float16", True)
+_sb("MS", (RO * NBK * MROWS, P), "float16"); _sb("MR", (RO * NBK * MROWS, P), "float16")
 _sb("OT", (8, P), "float16"); _sb("yno", NW, "float32", True)
 for _n, _k in (("wnf", NW + 1), ("E8", 128), ("cols", 8), ("ZF32", 128), ("YI", 56), ("RA", L), ("W5", 8), ("IDF", 128), ("NF", 2 * NW),
-               ("NLi", 2 * NW), ("NLf", 2 * NW), ("AC", 4), ("W32", 8), ("iv", 8), ("bs", 8), ("wf", 8)):
+               ("AC", 4), ("W32", 8), ("iv", 8), ("bs", 8), ("wf", 8)):
     _sb(_n, _k, "float32")
 for _n, _k in (("ci", 2), ("ATi", 1), ("ATj", 1), ("wa", 8), ("wb", 8)):
     _sb(_n, _k, "int32")
 for _n, _k in (("ID", 128), ("NEG", 128), ("N8", 128), ("N15", 128), ("JM", 128), ("W0", 128), ("W1", 128), ("W2", 128), ("W3", 128),
                ("ONE", 128), ("EW", 144), ("WW", 144), ("SEL", 2048), ("LUT", 16 * LS), ("VY", 56), ("K0", L), ("PAT", L), ("TWO", L),
-               ("MQ", 128), ("CK", L), ("VP", 8 * NX), ("DR", 16 * 144), ("BW", NB), ("ZF", NW), ("e1", NW), ("e2", NW), ("k1", 8), ("k3", 8),
+               ("MQ", 128), ("CK", L), ("VP", 3 * P), ("DR", 16 * 144), ("BW", NB), ("ZF", NW), ("e1", NW), ("e2", NW),
                ("ZB", 576), ("SH", 128), ("E9", 9)):
     _sb(_n, _k, "bfloat16")
-for _n, _k in (("RAMP", L), ("IN", 2 * NW)):
+for _n, _k in (("RAMP", L), ("IN", 2 * NW), ("IM", 2 * NW), ("NLi", 2 * NW)):
     _sb(_n, _k, "float16")
 for _i in range(4):
     _sb("PM%d" % _i, 128, "bfloat16"); _sb("QM%d" % _i, 128, "bfloat16"); _sb("XM%d" % _i, 128, "bfloat16")
@@ -65,66 +70,67 @@ _sb("nm", 2 * NW, "uint16"); _sb("WL", 8, "uint16")
 for _b in range(NBK):
     _s = str(_b)
     for _n, _k, _d in (("V", ROWS + 16, "bfloat16"), ("M", ROWS, "bfloat16"), ("Z", ROWS, "bfloat16"), ("D2", ROWS, "bfloat16"),
-                       ("AD", ROWS, "bfloat16"), ("S", 128, "bfloat16"), ("r", L, "bfloat16"), ("C", L, "bfloat16"), ("E", L, "bfloat16"),
-                       ("cm", L, "bfloat16"), ("c2", L, "bfloat16"), ("a", L, "float32"), ("na", L, "float32"), ("ni", L, "int32"),
+                       ("AD", (NX, CH), "bfloat16"), ("cs", 2 * L, "bfloat16"), ("lv", NB, "bfloat16"), ("S", 128, "bfloat16"), ("S2", 128, "bfloat16"), ("r", L, "bfloat16"), ("C", L, "bfloat16"), ("E", L, "bfloat16"),
+                       ("cm", L, "bfloat16"), ("c2", (NX, P), "bfloat16"), ("a", L, "float32"), ("na", L, "float32"), ("ni", L, "int32"),
                        ("y", L, "float32"), ("zo", NX, "uint16"), ("ui", L, "int32"), ("um", L, "int32"),
-                       ("v", L, "float32"), ("sq", L, "float32"), ("si", L, "int32"), ("hm", L, "int32"),
+                       ("v", L, "float32"), ("sq", L, "float32"), ("si", L, "int32"), ("hm", (NX, P), "int32"),
                        ("hu", L, "uint16"), ("nc", L, "float32"), ("nj", L, "int32"), ("of", NB, "uint16"),
                        ("CR0", CH, "bfloat16"), ("CR1", CH, "bfloat16"), ("CR2", CH, "bfloat16"), ("CR3", CH, "bfloat16"),
-                       ("n0", L, "int32"), ("n1", L, "int32"), ("WN", 3 * REG, "float32")):
+                       ("n0", (NX, P), "int32"), ("n1", (NX, P), "int32"), ("WN", 4 * REG, "float32")):
         _sb(_n + _s, _k, _d)
-    _sb("G" + _s, (NX, 192), "bfloat16"); _sb("IX" + _s, (NX, 16), "uint16"); _sb("NB" + _s, (NX, P), "float16")
+    _sb("G" + _s, 12 * NB, "bfloat16"); _sb("IX" + _s, (NX, 16), "uint16"); _sb("NB" + _s, (NX, P), "float16")
     _sb("N" + _s, 16 * NB, "float16"); _sb("yl" + _s, L, "float32", True)
-    for _t in range(RO):
-        _s = "%d%d" % (_t, _b)
-        for _n in ("cs", "ct", "cr0", "cr1"):
-            _sb(_n + _s, L, "bfloat16", True)
 for _d in FILL:
     SCRATCH["all_" + _d] = ("sbuf", [128, FILL[_d]], _d)
 
-SEMAPHORES = ["sv", "sa", "st", "sg", "loc"] + ["d%d" % i for i in range(7 + NBK)]
+SEMAPHORES = ["sv", "sa", "st", "sg", "loc"] + ["d%d" % i for i in range(8 + NBK)]
 SEMAPHORES += ["m%d%d%d%d" % (k, t, b, h) for k in range(3) for t in range(RO) for b in range(NBK) for h in (0, 1)]
 
 CY = 0.00083
-PE = 0.00055
+PE = 0.0005
+GA = 1.5
 FV = 0.05
 FA = 0.1
-HOP1, HOP2 = 3.5, 6.5
+XLOAD = 5.0
+HOP0 = 2.0
+HOP1 = 2.7
+PORT = 0.1
+WIDE = 0.0
+ONCE = 2.5
+WEIGHT = 3.0
 LINK = 0.1
-FIRST = 3.0
-URGE = 0.02
-PASSES = 6
-VPEN = 0.2
+SAME = 0.1
+CALL = 1.0
+FIRST = 1.0
+PASSES = 5
+RULES = [(3, u, v, (0, 0, 0)) for u in (0.02, 0.03, 0.05) for v in (0.1, 0.3, 0.5)]
+SLOW = 1.25
 
 
 def target(q, n, t, h):
     return (q + h + (1 if t < RO - 1 else 0)) % n
 
 
-def slot(t, b, h):
-    return ((t * NBK + b) * 2 + h) * 2 * L
+def calls(t, b):
+    s, r, u = MROWS * (t * NBK + b), MROWS * (t * NBK + b), NX // 2
+    if t < RO - 1:
+        return [(0, [(0, s + S_OWN, r + R_OWN, 2), (1, s + S_OVER, r + R_OVER, 2)]),
+                (1, [(0, s + S_N, r + R_N, NX), (1, s + S_N, r + R_UP, NX)]),
+                (2, [(0, s + S_N + NX, r + R_N + NX, NX)]), (2, [(1, s + S_N + NX, r + R_UP + NX, NX)])]
+    return [(0, [(1, s + S_OVER, r + R_OVER, 1)]), (1, [(1, s + S_UP, r + R_UP, u)]), (2, [(1, s + S_UP + u, r + R_UP + u, u)])]
 
 
-def landing(T, k, t, b, h):
-    if k == 0:
-        return T["cr%d%d%d" % (h, t, b)][:, :]
-    return T.MR[:, slot(t, b, h) + L * (k - 1):slot(t, b, h) + L * k]
-
-
-def relay_of(topo, src, dst, b):
+def leg(topo, src, dst, t, b, k):
     if topo.may_write(src, dst):
-        return None
+        return dst, topo.engines(src, dst)
     c = [x for x in topo.cores_of(src) if x != src and topo.die(x) == topo.die(src) and topo.may_write(x, dst)]
-    return c[b % len(c)]
+    e = topo.engines(src, c[0])
+    return c[b % len(c)], (e[len(e) // 2:] if k < 2 and t < RO - 1 else e)
 
 
-def engines(topo, src, dst, k):
-    return topo.engines(src, dst)[-8:] if k < 2 else topo.engines(src, dst)
-
-
-def transfer(T, topo, core, dst, src_ap, dst_ap, k, sem):
+def transfer(T, topo, core, dst, src_ap, dst_ap, engines, sem):
     rid, pid = topo.addr(dst, core)
-    return RemoteDMATransfer(dst_ids=[DstId(rid=rid, pnc=pid)], dma_engine_mask=sum(1 << e for e in engines(topo, core, dst, k)),
+    return RemoteDMATransfer(dst_ids=[DstId(rid=rid, pnc=pid)], dma_engine_mask=sum(1 << e for e in engines),
                              remote_sem=T.sem[sem], src=src_ap, dst=dst_ap)
 
 
@@ -132,17 +138,14 @@ def relay_program(g, core, T, topo):
     n = len(T.cores)
     tot = 0
     for t in range(RO):
-        for b in range(NBK):
-            for k in range(3):
-                for h in (0, 1):
-                    for q in range(n):
-                        d = target(q, n, t, h)
-                        if d != q and relay_of(topo, T.cores[q], T.cores[d], b) == core:
-                            sem = "m%d%d%d%d" % (k, t, b, h)
-                            g.wait_ge(T.sem[sem], len(engines(topo, T.cores[q], core, k)))
-                            x = landing(T, k, t, b, h)
-                            g.remote_dma_fused([transfer(T, topo, core, T.cores[d], x, x, k, sem)], local_sem=T.sem["loc"])
-                            tot += len(engines(topo, core, T.cores[d], k))
+        for b, k, h, r, m, q in [(b, k, h, r, m, q) for b in range(NBK) for k, ws in calls(t, b) for h, _, r, m in ws for q in range(n)]:
+            d = T.cores[target(q, n, t, h)]
+            if leg(topo, T.cores[q], d, t, b, k)[0] == core:
+                sem = "m%d%d%d%d" % (k, t, b, h)
+                g.wait_ge(T.sem[sem], len(leg(topo, T.cores[q], d, t, b, k)[1]))
+                x = T.MR[:, r:r + m, :]
+                g.remote_dma_fused([transfer(T, topo, core, d, x, x, topo.engines(core, d), sem)], local_sem=T.sem["loc"])
+                tot += len(topo.engines(core, d))
     if tot:
         g.wait_ge(T.sem["loc"], tot)
 
@@ -154,6 +157,8 @@ def clash(a, b):
         return True
     if a[2] <= b[1] or b[2] <= a[1]:
         return False
+    if len(a) > 4 and len(b) > 4:
+        return any(x[0] < y[1] and y[0] < x[1] for x in a[6] for y in b[6])
     if a[3] == b[3] and a[3] > 1 and (a[1] - b[1]) % a[3]:
         return False
     return True
@@ -211,11 +216,12 @@ def rank_program(g, core, T, topo):
     def R(name, lo=0, hi=None, step=1):
         return (name, lo, SIZE[name][0] if hi is None else hi, step)
 
-    def R3(name, w0, w1, lo, hi):
+    def R3(name, w0, w1, lo, hi, step=1):
         k = SCRATCH[name][1][2]
         if w1 is None:
-            return (name, k * w0 + lo, k * w0 + hi, 1, (slice(None), w0, slice(lo, hi)), hi - lo)
-        return (name, k * w0 + lo, k * (w1 - 1) + hi, 1, (slice(None), slice(w0, w1), slice(lo, hi)), (w1 - w0) * (hi - lo))
+            return (name, k * w0 + lo, k * w0 + hi, 1, (slice(None), w0, slice(lo, hi)), hi - lo, [(k * w0 + lo, k * w0 + hi)])
+        return (name, k * w0 + lo, k * (w1 - 1) + hi, 1, (slice(None), slice(w0, w1), slice(lo, hi, step) if step > 1 else slice(lo, hi)),
+                (w1 - w0) * -(-(hi - lo) // step), [(k * w + lo, k * w + hi) for w in range(w0, w1)])
 
     def num(r):
         return r[5] if len(r) > 4 else -(-(r[2] - r[1]) // r[3])
@@ -264,15 +270,18 @@ def rank_program(g, core, T, topo):
 
     def gather(e, o, win, off):
         f = lambda: A(win).indirect(A(off))
-        d = 0.06 + num(o) * CY * 1.5
-        return add(e, {"v": d, "a": d + 0.03}, [o], [win, off], lambda e: g.vector.tensor_copy(A(o), f()) if e == "v" else
+        d = 0.06 + num(o) * CY * GA
+        return add(e, {"v": d, "a": d + 0.015}, [o], [win, off], lambda e: g.vector.tensor_copy(A(o), f()) if e == "v" else
                    g.scalar.activation(A(o), f(), AF.Copy), ga=num(o))
 
-    def gts(o, win, off, s1, op0, s2=None, op1=None):
-        return add("v", 0.06 + num(o) * CY * 1.5, [o], [win, off], lambda: tsf(A(o), A(win).indirect(A(off)), s1, op0, s2, op1), ga=num(o))
+    def glin(o, win, off, k, c):
+        f = lambda: A(win).indirect(A(off))
+        d = 0.06 + num(o) * CY * GA
+        return add("va", {"v": d, "a": d + 0.015}, [o], [win, off], lambda e: g.vector.tensor_scalar(A(o), f(), k, c, OP.mult, OP.add)
+                   if e == "v" else g.scalar.activation(A(o), f(), AF.Identity, bias=c, scale=k), ga=num(o))
 
     def gtt(o, win, off, j):
-        return add("v", 0.06 + num(o) * CY * 1.5, [o], [win, off, j],
+        return add("v", 0.06 + num(o) * CY * GA, [o], [win, off, j],
                    lambda: g.vector.tensor_tensor(A(o), A(win).indirect(A(off)), A(j), OP.subtract), ga=num(o))
 
     def mms(lst):
@@ -304,22 +313,24 @@ def rank_program(g, core, T, topo):
 
     ndma = [0]
 
-    def dma(e, w, r, out, in_, dur=2.0):
+    def dma(e, w, r, out, in_, dur=2.0, behind=()):
         s = "d%d" % ndma[0]; ndma[0] += 1
-        return add(e, 0.1, w, r, lambda: eng[e].dma_start(out, in_), sem=s, inc=16, lat=dur)
+        i = add(e, 0.1, [], r, lambda: eng[e].dma_start(out, in_).then_inc(T.sem[s], 16), sem="loc", inc=0, after=behind)
+        add(None, 0.0, w, r, None, sem=s, inc=16, after=[i], lat=dur)
+        return i
 
     def iota(o, pattern, base, cm, ints=False):
         return add("g", 0.15 + num(o) * 2 * CY, [o], [], (lambda: g.iota(A(o), pattern, base, cm)) if ints else
                    (lambda: g.iota(A(o), pattern, base, cm, allow_small_or_imprecise_dtypes=True)))
 
-    dma("s", [R("XT", 0, W)], [], T.XT[:, 0:W], T.xv[:, :], 6.0)
-    dma("a", [R("wni")], [], T.wni[0:8, :], T.wn[:, :])
-    dma("a", [R("thi")], [], T.thi[0:8, :], T.th[:, :])
-    dma("a", [R("wli")], [], T.wli[:, :], T.wl[:, :], 2.5)
-    dma("s", [R("wti")], [], T.wti[:, :], T.wt[:, :])
+    x = dma("s", [R("wni")], [], T.wni[0:8, :], T.wn[:, :])
+    dma("s", [R("XT", 0, W)], [], T.XT[:, 0:W], T.xv[:, :], XLOAD, [x])
+    x = dma("a", [R("wli")], [], T.wli[:, :], T.wl[:, :], 2.5)
+    x = dma("a", [R("thi")], [], T.thi[0:8, :], T.th[:, :], 2.0, [x])
+    dma("a", [R("wti")], [], T.wti[:, :], T.wt[:, :], 2.0, [x])
     col = lambda i: R("cols", i, i + 1)
     ci = lambda i: R("ci", i, i + 1)
-    LA, LB, THR, TH, TN, WC, L32 = [col(i) for i in range(7)]
+    LA, LB, THR, TH, TN, WC, L32, LV = [col(i) for i in range(8)]
 
     def select(o, i, pattern, op, fill, base, cm=1):
         return add("g", 0.17 + num(o) * 2 * CY, [o], [i], lambda: g.affine_select(A(o), A(i), pattern, op, float(fill), base, cm))
@@ -334,21 +345,24 @@ def rank_program(g, core, T, topo):
     add("v", 0.1, [R("wnf", NW, NW + 1)], [R("thi")], lambda: g.vector.tensor_copy(A(R("wnf", NW, NW + 1), 8), A(R("thi"), 8)))
     bn = bank(NW + 1)
     add("p", 0.4, [bn], [R("E8"), R("wnf")], lambda: g.tensor.matmul(A(bn), A(R("E8"), 8), A(R("wnf"), 8), True, True))
-    for h, k in ((0, LA), (1, LB)):
-        ts(R("NLi", h, 2 * NW, 2), R(bn[0], 0, NW), k, OP.is_le, float(DEAD), OP.mult)
-    ts(THR, R(bn[0], NW, NW + 1), 0.5, OP.mult)
-    ts(TH, THR, 0.25, OP.add, 400.0, OP.mult); ts(TN, TH, -1.0, OP.mult)
-    tt(R("NLf"), R("NLi"), R("wli"), OP.max)
-    ts(R("IN"), R("NLf"), float(-HALF), OP.add)
-    add("v", 8 * 0.085, [R("OT")], [R("IN")],
-        lambda: [g.vector.transpose(A(R3("OT", w, None, 0, P)), A(R("IN", P * w, P * w + P))) for w in range(8)], inc=8)
     for x in range(4):
         pick(R("PM%d" % x), [[-32, 4], [1000, 2], [-2, 16]], -(x % 2) - 1000 * (x // 2))
-    mms([(R3("psz", 0, 8, 16 * y, 16 * y + 16), R("PM%d" % (2 * x + y)), R3("OT", 0, 8, 16 * x, 16 * x + 16), x == 0, x == 1)
-         for y in (0, 1) for x in (0, 1)])
     for b in range(NBK):
+        cur["plus"] = FIRST if b == 0 else 0.0
+        x, y = L * b, L * b + L
+        ts(R("IM", x, y), R("wli", x, y), float(-HALF), OP.add)
+        add("v", 2 * dv(R(bn[0], 0, NB)), [R("NLi", x, y)], [bn, LA, LB], lambda x=x, y=y, b=b: [g.vector.tensor_scalar(
+            A(R("NLi", x + h, y, 2)), A(R(bn[0], NB * b, NB * b + NB)), A(k), float(DEAD), OP.is_le, OP.mult) for h, k in ((0, LA), (1, LB))], inc=2)
+        tt(R("IN", x, y), R("NLi", x, y), R("IM", x, y), OP.add)
+        add("v", NX * 0.07, [R3("OT", NX * b, NX * b + NX, 0, P)], [R("IN", x, y)], lambda b=b: [
+            g.vector.transpose(A(R3("OT", w, None, 0, P)), A(R("IN", P * w, P * w + P))) for w in range(NX * b, NX * b + NX)], inc=NX)
+        mms([(R3("psz", NX * b, NX * b + NX, 16 * i, 16 * i + 16), R("PM%d" % (2 * j + i)), R3("OT", NX * b, NX * b + NX, 16 * j, 16 * j + 16),
+              j == 0, j == 1) for i in (0, 1) for j in (0, 1)])
         z = R3("psz", NX * b, NX * b + NX, 0, P)
-        ts(R("nm", L * b, L * b + L), z, float(HALF), OP.add); lin(R("NF", L * b, L * b + L), z, 1.0, float(HALF))
+        ts(R("nm", x, y), z, float(HALF), OP.add, float(DEAD), OP.min); lin(R("NF", x, y), z, 1.0, float(HALF))
+    cur["plus"] = 0.0
+    ts(THR, R(bn[0], NW, NW + 1), 0.5, OP.mult)
+    ts(TH, THR, 0.25, OP.add, 400.0, OP.mult); ts(TN, TH, -1.0, OP.mult)
     mset(R("XT", W, W + 16), 255.0)
     for n, k in (("ID", 1), ("NEG", -1), ("N8", -8192), ("N15", -1584), ("JM", REG - 15), ("W0", 1 - LS), ("W1", -LS),
                  ("W2", -2 * LS), ("W3", 4 * LS)):
@@ -360,22 +374,23 @@ def rank_program(g, core, T, topo):
     ts(R("WW", 15, 144, 16), R("EW", 15, 144, 16), WC, OP.mult)
     for n, k in (("K0", 0.0), ("PAT", 1.0), ("TWO", 2.0), ("MQ", -0.25), ("CK", 167.0 / 32), ("VP", 0.0)):
         mset(R(n), k)
-    mset(R("K0", 0, L, P), 16384.0); mset(R("PAT", 0, L, P), 0.0); mset(R("VP", 7, 8 * NX, 8), 8.0 * LS)
+    mset(R("K0", 0, L, P), 16384.0); mset(R("PAT", 0, L, P), 0.0); mset(R("VP", 3, 2 * P, 4), 8.0 * LS)
     for b in range(NBK):
         mset(R("V%d" % b, 0, 16), 0.0)
-        mset(R("WN%d" % b, 2 * REG), float(DEAD - HALF))
+        mset(R("WN%d" % b, 3 * REG), float(DEAD - HALF))
     mset(R("AC", 0, 1), -0.375)
     for x in range(0, 16, 4):
         pick(R("SEL", 128 * x, 128 * x + 512), [[-1, 4], [-16, 8], [0, 16]], -x)
     iota(R("RA"), [[16, L]], 0, 0); ts(R("RAMP"), R("RA"), LA, OP.add)
-    iota(R("BW"), [[P, NX], [0, 8], [L, 2]], 0, 0); iota(R("YI"), [[1, 56]], 0, 0); iota(R("W5"), [[512, 8]], 0, 0)
+    iota(R("BW"), [[0, 8], [NB, 2], [16, NX]], 0, 0); iota(R("YI"), [[1, 56]], 0, 0); iota(R("W5"), [[512, 8]], 0, 0)
     ts(L32, LA, 32.0, OP.mult); ts(R("W32"), R("W5"), L32, OP.add)
     for x in range(0, 16, 4):
         pick(R("DR", 144 * x, 144 * x + 576), [[-1, 4], [-16, 9], [1000, 16]], 16 - x - 15000)
     select(R("DR", 15, None, 144), R("DR", 15, None, 144), [[-1, 16]], OP.not_equal, 1, -112)
     for x in range(4):
         pick(R("XM%d" % x), [[-16, 8], [1000, 2], [-2, 8]], -(x % 2) - 1000 * (x // 2))
-    ts(R("VY"), R("YI"), LA, OP.is_le)
+    ts(LV, LA, 0.5, OP.add, 200.0, OP.mult)
+    add("a", 1.5, [R("VY")], [R("YI"), LV], lambda: g.scalar.activation(A(R("VY")), A(R("YI")), AF.Sigmoid, bias=A(LV), scale=-200.0))
     for part in range(2):
         b0 = bank(8 * LS); l = []
         for j in range(8):
@@ -388,60 +403,63 @@ def rank_program(g, core, T, topo):
     nloc = [0]
     win = lambda name, r: R(name, 15 - r, 143 - r)
 
-    def transmit(k, t, b, srcs):
-        todo = []
-        for h in (0, 1):
-            d = target(rank, nr, t, h)
-            if d != rank:
-                via = relay_of(topo, core, T.cores[d], b)
-                todo.append((h, T.cores[d] if via is None else via, via))
-                nloc[0] += len(engines(topo, core, todo[-1][1], k))
-        for part in ([todo] if k < 2 else [[x] for x in todo]):
-            sent[:] = [add("g", 1.0, [], [srcs[h] for h, _, _ in part], lambda part=part: g.remote_dma_fused(
-                [transfer(T, topo, core, to, A(srcs[h]), landing(T, k, t, b, h), k, "m%d%d%d%d" % (k, t, b, h)) for h, to, _ in part],
+    def transmit(k, t, b):
+        for ws in [ws for j, ws in calls(t, b) if j == k]:
+            ws = [x + leg(topo, core, T.cores[target(rank, nr, t, x[0])], t, b, k) for x in ws]
+            nloc[0] += sum(len(x[5]) for x in ws)
+            sent[:] = [add("g", CALL if sent else ONCE, [], [R3("MS", x[1], x[1] + x[3], 0, P) for x in ws], lambda ws=ws: g.remote_dma_fused(
+                [transfer(T, topo, core, to, T.MS[:, s:s + m, :], T.MR[:, r:r + m, :], e, "m%d%d%d%d" % (k, t, b, h)) for h, s, r, m, to, e in ws],
                 local_sem=T.sem["loc"]), sem="loc", inc=0, after=sent[:1] if k else [])]
-            for h, to, via in part:
-                src = [q for q in range(nr) if target(q, nr, t, h) == rank][0]
-                v2 = relay_of(topo, T.cores[src], core, b)
-                o = R("cr%d%d%d" % (h, t, b)) if k == 0 else names(t, b, k - 1, h)
-                add(None, 0.0, [o], [], None, sem="m%d%d%d%d" % (k, t, b, h), after=sent[:1], lat=HOP1 if via is None else HOP2,
-                    inc=len(engines(topo, T.cores[src] if v2 is None else v2, core, k)))
+            for h, _, r, m, _, _ in ws:
+                src = T.cores[[q for q in range(nr) if target(q, nr, t, h) == rank][0]]
+                to = leg(topo, src, core, t, b, k)[0]
+                last, more = sent[:1], (0.0 if k == 2 else WIDE)
+                if to != core:
+                    last = [add(None, 0.0, [], [], None, sem="loc", inc=0, after=last, lat=HOP0 + more)]
+                    last = [add(str(b % 2), CALL if t or k else ONCE, [], [], None, sem="loc", inc=0, after=last)]
+                last = [add("2", PORT * m / NX, [], [], None, sem="loc", inc=0, after=last)]
+                kind[len(nodes)] = k
+                add(None, 0.0, [R3("MR", r, r + m, 0, P)], [], None, sem="m%d%d%d%d" % (k, t, b, h), after=last, lat=HOP1 + more,
+                    inc=len(topo.engines(src if to == core else to, core)))
 
-    sent = []
+    sent, pad, kind = [], {}, {}
 
-    def names(t, b, e, h):
-        n, x = ("MS", slot(t, b, 0) // 2) if target(rank, nr, t, h) == rank else ("MR", slot(t, b, h))
-        return R(n, x + L * e, x + L * e + L)
+    def rows(n, t, b, first, m, lo=0, hi=P):
+        x = MROWS * (t * NBK + b) + first
+        return R3(n, x, x + m, lo, hi)
 
-    def put_names(e, t, b, x):
-        y, k = R("n%d%d" % (e, b)), slot(t, b, 0) // 2 + L * e
-        ts(y, x, W - 1, OP.bitwise_and)
-        ts(R("MS", k, k + L), y, float(-HALF), OP.add)
-        transmit(1 + e, t, b, [R("MS", k, k + L)] * 2)
+    def put_names(e, t, b, x, lo=0, hi=P):
+        n, u = "n%d%d" % (e, b), NX // 2
+        ts(R3(n, 0, NX, lo, hi), x, W - 1, OP.bitwise_and)
+        if t == RO - 1 and hi == P:
+            ts(rows("MS", t, b, S_UP + u * e, u), R3(n, 0, NX, 16, P), float(-HALF), OP.add)
+            transmit(1 + e, t, b)
+        ts(rows("MS", t, b, S_N + NX * e, NX, lo, hi), R3(n, 0, NX, lo, hi), float(-HALF), OP.add)
+        if t < RO - 1:
+            transmit(1 + e, t, b)
 
     def join(t, b):
         s = str(b)
-        own = ("cr0%d%d" if t < RO - 1 else "cs%d%d") % (t, b)
-        over = "cr1%d%d" % (t, b)
+        n, x, z = ("MR", R_OWN, R_N) if t < RO - 1 else ("MS", S_OWN, S_N)
+        copy(R3("IX" + s, 0, NX, 8, 16), rows(n, t, b, x, 1))
         f = bank(8 * NX)
-        acc(f, [(R("W%d" % i), R(own, i, L, 4)) for i in range(4)] + [(R("ID"), R("VP"))])
-        copy(R3("IX" + s, 0, NX, 8, 16), f)
-        f = bank(8 * NX)
-        acc(f, [(R("W%d" % i), R(over, i, L, 4)) for i in range(4)] +
-            [(R("ID"), R(own, P - 1, L, P), R(f[0], c, 8 * NX, 8)) for c in range(4, 8)] + [(R("ID"), R("VP"))])
+        acc(f, [(R("ID"), rows("MR", t, b, R_OVER, 1)), (R("ID"), rows(n, t, b, x + 1, 1))])
         copy(R3("IX" + s, 0, NX, 0, 8), f)
         for w in range(NX):
-            gather("va", R3("G" + s, w, None, 0, 192), R("LUT"), R3("IX" + s, w, None, 4, 16))
+            gather("va", R("G" + s, w, None, NX), R("LUT"), R3("IX" + s, w, None, 4, 16))
         f = bank(NB)
-        acc(f, [(R("ID"), R3("G" + s, 0, NX, 16 * c, 16 * c + 16)) for c in range(12)] + [(R("ID"), R("BW"))])
-        add("v", NX * (FV + 16 * CY), [R("of" + s)], [f], lambda f=f: [
-            g.vector.tensor_copy(A(R("of" + s, w, NB, NX)), A(R(f[0], 16 * w, 16 * w + 16))) for w in range(NX)], inc=NX)
+        acc(f, [(R("ID"), R("G" + s, NB * c, NB * c + NB)) for c in range(12)] + [(R("ID"), R("BW"))])
+        copy(R("of" + s), f)
         if t == RO - 1:
-            mset(R("WN" + s, 2 * REG + 16, 3 * REG, P), float(-HALF))
-        for h in (1, 0):
-            f = bank(REG)
-            mms([(R(f[0], L * y, L * y + L), R("XM%d" % (2 * e + y)), names(t, b, e, h), e == 0, e == 1) for y in (0, 1) for e in (0, 1)])
-            copy(R("WN" + s, REG * h, REG * h + REG), f, "va")
+            mset(R("WN" + s, 3 * REG, 4 * REG, 16), float(-HALF))
+        f = bank(REG)
+        mms([(R(f[0], NB * y, NB * y + NB), R("XM%d" % (2 * e + y)), rows("MR", t, b, R_UP + NX * e, NX, 16, P) if t < RO - 1 else
+              rows("MR", t, b, R_UP + NX // 2 * e, NX // 2), e == 0, e == 1) for y in (0, 1) for e in (0, 1)])
+        copy(R("WN" + s, 2 * REG, 3 * REG), f, "va")
+        f = bank(2 * REG)
+        mms([(R(f[0], REG * h + NB * y, REG * h + NB * y + NB), R("XM%d" % (2 * e + y)), rows(n, t, b, z + NX * e, NX, 16 * h, 16 * h + 16),
+              e == 0, e == 1) for h in (0, 1) for y in (0, 1) for e in (0, 1)])
+        copy(R("WN" + s, 0, 2 * REG), f, "va")
         f = bank(L)
         for y in range(0, 16, 4):
             gather("v", R("N" + s, NB * y, NB * y + 4 * NB), R("WN" + s), R("of" + s, NX * y, NX * y + 4 * NX))
@@ -451,7 +469,7 @@ def rank_program(g, core, T, topo):
         return f
 
     def step(o, i, k, more):
-        return add("va", {"v": dv(o, i), "a": da(o)}, [o], [i, TH, TN, THR],
+        return add("va", {"v": dv(o, i), "a": da(o)}, [o], [i, TH, TN, THR, R("VY")],
                    lambda e: g.vector.tensor_scalar(A(o), A(i), k, A(THR), OP.mult, OP.is_gt if more else OP.is_le) if e == "v" else
                    g.scalar.activation(A(o), A(i), AF.Sigmoid, bias=A(TN if more else TH), scale=(400.0 if more else -400.0) * k))
 
@@ -481,12 +499,20 @@ def rank_program(g, core, T, topo):
                     A(R(f[0], x, 128, 16), L), A(R("V" + s, 16 + x, 16 + ROWS, 16)), A(R("EW", 15, 143, 16)), True, True) for x in range(16)][-1])
                 add("va", {"v": dv(f), "a": da(f)}, [r("S")], [f], lambda e, f=f, s=s: g.vector.tensor_copy(A(R("S" + s), L), A(f, L))
                     if e == "v" else g.scalar.activation(A(R("S" + s), L), A(f, L), AF.Copy))
+                f = bank(128) if MT else None
                 for y in range(0, 16, 4):
                     scans([(r("M", L * x, L * x + L), r("V", x, ROWS, 16), r("V", 16 + x, 16 + ROWS, 16)) for x in range(y, y + 4)], 256.0, OP.min, OP.max)
-                    acc(D, [(win("EW", x), r("M", L * x, L * x + L)) for x in range(y, y + 4)], y == 0, False)
-                add("p", 0.05 + 2 * L * PE, [D], [r("S"), R("SH"), R("ID"), R("K0")], lambda D=D, s=s: [
-                    g.tensor.matmul(A(D), A(R("S" + s), L), A(R("SH", 0, L), L), False, False),
-                    g.tensor.matmul(A(D), A(R("ID")), A(R("K0")), False, True)][-1])
+                    if MT:
+                        add("p", 0.05 + 256 * PE, [f], [r("M", L * y, L * y + 4 * L), R("EW")], lambda f=f, s=s, y=y: [g.tensor.matmul(
+                            A(R(f[0], x, 128, 16)), A(R("M" + s, L * x, L * x + L)), A(R("EW", 15, 143, 16)), True, True) for x in range(y, y + 4)][-1])
+                    else:
+                        acc(D, [(win("EW", x), r("M", L * x, L * x + L)) for x in range(y, y + 4)], y == 0, False)
+                if MT:
+                    acc(D, [(r("S"), R("SH")), (R("ID"), R("K0"))], True, False)
+                    copy(r("S2"), f, "va")
+                    acc(D, [(r("S2"), R("ID"))], False)
+                else:
+                    acc(D, [(r("S"), R("SH")), (R("ID"), R("K0"))], False)
             half = 0.5 if DIFF[b] else 1.0
             step(r("C"), D, half, False)
             step(r("E", 0, L - 1), R(D[0], 1, L), half, True)
@@ -503,17 +529,20 @@ def rank_program(g, core, T, topo):
                 scans([(r("Z", x, ROWS, 16), R(n, L * (x - y), L * (x - y + 1)), r("V", 16 + x, 16 + ROWS, 16)) for x in range(y, y + per)],
                       0.0, OP.mult, OP.max)
                 acc(fu, [(win("WW", x), r("Z", x, ROWS, 16)) for x in range(y, y + per)], y == 0, y + per == 16)
-            cs, ct = R("cs%d%d" % (t, b)), R("ct%d%d" % (t, b))
-            scans([(cs, R("PAT"), r("E"))], 0.0, OP.mult, OP.add)
-            add("va", {"v": dv(ct, cs), "a": da(ct)}, [ct], [cs], lambda e, o=ct, i=cs: g.vector.tensor_scalar(A(o), A(i), -16.0, 0.0, OP.add, OP.max)
-                if e == "v" else g.scalar.activation(A(o), A(i), AF.Relu, bias=-16.0))
-            transmit(0, t, b, [cs, ct])
+            scans([(r("cs", L), R("PAT"), r("E"))], 0.0, OP.mult, OP.add)
+            act(r("cs", 0, L), r("cs", L), AF.Relu, -16.0)
+            f = bank(3 * P)
+            acc(f, [(R("ID"), R("VP"))] + [(R("ID"), r("cs", L + P - 1, None, P), R(f[0], 2 * P + c, 3 * P, 8)) for c in range(4, 8)] +
+                [(R("W%d" % i), r("cs", i, None, 4), R(f[0], 0, 2 * P)) for i in range(4)])
+            copy(rows("MS", t, b, S_OVER, 3), f)
+            transmit(0, t, b)
             scans([(r("cm"), r("C"), R("TWO"))], 0.0, OP.mult, OP.add)
-            lin(r("c2"), r("cm"), 1.0, 1.0)
+            c2, hm = R3("c2" + s, 0, NX, 0, P), R3("hm" + s, 0, NX, 0, P)
+            lin(c2, r("cm"), 1.0, 1.0)
             f = bank(L)
             acc(f, [(R("IDF"), nf), (R("N8"), r("C"))])
-            scans([(r("a"), r("C"), f)], 0.0, OP.mult, OP.max)
-            tt(r("na"), r("a"), r("c2"), OP.mult)
+            scans([(R(f[0], L, 2 * L), r("C"), f)], 0.0, OP.mult, OP.max)
+            tt(r("na"), R(f[0], L, 2 * L), c2, OP.mult)
             ts(r("ni"), r("na"), 0.25, OP.mult, R("AC", t, t + 1), OP.add)
             put_names(0, t, b, r("ni"))
             f = bank(L)
@@ -521,7 +550,7 @@ def rank_program(g, core, T, topo):
             scans([(r("y"), R("K0"), f)], 0.0, OP.add, OP.min)
             ts(r("zo"), r("y", P - 1, L, P), 8192.0, OP.add, float(ROWS - 1), OP.min)
             ts(R("iv", NX * b, NX * b + NX), r("y", P - 1, L, P), 0.0, OP.is_ge, float(W + 16), OP.mult)
-            gts(R("ZF", NB * b, NB * b + NB), r("Z"), r("zo"), -192.0, OP.add)
+            glin(R("ZF", NB * b, NB * b + NB), r("Z"), r("zo"), 1.0, -192.0)
             f = fu
             if USC:
                 lin(r("r"), f, -1.0, HALF - 0.5 - MAGIC)
@@ -535,34 +564,51 @@ def rank_program(g, core, T, topo):
             f = bank(L)
             acc(f, [(R("N8"), r("cm")), (R("N15"), r("cm")), (R("N8"), R("CK"))])
             tt(r("si"), r("sq"), f, OP.subtract)
-            ts(r("hm"), r("si"), 5, OP.arith_shift_right, W - 1, OP.bitwise_and)
-            copy(r("hu"), r("hm"))
-            fd = bank(L)
-            for w in range(NX):
-                o, off, z = r("D2", CH * w, CH * w + CH), r("hu", P * w, P * w + P), r("Z", CH * w, CH * w + CH)
-                if w < XA[b]:
+            ts(hm, r("si"), 5, OP.arith_shift_right, W - 1, OP.bitwise_and)
+            copy(r("hu"), hm)
+            xa = XA[t][b]
+
+            def distance(w, lo, hi):
+                o, z = r("D2", CH * w + lo, CH * w + hi), r("Z", CH * w + lo, CH * w + hi)
+                off = r("hu", P * w + lo // 16, P * w + hi // 16)
+                if w < xa:
                     gather("a", o, R("XT", 0, W), off)
-                    f = bank(CH)
+                    f = bank(hi - lo)
                     acc(f, [(R("NEG"), z), (R("ID"), o)])
-                    act(r("AD", CH * w, CH * w + CH), f, AF.Abs)
+                    act(R3("AD" + s, w, None, lo, hi), f, AF.Abs)
                 else:
                     gtt(o, R("XT", 0, W), off, z)
-                    act(r("AD", CH * w, CH * w + CH), o, AF.Abs)
-                if w % 2:
-                    acc(R(fd[0], P * w - P, P * w + P), [(win("EW", x), r("AD", CH * w - CH + x, CH * w + CH, 16)) for x in range(16)])
-            x, y = NB * b, NB * b + 16 * XA[b]
-            if XA[b]:
-                gtt(R("e1", x, y), r("D2"), r("zo", 0, XA[b]), R("ZF", x, y))
-                ts(R("e2", x, y), R("e1", x, y), 0.5, OP.mult, 95.75, OP.add)
-            if XA[b] < NX:
-                gts(R("e2", y, x + NB), r("D2"), r("zo", XA[b]), 0.5, OP.mult, 191.75, OP.add)
-            tt(r("nc"), fd, r("c2"), OP.mult)
-            tt(r("nj"), r("nc"), r("hm"), OP.add)
-            put_names(1, t, b, r("nj"))
+                    act(R3("AD" + s, w, None, lo, hi), o, AF.Abs)
+
+            if t < RO - 1:
+                fd = bank(L)
+                for w in range(NX):
+                    distance(w, 0, CH)
+                    if w % 2:
+                        acc(R(fd[0], P * w - P, P * w + P), [(win("EW", x), R3("AD" + s, w - 1, w + 1, x, CH, 16)) for x in range(16)])
+                tt(fd, fd, c2, OP.mult)
+                tt(r("nj"), fd, hm, OP.add)
+                put_names(1, t, b, r("nj"))
+            else:
+                y = L // 2
+                for h in (1, 0):
+                    fd = bank(y)
+                    for w in range(NX):
+                        distance(w, CH // 2 * h, CH // 2 * (h + 1))
+                    acc(fd, [(win("EW", x), R3("AD" + s, 0, NX, CH // 2 * h + x, CH // 2 * (h + 1), 16)) for x in range(16)])
+                    tt(fd, fd, R3("c2" + s, 0, NX, 16 * h, 16 * h + 16), OP.mult)
+                    tt(r("nj", y * h, y * h + y), fd, R3("hm" + s, 0, NX, 16 * h, 16 * h + 16), OP.add)
+                    put_names(1, t, b, r("nj", y * h, y * h + y), 16 * h, 16 * h + 16)
+            x, y = NB * b, NB * b + 16 * xa
+            if xa:
+                gtt(R("e1", x, y), r("D2"), r("zo", 0, xa), R("ZF", x, y))
+                lin(R("e2", x, y), R("e1", x, y), 0.5, 95.75)
+            if xa < NX:
+                glin(R("e2", y, x + NB), r("D2"), r("zo", xa), 0.5, 191.75)
         cur["plus"] = 0.0
         if t < RO - 1:
             f = bank(1)
-            acc(f, [(R("ONE"), R("cs%d%d" % (t, b), x, x + 1)) for b in range(NBK) for x in range(P - 1, L, P)])
+            acc(f, [(R("ONE"), R("cs%d" % b, x, x + 1)) for b in range(NBK) for x in range(L + P - 1, 2 * L, P)])
             copy(R("ATi"), f)
             ts(R("ATj"), R("ATi"), 255, OP.bitwise_and); ts(R("AC", t + 1, t + 2), R("ATj"), -0.375, OP.add)
         f = bank(8)
@@ -572,10 +618,15 @@ def rank_program(g, core, T, topo):
         add("v", 0.07 + NW * CY * 3.5, [R("XT")], [R("ZF"), R("e2"), R("WL")],
             lambda: g.vector.tensor_tensor(A(R("XT")).indirect(A(R("WL"))), A(R("ZF")), A(R("e2")), OP.add))
     for q in range(4):
-        f = bank(512)
-        acc(f, [(R("ID"), R("XT", 1024 * q + e, 1024 * q + 1024, 2)) for e in (0, 1)])
-        copy(R("YX", 512 * q, 512 * q + 512), f, "va")
-    dma("s", [("yx", 0, 1, 1)], [R("YX")], T.yx[:, :], T.YX[:, :])
+        if q in YV:
+            tt(R("YX", 512 * q, 512 * q + 512), R("XT", 1024 * q, 1024 * q + 1024, 2), R("XT", 1024 * q + 1, 1024 * q + 1024, 2), OP.add)
+        else:
+            f = bank(512)
+            acc(f, [(R("ID"), R("XT", 1024 * q + e, 1024 * q + 1024, 2)) for e in (0, 1)])
+            copy(R("YX", 512 * q, 512 * q + 512), f, "va")
+        if q % 2:
+            dma("s", [("yx", q, q + 1, 1)], [R("YX", 512 * q - 512, 512 * q + 512)], T.yx[:, 512 * q - 512:512 * q + 512],
+                T.YX[:, 512 * q - 512:512 * q + 512], 3.0)
     for x in range(4):
         pat, base = [[-32, 4], [-1, 16], [1000, 2]], -16 * (x // 2) - 16 - 1000 * (x % 2)
         pick(R("QM%d" % x), pat, base)
@@ -585,8 +636,12 @@ def rank_program(g, core, T, topo):
     for b in range(NBK):
         s = str(b)
         cur["plus"] = FIRST if b == 0 else 0.0
-        tt(R("k1", NX * b, NX * b + NX), R("cs%d%d" % (t, b), P - 1, L, P), R("cr1%d%d" % (t, b), P - 1, L, P), OP.add)
         f = join(t, b)
+        ts(R("lv" + s), R("of" + s), float(3 * REG), OP.is_lt, 2.0, OP.mult)
+        z = bank(NB)
+        add("p", 0.2, [z], [R("EW"), R("lv" + s)], lambda z=z, s=s: [g.tensor.matmul(
+            A(R(z[0], 16 * w, 16 * w + 16), 8), A(R("EW", 15, 143, 16)), A(R("lv" + s, w, NB, NX)), True, True) for w in range(NX)][-1])
+        add("v", 0.1, [R("yno", NB * b, NB * b + NB)], [z], lambda z=z, b=b: g.vector.tensor_copy(A(R("yno", NB * b, NB * b + NB), 8), A(z, 8)))
         ts(R3("NB" + s, 0, NX, 0, P), f, float(-HALF), OP.add)
         l = []
         for x in (0, 1):
@@ -598,11 +653,6 @@ def rank_program(g, core, T, topo):
             g.vector.transpose(A(R("yl" + s, P * w, P * w + P)), A(R3("psz", NX * b + w, None, 0, P))) for w in range(NX)], inc=NX)
         dma("s" if b else "a", [("yl", b, b + 1, 1)], [R("yl" + s)], T.yl[:, L * b:L * b + L], T["yl" + s][:, :])
     cur["plus"] = 0.0
-    ts(R("k3"), R("k1"), 16.0, OP.min, 2.0, OP.mult)
-    f = bank(NW)
-    add("p", 0.8, [f], [R("SEL"), R("k3")], lambda f=f: [g.tensor.matmul(A(R(f[0], x, NW, 16), 8), A(R("SEL", 128 * x, 128 * x + 128, 16)),
-                                                                      A(R("k3")), True, True) for x in range(16)][-1])
-    add("v", 0.2, [R("yno")], [f], lambda f=f: g.vector.tensor_copy(A(R("yno"), 8), A(f, 8)))
     dma("s", [("yn", 0, 1, 1)], [R("yno")], T.yn[:, :], T.yno[0:8, :])
 
     n = len(nodes)
@@ -614,11 +664,10 @@ def rank_program(g, core, T, topo):
     for i in range(n - 1, -1, -1):
         x = nodes[i]
         prio[i] = (min(x["d"].values()) if x["e"] == "va" else x["d"][x["e"]] if x["e"] else 0.0) + x["lat"] + LINK + max([prio[k] for k in users[i]] + [0.0])
-    for i in range(n):
-        prio[i] += nodes[i]["plus"]
-    free = {"v": 0.0, "a": 0.0, "p": 0.0, "g": 0.0, "s": 0.0}
+    free = {k: 0.0 for k in "vapgs012"}
+    gap = lambda a, b: LINK if a != b else 0.0 if a == "p" else SAME
 
-    def sweep(urgency, back, on):
+    def sweep(urgency, back, on, urge=0.03, vpen=0.3):
         before, after = (users, [x["deps"] for x in nodes]) if back else ([x["deps"] for x in nodes], users)
         left = [len(x) for x in before]
         ready_at, at, fin, took, more = [0.0] * n, [0.0] * n, [0.0] * n, [None] * n, [[] for _ in range(n)]
@@ -633,7 +682,8 @@ def rank_program(g, core, T, topo):
 
         def done(i):
             for k in after[i]:
-                ready_at[k] = max(ready_at[k], fin[i] + (0.0 if on[i] == on[k] == "p" else LINK) + nodes[k if back else i]["lat"])
+                ready_at[k] = max(ready_at[k], fin[i] + gap(took[i], on[k]) + nodes[k if back else i]["lat"]
+                                  + (0.0 if back else pad.get(i, 0.0)))
                 left[k] -= 1
                 if left[k] == 0:
                     release(k)
@@ -659,7 +709,7 @@ def rank_program(g, core, T, topo):
                         if not fr:
                             continue
                         st = max(st, min(fr))
-                    key = (st + (VPEN if len(on[k]) > 1 and e == "v" else 0.0) - URGE * urgency[k], -urgency[k])
+                    key = (st + (vpen if len(on[k]) > 1 and e == "v" else 0.0) - urge * urgency[k], -urgency[k])
                     if best is None or key < best[0]:
                         best = (key, e, k, st)
             _, e, k, st = best
@@ -682,12 +732,26 @@ def rank_program(g, core, T, topo):
             done(k)
         return max(fin[i] + nodes[i]["lat"] for i in range(n)), order, took, at, fin, banks, more
 
+    def again(res, slow):
+        fin, busy = [0.0] * n, dict(free)
+        for i in sorted(range(n), key=lambda i: (res[3][i], i)):
+            e = res[2][i]
+            st = max([fin[j] + gap(e, res[2][j]) for j in nodes[i]["deps"] + res[6][i]] + [busy[e] if e and e != "2" else 0.0])
+            if e:
+                busy[e] = st + nodes[i]["d"][e] * (slow if e in "2p" else 1.0)
+            fin[i] = busy[e] if e else st + nodes[i]["lat"] * (1.0 if nodes[i]["sem"][0] == "d" else slow)
+        return max(fin)
+
     kept = None
-    for _ in range(PASSES):
-        res = sweep(prio, False, [x["e"] for x in nodes])
-        if kept is None or res[0] < kept[0]:
-            kept = res
-        prio = sweep(res[4], True, res[2])[4]
+    for first, urge, vpen, wait in RULES:
+        late = [prio[i] + first * nodes[i]["plus"] for i in range(n)]
+        pad.update({i: wait[k] for i, k in kind.items()})
+        for _ in range(PASSES):
+            res = sweep(late, False, [x["e"] for x in nodes], urge, vpen)
+            both = again(res, 1.0) * WEIGHT + again(res, SLOW)
+            if kept is None or both < best:
+                kept, best = res, both
+            late = sweep(res[4], True, res[2], urge, vpen)[4]
     end, order, took, at, fin, banks, more = kept
     phys.update(banks)
     for i, x in enumerate(nodes):
@@ -708,6 +772,8 @@ def rank_program(g, core, T, topo):
     known = {k: {} for k in free}
     for k in order:
         x = nodes[k]
+        if x["e"] not in eng:
+            continue
         q = eng[x["e"]]
         need = {}
         for j in x["deps"]:

@@ -3,30 +3,36 @@ from concourse.bass import DstId, RemoteDMATransfer
 from concourse.mybir import dt, AluOpType, AxisListType, ActivationFunctionType
 
 NW, P, RO = 128, 32, 3
-NB = 64
-NBK = NW // NB
-NX = NB // 16
-L = P * NX
-ROWS = 16 * L
+NXS = (4, 4)
+NBK = len(NXS)
+W0 = [sum(NXS[:b]) for b in range(NBK)]
+LM = P * max(NXS)
 W = 4096
 DEAD = 4096
 HALF = 2048
-REG = L
-MROWS = 20
-S_OVER, S_OWN, S_N, S_UP = 0, 1, 3, 3 + 2 * NX
-R_OWN, R_N, R_OVER, R_UP = 0, 2, 2 + 2 * NX, 4 + 2 * NX
+REG = LM
+S_OVER, S_OWN, S_CNT, S_N = 0, 1, 2, 3
+MROWS = S_N + 8
 LS = 49
 CH = 512
 MAGIC = 786432.0
 AF = ActivationFunctionType
 OP = AluOpType
 
-DIFF = (0, 0)
-XA = ((2, 0), (2, 0), (2, 2))
-ZC = (3,)
-MT = 0
+XA = ((2, 2), (2, 2), (2, 2))
+ZC = ((1, 3), (1, 3))
 YV = (1,)
-USC = 1
+MERGE = 0
+LATE2 = 1
+ALT = 0
+DRG = 1
+PV = 0
+PJ = 0
+PN0 = 0
+PN1 = 0
+WHOLE = 12582912.0
+VG = "va"
+GG = "va"
 
 SCRATCH = {"psz": ("psum", [128, 16, 32], "float32")}
 NPS = 7
@@ -50,61 +56,40 @@ def _sb(name, n, dtype, own=False):
 
 _sb("XT", 2 * W + 16, "bfloat16", True); _sb("YX", 2048, "bfloat16", True)
 _sb("wli", 2 * NW, "int32", True); _sb("wni", NW, "int32", True); _sb("thi", 1, "int32", True); _sb("wti", 1, "int32", True)
-_sb("MS", (RO * NBK * MROWS, P), "float16"); _sb("MR", (RO * NBK * MROWS, P), "float16")
+_sb("MS", (RO * NBK * MROWS, P), "float16"); _sb("MR", (2 * RO * NBK * MROWS, P), "float16")
+_sb("US", (16, 16), "float16"); _sb("UR", (16, 16), "float16")
 _sb("OT", (8, P), "float16"); _sb("yno", NW, "float32", True)
-for _n, _k in (("wnf", NW + 1), ("E8", 128), ("cols", 8), ("ZF32", 128), ("YI", 56), ("RA", L), ("W5", 8), ("IDF", 128), ("NF", 2 * NW),
-               ("AC", 4), ("W32", 8), ("iv", 8), ("bs", 8), ("wf", 8)):
+for _n, _k in (("wnf", NW + 1), ("E8", 128), ("cols", 16), ("ZF32", 128), ("YI", 56), ("RA", LM), ("W5", 8), ("IDF", 128), ("NF", 2 * NW),
+               ("AC", 4), ("AB", 4), ("W32", 8), ("iv", 8), ("bs", 8), ("wf", 8), ("MK", 16), ("y", 2 * NW)):
     _sb(_n, _k, "float32")
-for _n, _k in (("ci", 2), ("ATi", 1), ("ATj", 1), ("wa", 8), ("wb", 8)):
+for _n, _k in (("ci", 3), ("ATi", 1), ("ATj", 1), ("wa", 8), ("wb", 8)):
     _sb(_n, _k, "int32")
-for _n, _k in (("ID", 128), ("NEG", 128), ("N8", 128), ("N15", 128), ("JM", 128), ("W0", 128), ("W1", 128), ("W2", 128), ("W3", 128),
-               ("ONE", 128), ("EW", 144), ("WW", 144), ("SEL", 2048), ("LUT", 16 * LS), ("VY", 56), ("K0", L), ("PAT", L), ("TWO", L),
-               ("MQ", 128), ("CK", L), ("VP", 3 * P), ("DR", 16 * 144), ("BW", NB), ("ZF", NW), ("e1", NW), ("e2", NW),
-               ("ZB", 576), ("SH", 128), ("E9", 9)):
+for _n, _k in (("ID", 128), ("NEG", 128), ("N8", 128), ("K15", 128), ("JM", 128), ("W0", 128), ("W1", 128), ("W2", 128), ("W3", 128),
+               ("ONE", 128), ("EW", 144), ("WW", 144), ("EN", 144), ("SEL", 2048), ("LUT", 16 * LS), ("VY", 56), ("K0", LM), ("PAT", LM),
+               ("TWO", LM), ("MQ", 128), ("CK", LM), ("VP", 3 * P), ("DR", 16 * 144), ("ZF", NW), ("e1", NW), ("e2", NW),
+               ("ZB", 576), ("SH", 128), ("E9", 9), ("CG", 128), ("BLK", 128)):
     _sb(_n, _k, "bfloat16")
-for _n, _k in (("RAMP", L), ("IN", 2 * NW), ("IM", 2 * NW), ("NLi", 2 * NW)):
+for _n, _k in (("N97", 128), ("RAMP", LM), ("IN", 2 * NW), ("IM", 2 * NW), ("NLi", 2 * NW)):
     _sb(_n, _k, "float16")
 for _i in range(4):
     _sb("PM%d" % _i, 128, "bfloat16"); _sb("QM%d" % _i, 128, "bfloat16"); _sb("XM%d" % _i, 128, "bfloat16")
+for _i in sorted(set(NXS)):
+    _sb("BW%d" % _i, 16 * _i, "bfloat16")
 _sb("nm", 2 * NW, "uint16"); _sb("WL", 8, "uint16")
-for _b in range(NBK):
-    _s = str(_b)
-    for _n, _k, _d in (("V", ROWS + 16, "bfloat16"), ("M", ROWS, "bfloat16"), ("Z", ROWS, "bfloat16"), ("D2", ROWS, "bfloat16"),
-                       ("AD", (NX, CH), "bfloat16"), ("cs", 2 * L, "bfloat16"), ("lv", NB, "bfloat16"), ("S", 128, "bfloat16"), ("S2", 128, "bfloat16"), ("r", L, "bfloat16"), ("C", L, "bfloat16"), ("E", L, "bfloat16"),
-                       ("cm", L, "bfloat16"), ("c2", (NX, P), "bfloat16"), ("a", L, "float32"), ("na", L, "float32"), ("ni", L, "int32"),
-                       ("y", L, "float32"), ("zo", NX, "uint16"), ("ui", L, "int32"), ("um", L, "int32"),
-                       ("v", L, "float32"), ("sq", L, "float32"), ("si", L, "int32"), ("hm", (NX, P), "int32"),
-                       ("hu", L, "uint16"), ("nc", L, "float32"), ("nj", L, "int32"), ("of", NB, "uint16"),
-                       ("CR0", CH, "bfloat16"), ("CR1", CH, "bfloat16"), ("CR2", CH, "bfloat16"), ("CR3", CH, "bfloat16"),
-                       ("n0", (NX, P), "int32"), ("n1", (NX, P), "int32"), ("WN", 4 * REG, "float32")):
+for _b, _x in enumerate(NXS):
+    _s, _l = str(_b), P * _x
+    for _n, _k, _d in (("V", 16 * _l + 16, "bfloat16"), ("M", 16 * _l, "bfloat16"), ("Z", 16 * _l, "bfloat16"), ("D2", 16 * _l, "bfloat16"),
+                       ("AD", (_x, CH), "bfloat16"), ("cs", 256, "bfloat16"), ("lv", 16 * _x, "bfloat16"), ("S", 128, "bfloat16"),
+                       ("r", _l, "bfloat16"), ("r0", _l, "bfloat16"), ("C", _l, "bfloat16"), ("E", _l, "bfloat16"),
+                       ("cm", _l, "bfloat16"), ("c2", (_x, P), "bfloat16"), ("na", _l, "float32"), ("ni", _l, "int32"),
+                       ("zo", _x, "uint16"), ("v", _l, "float32"), ("sq", _l, "float32"), ("si", _l, "int32"), ("hm", (_x, P), "int32"),
+                       ("hu", _l, "uint16"), ("nj", _l, "int32"), ("of", 16 * _x, "uint16"), ("CR", 16 * _l, "bfloat16"),
+                       ("n0", (_x, P), "int32"), ("n1", (_x, P), "int32"), ("WN", 4 * REG, "float32"), ("G", 192 * _x, "bfloat16"),
+                       ("IX", (_x, 16), "uint16"), ("NB", (_x, P), "float16"), ("N", 256 * _x, "float16")):
         _sb(_n + _s, _k, _d)
-    _sb("G" + _s, 12 * NB, "bfloat16"); _sb("IX" + _s, (NX, 16), "uint16"); _sb("NB" + _s, (NX, P), "float16")
-    _sb("N" + _s, 16 * NB, "float16"); _sb("yl" + _s, L, "float32", True)
+    _sb("yl" + _s, _l, "float32", True)
 for _d in FILL:
     SCRATCH["all_" + _d] = ("sbuf", [128, FILL[_d]], _d)
-
-SEMAPHORES = ["sv", "sa", "st", "sg", "loc"] + ["d%d" % i for i in range(8 + NBK)]
-SEMAPHORES += ["m%d%d%d%d" % (k, t, b, h) for k in range(3) for t in range(RO) for b in range(NBK) for h in (0, 1)]
-
-CY = 0.00083
-PE = 0.0005
-GA = 1.5
-FV = 0.05
-FA = 0.1
-XLOAD = 5.0
-HOP0 = 2.0
-HOP1 = 2.7
-PORT = 0.1
-WIDE = 0.0
-ONCE = 2.5
-WEIGHT = 3.0
-LINK = 0.1
-SAME = 0.1
-CALL = 1.0
-FIRST = 1.0
-PASSES = 5
-RULES = [(3, u, v, (0, 0, 0)) for u in (0.02, 0.03, 0.05) for v in (0.1, 0.3, 0.5)]
-SLOW = 1.25
 
 
 def target(q, n, t, h):
@@ -112,12 +97,39 @@ def target(q, n, t, h):
 
 
 def calls(t, b):
-    s, r, u = MROWS * (t * NBK + b), MROWS * (t * NBK + b), NX // 2
+    s, nx = MROWS * (t * NBK + b), NXS[b]
+    both = lambda lo, m: [(h, "M", s + lo, 2 * s + MROWS * h + lo, m) for h in (0, 1)]
     if t < RO - 1:
-        return [(0, [(0, s + S_OWN, r + R_OWN, 2), (1, s + S_OVER, r + R_OVER, 2)]),
-                (1, [(0, s + S_N, r + R_N, NX), (1, s + S_N, r + R_UP, NX)]),
-                (2, [(0, s + S_N + NX, r + R_N + NX, NX)]), (2, [(1, s + S_N + NX, r + R_UP + NX, NX)])]
-    return [(0, [(1, s + S_OVER, r + R_OVER, 1)]), (1, [(1, s + S_UP, r + R_UP, u)]), (2, [(1, s + S_UP + u, r + R_UP + u, u)])]
+        early = [(1, both(0, S_N + nx))] if MERGE else [(0, both(0, S_N)), (1, both(S_N, nx))]
+        late = both(S_N + nx, nx)
+        return early + ([(2, late[:1]), (2, late[1:])] if LATE2 else [(2, late)])
+    return [(0, both(S_OVER, 1)[1:])] + [(1 + e, [(1, "U", 2 * W0[b] + nx * e, 2 * W0[b] + nx * e, nx)]) for e in (0, 1)]
+
+
+SEMAPHORES = ["sv", "sa", "st", "sg", "loc"] + ["d%d" % i for i in range(8 + NBK)]
+SEMAPHORES += ["m%d%d%d%d" % (k, t, b, x[0]) for t in range(RO) for b in range(NBK) for k, ws in calls(t, b) for x in ws]
+
+SPEED = np.array([1.2, 1.03, 1.45, 1.1])
+CY = 0.00083 * SPEED
+PE = 0.00042 * SPEED
+GA = np.array([1.45, 1.2, 2.0, 1.3])
+FV = 0.015
+FA = 0.04
+XLOAD = 5.0
+HOP0 = np.array([1.8, 1.8, 1.8, 2.4])
+HOP1 = np.array([2.7, 2.7, 2.7, 3.8])
+CALL = np.array([1.0, 1.0, 1.0, 1.3])
+ONCE = 1.5
+LINK = 0.1
+SAME = 0.08
+WEIGHT = np.array([2.0, 1.0, 1.0, 1.0])
+PASSES = 4
+KEEP = 0.0
+BIG = 0.05
+TRIES = 6000
+SHAKE = 0.0001
+RULES = [(f, 0.03, v) for f in (1, 3, 6) for v in (0.1, 0.3, 0.6)]
+KEPT = {}
 
 
 def leg(topo, src, dst, t, b, k):
@@ -125,7 +137,8 @@ def leg(topo, src, dst, t, b, k):
         return dst, topo.engines(src, dst)
     c = [x for x in topo.cores_of(src) if x != src and topo.die(x) == topo.die(src) and topo.may_write(x, dst)]
     e = topo.engines(src, c[0])
-    return c[b % len(c)], (e[len(e) // 2:] if k < 2 and t < RO - 1 else e)
+    alone = t == RO - 1 or (k == 2 and LATE2)
+    return c[(b + (ALT if k < 2 else 0)) % len(c)], (e if alone else e[len(e) // 2:])
 
 
 def transfer(T, topo, core, dst, src_ap, dst_ap, engines, sem):
@@ -136,14 +149,19 @@ def transfer(T, topo, core, dst, src_ap, dst_ap, engines, sem):
 
 def relay_program(g, core, T, topo):
     n = len(T.cores)
+    if not [q for q in T.cores if core in topo.cores_of(q)]:
+        return
+    if not KEPT:
+        rank_program(None, T.cores[0], T, topo)
     tot = 0
-    for t in range(RO):
-        for b, k, h, r, m, q in [(b, k, h, r, m, q) for b in range(NBK) for k, ws in calls(t, b) for h, _, r, m in ws for q in range(n)]:
+    for t, b, k, ws in KEPT["sends"]:
+        for h, buf, _, r, m, q in [x + (q,) for x in ws for q in range(n)]:
             d = T.cores[target(q, n, t, h)]
-            if leg(topo, T.cores[q], d, t, b, k)[0] == core:
+            to, e = leg(topo, T.cores[q], d, t, b, k)
+            if to == core:
                 sem = "m%d%d%d%d" % (k, t, b, h)
-                g.wait_ge(T.sem[sem], len(leg(topo, T.cores[q], d, t, b, k)[1]))
-                x = T.MR[:, r:r + m, :]
+                g.wait_ge(T.sem[sem], len(e))
+                x = T[buf + "R"][:, r:r + m, :]
                 g.remote_dma_fused([transfer(T, topo, core, d, x, x, topo.engines(core, d), sem)], local_sem=T.sem["loc"])
                 tot += len(topo.engines(core, d))
     if tot:
@@ -164,6 +182,126 @@ def clash(a, b):
     return True
 
 
+def polish(nodes, users, sends):
+    n, m = len(nodes), len(SPEED)
+    res = KEPT["res"]
+    rng = np.random.default_rng(0)
+    deps = [x["deps"] for x in nodes]
+    dur = [[{e: float(x["dd"][e][k]) for e in x["dd"]} for x in nodes] for k in range(m)]
+    lat = [[float(x["ll"][k]) for x in nodes] for k in range(m)]
+    total = {}
+    for x in nodes:
+        for y in x["banks"]:
+            total[y] = total.get(y, 0) + 1
+
+    def run(order, on, k, plan):
+        fin, why, busy, last = [0.0] * n, [-1] * n, {}, {}
+        d, l = dur[k], lat[k]
+        make = plan is None
+        if make:
+            plan, banks, left, bfree, blast = [()] * n, {}, dict(total), [0.0] * NPS, [[] for _ in range(NPS)]
+        for i in order:
+            e = on[i]
+            if make:
+                for y in nodes[i]["banks"]:
+                    if y not in banks:
+                        z = [z for z in range(NPS) if bfree[z] is not None]
+                        if not z:
+                            return None
+                        z = min(z, key=lambda z: bfree[z])
+                        banks[y], bfree[z] = z, None
+                        plan[i] = plan[i] + tuple(blast[z])
+                        blast[z] = []
+            st, w = (busy.get(e, 0.0), last.get(e, -1)) if e else (0.0, -1)
+            for js in (deps[i], plan[i]):
+                for j in js:
+                    f = on[j]
+                    t = fin[j] + (LINK if e != f else 0.0 if e == "p" else SAME)
+                    if t > st:
+                        st, w = t, j
+            why[i] = w
+            if e:
+                fin[i] = busy[e] = st + d[i][e]
+                last[e] = i
+            else:
+                fin[i] = st + l[i]
+            if make:
+                for y in nodes[i]["banks"]:
+                    left[y] -= 1
+                    blast[banks[y]].append(i)
+                    if not left[y]:
+                        bfree[banks[y]] = fin[i]
+        return fin, why, plan, banks if make else None
+
+    def score(order, on):
+        a = run(order, on, 0, None)
+        if a is None:
+            return None
+        rs = [a] + [run(order, on, k, a[2]) for k in range(1, m)]
+        ends = np.array([max(z[0]) for z in rs])
+        return float(np.sum(WEIGHT * ends / KEPT["scale"])), ends, rs
+
+    order, on = sorted(range(n), key=lambda i: (res[3][i], i)), list(res[2])
+    cur = best = (score(order, on), order, on)
+    for it in range(TRIES):
+        (sc, ends, rs), order, on = cur
+        fin, why = rs[int(rng.integers(m))][:2]
+        i, path = max(range(n), key=lambda i: fin[i]), []
+        while i >= 0:
+            if why[i] >= 0 and on[i] and why[i] not in deps[i]:
+                path.append(i)
+            i = why[i]
+        if not path:
+            break
+        i = path[int(rng.integers(len(path)))]
+        j = why[i]
+        new, to = list(order), on
+        u = rng.random()
+        if u > 1 - BIG:
+            b = order.index(i)
+            a = max(0, b - int(rng.integers(5, 80)))
+            mv = set()
+            for k in reversed(order[a:b + 1]):
+                if nodes[k]["plus"] == nodes[i]["plus"] or any(y in mv for y in users[k]):
+                    mv.add(k)
+            new[a:b + 1] = [k for k in order[a:b + 1] if k in mv] + [k for k in order[a:b + 1] if k not in mv]
+        elif u < 0.25:
+            k = i if rng.random() < 0.5 else j
+            if nodes[k]["e"] != "va":
+                continue
+            to = list(on); to[k] = "v" if on[k] == "a" else "a"
+        else:
+            pos = {k: p for p, k in enumerate(order)}
+            a, b = pos[j], pos[i]
+            if u < 0.65:
+                mv = {i}
+                for k in reversed(order[a:b]):
+                    if any(y in mv for y in users[k]):
+                        mv.add(k)
+                if j in mv:
+                    continue
+                new[a:b + 1] = [k for k in order[a:b + 1] if k in mv] + [k for k in order[a:b + 1] if k not in mv]
+            else:
+                b = min(n - 1, b + int(rng.integers(0, 12)))
+                mv = {j}
+                for k in order[a + 1:b + 1]:
+                    if any(y in mv for y in deps[k]):
+                        mv.add(k)
+                if i in mv:
+                    continue
+                new[a:b + 1] = [k for k in order[a:b + 1] if k not in mv] + [k for k in order[a:b + 1] if k in mv]
+        z = score(new, to)
+        if z is not None and z[0] < sc - SHAKE * (1 - it / TRIES) * np.log(rng.random()):
+            cur = (z, new, to)
+            if z[0] < best[0][0]:
+                best = cur
+    (sc, ends, rs), order, on = best
+    fin, _, plan, banks = rs[0]
+    at = [fin[i] - (dur[0][i][on[i]] if on[i] else lat[0][i]) for i in range(n)]
+    order = [i for i in order if on[i]]
+    KEPT.update(res=(ends[0], order, on, at, fin, banks, [list(x) for x in plan]), both=sc, ends=ends, sends=[sends[k] for k in order if k in sends])
+
+
 def rank_program(g, core, T, topo):
     rank = T.rank_of(core)
     if rank is None:
@@ -172,10 +310,11 @@ def rank_program(g, core, T, topo):
     nodes = []
     cur = {"plus": 0.0}
     hist = {}
-    eng = {"v": g.vector, "a": g.scalar, "p": g.tensor, "g": g, "s": g.sync}
     esem = {"v": "sv", "a": "sa", "p": "st", "g": "sg"}
+    eng = {"v": g.vector, "a": g.scalar, "p": g.tensor, "g": g, "s": g.sync} if g is not None else {}
+    one = np.ones(len(SPEED))
 
-    def add(e, dur, w, r, fn, sem=None, inc=1, after=(), lat=0.0, ga=0):
+    def add(e, dur, w, r, fn, sem=None, inc=1, after=(), lat=0.0):
         i = len(nodes)
         deps = {}
         for x in r:
@@ -202,8 +341,10 @@ def rank_program(g, core, T, topo):
         if not isinstance(dur, dict):
             dur, f1 = {e: dur}, fn
             fn = lambda e: f1()
-        nodes.append({"e": e, "d": dur, "plus": cur["plus"], "banks": banks, "w": w, "deps": sorted(deps), "fn": fn, "sem": sem, "inc": inc,
-                      "lat": lat, "ga": ga, "soft": [j for j in deps if deps[j] == 2]})
+        dur = {k: dur[k] * one for k in dur}
+        nodes.append({"e": e, "dd": dur, "d": {k: float(dur[k][0]) for k in dur}, "plus": cur["plus"], "banks": banks, "w": w,
+                      "deps": sorted(deps), "fn": fn, "sem": sem, "inc": inc, "ll": lat * one, "lat": float((lat * one)[0]),
+                      "soft": [j for j in deps if deps[j] == 2]})
         return i
 
     def A(r, rows=None):
@@ -229,11 +370,16 @@ def rank_program(g, core, T, topo):
     def two(r):
         return r[0][:2] != "ps" and SIZE[r[0]][1] in ("bfloat16", "uint16", "float16")
 
+    cv = lambda n: FV + max(64, n) * CY
+
     def dv(o, *i):
-        return FV + num(o) * CY * (0.5 if two(o) and all(two(x) for x in i) else 1)
+        return cv(num(o) * (0.5 if two(o) and all(two(x) for x in i) else 1))
 
     def da(o):
         return FA + num(o) * CY
+
+    def dg(o):
+        return {"v": 0.05 + num(o) * CY * GA, "a": 0.065 + num(o) * CY * GA}
 
     val = lambda s: A(s) if isinstance(s, tuple) else s
 
@@ -250,12 +396,13 @@ def rank_program(g, core, T, topo):
         return add("v", dv(o, i), [o], [i] + [s for s in (s1, s2) if isinstance(s, tuple)], lambda: tsf(A(o), A(i), s1, op0, s2, op1))
 
     def lin(o, i, k, c, e="va"):
-        return add(e, {"v": dv(o, i), "a": da(o)}, [o], [i], lambda e: g.vector.tensor_scalar(A(o), A(i), k, c, OP.mult, OP.add)
-                   if e == "v" else g.scalar.activation(A(o), A(i), AF.Identity, bias=c, scale=k))
+        return add(e, {"v": dv(o, i), "a": da(o)}, [o], [i] + ([k] if isinstance(k, tuple) else []),
+                   lambda e: g.vector.tensor_scalar(A(o), A(i), val(k), c, OP.mult, OP.add)
+                   if e == "v" else g.scalar.activation(A(o), A(i), AF.Identity, bias=c, scale=val(k)))
 
     def tt(o, i, j, op):
         k = 1 if "ps" in (i[0][:2], j[0][:2]) else 2
-        return add("v", FV + k * num(o) * CY, [o], [i, j], lambda: g.vector.tensor_tensor(A(o), A(i), A(j), op))
+        return add("v", cv(k * num(o)), [o], [i, j], lambda: g.vector.tensor_tensor(A(o), A(i), A(j), op))
 
     def act(o, i, func, bias=0.0, scale=1.0):
         return add("a", da(o), [o], [i] + ([bias] if isinstance(bias, tuple) else []),
@@ -270,34 +417,33 @@ def rank_program(g, core, T, topo):
 
     def gather(e, o, win, off):
         f = lambda: A(win).indirect(A(off))
-        d = 0.06 + num(o) * CY * GA
-        return add(e, {"v": d, "a": d + 0.015}, [o], [win, off], lambda e: g.vector.tensor_copy(A(o), f()) if e == "v" else
-                   g.scalar.activation(A(o), f(), AF.Copy), ga=num(o))
+        return add(e, dg(o), [o], [win, off], lambda e: g.vector.tensor_copy(A(o), f()) if e == "v" else
+                   g.scalar.activation(A(o), f(), AF.Copy))
 
     def glin(o, win, off, k, c):
         f = lambda: A(win).indirect(A(off))
-        d = 0.06 + num(o) * CY * GA
-        return add("va", {"v": d, "a": d + 0.015}, [o], [win, off], lambda e: g.vector.tensor_scalar(A(o), f(), k, c, OP.mult, OP.add)
-                   if e == "v" else g.scalar.activation(A(o), f(), AF.Identity, bias=c, scale=k), ga=num(o))
+        return add("va", dg(o), [o], [win, off], lambda e: g.vector.tensor_scalar(A(o), f(), k, c, OP.mult, OP.add)
+                   if e == "v" else g.scalar.activation(A(o), f(), AF.Identity, bias=c, scale=k))
 
     def gtt(o, win, off, j):
-        return add("v", 0.06 + num(o) * CY * GA, [o], [win, off, j],
-                   lambda: g.vector.tensor_tensor(A(o), A(win).indirect(A(off)), A(j), OP.subtract), ga=num(o))
+        return add("v", dg(o)["v"], [o], [win, off, j],
+                   lambda: g.vector.tensor_tensor(A(o), A(win).indirect(A(off)), A(j), OP.subtract))
 
     def mms(lst):
-        w, r, d = [], [], 0.05
-        for o, l, x, s, p in lst:
-            if o not in w:
-                w.append(o)
-            for y in (l, x):
+        w, r, d = [], [], 0.03
+        for x in lst:
+            if x[0] not in w:
+                w.append(x[0])
+            for y in x[1:3]:
                 if y not in r:
                     r.append(y)
-            d += max(64, num(x)) * PE * (4 if not two(x) else 1)
+            d = d + max(64, num(x[2])) * PE * (4 if not two(x[2]) else 1)
 
         def fn():
             z = None
-            for o, l, x, s, p in lst:
-                z = g.tensor.matmul(A(o), A(l), A(x), s, p)
+            for x in lst:
+                k = x[5] if len(x) > 5 else None
+                z = g.tensor.matmul(A(x[0]), A(x[1], k), A(x[2], k), x[3], x[4])
             return z
         return add("p", d, w, r, fn)
 
@@ -320,7 +466,7 @@ def rank_program(g, core, T, topo):
         return i
 
     def iota(o, pattern, base, cm, ints=False):
-        return add("g", 0.15 + num(o) * 2 * CY, [o], [], (lambda: g.iota(A(o), pattern, base, cm)) if ints else
+        return add("g", 0.13 + num(o) * 2 * CY, [o], [], (lambda: g.iota(A(o), pattern, base, cm)) if ints else
                    (lambda: g.iota(A(o), pattern, base, cm, allow_small_or_imprecise_dtypes=True)))
 
     x = dma("s", [R("wni")], [], T.wni[0:8, :], T.wn[:, :])
@@ -330,7 +476,7 @@ def rank_program(g, core, T, topo):
     dma("a", [R("wti")], [], T.wti[:, :], T.wt[:, :], 2.0, [x])
     col = lambda i: R("cols", i, i + 1)
     ci = lambda i: R("ci", i, i + 1)
-    LA, LB, THR, TH, TN, WC, L32, LV = [col(i) for i in range(8)]
+    LA, LB, THR, TH, TN, WC, L32, LV, GP = [col(i) for i in range(9)]
 
     def select(o, i, pattern, op, fill, base, cm=1):
         return add("g", 0.17 + num(o) * 2 * CY, [o], [i], lambda: g.affine_select(A(o), A(i), pattern, op, float(fill), base, cm))
@@ -338,59 +484,75 @@ def rank_program(g, core, T, topo):
     def pick(o, pattern, base, k=1.0, zero="ZB"):
         return select(o, R(zero, 0, num(o)), pattern, OP.not_equal, k, base)
 
-    mset(R("ZF32"), 0.0); mset(R("ZB", 0, 144), 0.0); mset(R("ZB", 144), 0.0)
+    mset(R("ZF32"), 0.0); mset(R("ZB", 0, 144), 0.0)
     iota(ci(0), [[0, 1]], 0, 1, True); ts(ci(1), ci(0), 15, OP.bitwise_and); copy(LA, ci(1)); ts(LB, LA, 16.0, OP.add)
+    ts(ci(2), ci(0), 4, OP.arith_shift_right); copy(GP, ci(2))
     pick(R("E8"), [[-1, 8], [0, 16]], 0, zero="ZF32")
-    add("v", 0.2, [R("wnf", 0, NW)], [R("wni")], lambda: g.vector.tensor_copy(A(R("wnf", 0, NW), 8), A(R("wni"), 8)))
-    add("v", 0.1, [R("wnf", NW, NW + 1)], [R("thi")], lambda: g.vector.tensor_copy(A(R("wnf", NW, NW + 1), 8), A(R("thi"), 8)))
+    add("v", cv(128), [R("wnf", 0, NW)], [R("wni")], lambda: g.vector.tensor_copy(A(R("wnf", 0, NW), 8), A(R("wni"), 8)))
+    add("v", cv(1), [R("wnf", NW, NW + 1)], [R("thi")], lambda: g.vector.tensor_copy(A(R("wnf", NW, NW + 1), 8), A(R("thi"), 8)))
     bn = bank(NW + 1)
-    add("p", 0.4, [bn], [R("E8"), R("wnf")], lambda: g.tensor.matmul(A(bn), A(R("E8"), 8), A(R("wnf"), 8), True, True))
+    add("p", 0.3, [bn], [R("E8"), R("wnf")], lambda: g.tensor.matmul(A(bn), A(R("E8"), 8), A(R("wnf"), 8), True, True))
     for x in range(4):
         pick(R("PM%d" % x), [[-32, 4], [1000, 2], [-2, 16]], -(x % 2) - 1000 * (x // 2))
-    for b in range(NBK):
-        cur["plus"] = FIRST if b == 0 else 0.0
-        x, y = L * b, L * b + L
+    for b, nx in enumerate(NXS):
+        cur["plus"] = NBK - 1 - b
+        w0, w1 = W0[b], W0[b] + nx
+        x, y = P * w0, P * w1
         ts(R("IM", x, y), R("wli", x, y), float(-HALF), OP.add)
-        add("v", 2 * dv(R(bn[0], 0, NB)), [R("NLi", x, y)], [bn, LA, LB], lambda x=x, y=y, b=b: [g.vector.tensor_scalar(
-            A(R("NLi", x + h, y, 2)), A(R(bn[0], NB * b, NB * b + NB)), A(k), float(DEAD), OP.is_le, OP.mult) for h, k in ((0, LA), (1, LB))], inc=2)
+        add("v", 2 * cv(16 * nx), [R("NLi", x, y)], [bn, LA, LB], lambda x=x, y=y: [g.vector.tensor_scalar(
+            A(R("NLi", x + h, y, 2)), A(R(bn[0], x // 2, y // 2)), A(k), float(DEAD), OP.is_le, OP.mult) for h, k in ((0, LA), (1, LB))], inc=2)
         tt(R("IN", x, y), R("NLi", x, y), R("IM", x, y), OP.add)
-        add("v", NX * 0.07, [R3("OT", NX * b, NX * b + NX, 0, P)], [R("IN", x, y)], lambda b=b: [
-            g.vector.transpose(A(R3("OT", w, None, 0, P)), A(R("IN", P * w, P * w + P))) for w in range(NX * b, NX * b + NX)], inc=NX)
-        mms([(R3("psz", NX * b, NX * b + NX, 16 * i, 16 * i + 16), R("PM%d" % (2 * j + i)), R3("OT", NX * b, NX * b + NX, 16 * j, 16 * j + 16),
+        add("v", nx * cv(1), [R3("OT", w0, w1, 0, P)], [R("IN", x, y)], lambda w0=w0, w1=w1: [
+            g.vector.transpose(A(R3("OT", w, None, 0, P)), A(R("IN", P * w, P * w + P))) for w in range(w0, w1)], inc=nx)
+        mms([(R3("psz", w0, w1, 16 * i, 16 * i + 16), R("PM%d" % (2 * j + i)), R3("OT", w0, w1, 16 * j, 16 * j + 16),
               j == 0, j == 1) for i in (0, 1) for j in (0, 1)])
-        z = R3("psz", NX * b, NX * b + NX, 0, P)
+        z = R3("psz", w0, w1, 0, P)
         ts(R("nm", x, y), z, float(HALF), OP.add, float(DEAD), OP.min); lin(R("NF", x, y), z, 1.0, float(HALF))
     cur["plus"] = 0.0
     ts(THR, R(bn[0], NW, NW + 1), 0.5, OP.mult)
     ts(TH, THR, 0.25, OP.add, 400.0, OP.mult); ts(TN, TH, -1.0, OP.mult)
     mset(R("XT", W, W + 16), 255.0)
-    for n, k in (("ID", 1), ("NEG", -1), ("N8", -8192), ("N15", -1584), ("JM", REG - 15), ("W0", 1 - LS), ("W1", -LS),
-                 ("W2", -2 * LS), ("W3", 4 * LS)):
-        pick(R(n), [[-1, 128]], 0, k)
-    pick(R("IDF"), [[-1, 128]], 0, zero="ZF32")
+    pick(R("ID"), [[-1, 128]], 0)
+    lin(R("N97"), R("ID"), -9776.0, 0.0, "v")
+    for n, k in (("NEG", -1), ("N8", -8192), ("JM", REG - 15), ("W0", 1 - LS), ("W1", -LS), ("W2", -2 * LS),
+                 ("W3", 4 * LS), ("IDF", 1)):
+        lin(R(n), R("ID"), float(k), 0.0)
     pick(R("SH"), [[-1, 128]], 0, -0.5); select(R("SH"), R("SH"), [[-1, 128]], OP.not_equal, -0.5, 1)
     copy(WC, R("wti")); mset(R("EW"), 0.0); mset(R("WW"), 0.0); mset(R("ONE"), 1.0)
     select(R("E9"), R("ONE", 0, 9), [[-16, 9]], OP.is_ge, 0, 0); select(R("EW", 15, 144, 16), R("E9"), [[16, 9]], OP.is_ge, 0, 15, -1)
     ts(R("WW", 15, 144, 16), R("EW", 15, 144, 16), WC, OP.mult)
     for n, k in (("K0", 0.0), ("PAT", 1.0), ("TWO", 2.0), ("MQ", -0.25), ("CK", 167.0 / 32), ("VP", 0.0)):
         mset(R(n), k)
-    mset(R("K0", 0, L, P), 16384.0); mset(R("PAT", 0, L, P), 0.0); mset(R("VP", 3, 2 * P, 4), 8.0 * LS)
-    for b in range(NBK):
+    mset(R("K0", 0, LM, P), 16384.0); mset(R("PAT", 0, LM, P), 0.0); mset(R("VP", 3, 2 * P, 4), 8.0 * LS)
+    for b, nx in enumerate(NXS):
         mset(R("V%d" % b, 0, 16), 0.0)
-        mset(R("WN%d" % b, 3 * REG), float(DEAD - HALF))
-    mset(R("AC", 0, 1), -0.375)
-    for x in range(0, 16, 4):
-        pick(R("SEL", 128 * x, 128 * x + 512), [[-1, 4], [-16, 8], [0, 16]], -x)
-    iota(R("RA"), [[16, L]], 0, 0); ts(R("RAMP"), R("RA"), LA, OP.add)
-    iota(R("BW"), [[0, 8], [NB, 2], [16, NX]], 0, 0); iota(R("YI"), [[1, 56]], 0, 0); iota(R("W5"), [[512, 8]], 0, 0)
+        mset(R("WN%d" % b, 3 * REG if P * nx == REG else 0), float(DEAD - HALF))
+        if nx < 4:
+            mset(R("cs%d" % b), 0.0)
+    if PN0:
+        mset(R("AC", 0, 1), WHOLE); mset(R("AB", 0, 1), HALF - 0.5 - MAGIC); mset(R("K15"), 1.5)
+    iota(R("YI"), [[1, 56]], 0, 0); iota(R("CG"), [[1, 8], [0, 16]], 0, 0)
+    ts(R("MK"), R("YI", 0, 16), LA, OP.is_equal); ts(R("BLK"), R("CG"), GP, OP.is_equal)
+    for x in range(16):
+        lin(R("SEL", 128 * x, 128 * x + 128), R("BLK"), R("MK", x, x + 1), 0.0)
+    iota(R("RA"), [[16, LM]], 0, 0); ts(R("RAMP"), R("RA"), LA, OP.add)
+    for x in sorted(set(NXS)):
+        iota(R("BW%d" % x), [[0, 8], [16 * x, 2], [16, x]], 0, 0)
+    iota(R("W5"), [[512, 8]], 0, 0)
     ts(L32, LA, 32.0, OP.mult); ts(R("W32"), R("W5"), L32, OP.add)
-    for x in range(0, 16, 4):
-        pick(R("DR", 144 * x, 144 * x + 576), [[-1, 4], [-16, 9], [1000, 16]], 16 - x - 15000)
-    select(R("DR", 15, None, 144), R("DR", 15, None, 144), [[-1, 16]], OP.not_equal, 1, -112)
+    if DRG:
+        mset(R("ZB", 144), 0.0)
+        for x in range(0, 16, 4):
+            pick(R("DR", 144 * x, 144 * x + 576), [[-1, 4], [-16, 9], [1000, 16]], 16 - x - 15000)
+        select(R("DR", 15, None, 144), R("DR", 15, None, 144), [[-1, 16]], OP.not_equal, 1, -112)
+    else:
+        mset(R("EN"), 0.0); copy(R("EN", 31, 128, 16), R("EW", 15, 112, 16)); copy(R("EN", 15, 16), R("EW", 127, 128))
+        for x in range(16):
+            lin(R("DR", 144 * x, 144 * x + 144), R("EN"), R("MK", x, x + 1), 0.0)
     for x in range(4):
         pick(R("XM%d" % x), [[-16, 8], [1000, 2], [-2, 8]], -(x % 2) - 1000 * (x // 2))
     ts(LV, LA, 0.5, OP.add, 200.0, OP.mult)
-    add("a", 1.5, [R("VY")], [R("YI"), LV], lambda: g.scalar.activation(A(R("VY")), A(R("YI")), AF.Sigmoid, bias=A(LV), scale=-200.0))
+    add("a", 1.45, [R("VY")], [R("YI"), LV], lambda: g.scalar.activation(A(R("VY")), A(R("YI")), AF.Sigmoid, bias=A(LV), scale=-200.0))
     for part in range(2):
         b0 = bank(8 * LS); l = []
         for j in range(8):
@@ -402,171 +564,180 @@ def rank_program(g, core, T, topo):
         copy(R("LUT", 8 * LS * part, 8 * LS * (part + 1)), b0, "va")
     nloc = [0]
     win = lambda name, r: R(name, 15 - r, 143 - r)
+    sends, used = {}, set()
 
     def transmit(k, t, b):
-        for ws in [ws for j, ws in calls(t, b) if j == k]:
-            ws = [x + leg(topo, core, T.cores[target(rank, nr, t, x[0])], t, b, k) for x in ws]
-            nloc[0] += sum(len(x[5]) for x in ws)
-            sent[:] = [add("g", CALL if sent else ONCE, [], [R3("MS", x[1], x[1] + x[3], 0, P) for x in ws], lambda ws=ws: g.remote_dma_fused(
-                [transfer(T, topo, core, to, T.MS[:, s:s + m, :], T.MR[:, r:r + m, :], e, "m%d%d%d%d" % (k, t, b, h)) for h, s, r, m, to, e in ws],
-                local_sem=T.sem["loc"]), sem="loc", inc=0, after=sent[:1] if k else [])]
-            for h, _, r, m, _, _ in ws:
+        before = []
+        for parts in [ws for j, ws in calls(t, b) if j == k]:
+            ws = [x + leg(topo, core, T.cores[target(rank, nr, t, x[0])], t, b, k) for x in parts]
+            nloc[0] += sum(len(x[6]) for x in ws)
+            i = add("g", CALL + (0.0 if sends else ONCE), [], [R3(x[1] + "S", x[2], x[2] + x[4], 0, SCRATCH[x[1] + "S"][1][2]) for x in ws],
+                    lambda ws=ws: g.remote_dma_fused(
+                        [transfer(T, topo, core, to, T[u + "S"][:, s:s + m, :], T[u + "R"][:, r:r + m, :], e, "m%d%d%d%d" % (k, t, b, h))
+                         for h, u, s, r, m, to, e in ws], local_sem=T.sem["loc"]), sem="loc", inc=0, after=before)
+            sends[i] = (t, b, k, parts)
+            before = [i]
+            for h, u, _, r, m, out, _ in ws:
                 src = T.cores[[q for q in range(nr) if target(q, nr, t, h) == rank][0]]
                 to = leg(topo, src, core, t, b, k)[0]
-                last, more = sent[:1], (0.0 if k == 2 else WIDE)
+                last = [i]
                 if to != core:
-                    last = [add(None, 0.0, [], [], None, sem="loc", inc=0, after=last, lat=HOP0 + more)]
-                    last = [add(str(b % 2), CALL if t or k else ONCE, [], [], None, sem="loc", inc=0, after=last)]
-                last = [add("2", PORT * m / NX, [], [], None, sem="loc", inc=0, after=last)]
-                kind[len(nodes)] = k
-                add(None, 0.0, [R3("MR", r, r + m, 0, P)], [], None, sem="m%d%d%d%d" % (k, t, b, h), after=last, lat=HOP1 + more,
-                    inc=len(topo.engines(src if to == core else to, core)))
+                    last = [add(None, 0.0, [], [], None, sem="loc", inc=0, after=last, lat=HOP0)]
+                    last = [add(str(out % 2), CALL + (0.0 if out in used else ONCE), [], [], None, sem="loc", inc=0, after=last)]
+                    used.add(out)
+                add(None, 0.0, [R3(u + "R", r, r + m, 0, SCRATCH[u + "R"][1][2])], [], None, sem="m%d%d%d%d" % (k, t, b, h), after=last,
+                    lat=HOP1, inc=len(topo.engines(src if to == core else to, core)))
 
-    sent, pad, kind = [], {}, {}
+    def rows(h, t, b, first, m, lo=0, hi=P):
+        x = MROWS * (t * NBK + b)
+        n, x = ("MS", x + first) if h is None else ("MR", 2 * x + MROWS * h + first)
+        return R3(n, x, None if m is None else x + m, lo, hi)
 
-    def rows(n, t, b, first, m, lo=0, hi=P):
-        x = MROWS * (t * NBK + b) + first
-        return R3(n, x, x + m, lo, hi)
-
-    def put_names(e, t, b, x, lo=0, hi=P):
-        n, u = "n%d%d" % (e, b), NX // 2
-        ts(R3(n, 0, NX, lo, hi), x, W - 1, OP.bitwise_and)
+    def put_names(e, t, b, x, lo=0, hi=P, shift=0, plus=None):
+        n, nx = "n%d%d" % (e, b), NXS[b]
+        u = 2 * W0[b] + nx * e
+        if plus is not None:
+            ts(rows(None, t, b, S_N + nx * e, nx, lo, hi), x, plus, OP.add)
+            if t == RO - 1:
+                copy(R3("US", u, u + nx, 0, 16), rows(None, t, b, S_N + nx * e, nx, 16, P))
+            return transmit(1 + e, t, b)
+        if shift:
+            ts(R3(n, 0, nx, lo, hi), x, shift, OP.arith_shift_right, W - 1, OP.bitwise_and)
+        else:
+            ts(R3(n, 0, nx, lo, hi), x, W - 1, OP.bitwise_and)
         if t == RO - 1 and hi == P:
-            ts(rows("MS", t, b, S_UP + u * e, u), R3(n, 0, NX, 16, P), float(-HALF), OP.add)
+            ts(R3("US", u, u + nx, 0, 16), R3(n, 0, nx, 16, P), float(-HALF), OP.add)
             transmit(1 + e, t, b)
-        ts(rows("MS", t, b, S_N + NX * e, NX, lo, hi), R3(n, 0, NX, lo, hi), float(-HALF), OP.add)
+        ts(rows(None, t, b, S_N + nx * e, nx, lo, hi), R3(n, 0, nx, lo, hi), float(-HALF), OP.add)
         if t < RO - 1:
             transmit(1 + e, t, b)
 
     def join(t, b):
-        s = str(b)
-        n, x, z = ("MR", R_OWN, R_N) if t < RO - 1 else ("MS", S_OWN, S_N)
-        copy(R3("IX" + s, 0, NX, 8, 16), rows(n, t, b, x, 1))
-        f = bank(8 * NX)
-        acc(f, [(R("ID"), rows("MR", t, b, R_OVER, 1)), (R("ID"), rows(n, t, b, x + 1, 1))])
-        copy(R3("IX" + s, 0, NX, 0, 8), f)
-        for w in range(NX):
-            gather("va", R("G" + s, w, None, NX), R("LUT"), R3("IX" + s, w, None, 4, 16))
-        f = bank(NB)
-        acc(f, [(R("ID"), R("G" + s, NB * c, NB * c + NB)) for c in range(12)] + [(R("ID"), R("BW"))])
+        s, nx = str(b), NXS[b]
+        nb, l, own = 16 * nx, P * nx, 0 if t < RO - 1 else None
+        copy(R3("IX" + s, 0, nx, 8, 16), rows(own, t, b, S_OWN, None, 0, 8 * nx))
+        f = bank(8 * nx)
+        acc(f, [(R("ID"), rows(1, t, b, S_OVER, None, 0, 8 * nx)), (R("ID"), rows(own, t, b, S_CNT, None, 0, 8 * nx))])
+        copy(R3("IX" + s, 0, nx, 0, 8), f)
+        for w in range(nx):
+            gather(GG, R("G" + s, w, None, nx), R("LUT"), R3("IX" + s, w, None, 4, 16))
+        f = bank(nb)
+        acc(f, [(R("ID"), R("G" + s, nb * c, nb * c + nb)) for c in range(12)] + [(R("ID"), R("BW%d" % nx))])
         copy(R("of" + s), f)
         if t == RO - 1:
             mset(R("WN" + s, 3 * REG, 4 * REG, 16), float(-HALF))
-        f = bank(REG)
-        mms([(R(f[0], NB * y, NB * y + NB), R("XM%d" % (2 * e + y)), rows("MR", t, b, R_UP + NX * e, NX, 16, P) if t < RO - 1 else
-              rows("MR", t, b, R_UP + NX // 2 * e, NX // 2), e == 0, e == 1) for y in (0, 1) for e in (0, 1)])
-        copy(R("WN" + s, 2 * REG, 3 * REG), f, "va")
-        f = bank(2 * REG)
-        mms([(R(f[0], REG * h + NB * y, REG * h + NB * y + NB), R("XM%d" % (2 * e + y)), rows(n, t, b, z + NX * e, NX, 16 * h, 16 * h + 16),
-              e == 0, e == 1) for h in (0, 1) for y in (0, 1) for e in (0, 1)])
-        copy(R("WN" + s, 0, 2 * REG), f, "va")
-        f = bank(L)
+        f = bank(l)
+        up = lambda e: rows(1, t, b, S_N + nx * e, nx, 16, P) if t < RO - 1 else R3("UR", 2 * W0[b] + nx * e, 2 * W0[b] + nx * e + nx, 0, 16)
+        mms([(R(f[0], nb * y, nb * y + nb), R("XM%d" % (2 * e + y)), up(e), e == 0, e == 1) for y in (0, 1) for e in (0, 1)])
+        copy(R("WN" + s, 2 * REG, 2 * REG + l), f, "va")
+        for hs in ([(0, 1)] if l == REG else [(0,), (1,)]):
+            f = bank(l * len(hs))
+            mms([(R(f[0], l * i + nb * y, l * i + nb * y + nb), R("XM%d" % (2 * e + y)), rows(own, t, b, S_N + nx * e, nx, 16 * h, 16 * h + 16),
+                  e == 0, e == 1) for i, h in enumerate(hs) for y in (0, 1) for e in (0, 1)])
+            copy(R("WN" + s, REG * hs[0], REG * hs[0] + f[2]), f, "va")
+        f = bank(l)
         for y in range(0, 16, 4):
-            gather("v", R("N" + s, NB * y, NB * y + 4 * NB), R("WN" + s), R("of" + s, NX * y, NX * y + 4 * NX))
-            acc(f, ([(R("N8"), R("MQ", 0, L))] if y == 0 else []) +
-                [(R("DR", 144 * (8 * e + x // 2) + 15 - x, 144 * (8 * e + x // 2) + 143 - x), R("N" + s, NB * x, NB * x + NB), R(f[0], e, L, 2))
-                 for x in range(y, y + 4) for e in (0, 1)], y == 0, y == 12)
+            gather("v", R("N" + s, nb * y, nb * y + 4 * nb), R("WN" + s), R("of" + s, nx * y, nx * y + 4 * nx))
+            acc(f, ([(R("N8"), R("MQ", 0, l))] if y == 0 else []) +
+                [(R("DR", 144 * (8 * e + x // 2) + 15 - x, 144 * (8 * e + x // 2) + 143 - x), R("N" + s, nb * x, nb * x + nb), R(f[0], e, l, 2))
+                 for x in range(y, y + 4) for e in (0, 1)], y == 0, y == 12 and (t == RO - 1 or not PJ))
         return f
 
-    def step(o, i, k, more):
+    def step(o, i, more):
         return add("va", {"v": dv(o, i), "a": da(o)}, [o], [i, TH, TN, THR, R("VY")],
-                   lambda e: g.vector.tensor_scalar(A(o), A(i), k, A(THR), OP.mult, OP.is_gt if more else OP.is_le) if e == "v" else
-                   g.scalar.activation(A(o), A(i), AF.Sigmoid, bias=A(TN if more else TH), scale=(400.0 if more else -400.0) * k))
+                   lambda e: g.vector.tensor_scalar(A(o), A(i), A(THR), None, OP.is_gt if more else OP.is_le) if e == "v" else
+                   g.scalar.activation(A(o), A(i), AF.Sigmoid, bias=A(TN if more else TH), scale=400.0 if more else -400.0))
 
     for t in range(RO):
-        for b in range(NBK):
+        for b, NX in enumerate(NXS):
             s = str(b)
+            L, LO, WO = P * NX, P * W0[b], 16 * W0[b]
+            ROWS = 16 * L
             r = lambda n, lo=0, hi=None, step=1: R(n + s, lo, hi, step)
-            cur["plus"] = FIRST if b == 0 else 0.0
-            nm, nf = R("nm", L * b, L * b + L), R("NF", L * b, L * b + L)
+            cur["plus"] = NBK - 1 - b
+            nm, nf = R("nm", LO, LO + L), R("NF", LO, LO + L)
             if t:
-                f = join(t - 1, b)
-                copy(nm, f); copy(nf, f, "va")
+                fj = join(t - 1, b)
+                copy(nm, fj)
+                if not PJ:
+                    copy(nf, fj, "va")
             for w in range(NX):
-                gather("va", r("V", 16 + CH * w, 16 + CH * w + CH), R("XT", 0, W + 16), R("nm", L * b + P * w, L * b + P * w + P))
+                gather(VG, r("V", 16 + CH * w, 16 + CH * w + CH), R("XT", 0, W + 16), R("nm", LO + P * w, LO + P * w + P))
             D = bank(L)
-            if DIFF[b]:
-                for x in range(0, ROWS, CH):
-                    f = bank(CH)
-                    acc(f, [(R("ID"), r("V", 16 + x, 16 + x + CH)), (R("NEG"), r("V", x, x + CH))])
-                    act(r("M", x, x + CH), f, AF.Abs)
-                    if x % (2 * CH):
-                        y = (x - CH) // 16
-                        acc(R(D[0], y, y + 64), [(win("EW", z), r("M", 16 * y + z, x + CH, 16)) for z in range(16)] + [(R("ID"), R("K0", 0, 64))])
-            else:
-                f = bank(128)
-                add("p", 0.05 + 1024 * PE, [f], [r("V"), R("EW")], lambda f=f, s=s: [g.tensor.matmul(
-                    A(R(f[0], x, 128, 16), L), A(R("V" + s, 16 + x, 16 + ROWS, 16)), A(R("EW", 15, 143, 16)), True, True) for x in range(16)][-1])
-                add("va", {"v": dv(f), "a": da(f)}, [r("S")], [f], lambda e, f=f, s=s: g.vector.tensor_copy(A(R("S" + s), L), A(f, L))
-                    if e == "v" else g.scalar.activation(A(R("S" + s), L), A(f, L), AF.Copy))
-                f = bank(128) if MT else None
-                for y in range(0, 16, 4):
-                    scans([(r("M", L * x, L * x + L), r("V", x, ROWS, 16), r("V", 16 + x, 16 + ROWS, 16)) for x in range(y, y + 4)], 256.0, OP.min, OP.max)
-                    if MT:
-                        add("p", 0.05 + 256 * PE, [f], [r("M", L * y, L * y + 4 * L), R("EW")], lambda f=f, s=s, y=y: [g.tensor.matmul(
-                            A(R(f[0], x, 128, 16)), A(R("M" + s, L * x, L * x + L)), A(R("EW", 15, 143, 16)), True, True) for x in range(y, y + 4)][-1])
-                    else:
-                        acc(D, [(win("EW", x), r("M", L * x, L * x + L)) for x in range(y, y + 4)], y == 0, False)
-                if MT:
-                    acc(D, [(r("S"), R("SH")), (R("ID"), R("K0"))], True, False)
-                    copy(r("S2"), f, "va")
-                    acc(D, [(r("S2"), R("ID"))], False)
-                else:
-                    acc(D, [(r("S"), R("SH")), (R("ID"), R("K0"))], False)
-            half = 0.5 if DIFF[b] else 1.0
-            step(r("C"), D, half, False)
-            step(r("E", 0, L - 1), R(D[0], 1, L), half, True)
-            ts(r("E", P - 1, L, P), R("nm", L * b + P - 1, L * b + L, P), float(DEAD), OP.is_lt)
-            per = CH // L
+            f = bank(128)
+            add("p", 0.03 + 1024 * PE, [f], [r("V"), R("EW")], lambda f=f, s=s, L=L: [g.tensor.matmul(
+                A(R(f[0], x, 128, 16), L), A(R("V" + s, 16 + x, 16 + 16 * L, 16)), A(R("EW", 15, 143, 16)), True, True) for x in range(16)][-1])
+            add("va", {"v": dv(f), "a": da(f)}, [r("S")], [f], lambda e, f=f, s=s, L=L: g.vector.tensor_copy(A(R("S" + s), L), A(f, L))
+                if e == "v" else g.scalar.activation(A(R("S" + s), L), A(f, L), AF.Copy))
+            for y in range(0, 16, 4):
+                scans([(r("M", L * x, L * x + L), r("V", x, ROWS, 16), r("V", 16 + x, 16 + ROWS, 16)) for x in range(y, y + 4)], 256.0, OP.min, OP.max)
+                acc(D, [(win("EW", x), r("M", L * x, L * x + L)) for x in range(y, y + 4)], y == 0, False)
+            mms([(D, r("S"), R("SH", 0, L), False, False, L), (D, R("ID"), R("K0", 0, L), False, True)])
+            step(r("C"), D, False)
+            step(r("E", 0, L - 1), R(D[0], 1, L), True)
+            ts(r("E", P - 1, L, P), R("nm", LO + P - 1, LO + L, P), float(DEAD), OP.is_lt)
+            per = 4 if NX > 2 else 8
             fu = bank(L)
             for y in range(0, 16, per):
-                f = bank(CH)
+                f = bank(per * L)
                 mms([(R(f[0], L * (x - y), L * (x - y + 1)), R("SEL", 128 * x, 128 * x + 128), r("C"), True, True) for x in range(y, y + per)])
-                n = f[0]
-                if y // per in ZC:
-                    n = "CR%d%s" % (y // per, s)
-                    copy(R(n), f, "a")
-                scans([(r("Z", x, ROWS, 16), R(n, L * (x - y), L * (x - y + 1)), r("V", 16 + x, 16 + ROWS, 16)) for x in range(y, y + per)],
+                n, o = f[0], 0
+                if y // per in ZC[b]:
+                    n, o = "CR" + s, L * y
+                    copy(R(n, o, o + per * L), f, "a")
+                scans([(r("Z", x, ROWS, 16), R(n, o + L * (x - y), o + L * (x - y + 1)), r("V", 16 + x, 16 + ROWS, 16)) for x in range(y, y + per)],
                       0.0, OP.mult, OP.max)
-                acc(fu, [(win("WW", x), r("Z", x, ROWS, 16)) for x in range(y, y + per)], y == 0, y + per == 16)
-            scans([(r("cs", L), R("PAT"), r("E"))], 0.0, OP.mult, OP.add)
-            act(r("cs", 0, L), r("cs", L), AF.Relu, -16.0)
+                acc(fu, [(win("WW", x), r("Z", x, ROWS, 16)) for x in range(y, y + per)], y == 0, y + per == 16 and not PV)
+            scans([(r("cs", 128, 128 + L), R("PAT", 0, L), r("E"))], 0.0, OP.mult, OP.add)
+            act(r("cs", 0, L), r("cs", 128, 128 + L), AF.Relu, -16.0)
             f = bank(3 * P)
-            acc(f, [(R("ID"), R("VP"))] + [(R("ID"), r("cs", L + P - 1, None, P), R(f[0], 2 * P + c, 3 * P, 8)) for c in range(4, 8)] +
+            acc(f, [(R("ID"), R("VP"))] + [(R("ID"), r("cs", 128 + P - 1, 128 + L, P), R(f[0], 2 * P + c, 2 * P + 8 * NX, 8)) for c in range(4, 8)] +
                 [(R("W%d" % i), r("cs", i, None, 4), R(f[0], 0, 2 * P)) for i in range(4)])
-            copy(rows("MS", t, b, S_OVER, 3), f)
+            copy(rows(None, t, b, 0, 3), f)
             transmit(0, t, b)
-            scans([(r("cm"), r("C"), R("TWO"))], 0.0, OP.mult, OP.add)
+            scans([(r("cm"), r("C"), R("TWO", 0, L))], 0.0, OP.mult, OP.add)
             c2, hm = R3("c2" + s, 0, NX, 0, P), R3("hm" + s, 0, NX, 0, P)
             lin(c2, r("cm"), 1.0, 1.0)
-            f = bank(L)
-            acc(f, [(R("IDF"), nf), (R("N8"), r("C"))])
+            if t and PJ:
+                f = fj
+                acc(f, [(R("N8"), r("C"))], False, not PN0)
+            else:
+                f = bank(L)
+                acc(f, [(R("IDF"), nf), (R("N8"), r("C"))], True, not PN0)
             scans([(R(f[0], L, 2 * L), r("C"), f)], 0.0, OP.mult, OP.max)
-            tt(r("na"), R(f[0], L, 2 * L), c2, OP.mult)
-            ts(r("ni"), r("na"), 0.25, OP.mult, R("AC", t, t + 1), OP.add)
-            put_names(0, t, b, r("ni"))
+            if PN0:
+                tt(f, R(f[0], L, 2 * L), c2, OP.mult)
+                acc(f, [(R("NEG"), R("K15", 0, L))], False, False)
+                act(r("r0"), f, AF.Identity, R("AB", t, t + 1), -0.25)
+                act(f, f, AF.Identity, R("AC", t, t + 1), 0.25)
+                acc(f, [(R("ID"), r("r0"))], False)
+                put_names(0, t, b, f, plus=MAGIC - WHOLE - HALF)
+            elif t == 0:
+                tt(r("ni"), R(f[0], L, 2 * L), c2, OP.mult)
+                put_names(0, t, b, r("ni"), shift=2)
+            else:
+                tt(r("na"), R(f[0], L, 2 * L), c2, OP.mult)
+                ts(r("ni"), r("na"), 0.25, OP.mult, R("AC", t, t + 1), OP.add)
+                put_names(0, t, b, r("ni"))
             f = bank(L)
-            acc(f, [(R("ID"), R("RAMP")), (R("N8"), r("E"))])
-            scans([(r("y"), R("K0"), f)], 0.0, OP.add, OP.min)
-            ts(r("zo"), r("y", P - 1, L, P), 8192.0, OP.add, float(ROWS - 1), OP.min)
-            ts(R("iv", NX * b, NX * b + NX), r("y", P - 1, L, P), 0.0, OP.is_ge, float(W + 16), OP.mult)
-            glin(R("ZF", NB * b, NB * b + NB), r("Z"), r("zo"), 1.0, -192.0)
+            acc(f, [(R("ID"), R("RAMP", 0, L)), (R("N8"), r("E"))])
+            scans([(R("y", LO, LO + L), R("K0", 0, L), f)], 0.0, OP.add, OP.min)
+            ts(r("zo"), R("y", LO + P - 1, LO + L, P), 8192.0, OP.add, float(ROWS - 1), OP.min)
+            glin(R("ZF", WO, WO + 16 * NX), r("Z"), r("zo"), 1.0, -192.0)
             f = fu
-            if USC:
-                lin(r("r"), f, -1.0, HALF - 0.5 - MAGIC)
+            lin(r("r"), f, -1.0, HALF - 0.5 - MAGIC)
+            if PV:
+                acc(f, [(R("ID"), r("r"))], False)
+                act(r("sq"), f, AF.Square, 592.0 + MAGIC)
+            else:
                 tt(r("v"), f, r("r"), OP.add)
                 act(r("sq"), r("v"), AF.Square, 592.0 + MAGIC)
-            else:
-                copy(r("ui"), f)
-                ts(r("um"), r("ui"), W - 1, OP.bitwise_and)
-                ts(r("v"), r("um"), 592.0, OP.add)
-                tt(r("sq"), r("v"), r("v"), OP.mult)
             f = bank(L)
-            acc(f, [(R("N8"), r("cm")), (R("N15"), r("cm")), (R("N8"), R("CK"))])
+            acc(f, [(R("N97"), r("cm")), (R("N8"), R("CK", 0, L))])
             tt(r("si"), r("sq"), f, OP.subtract)
             ts(hm, r("si"), 5, OP.arith_shift_right, W - 1, OP.bitwise_and)
             copy(r("hu"), hm)
-            xa = XA[t][b]
+            xa = min(XA[t][b], NX)
 
             def distance(w, lo, hi):
                 o, z = r("D2", CH * w + lo, CH * w + hi), r("Z", CH * w + lo, CH * w + hi)
@@ -584,11 +755,19 @@ def rank_program(g, core, T, topo):
                 fd = bank(L)
                 for w in range(NX):
                     distance(w, 0, CH)
-                    if w % 2:
-                        acc(R(fd[0], P * w - P, P * w + P), [(win("EW", x), R3("AD" + s, w - 1, w + 1, x, CH, 16)) for x in range(16)])
+                    if w == NX - 1 or (w == 1 and NX == 4):
+                        z = 2 if w == 3 else 0
+                        acc(R(fd[0], P * z, P * w + P), [(win("EW", x), R3("AD" + s, z, w + 1, x, CH, 16)) for x in range(16)],
+                            z == 0, w == NX - 1 and not PN1)
                 tt(fd, fd, c2, OP.mult)
-                tt(r("nj"), fd, hm, OP.add)
-                put_names(1, t, b, r("nj"))
+                if PN1:
+                    tt(fd, fd, hm, OP.add)
+                    act(r("r0"), fd, AF.Identity, HALF - 0.5 - MAGIC, -1.0)
+                    acc(fd, [(R("ID"), r("r0"))], False)
+                    put_names(1, t, b, fd, plus=MAGIC - HALF)
+                else:
+                    tt(r("nj"), fd, hm, OP.add)
+                    put_names(1, t, b, r("nj"))
             else:
                 y = L // 2
                 for h in (1, 0):
@@ -599,23 +778,26 @@ def rank_program(g, core, T, topo):
                     tt(fd, fd, R3("c2" + s, 0, NX, 16 * h, 16 * h + 16), OP.mult)
                     tt(r("nj", y * h, y * h + y), fd, R3("hm" + s, 0, NX, 16 * h, 16 * h + 16), OP.add)
                     put_names(1, t, b, r("nj", y * h, y * h + y), 16 * h, 16 * h + 16)
-            x, y = NB * b, NB * b + 16 * xa
+            x, y, z = WO, WO + 16 * xa, xa - xa % 2
+            if xa < NX:
+                glin(R("e2", x + 16 * z, x + 16 * NX), r("D2"), r("zo", z), 0.5, 191.75)
             if xa:
                 gtt(R("e1", x, y), r("D2"), r("zo", 0, xa), R("ZF", x, y))
                 lin(R("e2", x, y), R("e1", x, y), 0.5, 95.75)
-            if xa < NX:
-                glin(R("e2", y, x + NB), r("D2"), r("zo", xa), 0.5, 191.75)
         cur["plus"] = 0.0
         if t < RO - 1:
             f = bank(1)
-            acc(f, [(R("ONE"), R("cs%d" % b, x, x + 1)) for b in range(NBK) for x in range(L + P - 1, 2 * L, P)])
+            acc(f, [(R("ONE"), R("cs%d" % b, x, x + 1)) for b in range(NBK) for x in range(128 + P - 1, 128 + P * NXS[b], P)])
             copy(R("ATi"), f)
-            ts(R("ATj"), R("ATi"), 255, OP.bitwise_and); ts(R("AC", t + 1, t + 2), R("ATj"), -0.375, OP.add)
+            ts(R("ATj"), R("ATi"), 255, OP.bitwise_and); ts(R("AC", t + 1, t + 2), R("ATj"), WHOLE if PN0 else -0.375, OP.add)
+            if PN0:
+                ts(R("AB", t + 1, t + 2), R("ATj"), -1.0, OP.mult, HALF - 0.5 - MAGIC, OP.add)
         f = bank(8)
         acc(f, [(win("WW", x), R("ZF", x, NW, 16)) for x in range(16)])
         copy(R("wa"), f); ts(R("wb"), R("wa"), 31, OP.bitwise_and)
+        ts(R("iv"), R("y", P - 1, 2 * NW, P), 0.0, OP.is_ge, float(W + 16), OP.mult)
         tt(R("bs"), R("iv"), R("W32"), OP.add); tt(R("wf"), R("wb"), R("bs"), OP.add); copy(R("WL"), R("wf"))
-        add("v", 0.07 + NW * CY * 3.5, [R("XT")], [R("ZF"), R("e2"), R("WL")],
+        add("v", 0.05 + NW * CY * 3.5, [R("XT")], [R("ZF"), R("e2"), R("WL")],
             lambda: g.vector.tensor_tensor(A(R("XT")).indirect(A(R("WL"))), A(R("ZF")), A(R("e2")), OP.add))
     for q in range(4):
         if q in YV:
@@ -633,25 +815,25 @@ def rank_program(g, core, T, topo):
         if x // 2:
             select(R("QM%d" % x), R("QM%d" % x), pat, OP.not_equal, 1, base + 128)
     t = RO - 1
-    for b in range(NBK):
-        s = str(b)
-        cur["plus"] = FIRST if b == 0 else 0.0
+    for b, nx in enumerate(NXS):
+        s, nb, w0, wo = str(b), 16 * nx, W0[b], 16 * W0[b]
+        cur["plus"] = NBK - 1 - b
         f = join(t, b)
         ts(R("lv" + s), R("of" + s), float(3 * REG), OP.is_lt, 2.0, OP.mult)
-        z = bank(NB)
-        add("p", 0.2, [z], [R("EW"), R("lv" + s)], lambda z=z, s=s: [g.tensor.matmul(
-            A(R(z[0], 16 * w, 16 * w + 16), 8), A(R("EW", 15, 143, 16)), A(R("lv" + s, w, NB, NX)), True, True) for w in range(NX)][-1])
-        add("v", 0.1, [R("yno", NB * b, NB * b + NB)], [z], lambda z=z, b=b: g.vector.tensor_copy(A(R("yno", NB * b, NB * b + NB), 8), A(z, 8)))
-        ts(R3("NB" + s, 0, NX, 0, P), f, float(-HALF), OP.add)
+        z = bank(nb)
+        add("p", 0.15, [z], [R("EW"), R("lv" + s)], lambda z=z, s=s, nx=nx: [g.tensor.matmul(
+            A(R(z[0], 16 * w, 16 * w + 16), 8), A(R("EW", 15, 143, 16)), A(R("lv" + s, w, 16 * nx, nx)), True, True) for w in range(nx)][-1])
+        add("v", cv(1), [R("yno", wo, wo + nb)], [z], lambda z=z, wo=wo, nb=nb: g.vector.tensor_copy(A(R("yno", wo, wo + nb), 8), A(z, 8)))
+        ts(R3("NB" + s, 0, nx, 0, P), f, float(-HALF), OP.add)
         l = []
         for x in (0, 1):
-            o = R3("psz", NX * b, NX * b + NX, 16 * x, 16 * x + 16)
-            l += [(o, R("QM%d" % (2 * x), 0, 128), R3("NB" + s, 0, NX, 0, 16), True, False), (o, R("N8"), R("MQ", 0, NB), False, False),
-                  (o, R("QM%d" % (2 * x + 1), 0, 128), R3("NB" + s, 0, NX, 16, P), False, True)]
+            o = R3("psz", w0, w0 + nx, 16 * x, 16 * x + 16)
+            l += [(o, R("QM%d" % (2 * x), 0, 128), R3("NB" + s, 0, nx, 0, 16), True, False), (o, R("N8"), R("MQ", 0, nb), False, False),
+                  (o, R("QM%d" % (2 * x + 1), 0, 128), R3("NB" + s, 0, nx, 16, P), False, True)]
         mms(l)
-        add("v", NX * 0.1, [R("yl" + s)], [R("psz")], lambda b=b, s=s: [
-            g.vector.transpose(A(R("yl" + s, P * w, P * w + P)), A(R3("psz", NX * b + w, None, 0, P))) for w in range(NX)], inc=NX)
-        dma("s" if b else "a", [("yl", b, b + 1, 1)], [R("yl" + s)], T.yl[:, L * b:L * b + L], T["yl" + s][:, :])
+        add("v", nx * cv(1), [R("yl" + s)], [R("psz")], lambda w0=w0, s=s, nx=nx: [
+            g.vector.transpose(A(R("yl" + s, P * w, P * w + P)), A(R3("psz", w0 + w, None, 0, P))) for w in range(nx)], inc=nx)
+        dma("s" if b % 2 else "a", [("yl", b, b + 1, 1)], [R("yl" + s)], T.yl[:, P * w0:P * w0 + P * nx], T["yl" + s][:, :])
     cur["plus"] = 0.0
     dma("s", [("yn", 0, 1, 1)], [R("yno")], T.yn[:, :], T.yno[0:8, :])
 
@@ -664,10 +846,10 @@ def rank_program(g, core, T, topo):
     for i in range(n - 1, -1, -1):
         x = nodes[i]
         prio[i] = (min(x["d"].values()) if x["e"] == "va" else x["d"][x["e"]] if x["e"] else 0.0) + x["lat"] + LINK + max([prio[k] for k in users[i]] + [0.0])
-    free = {k: 0.0 for k in "vapgs012"}
+    free = {k: 0.0 for k in "vapgs01"}
     gap = lambda a, b: LINK if a != b else 0.0 if a == "p" else SAME
 
-    def sweep(urgency, back, on, urge=0.03, vpen=0.3):
+    def sweep(urgency, back, on, urge, vpen):
         before, after = (users, [x["deps"] for x in nodes]) if back else ([x["deps"] for x in nodes], users)
         left = [len(x) for x in before]
         ready_at, at, fin, took, more = [0.0] * n, [0.0] * n, [0.0] * n, [None] * n, [[] for _ in range(n)]
@@ -682,8 +864,7 @@ def rank_program(g, core, T, topo):
 
         def done(i):
             for k in after[i]:
-                ready_at[k] = max(ready_at[k], fin[i] + gap(took[i], on[k]) + nodes[k if back else i]["lat"]
-                                  + (0.0 if back else pad.get(i, 0.0)))
+                ready_at[k] = max(ready_at[k], fin[i] + gap(took[i], on[k]) + nodes[k if back else i]["lat"])
                 left[k] -= 1
                 if left[k] == 0:
                     release(k)
@@ -732,27 +913,34 @@ def rank_program(g, core, T, topo):
             done(k)
         return max(fin[i] + nodes[i]["lat"] for i in range(n)), order, took, at, fin, banks, more
 
-    def again(res, slow):
-        fin, busy = [0.0] * n, dict(free)
+    def again(res):
+        fin, busy = [None] * n, {k: 0.0 * one for k in free}
         for i in sorted(range(n), key=lambda i: (res[3][i], i)):
             e = res[2][i]
-            st = max([fin[j] + gap(e, res[2][j]) for j in nodes[i]["deps"] + res[6][i]] + [busy[e] if e and e != "2" else 0.0])
+            st = busy[e] if e else 0.0 * one
+            for j in nodes[i]["deps"] + res[6][i]:
+                st = np.maximum(st, fin[j] + gap(e, res[2][j]))
             if e:
-                busy[e] = st + nodes[i]["d"][e] * (slow if e in "2p" else 1.0)
-            fin[i] = busy[e] if e else st + nodes[i]["lat"] * (1.0 if nodes[i]["sem"][0] == "d" else slow)
-        return max(fin)
+                busy[e] = st + nodes[i]["dd"][e]
+            fin[i] = busy[e] if e else st + nodes[i]["ll"]
+        return np.max(fin, axis=0)
 
-    kept = None
-    for first, urge, vpen, wait in RULES:
-        late = [prio[i] + first * nodes[i]["plus"] for i in range(n)]
-        pad.update({i: wait[k] for i, k in kind.items()})
-        for _ in range(PASSES):
-            res = sweep(late, False, [x["e"] for x in nodes], urge, vpen)
-            both = again(res, 1.0) * WEIGHT + again(res, SLOW)
-            if kept is None or both < best:
-                kept, best = res, both
-            late = sweep(res[4], True, res[2], urge, vpen)[4]
-    end, order, took, at, fin, banks, more = kept
+    if not KEPT:
+        for first, urge, vpen in RULES:
+            late = [prio[i] + first * nodes[i]["plus"] for i in range(n)]
+            for _ in range(PASSES):
+                res = sweep(late, False, [x["e"] for x in nodes], urge, vpen)
+                ends = again(res)
+                KEPT.setdefault("scale", ends)
+                both = float(np.sum(WEIGHT * ends / KEPT["scale"]))
+                if "res" not in KEPT or both < KEPT["both"]:
+                    KEPT.update(res=res, both=both, ends=ends, sends=[sends[k] for k in res[1] if k in sends], rule=(first, urge, vpen))
+                late = [z + KEEP * first * x["plus"] for z, x in zip(sweep(res[4], True, res[2], urge, vpen)[4], nodes)]
+        if TRIES:
+            polish(nodes, users, sends)
+    if g is None:
+        return
+    end, order, took, at, fin, banks, more = KEPT["res"]
     phys.update(banks)
     for i, x in enumerate(nodes):
         x["e"], x["t"], x["deps"] = took[i], at[i], sorted(set(x["deps"] + more[i]))

@@ -10,10 +10,11 @@ LM = P * max(NXS)
 W = 4096
 DEAD = 4096
 HALF = 2048
-REG = LM
-S_OVER, S_OWN, S_CNT, S_N = 0, 1, 2, 3
-MROWS = S_N + 8
-LS = 49
+CELLS = 50
+NR, S_C, MROWS = (4, 0), 8, 9
+FULL = 2048
+STAGE = ("psz", "psy")
+UK = [127] + [-2 ** _i for _i in range(6)] + [64, 128]
 CH = 512
 MAGIC = 786432.0
 AF = ActivationFunctionType
@@ -21,25 +22,31 @@ OP = AluOpType
 
 XA = ((2, 2), (2, 2), (2, 2))
 ZC = ((1, 3), (1, 3))
-YV = (1,)
+YV = ()
 MERGE = 0
-LATE2 = 1
+MERGEL = 0
+PACK = 1
+FUSE = 0
+UROWS = 10
 ALT = 0
-DRG = 1
-PV = 0
-PJ = 0
-PN0 = 0
-PN1 = 0
-WHOLE = 12582912.0
+HO = (1, 0)
+CQ = "a"
+SG = ()
+UG = ()
+HW = ((0, 4),)
+HH = ((HW, HW),) * 3
+RV = (((), ()),) * 3
 VG = "va"
-GG = "va"
+NP = (("v", 0, 4), ("v", 4, 8))
+NJ = (((NP, NP), (NP, NP)),) * 2
+GG = "a"
 
-SCRATCH = {"psz": ("psum", [128, 16, 32], "float32")}
-NPS = 7
+SCRATCH = {_n: ("psum", [128, 8, 64], "float32") for _n in STAGE}
+NPS = 8 - len(SCRATCH)
 for _i in range(NPS):
     SCRATCH["ps%d" % _i] = ("psum", [128, 512], "float32")
 
-SIZE, PLACE, FILL = {"psz": (512, "float32")}, {}, {"float32": 0, "int32": 0, "uint16": 0, "bfloat16": 0, "float16": 0}
+SIZE, PLACE, FILL = {_n: (512, "float32") for _n in STAGE}, {}, {"float32": 0, "int32": 0, "uint16": 0, "bfloat16": 0, "float16": 0}
 
 
 def _sb(name, n, dtype, own=False):
@@ -57,35 +64,35 @@ def _sb(name, n, dtype, own=False):
 _sb("XT", 2 * W + 16, "bfloat16", True); _sb("YX", 2048, "bfloat16", True)
 _sb("wli", 2 * NW, "int32", True); _sb("wni", NW, "int32", True); _sb("thi", 1, "int32", True); _sb("wti", 1, "int32", True)
 _sb("MS", (RO * NBK * MROWS, P), "float16"); _sb("MR", (2 * RO * NBK * MROWS, P), "float16")
-_sb("US", (16, 16), "float16"); _sb("UR", (16, 16), "float16")
+_sb("US", (UROWS * NBK + 16, 16), "float16"); _sb("UR", (UROWS * NBK + 16, 16), "float16")
 _sb("OT", (8, P), "float16"); _sb("yno", NW, "float32", True)
-for _n, _k in (("wnf", NW + 1), ("E8", 128), ("cols", 16), ("ZF32", 128), ("YI", 56), ("RA", LM), ("W5", 8), ("IDF", 128), ("NF", 2 * NW),
-               ("AC", 4), ("AB", 4), ("W32", 8), ("iv", 8), ("bs", 8), ("wf", 8), ("MK", 16), ("y", 2 * NW)):
+for _n, _k in (("wnf", NW + 1), ("E8", 128), ("cols", 16), ("ZF32", 128), ("YI", 16), ("HF", 8), ("R2", 8), ("bf", 8), ("pre", 8), ("pb", 8), ("RA", LM), ("W5", 8), ("IDF", 128), ("XB", 512), ("MK8", 8), ("DF", 1024),
+               ("AC", 4), ("W32", 8), ("iv", 8), ("bs", 8), ("wf", 8), ("MK", 16), ("y", 2 * NW)):
     _sb(_n, _k, "float32")
-for _n, _k in (("ci", 3), ("ATi", 1), ("ATj", 1), ("wa", 8), ("wb", 8)):
+for _n, _k in (("ci", 3), ("ATi", 1), ("ATj", 1), ("bi", 8), ("bj", 8), ("wa", 8), ("wb", 8)):
     _sb(_n, _k, "int32")
-for _n, _k in (("ID", 128), ("NEG", 128), ("N8", 128), ("K15", 128), ("JM", 128), ("W0", 128), ("W1", 128), ("W2", 128), ("W3", 128),
-               ("ONE", 128), ("EW", 144), ("WW", 144), ("EN", 144), ("SEL", 2048), ("LUT", 16 * LS), ("VY", 56), ("K0", LM), ("PAT", LM),
-               ("TWO", LM), ("MQ", 128), ("CK", LM), ("VP", 3 * P), ("DR", 16 * 144), ("ZF", NW), ("e1", NW), ("e2", NW),
-               ("ZB", 576), ("SH", 128), ("E9", 9), ("CG", 128), ("BLK", 128)):
+for _n, _k in (("ID", 128), ("NEG", 128), ("N8", 128), ("K15", 128), ("U", 9 * 128), ("TD", 128), ("WD", 144),
+               ("ONE", 128), ("EW", 144), ("WW", 144), ("EN", 144), ("SEL", 2048), ("LUT", FULL + 16), ("VY", 7 * 16), ("K0", LM + 4), ("PAT", LM),
+               ("TWO", LM), ("MQ", 128), ("CK", LM), ("DR", 16 * 144), ("ZF", NW), ("e1", NW), ("e2", NW),
+               ("ZB", 576), ("SH", 132), ("SHF", 128), ("DE", 1024), ("BH", 64), ("E9", 9), ("CG", 128), ("BLK", 128)):
     _sb(_n, _k, "bfloat16")
 for _n, _k in (("N97", 128), ("RAMP", LM), ("IN", 2 * NW), ("IM", 2 * NW), ("NLi", 2 * NW)):
     _sb(_n, _k, "float16")
 for _i in range(4):
     _sb("PM%d" % _i, 128, "bfloat16"); _sb("QM%d" % _i, 128, "bfloat16"); _sb("XM%d" % _i, 128, "bfloat16")
 for _i in sorted(set(NXS)):
-    _sb("BW%d" % _i, 16 * _i, "bfloat16")
-_sb("nm", 2 * NW, "uint16"); _sb("WL", 8, "uint16")
+    _sb("BW%d" % _i, 16 * _i, "bfloat16"); _sb("BE%d" % _i, 16 * _i, "bfloat16")
+_sb("nm", (2 * NBK, 64), "uint16"); _sb("NF", (2 * NBK, 64), "float32"); _sb("WL", 8, "uint16")
 for _b, _x in enumerate(NXS):
     _s, _l = str(_b), P * _x
     for _n, _k, _d in (("V", 16 * _l + 16, "bfloat16"), ("M", 16 * _l, "bfloat16"), ("Z", 16 * _l, "bfloat16"), ("D2", 16 * _l, "bfloat16"),
-                       ("AD", (_x, CH), "bfloat16"), ("cs", 256, "bfloat16"), ("lv", 16 * _x, "bfloat16"), ("S", 128, "bfloat16"),
+                       ("AD", (_x, CH), "bfloat16"), ("cs", 2 * _l, "bfloat16"), ("lv", 16 * _x, "bfloat16"), ("S", 128, "bfloat16"),
                        ("r", _l, "bfloat16"), ("r0", _l, "bfloat16"), ("C", _l, "bfloat16"), ("E", _l, "bfloat16"),
                        ("cm", _l, "bfloat16"), ("c2", (_x, P), "bfloat16"), ("na", _l, "float32"), ("ni", _l, "int32"),
                        ("zo", _x, "uint16"), ("v", _l, "float32"), ("sq", _l, "float32"), ("si", _l, "int32"), ("hm", (_x, P), "int32"),
                        ("hu", _l, "uint16"), ("nj", _l, "int32"), ("of", 16 * _x, "uint16"), ("CR", 16 * _l, "bfloat16"),
-                       ("n0", (_x, P), "int32"), ("n1", (_x, P), "int32"), ("WN", 4 * REG, "float32"), ("G", 192 * _x, "bfloat16"),
-                       ("IX", (_x, 16), "uint16"), ("NB", (_x, P), "float16"), ("N", 256 * _x, "float16")):
+                       ("n0", (_x, P), "int32"), ("n1", (_x, P), "int32"), ("WN", 2 * _x * CELLS, "float32"), ("G", 96 * _x, "bfloat16"), ("GH", (2, 48 * _x), "bfloat16"),
+                       ("IX", (_x, 8), "uint16"), ("NB", (_x, P), "float16"), ("N", 256 * _x, "float16"), ("NA", 256 * _x, "float32")):
         _sb(_n + _s, _k, _d)
     _sb("yl" + _s, _l, "float32", True)
 for _d in FILL:
@@ -100,35 +107,42 @@ def calls(t, b):
     s, nx = MROWS * (t * NBK + b), NXS[b]
     both = lambda lo, m: [(h, "M", s + lo, 2 * s + MROWS * h + lo, m) for h in (0, 1)]
     if t < RO - 1:
-        early = [(1, both(0, S_N + nx))] if MERGE else [(0, both(0, S_N)), (1, both(S_N, nx))]
-        late = both(S_N + nx, nx)
-        return early + ([(2, late[:1]), (2, late[1:])] if LATE2 else [(2, late)])
-    return [(0, both(S_OVER, 1)[1:])] + [(1 + e, [(1, "U", 2 * W0[b] + nx * e, 2 * W0[b] + nx * e, nx)]) for e in (0, 1)]
+        early = [[(0, both(S_C, 1)), (1, both(NR[0], nx))], [(1, both(NR[0], nx + 1))], [(0, both(S_C, 1))]][MERGE]
+        more = nx if MERGE == 2 else 0
+        late = [(2 + h, both(2 * h, 2 + more * h)) for h in HO]
+        u = UROWS * NBK + nx * (t * NBK + b)
+        return early + (late if FUSE else [(k, x[:1]) for k, x in late] + [(4, [(1, "U", u, u, nx)] if PACK else both(0, nx + more)[1:])])
+    up = lambda lo, m: [(1, "U", UROWS * b + lo, UROWS * b + lo, m)]
+    return [[(0, up(0, 2)), (1, up(2, nx)), (2, up(2 + nx, nx))], [(1, up(0, 2 + nx)), (2, up(2 + nx, nx))], [(0, up(0, 2)), (2, up(2, 2 * nx))]][MERGEL]
 
 
 SEMAPHORES = ["sv", "sa", "st", "sg", "loc"] + ["d%d" % i for i in range(8 + NBK)]
 SEMAPHORES += ["m%d%d%d%d" % (k, t, b, x[0]) for t in range(RO) for b in range(NBK) for k, ws in calls(t, b) for x in ws]
 
-SPEED = np.array([1.2, 1.03, 1.45, 1.1])
+SPEED = np.array([1.2, 1.45, 1.03, 1.05, 1.0])
 CY = 0.00083 * SPEED
 PE = 0.00042 * SPEED
-GA = np.array([1.45, 1.2, 2.0, 1.3])
+GA = np.array([1.5, 1.9, 1.2, 1.56, 1.1])
 FV = 0.015
 FA = 0.04
 XLOAD = 5.0
-HOP0 = np.array([1.8, 1.8, 1.8, 2.4])
-HOP1 = np.array([2.7, 2.7, 2.7, 3.8])
-CALL = np.array([1.0, 1.0, 1.0, 1.3])
+HOP0 = np.array([1.4, 1.4, 1.8, 1.2, 2.0])
+HOP1 = np.array([2.1, 2.1, 2.7, 2.0, 3.2])
+CALL = np.array([0.9, 0.9, 1.0, 0.8, 0.7])
+HALFE = 0.3
+BYTE = 0.0015
 ONCE = 1.5
-LINK = 0.1
-SAME = 0.08
-WEIGHT = np.array([2.0, 1.0, 1.0, 1.0])
-PASSES = 4
-KEEP = 0.0
+LINK = np.array([0.13, 0.1, 0.1, 0.18, 0.12])
+SAME = np.array([0.11, 0.1, 0.08, 0.16, 0.1])
+SEED = 0
+LEFT = 0.2
+WEIGHT = np.array([1.5, 0.8, 1.2, 1.0, 0.5])
+PASSES = 5
 BIG = 0.05
-TRIES = 6000
-SHAKE = 0.0001
-RULES = [(f, 0.03, v) for f in (1, 3, 6) for v in (0.1, 0.3, 0.6)]
+ROUNDS = ((4, 1000), (1, 26000))
+SHAKE = 0.005
+RULES = [(f, u, v) for f in (1, 3, 6) for u in (0.015, 0.04) for v in (0.1, 0.3)]
+AGAIN, POOL, NOISE = 100, 8, 0.7
 KEPT = {}
 
 
@@ -137,8 +151,8 @@ def leg(topo, src, dst, t, b, k):
         return dst, topo.engines(src, dst)
     c = [x for x in topo.cores_of(src) if x != src and topo.die(x) == topo.die(src) and topo.may_write(x, dst)]
     e = topo.engines(src, c[0])
-    alone = t == RO - 1 or (k == 2 and LATE2)
-    return c[(b + (ALT if k < 2 else 0)) % len(c)], (e if alone else e[len(e) // 2:])
+    alone = t == RO - 1 or (k >= 2 and not FUSE)
+    return c[(b + (ALT if k == 3 else 0)) % len(c)], (e if alone else e[len(e) // 2:])
 
 
 def transfer(T, topo, core, dst, src_ap, dst_ap, engines, sem):
@@ -182,80 +196,150 @@ def clash(a, b):
     return True
 
 
-def polish(nodes, users, sends):
+def polish(nodes, sends, starts):
     n, m = len(nodes), len(SPEED)
-    res = KEPT["res"]
-    rng = np.random.default_rng(0)
-    deps = [x["deps"] for x in nodes]
+    rng = np.random.default_rng(SEED)
+    deps, reach, users = [], [], [[] for _ in range(n)]
+    for i, x in enumerate(nodes):
+        cover = 0
+        for j in x["deps"]:
+            cover |= reach[j]
+        deps.append([j for j in x["deps"] if not cover >> j & 1])
+        reach.append(cover | sum(1 << j for j in x["deps"]))
+        for j in deps[i]:
+            users[j].append(i)
     dur = [[{e: float(x["dd"][e][k]) for e in x["dd"]} for x in nodes] for k in range(m)]
     lat = [[float(x["ll"][k]) for x in nodes] for k in range(m)]
+    gaps = [(0.0, float(SAME[k]), float(LINK[k])) for k in range(m)]
+    held = [x["banks"] for x in nodes]
     total = {}
     for x in nodes:
         for y in x["banks"]:
             total[y] = total.get(y, 0) + 1
+    kind = lambda e, f: 2 if e != f else 0 if e == "p" else 1
+    STEP = 32
 
-    def run(order, on, k, plan):
-        fin, why, busy, last = [0.0] * n, [-1] * n, {}, {}
-        d, l = dur[k], lat[k]
-        make = plan is None
-        if make:
-            plan, banks, left, bfree, blast = [()] * n, {}, dict(total), [0.0] * NPS, [[] for _ in range(NPS)]
-        for i in order:
-            e = on[i]
-            if make:
-                for y in nodes[i]["banks"]:
-                    if y not in banks:
-                        z = [z for z in range(NPS) if bfree[z] is not None]
-                        if not z:
-                            return None
-                        z = min(z, key=lambda z: bfree[z])
-                        banks[y], bfree[z] = z, None
-                        plan[i] = plan[i] + tuple(blast[z])
-                        blast[z] = []
-            st, w = (busy.get(e, 0.0), last.get(e, -1)) if e else (0.0, -1)
-            for js in (deps[i], plan[i]):
-                for j in js:
-                    f = on[j]
-                    t = fin[j] + (LINK if e != f else 0.0 if e == "p" else SAME)
-                    if t > st:
-                        st, w = t, j
-            why[i] = w
+    def first(order, on, base, a, old):
+        d, l, gp = dur[0], lat[0], gaps[0]
+        fin, waits, plan, marks = list(old[0]), list(old[1]), list(old[2]), old[4][:a // STEP + 1]
+        banks, left, bfree, blast, last = marks[-1]
+        banks, left, bfree, blast, last = dict(banks), dict(left), list(bfree), list(blast), dict(last)
+        busy = {e: fin[last[e]] if e in last else 0.0 for e in "vapgs01"}
+        for p in range(a, n):
+            if p % STEP == 0 and p > a:
+                marks.append((dict(banks), dict(left), list(bfree), list(blast), dict(last)))
+            i = order[p]
+            e, h, w = on[i], held[i], base[i]
+            plan[i] = ()
+            for y in h:
+                if y not in banks:
+                    z = [z for z in range(NPS) if bfree[z] is not None]
+                    if not z:
+                        return None
+                    z = min(z, key=lambda z: bfree[z])
+                    banks[y], bfree[z] = z, None
+                    plan[i] += blast[z]
+                    w = w + [(j, kind(e, on[j])) for j in blast[z]]
+                    blast[z] = ()
+            waits[i] = w
+            st = busy[e] if e else 0.0
+            for j, c in w:
+                t = fin[j] + gp[c]
+                if t > st:
+                    st = t
             if e:
                 fin[i] = busy[e] = st + d[i][e]
                 last[e] = i
             else:
                 fin[i] = st + l[i]
-            if make:
-                for y in nodes[i]["banks"]:
-                    left[y] -= 1
-                    blast[banks[y]].append(i)
-                    if not left[y]:
-                        bfree[banks[y]] = fin[i]
-        return fin, why, plan, banks if make else None
+            for y in h:
+                left[y] -= 1
+                blast[banks[y]] += (i,)
+                if not left[y]:
+                    bfree[banks[y]] = fin[i]
+        return fin, waits, plan, banks, marks
 
-    def score(order, on):
-        a = run(order, on, 0, None)
-        if a is None:
+    def run(order, on, k, waits, a, old, last):
+        fin, d, l, gp = list(old[k]), dur[k], lat[k], gaps[k]
+        fin2, d2, l2, gp2 = list(old[k + 1]), dur[k + 1], lat[k + 1], gaps[k + 1]
+        busy = {e: (fin[last[e]], fin2[last[e]]) if e in last else (0.0, 0.0) for e in "vapgs01"}
+        busy[None] = (0.0, 0.0)
+        for i in order[a:]:
+            e = on[i]
+            st, st2 = busy[e]
+            for j, c in waits[i]:
+                t = fin[j] + gp[c]
+                if t > st:
+                    st = t
+                t = fin2[j] + gp2[c]
+                if t > st2:
+                    st2 = t
+            if e:
+                fin[i], fin2[i] = busy[e] = st + d[i][e], st2 + d2[i][e]
+            else:
+                fin[i], fin2[i] = st + l[i], st2 + l2[i]
+        return fin, fin2
+
+    def score(order, on, base, a, old, limit):
+        a -= a % STEP
+        x = first(order, on, base, a, old[3])
+        if x is None:
             return None
-        rs = [a] + [run(order, on, k, a[2]) for k in range(1, m)]
-        ends = np.array([max(z[0]) for z in rs])
-        return float(np.sum(WEIGHT * ends / KEPT["scale"])), ends, rs
+        fins, part = [x[0]], [wt[0] * (max(x[0]) + LEFT * sum(x[0]) / n)]
+        for k in range(1, m, 2):
+            if sum(part) + 0.997 * sum(old[4][k:]) > limit:
+                return None
+            fins += run(order, on, k, x[1], a, old[2], x[4][a // STEP][4])
+            part += [wt[j] * (max(fins[j]) + LEFT * sum(fins[j]) / n) for j in (k, k + 1)]
+        return sum(part), [max(z) for z in fins], fins, x, part
 
-    order, on = sorted(range(n), key=lambda i: (res[3][i], i)), list(res[2])
-    cur = best = (score(order, on), order, on)
-    for it in range(TRIES):
-        (sc, ends, rs), order, on = cur
-        fin, why = rs[int(rng.integers(m))][:2]
-        i, path = max(range(n), key=lambda i: fin[i]), []
-        while i >= 0:
-            if why[i] >= 0 and on[i] and why[i] not in deps[i]:
-                path.append(i)
-            i = why[i]
-        if not path:
-            break
-        i = path[int(rng.integers(len(path)))]
-        j = why[i]
-        new, to = list(order), on
+    def chain(z, order, on, k):
+        fin, waits, gp, d = z[2][k], z[3][1], gaps[k], dur[k]
+        i, path = fin.index(max(fin)), []
+        p = order.index(i)
+        while True:
+            st, w, e = 0.0, -1, on[i]
+            for j, c in waits[i]:
+                if fin[j] + gp[c] > st:
+                    st, w = fin[j] + gp[c], j
+            if e and fin[i] - d[i][e] > st + 1e-9:
+                p -= 1
+                while on[order[p]] != e:
+                    p -= 1
+                w = order[p]
+            elif w < 0:
+                return path
+            else:
+                while order[p] != w:
+                    p -= 1
+            if e and w not in deps[i]:
+                path.append((i, w))
+            i = w
+
+    wt = [float(x) for x in WEIGHT / KEPT["scale"]]
+    runs = []
+    for res in starts:
+        order, on = sorted(range(n), key=lambda i: (res[3][i], i)), list(res[2])
+        base = [[(j, kind(on[i], on[j])) for j in deps[i]] for i in range(n)]
+        none = (0.0, [0.0] * m, [[0.0] * n] * m, ([0.0] * n, base, [()] * n, {}, [({}, total, [0.0] * NPS, [()] * NPS, {})]), [0.0] * m)
+        runs.append((score(order, on, base, 0, none, 1e9), order, on, base))
+    plan = [(r, x, it) for r, (k, tries) in enumerate(ROUNDS) for x in range(min(k, len(runs))) for it in range(tries)]
+    for r, x, it in plan:
+        if it == 0:
+            if x == 0:
+                runs.sort(key=lambda z: z[0][0])
+            cur = best = runs[x]
+            paths = {}
+        runs[x] = best
+        heat = SHAKE * (1 - it / ROUNDS[r][1] if r == len(ROUNDS) - 1 else 1)
+        old, order, on, base = cur
+        sc = old[0]
+        k = int(rng.integers(m))
+        if k not in paths:
+            paths[k] = chain(old, order, on, k)
+        path = paths[k]
+        i, j = path[int(rng.integers(len(path)))]
+        new, to, eb = list(order), on, base
         u = rng.random()
         if u > 1 - BIG:
             b = order.index(i)
@@ -270,9 +354,11 @@ def polish(nodes, users, sends):
             if nodes[k]["e"] != "va":
                 continue
             to = list(on); to[k] = "v" if on[k] == "a" else "a"
+            a, eb = order.index(k), list(base)
+            for y in [k] + users[k]:
+                eb[y] = [(x, kind(to[y], to[x])) for x in deps[y]]
         else:
-            pos = {k: p for p, k in enumerate(order)}
-            a, b = pos[j], pos[i]
+            a, b = order.index(j), order.index(i)
             if u < 0.65:
                 mv = {i}
                 for k in reversed(order[a:b]):
@@ -290,13 +376,13 @@ def polish(nodes, users, sends):
                 if i in mv:
                     continue
                 new[a:b + 1] = [k for k in order[a:b + 1] if k not in mv] + [k for k in order[a:b + 1] if k in mv]
-        z = score(new, to)
-        if z is not None and z[0] < sc - SHAKE * (1 - it / TRIES) * np.log(rng.random()):
-            cur = (z, new, to)
+        limit = sc - heat * np.log(rng.random())
+        z = score(new, to, eb, a, old, limit)
+        if z is not None and z[0] < limit:
+            cur, paths = (z, new, to, eb), {}
             if z[0] < best[0][0]:
                 best = cur
-    (sc, ends, rs), order, on = best
-    fin, _, plan, banks = rs[0]
+    (sc, ends, _, (fin, _, plan, banks, _), _), order, on, _ = best
     at = [fin[i] - (dur[0][i][on[i]] if on[i] else lat[0][i]) for i in range(n)]
     order = [i for i in order if on[i]]
     KEPT.update(res=(ends[0], order, on, at, fin, banks, [list(x) for x in plan]), both=sc, ends=ends, sends=[sends[k] for k in order if k in sends])
@@ -360,7 +446,8 @@ def rank_program(g, core, T, topo):
     def R3(name, w0, w1, lo, hi, step=1):
         k = SCRATCH[name][1][2]
         if w1 is None:
-            return (name, k * w0 + lo, k * w0 + hi, 1, (slice(None), w0, slice(lo, hi)), hi - lo, [(k * w0 + lo, k * w0 + hi)])
+            return (name, k * w0 + lo, k * w0 + hi, 1, (slice(None), w0, slice(lo, hi, step) if step > 1 else slice(lo, hi)),
+                    -(-(hi - lo) // step), [(k * w0 + lo, k * w0 + hi)])
         return (name, k * w0 + lo, k * (w1 - 1) + hi, 1, (slice(None), slice(w0, w1), slice(lo, hi, step) if step > 1 else slice(lo, hi)),
                 (w1 - w0) * -(-(hi - lo) // step), [(k * w + lo, k * w + hi) for w in range(w0, w1)])
 
@@ -469,9 +556,9 @@ def rank_program(g, core, T, topo):
         return add("g", 0.13 + num(o) * 2 * CY, [o], [], (lambda: g.iota(A(o), pattern, base, cm)) if ints else
                    (lambda: g.iota(A(o), pattern, base, cm, allow_small_or_imprecise_dtypes=True)))
 
-    x = dma("s", [R("wni")], [], T.wni[0:8, :], T.wn[:, :])
-    dma("s", [R("XT", 0, W)], [], T.XT[:, 0:W], T.xv[:, :], XLOAD, [x])
-    x = dma("a", [R("wli")], [], T.wli[:, :], T.wl[:, :], 2.5)
+    dma("s", [R("XT", 0, W)], [], T.XT[:, 0:W], T.xv[:, :], XLOAD)
+    x = dma("a", [R("wni")], [], T.wni[0:8, :], T.wn[:, :])
+    x = dma("a", [R("wli")], [], T.wli[:, :], T.wl[:, :], 2.5, [x])
     x = dma("a", [R("thi")], [], T.thi[0:8, :], T.th[:, :], 2.0, [x])
     dma("a", [R("wti")], [], T.wti[:, :], T.wt[:, :], 2.0, [x])
     col = lambda i: R("cols", i, i + 1)
@@ -507,61 +594,78 @@ def rank_program(g, core, T, topo):
         mms([(R3("psz", w0, w1, 16 * i, 16 * i + 16), R("PM%d" % (2 * j + i)), R3("OT", w0, w1, 16 * j, 16 * j + 16),
               j == 0, j == 1) for i in (0, 1) for j in (0, 1)])
         z = R3("psz", w0, w1, 0, P)
-        ts(R("nm", x, y), z, float(HALF), OP.add, float(DEAD), OP.min); lin(R("NF", x, y), z, 1.0, float(HALF))
+        ts(R3("nm", 2 * b, 2 * b + 2, 0, 64), z, float(HALF), OP.add, float(DEAD), OP.min)
+        lin(R3("NF", 2 * b, 2 * b + 2, 0, 64), z, 1.0, float(HALF))
     cur["plus"] = 0.0
     ts(THR, R(bn[0], NW, NW + 1), 0.5, OP.mult)
     ts(TH, THR, 0.25, OP.add, 400.0, OP.mult); ts(TN, TH, -1.0, OP.mult)
     mset(R("XT", W, W + 16), 255.0)
     pick(R("ID"), [[-1, 128]], 0)
     lin(R("N97"), R("ID"), -9776.0, 0.0, "v")
-    for n, k in (("NEG", -1), ("N8", -8192), ("JM", REG - 15), ("W0", 1 - LS), ("W1", -LS), ("W2", -2 * LS),
-                 ("W3", 4 * LS), ("IDF", 1)):
+    for n, k in (("NEG", -1), ("N8", -8192), ("IDF", 1)):
         lin(R(n), R("ID"), float(k), 0.0)
-    pick(R("SH"), [[-1, 128]], 0, -0.5); select(R("SH"), R("SH"), [[-1, 128]], OP.not_equal, -0.5, 1)
+    U = [R("NEG") if k == -1 else R("U", 128 * i, 128 * i + 128) for i, k in enumerate(UK)]
+    for i, k in enumerate(UK):
+        if i in UG:
+            pick(U[i], [[-1, 128]], 0, k)
+        elif k != -1:
+            lin(U[i], R("ID"), float(k), 0.0, CQ)
+    pick(R("SH", 0, 128), [[-1, 128]], 0, -0.5); select(R("SH", 0, 128), R("SH", 0, 128), [[-1, 128]], OP.not_equal, -0.5, 1)
+    pick(R("SH", 128), [[-P, 4]], 1 - P, -0.5)
     copy(WC, R("wti")); mset(R("EW"), 0.0); mset(R("WW"), 0.0); mset(R("ONE"), 1.0)
     select(R("E9"), R("ONE", 0, 9), [[-16, 9]], OP.is_ge, 0, 0); select(R("EW", 15, 144, 16), R("E9"), [[16, 9]], OP.is_ge, 0, 15, -1)
     ts(R("WW", 15, 144, 16), R("EW", 15, 144, 16), WC, OP.mult)
-    for n, k in (("K0", 0.0), ("PAT", 1.0), ("TWO", 2.0), ("MQ", -0.25), ("CK", 167.0 / 32), ("VP", 0.0)):
+    if any(map(any, RV)):
+        lin(R("EN"), R("EW"), -1.0, 0.0)
+    for n, k in (("K0", 0.0), ("PAT", 1.0), ("TWO", 2.0), ("MQ", -0.25), ("CK", 167.0 / 32), ("HF", 0.5)):
         mset(R(n), k)
-    mset(R("K0", 0, LM, P), 16384.0); mset(R("PAT", 0, LM, P), 0.0); mset(R("VP", 3, 2 * P, 4), 8.0 * LS)
+    mset(R("K0", 0, LM, P), 16384.0); mset(R("K0", LM), 8 * 255.0); mset(R("PAT", 0, LM, P), 0.0); mset(R("LUT", FULL), 0.0)
     for b, nx in enumerate(NXS):
         mset(R("V%d" % b, 0, 16), 0.0)
-        mset(R("WN%d" % b, 3 * REG if P * nx == REG else 0), float(DEAD - HALF))
-        if nx < 4:
-            mset(R("cs%d" % b), 0.0)
-    if PN0:
-        mset(R("AC", 0, 1), WHOLE); mset(R("AB", 0, 1), HALF - 0.5 - MAGIC); mset(R("K15"), 1.5)
-    iota(R("YI"), [[1, 56]], 0, 0); iota(R("CG"), [[1, 8], [0, 16]], 0, 0)
+    for n in sorted(set(STAGE)):
+        mset(R3(n, 0, 8, 48, CELLS), float(DEAD - HALF))
+    iota(R("YI"), [[1, 16]], 0, 0); iota(R("CG"), [[1, 8], [0, 16]], 0, 0)
     ts(R("MK"), R("YI", 0, 16), LA, OP.is_equal); ts(R("BLK"), R("CG"), GP, OP.is_equal)
-    for x in range(16):
-        lin(R("SEL", 128 * x, 128 * x + 128), R("BLK"), R("MK", x, x + 1), 0.0)
+    mset(R("ZB", 144), 0.0)
+    for x in range(0, 16, 4):
+        if x // 4 in SG:
+            pick(R("SEL", 128 * x, 128 * x + 512), [[-1, 4], [-16, 8], [0, 16]], -x)
+        else:
+            for y in range(x, x + 4):
+                lin(R("SEL", 128 * y, 128 * y + 128), R("BLK"), R("MK", y, y + 1), 0.0)
     iota(R("RA"), [[16, LM]], 0, 0); ts(R("RAMP"), R("RA"), LA, OP.add)
     for x in sorted(set(NXS)):
-        iota(R("BW%d" % x), [[0, 8], [16 * x, 2], [16, x]], 0, 0)
-    iota(R("W5"), [[512, 8]], 0, 0)
+        iota(R("BW%d" % x), [[0, 8], [CELLS * x, 2], [CELLS, x]], 0, 0); lin(R("BE%d" % x), R("BW%d" % x), 1.0, 48.0)
+    iota(R("W5"), [[512, 8]], 0, 0); iota(R("BH"), [[0, 16], [CELLS, 4]], 0, 0)
+    pick(R("SHF"), [[-1, 128]], 16); select(R("SHF"), R("SHF"), [[-1, 128]], OP.not_equal, 1, -112)
+    tt(R("MK8"), R("MK", 0, 8), R("MK", 8, 16), OP.add)
+    for e, j in sorted({(e, j) for x in NJ for y in x for z in y for e, j0, j1 in z for j in range(j0, j1)}):
+        lin(R("DE" if e == "v" else "DF", 128 * j, 128 * j + 128), R("SHF"), R("MK8", j, j + 1), 0.0, CQ)
+    for x in range(4):
+        pick(R("XB", 128 * x, 128 * x + 128), [[-16, 8], [-1, 8], [1000, 2]], -8 * (x // 2) - 1000 * (x % 2), zero="ZF32")
     ts(L32, LA, 32.0, OP.mult); ts(R("W32"), R("W5"), L32, OP.add)
-    if DRG:
-        mset(R("ZB", 144), 0.0)
-        for x in range(0, 16, 4):
-            pick(R("DR", 144 * x, 144 * x + 576), [[-1, 4], [-16, 9], [1000, 16]], 16 - x - 15000)
-        select(R("DR", 15, None, 144), R("DR", 15, None, 144), [[-1, 16]], OP.not_equal, 1, -112)
-    else:
-        mset(R("EN"), 0.0); copy(R("EN", 31, 128, 16), R("EW", 15, 112, 16)); copy(R("EN", 15, 16), R("EW", 127, 128))
-        for x in range(16):
-            lin(R("DR", 144 * x, 144 * x + 144), R("EN"), R("MK", x, x + 1), 0.0)
+    for x in range(0, 16, 4):
+        pick(R("DR", 144 * x, 144 * x + 576), [[-1, 4], [-16, 9], [1000, 16]], 16 - x - 15000)
+    select(R("DR", 15, None, 144), R("DR", 15, None, 144), [[-1, 16]], OP.not_equal, 1, -112)
     for x in range(4):
         pick(R("XM%d" % x), [[-16, 8], [1000, 2], [-2, 8]], -(x % 2) - 1000 * (x // 2))
-    ts(LV, LA, 0.5, OP.add, 200.0, OP.mult)
-    add("a", 1.45, [R("VY")], [R("YI"), LV], lambda: g.scalar.activation(A(R("VY")), A(R("YI")), AF.Sigmoid, bias=A(LV), scale=-200.0))
-    for part in range(2):
-        b0 = bank(8 * LS); l = []
-        for j in range(8):
-            c = 0
-            for p in range(4):
-                c += (j >> (p - 1) & 1) if p else 0
-                l.append((R(b0[0], LS * j, LS * j + LS), R("JM" if part and p == 3 else "ID"), R("VY", c, c + LS), p == 0, p == 3))
-        mms(l)
-        copy(R("LUT", 8 * LS * part, 8 * LS * (part + 1)), b0, "va")
+    copy(LV, ci(0))
+    scans([(R("R2"), R("HF"), R("ZB", 0, 8))], 2.0, OP.mult, OP.add)
+    ts(R("bi"), R("R2"), LV, OP.mult, -0.49, OP.add); ts(R("bj"), R("bi"), 1, OP.bitwise_and); copy(R("bf"), R("bj"))
+    scans([(R("pre"), R("ONE", 0, 8), R("bf"))], 0.0, OP.mult, OP.add)
+    ts(R("pb"), R("pre"), -200.0, OP.mult, 100.0, OP.add)
+    add("a", 1.3 + 7 * (FA + 16 * CY), [R("VY")], [R("YI"), R("pb")], lambda: [g.scalar.activation(
+        A(R("VY", 16 * p, 16 * p + 16)), A(R("YI")), AF.Sigmoid, bias=A(R("pb", p, p + 1)), scale=200.0) for p in range(7)], inc=7)
+    f = bank(128)
+    add("p", 0.03 + 1024 * PE, [f], [R("VY"), R("ONE"), R("ID")], lambda f=f: [g.tensor.matmul(
+        A(f, 16), A(R("VY", 16 * p, 16 * p + 16) if p < 7 else R("ONE", 0, 16)), A(R("ID")), p == 0, p == 7) for p in range(8)][-1])
+    add("va", {"v": dv(f), "a": da(f)}, [R("TD")], [f], lambda e, f=f: g.vector.tensor_copy(A(R("TD"), 16), A(f, 16))
+        if e == "v" else g.scalar.activation(A(R("TD"), 16), A(f, 16), AF.Copy))
+    pick(R("WD"), [[0, 9], [-1, 16]], 0)
+    for y in range(0, 16, 4):
+        f = bank(512)
+        mms([(R(f[0], 128 * (c - y), 128 * (c - y + 1)), R("WD", 16 - c, 144 - c), R("TD"), True, True, 16 - c) for c in range(y, y + 4)])
+        copy(R("LUT", 128 * y, 128 * y + 512), f, CQ)
     nloc = [0]
     win = lambda name, r: R(name, 15 - r, 143 - r)
     sends, used = {}, set()
@@ -580,27 +684,29 @@ def rank_program(g, core, T, topo):
             for h, u, _, r, m, out, _ in ws:
                 src = T.cores[[q for q in range(nr) if target(q, nr, t, h) == rank][0]]
                 to = leg(topo, src, core, t, b, k)[0]
-                last = [i]
+                last, size = [i], BYTE * (2 * m * SCRATCH[u + "S"][1][2] - 128)
                 if to != core:
-                    last = [add(None, 0.0, [], [], None, sem="loc", inc=0, after=last, lat=HOP0)]
+                    last = [add(None, 0.0, [], [], None, sem="loc", inc=0, after=last,
+                                lat=HOP0 + (HALFE + size if len(ws) > 1 else size / 2))]
                     last = [add(str(out % 2), CALL + (0.0 if out in used else ONCE), [], [], None, sem="loc", inc=0, after=last)]
                     used.add(out)
                 add(None, 0.0, [R3(u + "R", r, r + m, 0, SCRATCH[u + "R"][1][2])], [], None, sem="m%d%d%d%d" % (k, t, b, h), after=last,
-                    lat=HOP1, inc=len(topo.engines(src if to == core else to, core)))
+                    lat=HOP1 + size, inc=len(topo.engines(src if to == core else to, core)))
 
     def rows(h, t, b, first, m, lo=0, hi=P):
         x = MROWS * (t * NBK + b)
         n, x = ("MS", x + first) if h is None else ("MR", 2 * x + MROWS * h + first)
         return R3(n, x, None if m is None else x + m, lo, hi)
 
-    def put_names(e, t, b, x, lo=0, hi=P, shift=0, plus=None):
+    def put_half(t, b, h, x):
+        n, nx = R3("n1%d" % b, 2 * h, 2 * h + 2, 0, P), NXS[b]
+        ts(n, x, W - 1, OP.bitwise_and)
+        ts(rows(None, t, b, NR[1] + 2 * h, 2), n, float(-HALF), OP.add)
+        transmit(2 + h, t, b)
+
+    def put_names(e, t, b, x, lo=0, hi=P, shift=0):
         n, nx = "n%d%d" % (e, b), NXS[b]
-        u = 2 * W0[b] + nx * e
-        if plus is not None:
-            ts(rows(None, t, b, S_N + nx * e, nx, lo, hi), x, plus, OP.add)
-            if t == RO - 1:
-                copy(R3("US", u, u + nx, 0, 16), rows(None, t, b, S_N + nx * e, nx, 16, P))
-            return transmit(1 + e, t, b)
+        u = UROWS * b + 2 + nx * e
         if shift:
             ts(R3(n, 0, nx, lo, hi), x, shift, OP.arith_shift_right, W - 1, OP.bitwise_and)
         else:
@@ -608,39 +714,75 @@ def rank_program(g, core, T, topo):
         if t == RO - 1 and hi == P:
             ts(R3("US", u, u + nx, 0, 16), R3(n, 0, nx, 16, P), float(-HALF), OP.add)
             transmit(1 + e, t, b)
-        ts(rows(None, t, b, S_N + nx * e, nx, lo, hi), R3(n, 0, nx, lo, hi), float(-HALF), OP.add)
+        ts(rows(None, t, b, NR[e], nx, lo, hi), R3(n, 0, nx, lo, hi), float(-HALF), OP.add)
         if t < RO - 1:
             transmit(1 + e, t, b)
+
+    def chunks(t, b):
+        s, nx, own = str(b), NXS[b], 0 if t < RO - 1 else None
+        num16 = lambda h, y, hi=16: (rows(h, t, b, S_C, None, 16 * y, 16 * y + hi) if t < RO - 1 else
+                                     R3("US" if h is None else "UR", UROWS * b + y, None, 0, hi))
+        copy(R3("IX" + s, 0, nx, 4, 8), num16(own, 1))
+        f = bank(4 * nx)
+        acc(f, [(R("ID"), num16(1, 0)), (R("ID"), num16(own, 0, 14), R(f[0], 2, 4 * nx))])
+        ts(R3("IX" + s, 0, nx, 0, 4), f, float(FULL), OP.min)
+
+    def join_halves(t, b):
+        s, nx = str(b), NXS[b]
+        chunks(t, b)
+        for w in range(nx):
+            gather(GG, R3("GH" + s, w // 2, None, w % 2, 192, 2), R("LUT"), R3("IX" + s, w, None, 2, 8))
+        f = bank(64)
+        acc(f, [(R("ID"), R3("GH" + s, 0, 2, 32 * c, 32 * c + 32)) for c in range(6)] + [(R("ID"), R("BH"))])
+        copy(R("of" + s), f)
+        for h in HO:
+            st = STAGE[h]
+            u = UROWS * NBK + nx * (t * NBK + b) + 2 * h
+            for lo, hi, part in ((P, 48, 1), (0, P, 0)):
+                mms([(R3(st, 4 * h + 2 * y, 4 * h + 2 * y + 2, lo, hi), R("XM%d" % (2 * e + y)),
+                      R3("UR", u, u + 2, 0, 16) if PACK and part and e else rows(part, t, b, NR[e] + 2 * h, 2, 16 * part, P), e == 0, e == 1)
+                     for y in (0, 1) for e in (0, 1)])
+            wn = R("WN" + s, 4 * CELLS * h, 4 * CELLS * (h + 1))
+            copy(wn, R3(st, 4 * h, 4 * h + 4, 0, CELLS), "va")
+            f = bank(64)
+            for i, (e, j0, j1) in enumerate(NJ[t][b][h]):
+                x, n, d = 512 * h + 64 * j0, "N" if e == "v" else "NA", "DE" if e == "v" else "DF"
+                gather(e, R(n + s, x, x + 64 * (j1 - j0)), wn, R("of" + s, x // 16, x // 16 + 4 * (j1 - j0)))
+                acc(f, ([(R("N8"), R("MQ", 0, 64))] if i == 0 else []) +
+                    [(R(d, 128 * j, 128 * j + 128), R(n + s, 512 * h + 64 * j, 512 * h + 64 * j + 64)) for j in range(j0, j1)],
+                    i == 0, i == len(NJ[t][b][h]) - 1)
+            copy(R3("nm", 2 * b, 2 * b + 2, 32 * h, 32 * h + 32), f)
+            copy(R3("NF", 2 * b, 2 * b + 2, 32 * h, 32 * h + 32), f, "va")
 
     def join(t, b):
         s, nx = str(b), NXS[b]
         nb, l, own = 16 * nx, P * nx, 0 if t < RO - 1 else None
-        copy(R3("IX" + s, 0, nx, 8, 16), rows(own, t, b, S_OWN, None, 0, 8 * nx))
-        f = bank(8 * nx)
-        acc(f, [(R("ID"), rows(1, t, b, S_OVER, None, 0, 8 * nx)), (R("ID"), rows(own, t, b, S_CNT, None, 0, 8 * nx))])
-        copy(R3("IX" + s, 0, nx, 0, 8), f)
+        chunks(t, b)
         for w in range(nx):
-            gather(GG, R("G" + s, w, None, nx), R("LUT"), R3("IX" + s, w, None, 4, 16))
+            gather(GG, R("G" + s, w, None, nx), R("LUT"), R3("IX" + s, w, None, 2, 8))
         f = bank(nb)
-        acc(f, [(R("ID"), R("G" + s, nb * c, nb * c + nb)) for c in range(12)] + [(R("ID"), R("BW%d" % nx))])
+        acc(f, [(R("ID"), R("G" + s, nb * c, nb * c + nb)) for c in range(6)] + [(R("ID"), R("BW%d" % nx))])
         copy(R("of" + s), f)
+        st = STAGE[b]
         if t == RO - 1:
-            mset(R("WN" + s, 3 * REG, 4 * REG, 16), float(-HALF))
-        f = bank(l)
-        up = lambda e: rows(1, t, b, S_N + nx * e, nx, 16, P) if t < RO - 1 else R3("UR", 2 * W0[b] + nx * e, 2 * W0[b] + nx * e + nx, 0, 16)
-        mms([(R(f[0], nb * y, nb * y + nb), R("XM%d" % (2 * e + y)), up(e), e == 0, e == 1) for y in (0, 1) for e in (0, 1)])
-        copy(R("WN" + s, 2 * REG, 2 * REG + l), f, "va")
-        for hs in ([(0, 1)] if l == REG else [(0,), (1,)]):
-            f = bank(l * len(hs))
-            mms([(R(f[0], l * i + nb * y, l * i + nb * y + nb), R("XM%d" % (2 * e + y)), rows(own, t, b, S_N + nx * e, nx, 16 * h, 16 * h + 16),
-                  e == 0, e == 1) for i, h in enumerate(hs) for y in (0, 1) for e in (0, 1)])
-            copy(R("WN" + s, REG * hs[0], REG * hs[0] + f[2]), f, "va")
+            tt(R("lv" + s), f, R("BE%d" % nx), OP.is_lt)
+            if st not in STAGE[:b]:
+                mset(R3(st, 0, 8, 48, CELLS), float(-HALF))
+        up = lambda e: R3("UR", UROWS * b + 2 + nx * e, UROWS * b + 2 + nx * e + nx, 0, 16)
+        parts = [(P, 48, up), (0, P, lambda e: rows(own, t, b, NR[e], nx))]
+        for lo, hi, x in (parts if t < RO - 1 else parts[::-1]):
+            mms([(R3(st, nx * y, nx * y + nx, lo, hi), R("XM%d" % (2 * e + y)), x(e), e == 0, e == 1) for y in (0, 1) for e in (0, 1)])
+        copy(R("WN" + s), R3(st, 0, 2 * nx, 0, CELLS), "va")
+
+    def joined(t, b):
+        s, nx = str(b), NXS[b]
+        nb, l = 16 * nx, P * nx
         f = bank(l)
         for y in range(0, 16, 4):
             gather("v", R("N" + s, nb * y, nb * y + 4 * nb), R("WN" + s), R("of" + s, nx * y, nx * y + 4 * nx))
             acc(f, ([(R("N8"), R("MQ", 0, l))] if y == 0 else []) +
                 [(R("DR", 144 * (8 * e + x // 2) + 15 - x, 144 * (8 * e + x // 2) + 143 - x), R("N" + s, nb * x, nb * x + nb), R(f[0], e, l, 2))
-                 for x in range(y, y + 4) for e in (0, 1)], y == 0, y == 12 and (t == RO - 1 or not PJ))
+                 for x in range(y, y + 4) for e in (0, 1)], y == 0, y == 12)
         return f
 
     def step(o, i, more):
@@ -655,27 +797,30 @@ def rank_program(g, core, T, topo):
             ROWS = 16 * L
             r = lambda n, lo=0, hi=None, step=1: R(n + s, lo, hi, step)
             cur["plus"] = NBK - 1 - b
-            nm, nf = R("nm", LO, LO + L), R("NF", LO, LO + L)
             if t:
-                fj = join(t - 1, b)
-                copy(nm, fj)
-                if not PJ:
-                    copy(nf, fj, "va")
+                join_halves(t - 1, b)
             for w in range(NX):
-                gather(VG, r("V", 16 + CH * w, 16 + CH * w + CH), R("XT", 0, W + 16), R("nm", LO + P * w, LO + P * w + P))
-            D = bank(L)
+                gather(VG, r("V", 16 + CH * w, 16 + CH * w + CH), R("XT", 0, W + 16), R3("nm", 2 * b + w // 2, None, P * (w % 2), P * (w % 2) + P))
+            if t:
+                vs = lambda x, back=0: r("V", 16 + 8 * L * (x % 2) + x // 2 - 8 * back, 16 + 8 * L * (x % 2 + 1) - 8 * back, 8)
+                lanes = list(range(0, 16, 2)) + list(range(1, 16, 2))
+            else:
+                vs = lambda x, back=0: r("V", 16 + x - 16 * back, 16 + ROWS - 16 * back, 16)
+                lanes = list(range(16))
+            D = bank(L + 4)
+            DL = R(D[0], 0, L)
             f = bank(128)
-            add("p", 0.03 + 1024 * PE, [f], [r("V"), R("EW")], lambda f=f, s=s, L=L: [g.tensor.matmul(
-                A(R(f[0], x, 128, 16), L), A(R("V" + s, 16 + x, 16 + 16 * L, 16)), A(R("EW", 15, 143, 16)), True, True) for x in range(16)][-1])
+            for y in (0, 8):
+                mms([(R(f[0], x, 128, 16), vs(x), R("EW", 15, 143, 16), True, True) for x in lanes[y:y + 8]])
             add("va", {"v": dv(f), "a": da(f)}, [r("S")], [f], lambda e, f=f, s=s, L=L: g.vector.tensor_copy(A(R("S" + s), L), A(f, L))
                 if e == "v" else g.scalar.activation(A(R("S" + s), L), A(f, L), AF.Copy))
             for y in range(0, 16, 4):
-                scans([(r("M", L * x, L * x + L), r("V", x, ROWS, 16), r("V", 16 + x, 16 + ROWS, 16)) for x in range(y, y + 4)], 256.0, OP.min, OP.max)
-                acc(D, [(win("EW", x), r("M", L * x, L * x + L)) for x in range(y, y + 4)], y == 0, False)
-            mms([(D, r("S"), R("SH", 0, L), False, False, L), (D, R("ID"), R("K0", 0, L), False, True)])
-            step(r("C"), D, False)
-            step(r("E", 0, L - 1), R(D[0], 1, L), True)
-            ts(r("E", P - 1, L, P), R("nm", LO + P - 1, LO + L, P), float(DEAD), OP.is_lt)
+                scans([(r("M", L * x, L * x + L), vs(x, 1), vs(x)) for x in lanes[y:y + 4]], 256.0, OP.min, OP.max)
+                acc(DL, ([(R("ID"), R("K0"), D)] if y == 0 else []) + [(win("EW", x), r("M", L * x, L * x + L)) for x in lanes[y:y + 4]], y == 0, False)
+            mms([(D, r("S"), R("SH"), False, True)])
+            step(r("C"), DL, False)
+            lin(r("E", 0, L - 1), r("C", 1, L), -1.0, 1.0)
+            step(r("E", P - 1, L, P), R(D[0], L, L + 4), True)
             per = 4 if NX > 2 else 8
             fu = bank(L)
             for y in range(0, 16, per):
@@ -685,34 +830,29 @@ def rank_program(g, core, T, topo):
                 if y // per in ZC[b]:
                     n, o = "CR" + s, L * y
                     copy(R(n, o, o + per * L), f, "a")
-                scans([(r("Z", x, ROWS, 16), R(n, o + L * (x - y), o + L * (x - y + 1)), r("V", 16 + x, 16 + ROWS, 16)) for x in range(y, y + per)],
+                scans([(r("Z", x, ROWS, 16), R(n, o + L * (x - y), o + L * (x - y + 1)), vs(x)) for x in range(y, y + per)],
                       0.0, OP.mult, OP.max)
-                acc(fu, [(win("WW", x), r("Z", x, ROWS, 16)) for x in range(y, y + per)], y == 0, y + per == 16 and not PV)
-            scans([(r("cs", 128, 128 + L), R("PAT", 0, L), r("E"))], 0.0, OP.mult, OP.add)
-            act(r("cs", 0, L), r("cs", 128, 128 + L), AF.Relu, -16.0)
-            f = bank(3 * P)
-            acc(f, [(R("ID"), R("VP"))] + [(R("ID"), r("cs", 128 + P - 1, 128 + L, P), R(f[0], 2 * P + c, 2 * P + 8 * NX, 8)) for c in range(4, 8)] +
-                [(R("W%d" % i), r("cs", i, None, 4), R(f[0], 0, 2 * P)) for i in range(4)])
-            copy(rows(None, t, b, 0, 3), f)
+                acc(fu, [(win("WW", x), r("Z", x, ROWS, 16)) for x in range(y, y + per)], y == 0, y + per == 16)
+            scans([(r("cs", L), R("PAT", 0, L), r("E"))], 0.0, OP.mult, OP.add)
+            x, y = r("cs", 0, L), r("cs", L)
+            add("va", {"v": dv(x, y), "a": da(x)}, [x], [y], lambda e, x=x, y=y: g.vector.tensor_scalar(A(x), A(y), -16.0, 0.0, OP.add, OP.max)
+                if e == "v" else g.scalar.activation(A(x), A(y), AF.Relu, bias=-16.0))
+            f = bank(8 * NX)
+            acc(f, [(U[i], r("cs", i, None, 8)) for i in range(8)] +
+                [(U[8], r("cs", L + P - 1, None, P), R(f[0], c, 4 * NX, 4)) for c in (0, 1)])
+            ts(rows(None, t, b, S_C, None) if t < RO - 1 else R3("US", UROWS * b, UROWS * b + 2, 0, 16), f, float(FULL), OP.min)
             transmit(0, t, b)
             scans([(r("cm"), r("C"), R("TWO", 0, L))], 0.0, OP.mult, OP.add)
             c2, hm = R3("c2" + s, 0, NX, 0, P), R3("hm" + s, 0, NX, 0, P)
             lin(c2, r("cm"), 1.0, 1.0)
-            if t and PJ:
-                f = fj
-                acc(f, [(R("N8"), r("C"))], False, not PN0)
+            f = bank(L)
+            if t:
+                acc(f, [(R("N8"), r("C"))] + [(R("XB", 128 * (2 * e + y), 128 * (2 * e + y + 1)), R3("NF", 2 * b + y, None, 0, 64), R(f[0], e, L, 2))
+                                              for y in (0, 1) for e in (0, 1)])
             else:
-                f = bank(L)
-                acc(f, [(R("IDF"), nf), (R("N8"), r("C"))], True, not PN0)
+                acc(f, [(R("IDF"), R3("NF", 2 * b, 2 * b + 2, 0, 64)), (R("N8"), r("C"))])
             scans([(R(f[0], L, 2 * L), r("C"), f)], 0.0, OP.mult, OP.max)
-            if PN0:
-                tt(f, R(f[0], L, 2 * L), c2, OP.mult)
-                acc(f, [(R("NEG"), R("K15", 0, L))], False, False)
-                act(r("r0"), f, AF.Identity, R("AB", t, t + 1), -0.25)
-                act(f, f, AF.Identity, R("AC", t, t + 1), 0.25)
-                acc(f, [(R("ID"), r("r0"))], False)
-                put_names(0, t, b, f, plus=MAGIC - WHOLE - HALF)
-            elif t == 0:
+            if t == 0:
                 tt(r("ni"), R(f[0], L, 2 * L), c2, OP.mult)
                 put_names(0, t, b, r("ni"), shift=2)
             else:
@@ -724,19 +864,16 @@ def rank_program(g, core, T, topo):
             scans([(R("y", LO, LO + L), R("K0", 0, L), f)], 0.0, OP.add, OP.min)
             ts(r("zo"), R("y", LO + P - 1, LO + L, P), 8192.0, OP.add, float(ROWS - 1), OP.min)
             glin(R("ZF", WO, WO + 16 * NX), r("Z"), r("zo"), 1.0, -192.0)
-            f = fu
-            lin(r("r"), f, -1.0, HALF - 0.5 - MAGIC)
-            if PV:
-                acc(f, [(R("ID"), r("r"))], False)
-                act(r("sq"), f, AF.Square, 592.0 + MAGIC)
-            else:
-                tt(r("v"), f, r("r"), OP.add)
-                act(r("sq"), r("v"), AF.Square, 592.0 + MAGIC)
             f = bank(L)
             acc(f, [(R("N97"), r("cm")), (R("N8"), R("CK", 0, L))])
-            tt(r("si"), r("sq"), f, OP.subtract)
-            ts(hm, r("si"), 5, OP.arith_shift_right, W - 1, OP.bitwise_and)
-            copy(r("hu"), hm)
+            for w0, w1 in HH[t][b]:
+                x, y = P * w0, P * w1
+                lin(r("r", x, y), R(fu[0], x, y), -1.0, HALF - 0.5 - MAGIC)
+                tt(r("v", x, y), R(fu[0], x, y), r("r", x, y), OP.add)
+                act(r("sq", x, y), r("v", x, y), AF.Square, 592.0 + MAGIC)
+                tt(r("si", x, y), r("sq", x, y), R(f[0], x, y), OP.subtract)
+                ts(R3("hm" + s, w0, w1, 0, P), r("si", x, y), 5, OP.arith_shift_right, W - 1, OP.bitwise_and)
+                copy(r("hu", x, y), R3("hm" + s, w0, w1, 0, P))
             xa = min(XA[t][b], NX)
 
             def distance(w, lo, hi):
@@ -749,25 +886,27 @@ def rank_program(g, core, T, topo):
                     act(R3("AD" + s, w, None, lo, hi), f, AF.Abs)
                 else:
                     gtt(o, R("XT", 0, W), off, z)
-                    act(R3("AD" + s, w, None, lo, hi), o, AF.Abs)
+                    if w in RV[t][b]:
+                        ts(R3("AD" + s, w, None, lo, hi), o, 0.0, OP.max, 2.0, OP.mult)
+                    else:
+                        act(R3("AD" + s, w, None, lo, hi), o, AF.Abs)
 
             if t < RO - 1:
-                fd = bank(L)
-                for w in range(NX):
-                    distance(w, 0, CH)
-                    if w == NX - 1 or (w == 1 and NX == 4):
-                        z = 2 if w == 3 else 0
-                        acc(R(fd[0], P * z, P * w + P), [(win("EW", x), R3("AD" + s, z, w + 1, x, CH, 16)) for x in range(16)],
-                            z == 0, w == NX - 1 and not PN1)
-                tt(fd, fd, c2, OP.mult)
-                if PN1:
-                    tt(fd, fd, hm, OP.add)
-                    act(r("r0"), fd, AF.Identity, HALF - 0.5 - MAGIC, -1.0)
-                    acc(fd, [(R("ID"), r("r0"))], False)
-                    put_names(1, t, b, fd, plus=MAGIC - HALF)
-                else:
-                    tt(r("nj"), fd, hm, OP.add)
-                    put_names(1, t, b, r("nj"))
+                for h in HO:
+                    fd = bank(64)
+                    for w in (2 * h, 2 * h + 1):
+                        distance(w, 0, CH)
+                    less = 2 * h in RV[t][b]
+                    if less:
+                        acc(fd, [(win("EN", x), r("D2", 2 * CH * h + x, 2 * CH * (h + 1), 16)) for x in range(16)], True, False)
+                    acc(fd, [(win("EW", x), R3("AD" + s, 2 * h, 2 * h + 2, x, CH, 16)) for x in range(16)], not less)
+                    tt(fd, fd, R3("c2" + s, 2 * h, 2 * h + 2, 0, P), OP.mult)
+                    tt(r("nj", 64 * h, 64 * h + 64), fd, R3("hm" + s, 2 * h, 2 * h + 2, 0, P), OP.add)
+                    put_half(t, b, h, r("nj", 64 * h, 64 * h + 64))
+                if PACK:
+                    u = UROWS * NBK + NX * (t * NBK + b)
+                    ts(R3("US", u, u + NX, 0, 16), R3("n1" + s, 0, NX, 16, P), float(-HALF), OP.add)
+                transmit(4, t, b)
             else:
                 y = L // 2
                 for h in (1, 0):
@@ -787,11 +926,9 @@ def rank_program(g, core, T, topo):
         cur["plus"] = 0.0
         if t < RO - 1:
             f = bank(1)
-            acc(f, [(R("ONE"), R("cs%d" % b, x, x + 1)) for b in range(NBK) for x in range(128 + P - 1, 128 + P * NXS[b], P)])
+            acc(f, [(R("ONE"), R("cs%d" % b, x, x + 1)) for b in range(NBK) for x in range(P * NXS[b] + P - 1, 2 * P * NXS[b], P)])
             copy(R("ATi"), f)
-            ts(R("ATj"), R("ATi"), 255, OP.bitwise_and); ts(R("AC", t + 1, t + 2), R("ATj"), WHOLE if PN0 else -0.375, OP.add)
-            if PN0:
-                ts(R("AB", t + 1, t + 2), R("ATj"), -1.0, OP.mult, HALF - 0.5 - MAGIC, OP.add)
+            ts(R("ATj"), R("ATi"), 255, OP.bitwise_and); ts(R("AC", t + 1, t + 2), R("ATj"), -0.375, OP.add)
         f = bank(8)
         acc(f, [(win("WW", x), R("ZF", x, NW, 16)) for x in range(16)])
         copy(R("wa"), f); ts(R("wb"), R("wa"), 31, OP.bitwise_and)
@@ -815,15 +952,17 @@ def rank_program(g, core, T, topo):
         if x // 2:
             select(R("QM%d" % x), R("QM%d" % x), pat, OP.not_equal, 1, base + 128)
     t = RO - 1
+    for b in range(NBK):
+        cur["plus"] = NBK - 1 - b
+        join(t, b)
     for b, nx in enumerate(NXS):
         s, nb, w0, wo = str(b), 16 * nx, W0[b], 16 * W0[b]
         cur["plus"] = NBK - 1 - b
-        f = join(t, b)
-        ts(R("lv" + s), R("of" + s), float(3 * REG), OP.is_lt, 2.0, OP.mult)
+        f = joined(t, b)
         z = bank(nb)
         add("p", 0.15, [z], [R("EW"), R("lv" + s)], lambda z=z, s=s, nx=nx: [g.tensor.matmul(
             A(R(z[0], 16 * w, 16 * w + 16), 8), A(R("EW", 15, 143, 16)), A(R("lv" + s, w, 16 * nx, nx)), True, True) for w in range(nx)][-1])
-        add("v", cv(1), [R("yno", wo, wo + nb)], [z], lambda z=z, wo=wo, nb=nb: g.vector.tensor_copy(A(R("yno", wo, wo + nb), 8), A(z, 8)))
+        add("v", cv(1), [R("yno", wo, wo + nb)], [z], lambda z=z, wo=wo, nb=nb: g.vector.tensor_scalar(A(R("yno", wo, wo + nb), 8), A(z, 8), 2.0, None, OP.mult))
         ts(R3("NB" + s, 0, nx, 0, P), f, float(-HALF), OP.add)
         l = []
         for x in (0, 1):
@@ -845,9 +984,10 @@ def rank_program(g, core, T, topo):
     prio = [0.0] * n
     for i in range(n - 1, -1, -1):
         x = nodes[i]
-        prio[i] = (min(x["d"].values()) if x["e"] == "va" else x["d"][x["e"]] if x["e"] else 0.0) + x["lat"] + LINK + max([prio[k] for k in users[i]] + [0.0])
+        prio[i] = (min(x["d"].values()) if x["e"] == "va" else x["d"][x["e"]] if x["e"] else 0.0) + x["lat"] + LINK[0] + max([prio[k] for k in users[i]] + [0.0])
     free = {k: 0.0 for k in "vapgs01"}
-    gap = lambda a, b: LINK if a != b else 0.0 if a == "p" else SAME
+    gaps = lambda a, b: LINK if a != b else 0.0 if a == "p" else SAME
+    gap = lambda a, b, g0=(float(LINK[0]), float(SAME[0])): g0[0] if a != b else 0.0 if a == "p" else g0[1]
 
     def sweep(urgency, back, on, urge, vpen):
         before, after = (users, [x["deps"] for x in nodes]) if back else ([x["deps"] for x in nodes], users)
@@ -907,7 +1047,7 @@ def rank_program(g, core, T, topo):
                 bleft[y] -= 1
                 blast[banks[y]].append(k)
                 if bleft[y] == 0:
-                    bfree[banks[y]] = fin[k] + LINK
+                    bfree[banks[y]] = fin[k] + LINK[0]
             busy[e] = fin[k]
             order.append(k)
             done(k)
@@ -919,25 +1059,36 @@ def rank_program(g, core, T, topo):
             e = res[2][i]
             st = busy[e] if e else 0.0 * one
             for j in nodes[i]["deps"] + res[6][i]:
-                st = np.maximum(st, fin[j] + gap(e, res[2][j]))
+                st = np.maximum(st, fin[j] + gaps(e, res[2][j]))
             if e:
                 busy[e] = st + nodes[i]["dd"][e]
             fin[i] = busy[e] if e else st + nodes[i]["ll"]
         return np.max(fin, axis=0)
 
     if not KEPT:
-        for first, urge, vpen in RULES:
-            late = [prio[i] + first * nodes[i]["plus"] for i in range(n)]
-            for _ in range(PASSES):
+        pool, rng = [], np.random.default_rng(SEED)
+
+        def passes(late, urge, vpen, k):
+            for _ in range(k):
                 res = sweep(late, False, [x["e"] for x in nodes], urge, vpen)
                 ends = again(res)
                 KEPT.setdefault("scale", ends)
                 both = float(np.sum(WEIGHT * ends / KEPT["scale"]))
-                if "res" not in KEPT or both < KEPT["both"]:
-                    KEPT.update(res=res, both=both, ends=ends, sends=[sends[k] for k in res[1] if k in sends], rule=(first, urge, vpen))
-                late = [z + KEEP * first * x["plus"] for z, x in zip(sweep(res[4], True, res[2], urge, vpen)[4], nodes)]
-        if TRIES:
-            polish(nodes, users, sends)
+                late = sweep(res[4], True, res[2], urge, vpen)[4]
+                if all(abs(both - z[0]) > 1e-4 for z in pool):
+                    pool.append((both, res, late, urge, vpen))
+
+        for first, urge, vpen in RULES:
+            passes([prio[i] + first * nodes[i]["plus"] for i in range(n)], urge, vpen, PASSES)
+        for _ in range(AGAIN):
+            pool.sort(key=lambda z: z[0])
+            del pool[POOL:]
+            _, _, late, urge, vpen = pool[int(rng.integers(len(pool)))]
+            k = NOISE * rng.random()
+            passes([z + y for z, y in zip(late, k * rng.standard_normal(n))], urge, vpen, 2)
+        pool.sort(key=lambda z: z[0])
+        KEPT["first"] = [z[0] for z in pool]
+        polish(nodes, sends, [z[1] for z in pool[:POOL]])
     if g is None:
         return
     end, order, took, at, fin, banks, more = KEPT["res"]

import numpy as np
from concourse.bass import DstId, RemoteDMATransfer
from concourse.mybir import dt, AluOpType, AxisListType, ActivationFunctionType

NW, P, RO = 128, 32, 3
NXS = (4, 4)
NBK = len(NXS)
W0 = [sum(NXS[:b]) for b in range(NBK)]
LM = P * max(NXS)
W = 4096
DEAD = 4096
HALF = 2048
CELLS = 50
NR, S_C, MROWS = (4, 0), 8, 9
FULL = 2048
STAGE = ("psz", "psy")
UK = [127] + [-2 ** _i for _i in range(6)] + [64, 128]
CH = 512
MAGIC = 786432.0
AF = ActivationFunctionType
OP = AluOpType

XA = ((2, 2), (2, 2), (2, 2))
ZC = ((1, 3), (1, 3))
YV = ()
MERGE = 0
MERGEL = 0
PACK = 1
FUSE = 0
UROWS = 10
ALT = 0
HO = (1, 0)
CQ = "a"
SG = ()
UG = ()
HW = ((0, 4),)
HH = ((HW, HW),) * 3
RV = (((), ()),) * 3
VG = "va"
NP = (("v", 0, 4), ("v", 4, 8))
NJ = (((NP, NP), (NP, NP)),) * 2
GG = "a"

SCRATCH = {_n: ("psum", [128, 8, 64], "float32") for _n in STAGE}
NPS = 8 - len(SCRATCH)
for _i in range(NPS):
    SCRATCH["ps%d" % _i] = ("psum", [128, 512], "float32")

SIZE, PLACE, FILL = {_n: (512, "float32") for _n in STAGE}, {}, {"float32": 0, "int32": 0, "uint16": 0, "bfloat16": 0, "float16": 0}


def _sb(name, n, dtype, own=False):
    if own or not isinstance(n, int):
        shape = [n] if isinstance(n, int) else list(n)
        SIZE[name] = (int(np.prod(shape)), dtype)
        SCRATCH[name] = ("sbuf", [128] + shape, dtype)
        PLACE[name] = (name, 0)
    else:
        SIZE[name] = (n, dtype)
        PLACE[name] = ("all_" + dtype, FILL[dtype])
        FILL[dtype] += -(-n // 16) * 16


_sb("XT", 2 * W + 16, "bfloat16", True); _sb("YX", 2048, "bfloat16", True)
_sb("wli", 2 * NW, "int32", True); _sb("wni", NW, "int32", True); _sb("thi", 1, "int32", True); _sb("wti", 1, "int32", True)
_sb("MS", (RO * NBK * MROWS, P), "float16"); _sb("MR", (2 * RO * NBK * MROWS, P), "float16")
_sb("US", (UROWS * NBK + 16, 16), "float16"); _sb("UR", (UROWS * NBK + 16, 16), "float16")
_sb("OT", (8, P), "float16"); _sb("yno", NW, "float32", True)
for _n, _k in (("wnf", NW + 1), ("E8", 128), ("cols", 16), ("ZF32", 128), ("YI", 16), ("HF", 8), ("R2", 8), ("bf", 8), ("pre", 8), ("pb", 8), ("RA", LM), ("W5", 8), ("IDF", 128), ("XB", 512), ("MK8", 8), ("DF", 1024),
               ("AC", 4), ("W32", 8), ("iv", 8), ("bs", 8), ("wf", 8), ("MK", 16), ("y", 2 * NW)):
    _sb(_n, _k, "float32")
for _n, _k in (("ci", 3), ("ATi", 1), ("ATj", 1), ("bi", 8), ("bj", 8), ("wa", 8), ("wb", 8)):
    _sb(_n, _k, "int32")
for _n, _k in (("ID", 128), ("NEG", 128), ("N8", 128), ("K15", 128), ("U", 9 * 128), ("TD", 128), ("WD", 144),
               ("ONE", 128), ("EW", 144), ("WW", 144), ("EN", 144), ("SEL", 2048), ("LUT", FULL + 16), ("VY", 7 * 16), ("K0", LM + 4), ("PAT", LM),
               ("TWO", LM), ("MQ", 128), ("CK", LM), ("DR", 16 * 144), ("ZF", NW), ("e1", NW), ("e2", NW),
               ("ZB", 576), ("SH", 132), ("SHF", 128), ("DE", 1024), ("BH", 64), ("E9", 9), ("CG", 128), ("BLK", 128)):
    _sb(_n, _k, "bfloat16")
for _n, _k in (("N97", 128), ("RAMP", LM), ("IN", 2 * NW), ("IM", 2 * NW), ("NLi", 2 * NW)):
    _sb(_n, _k, "float16")
for _i in range(4):
    _sb("PM%d" % _i, 128, "bfloat16"); _sb("QM%d" % _i, 128, "bfloat16"); _sb("XM%d" % _i, 128, "bfloat16")
for _i in sorted(set(NXS)):
    _sb("BW%d" % _i, 16 * _i, "bfloat16"); _sb("BE%d" % _i, 16 * _i, "bfloat16")
_sb("nm", (2 * NBK, 64), "uint16"); _sb("NF", (2 * NBK, 64), "float32"); _sb("WL", 8, "uint16")
for _b, _x in enumerate(NXS):
    _s, _l = str(_b), P * _x
    for _n, _k, _d in (("V", 16 * _l + 16, "bfloat16"), ("M", 16 * _l, "bfloat16"), ("Z", 16 * _l, "bfloat16"), ("D2", 16 * _l, "bfloat16"),
                       ("AD", (_x, CH), "bfloat16"), ("cs", 2 * _l, "bfloat16"), ("lv", 16 * _x, "bfloat16"), ("S", 128, "bfloat16"),
                       ("r", _l, "bfloat16"), ("r0", _l, "bfloat16"), ("C", _l, "bfloat16"), ("E", _l, "bfloat16"),
                       ("cm", _l, "bfloat16"), ("c2", (_x, P), "bfloat16"), ("na", _l, "float32"), ("ni", _l, "int32"),
                       ("zo", _x, "uint16"), ("v", _l, "float32"), ("sq", _l, "float32"), ("si", _l, "int32"), ("hm", (_x, P), "int32"),
                       ("hu", _l, "uint16"), ("nj", _l, "int32"), ("of", 16 * _x, "uint16"), ("CR", 16 * _l, "bfloat16"),
                       ("n0", (_x, P), "int32"), ("n1", (_x, P), "int32"), ("WN", 2 * _x * CELLS, "float32"), ("G", 96 * _x, "bfloat16"), ("GH", (2, 48 * _x), "bfloat16"),
                       ("IX", (_x, 8), "uint16"), ("NB", (_x, P), "float16"), ("N", 256 * _x, "float16"), ("NA", 256 * _x, "float32")):
        _sb(_n + _s, _k, _d)
    _sb("yl" + _s, _l, "float32", True)
for _d in FILL:
    SCRATCH["all_" + _d] = ("sbuf", [128, FILL[_d]], _d)


def target(q, n, t, h):
    return (q + h + (1 if t < RO - 1 else 0)) % n


def calls(t, b):
    s, nx = MROWS * (t * NBK + b), NXS[b]
    both = lambda lo, m: [(h, "M", s + lo, 2 * s + MROWS * h + lo, m) for h in (0, 1)]
    if t < RO - 1:
        early = [[(0, both(S_C, 1)), (1, both(NR[0], nx))], [(1, both(NR[0], nx + 1))], [(0, both(S_C, 1))]][MERGE]
        more = nx if MERGE == 2 else 0
        late = [(2 + h, both(2 * h, 2 + more * h)) for h in HO]
        u = UROWS * NBK + nx * (t * NBK + b)
        return early + (late if FUSE else [(k, x[:1]) for k, x in late] + [(4, [(1, "U", u, u, nx)] if PACK else both(0, nx + more)[1:])])
    up = lambda lo, m: [(1, "U", UROWS * b + lo, UROWS * b + lo, m)]
    return [[(0, up(0, 2)), (1, up(2, nx)), (2, up(2 + nx, nx))], [(1, up(0, 2 + nx)), (2, up(2 + nx, nx))], [(0, up(0, 2)), (2, up(2, 2 * nx))]][MERGEL]


SEMAPHORES = ["sv", "sa", "st", "sg", "loc"] + ["d%d" % i for i in range(8 + NBK)]
SEMAPHORES += ["m%d%d%d%d" % (k, t, b, x[0]) for t in range(RO) for b in range(NBK) for k, ws in calls(t, b) for x in ws]

SPEED = np.array([1.2, 1.45, 1.03, 1.05, 1.0])
CY = 0.00083 * SPEED
PE = 0.00042 * SPEED
GA = np.array([1.5, 1.9, 1.2, 1.56, 1.1])
FV = 0.015
FA = 0.04
XLOAD = 5.0
HOP0 = np.array([1.4, 1.4, 1.8, 1.2, 2.0])
HOP1 = np.array([2.1, 2.1, 2.7, 2.0, 3.2])
CALL = np.array([0.9, 0.9, 1.0, 0.8, 0.7])
HALFE = 0.3
BYTE = 0.0015
ONCE = 1.5
LINK = np.array([0.13, 0.1, 0.1, 0.18, 0.12])
SAME = np.array([0.11, 0.1, 0.08, 0.16, 0.1])
SEED = 0
LEFT = 0.2
WEIGHT = np.array([1.5, 0.8, 1.2, 1.0, 0.5])
PASSES = 5
BIG = 0.05
ROUNDS = ((4, 1000), (1, 26000))
SHAKE = 0.005
RULES = [(f, u, v) for f in (1, 3, 6) for u in (0.015, 0.04) for v in (0.1, 0.3)]
AGAIN, POOL, NOISE = 100, 8, 0.7
KEPT = {}


def leg(topo, src, dst, t, b, k):
    if topo.may_write(src, dst):
        return dst, topo.engines(src, dst)
    c = [x for x in topo.cores_of(src) if x != src and topo.die(x) == topo.die(src) and topo.may_write(x, dst)]
    e = topo.engines(src, c[0])
    alone = t == RO - 1 or (k >= 2 and not FUSE)
    return c[(b + (ALT if k == 3 else 0)) % len(c)], (e if alone else e[len(e) // 2:])


def transfer(T, topo, core, dst, src_ap, dst_ap, engines, sem):
    rid, pid = topo.addr(dst, core)
    return RemoteDMATransfer(dst_ids=[DstId(rid=rid, pnc=pid)], dma_engine_mask=sum(1 << e for e in engines),
                             remote_sem=T.sem[sem], src=src_ap, dst=dst_ap)


def relay_program(g, core, T, topo):
    n = len(T.cores)
    if not [q for q in T.cores if core in topo.cores_of(q)]:
        return
    if not KEPT:
        rank_program(None, T.cores[0], T, topo)
    tot = 0
    for t, b, k, ws in KEPT["sends"]:
        for h, buf, _, r, m, q in [x + (q,) for x in ws for q in range(n)]:
            d = T.cores[target(q, n, t, h)]
            to, e = leg(topo, T.cores[q], d, t, b, k)
            if to == core:
                sem = "m%d%d%d%d" % (k, t, b, h)
                g.wait_ge(T.sem[sem], len(e))
                x = T[buf + "R"][:, r:r + m, :]
                g.remote_dma_fused([transfer(T, topo, core, d, x, x, topo.engines(core, d), sem)], local_sem=T.sem["loc"])
                tot += len(topo.engines(core, d))
    if tot:
        g.wait_ge(T.sem["loc"], tot)


def clash(a, b):
    if a[0] != b[0]:
        return False
    if a[0][:2] == "ps":
        return True
    if a[2] <= b[1] or b[2] <= a[1]:
        return False
    if len(a) > 4 and len(b) > 4:
        return any(x[0] < y[1] and y[0] < x[1] for x in a[6] for y in b[6])
    if a[3] == b[3] and a[3] > 1 and (a[1] - b[1]) % a[3]:
        return False
    return True


def polish(nodes, sends, starts):
    n, m = len(nodes), len(SPEED)
    rng = np.random.default_rng(SEED)
    deps, reach, users = [], [], [[] for _ in range(n)]
    for i, x in enumerate(nodes):
        cover = 0
        for j in x["deps"]:
            cover |= reach[j]
        deps.append([j for j in x["deps"] if not cover >> j & 1])
        reach.append(cover | sum(1 << j for j in x["deps"]))
        for j in deps[i]:
            users[j].append(i)
    dur = [[{e: float(x["dd"][e][k]) for e in x["dd"]} for x in nodes] for k in range(m)]
    lat = [[float(x["ll"][k]) for x in nodes] for k in range(m)]
    gaps = [(0.0, float(SAME[k]), float(LINK[k])) for k in range(m)]
    held = [x["banks"] for x in nodes]
    total = {}
    for x in nodes:
        for y in x["banks"]:
            total[y] = total.get(y, 0) + 1
    kind = lambda e, f: 2 if e != f else 0 if e == "p" else 1
    STEP = 32

    def first(order, on, base, a, old):
        d, l, gp = dur[0], lat[0], gaps[0]
        fin, waits, plan, marks = list(old[0]), list(old[1]), list(old[2]), old[4][:a // STEP + 1]
        banks, left, bfree, blast, last = marks[-1]
        banks, left, bfree, blast, last = dict(banks), dict(left), list(bfree), list(blast), dict(last)
        busy = {e: fin[last[e]] if e in last else 0.0 for e in "vapgs01"}
        for p in range(a, n):
            if p % STEP == 0 and p > a:
                marks.append((dict(banks), dict(left), list(bfree), list(blast), dict(last)))
            i = order[p]
            e, h, w = on[i], held[i], base[i]
            plan[i] = ()
            for y in h:
                if y not in banks:
                    z = [z for z in range(NPS) if bfree[z] is not None]
                    if not z:
                        return None
                    z = min(z, key=lambda z: bfree[z])
                    banks[y], bfree[z] = z, None
                    plan[i] += blast[z]
                    w = w + [(j, kind(e, on[j])) for j in blast[z]]
                    blast[z] = ()
            waits[i] = w
            st = busy[e] if e else 0.0
            for j, c in w:
                t = fin[j] + gp[c]
                if t > st:
                    st = t
            if e:
                fin[i] = busy[e] = st + d[i][e]
                last[e] = i
            else:
                fin[i] = st + l[i]
            for y in h:
                left[y] -= 1
                blast[banks[y]] += (i,)
                if not left[y]:
                    bfree[banks[y]] = fin[i]
        return fin, waits, plan, banks, marks

    def run(order, on, k, waits, a, old, last):
        fin, d, l, gp = list(old[k]), dur[k], lat[k], gaps[k]
        fin2, d2, l2, gp2 = list(old[k + 1]), dur[k + 1], lat[k + 1], gaps[k + 1]
        busy = {e: (fin[last[e]], fin2[last[e]]) if e in last else (0.0, 0.0) for e in "vapgs01"}
        busy[None] = (0.0, 0.0)
        for i in order[a:]:
            e = on[i]
            st, st2 = busy[e]
            for j, c in waits[i]:
                t = fin[j] + gp[c]
                if t > st:
                    st = t
                t = fin2[j] + gp2[c]
                if t > st2:
                    st2 = t
            if e:
                fin[i], fin2[i] = busy[e] = st + d[i][e], st2 + d2[i][e]
            else:
                fin[i], fin2[i] = st + l[i], st2 + l2[i]
        return fin, fin2

    def score(order, on, base, a, old, limit):
        a -= a % STEP
        x = first(order, on, base, a, old[3])
        if x is None:
            return None
        fins, part = [x[0]], [wt[0] * (max(x[0]) + LEFT * sum(x[0]) / n)]
        for k in range(1, m, 2):
            if sum(part) + 0.997 * sum(old[4][k:]) > limit:
                return None
            fins += run(order, on, k, x[1], a, old[2], x[4][a // STEP][4])
            part += [wt[j] * (max(fins[j]) + LEFT * sum(fins[j]) / n) for j in (k, k + 1)]
        return sum(part), [max(z) for z in fins], fins, x, part

    def chain(z, order, on, k):
        fin, waits, gp, d = z[2][k], z[3][1], gaps[k], dur[k]
        i, path = fin.index(max(fin)), []
        p = order.index(i)
        while True:
            st, w, e = 0.0, -1, on[i]
            for j, c in waits[i]:
                if fin[j] + gp[c] > st:
                    st, w = fin[j] + gp[c], j
            if e and fin[i] - d[i][e] > st + 1e-9:
                p -= 1
                while on[order[p]] != e:
                    p -= 1
                w = order[p]
            elif w < 0:
                return path
            else:
                while order[p] != w:
                    p -= 1
            if e and w not in deps[i]:
                path.append((i, w))
            i = w

    wt = [float(x) for x in WEIGHT / KEPT["scale"]]
    runs = []
    for res in starts:
        order, on = sorted(range(n), key=lambda i: (res[3][i], i)), list(res[2])
        base = [[(j, kind(on[i], on[j])) for j in deps[i]] for i in range(n)]
        none = (0.0, [0.0] * m, [[0.0] * n] * m, ([0.0] * n, base, [()] * n, {}, [({}, total, [0.0] * NPS, [()] * NPS, {})]), [0.0] * m)
        runs.append((score(order, on, base, 0, none, 1e9), order, on, base))
    plan = [(r, x, it) for r, (k, tries) in enumerate(ROUNDS) for x in range(min(k, len(runs))) for it in range(tries)]
    for r, x, it in plan:
        if it == 0:
            if x == 0:
                runs.sort(key=lambda z: z[0][0])
            cur = best = runs[x]
            paths = {}
        runs[x] = best
        heat = SHAKE * (1 - it / ROUNDS[r][1] if r == len(ROUNDS) - 1 else 1)
        old, order, on, base = cur
        sc = old[0]
        k = int(rng.integers(m))
        if k not in paths:
            paths[k] = chain(old, order, on, k)
        path = paths[k]
        i, j = path[int(rng.integers(len(path)))]
        new, to, eb = list(order), on, base
        u = rng.random()
        if u > 1 - BIG:
            b = order.index(i)
            a = max(0, b - int(rng.integers(5, 80)))
            mv = set()
            for k in reversed(order[a:b + 1]):
                if nodes[k]["plus"] == nodes[i]["plus"] or any(y in mv for y in users[k]):
                    mv.add(k)
            new[a:b + 1] = [k for k in order[a:b + 1] if k in mv] + [k for k in order[a:b + 1] if k not in mv]
        elif u < 0.25:
            k = i if rng.random() < 0.5 else j
            if nodes[k]["e"] != "va":
                continue
            to = list(on); to[k] = "v" if on[k] == "a" else "a"
            a, eb = order.index(k), list(base)
            for y in [k] + users[k]:
                eb[y] = [(x, kind(to[y], to[x])) for x in deps[y]]
        else:
            a, b = order.index(j), order.index(i)
            if u < 0.65:
                mv = {i}
                for k in reversed(order[a:b]):
                    if any(y in mv for y in users[k]):
                        mv.add(k)
                if j in mv:
                    continue
                new[a:b + 1] = [k for k in order[a:b + 1] if k in mv] + [k for k in order[a:b + 1] if k not in mv]
            else:
                b = min(n - 1, b + int(rng.integers(0, 12)))
                mv = {j}
                for k in order[a + 1:b + 1]:
                    if any(y in mv for y in deps[k]):
                        mv.add(k)
                if i in mv:
                    continue
                new[a:b + 1] = [k for k in order[a:b + 1] if k not in mv] + [k for k in order[a:b + 1] if k in mv]
        limit = sc - heat * np.log(rng.random())
        z = score(new, to, eb, a, old, limit)
        if z is not None and z[0] < limit:
            cur, paths = (z, new, to, eb), {}
            if z[0] < best[0][0]:
                best = cur
    (sc, ends, _, (fin, _, plan, banks, _), _), order, on, _ = best
    at = [fin[i] - (dur[0][i][on[i]] if on[i] else lat[0][i]) for i in range(n)]
    order = [i for i in order if on[i]]
    KEPT.update(res=(ends[0], order, on, at, fin, banks, [list(x) for x in plan]), both=sc, ends=ends, sends=[sends[k] for k in order if k in sends])


def rank_program(g, core, T, topo):
    rank = T.rank_of(core)
    if rank is None:
        return relay_program(g, core, T, topo)
    nr = len(T.cores)
    nodes = []
    cur = {"plus": 0.0}
    hist = {}
    esem = {"v": "sv", "a": "sa", "p": "st", "g": "sg"}
    eng = {"v": g.vector, "a": g.scalar, "p": g.tensor, "g": g, "s": g.sync} if g is not None else {}
    one = np.ones(len(SPEED))

    def add(e, dur, w, r, fn, sem=None, inc=1, after=(), lat=0.0):
        i = len(nodes)
        deps = {}
        for x in r:
            ps = x[0][:2] == "ps"
            for (j, y, k) in hist.get(x[0], ()):
                if (k or ps) and clash(x, y):
                    deps[j] = min(deps.get(j, 2), 1 if k else 2)
        for x in w:
            for (j, y, k) in hist.get(x[0], ()):
                if clash(x, y):
                    deps[j] = min(deps.get(j, 2), 2 if e == "p" and nodes[j]["e"] == "p" else 1)
        for j in after:
            deps[j] = 1
        for x in w:
            h = hist.setdefault(x[0], [])
            h[:] = [z for z in h if not (x[3] == 1 and len(x) == 4 and x[1] <= z[1][1] and z[1][2] <= x[2])] if x[0][:2] != "ps" else []
            h.append((i, x, 1))
        for x in r:
            hist.setdefault(x[0], []).append((i, x, 0))
        banks = []
        for x in list(w) + list(r):
            if x[0][:3] == "ps@" and x[0] not in banks:
                banks.append(x[0])
        if not isinstance(dur, dict):
            dur, f1 = {e: dur}, fn
            fn = lambda e: f1()
        dur = {k: dur[k] * one for k in dur}
        nodes.append({"e": e, "dd": dur, "d": {k: float(dur[k][0]) for k in dur}, "plus": cur["plus"], "banks": banks, "w": w,
                      "deps": sorted(deps), "fn": fn, "sem": sem, "inc": inc, "ll": lat * one, "lat": float((lat * one)[0]),
                      "soft": [j for j in deps if deps[j] == 2]})
        return i

    def A(r, rows=None):
        if len(r) > 4:
            return T[r[0]][r[4]]
        n, o = ("ps%d" % phys[r[0]], 0) if r[0][:3] == "ps@" else PLACE[r[0]]
        p = slice(None) if rows is None else slice(0, rows)
        return T[n][p, o + r[1]:o + r[2]:r[3]] if r[3] > 1 else T[n][p, o + r[1]:o + r[2]]

    def R(name, lo=0, hi=None, step=1):
        return (name, lo, SIZE[name][0] if hi is None else hi, step)

    def R3(name, w0, w1, lo, hi, step=1):
        k = SCRATCH[name][1][2]
        if w1 is None:
            return (name, k * w0 + lo, k * w0 + hi, 1, (slice(None), w0, slice(lo, hi, step) if step > 1 else slice(lo, hi)),
                    -(-(hi - lo) // step), [(k * w0 + lo, k * w0 + hi)])
        return (name, k * w0 + lo, k * (w1 - 1) + hi, 1, (slice(None), slice(w0, w1), slice(lo, hi, step) if step > 1 else slice(lo, hi)),
                (w1 - w0) * -(-(hi - lo) // step), [(k * w + lo, k * w + hi) for w in range(w0, w1)])

    def num(r):
        return r[5] if len(r) > 4 else -(-(r[2] - r[1]) // r[3])

    def two(r):
        return r[0][:2] != "ps" and SIZE[r[0]][1] in ("bfloat16", "uint16", "float16")

    cv = lambda n: FV + max(64, n) * CY

    def dv(o, *i):
        return cv(num(o) * (0.5 if two(o) and all(two(x) for x in i) else 1))

    def da(o):
        return FA + num(o) * CY

    def dg(o):
        return {"v": 0.05 + num(o) * CY * GA, "a": 0.065 + num(o) * CY * GA}

    val = lambda s: A(s) if isinstance(s, tuple) else s

    def copy(o, i, e="v"):
        return add(e, {"v": dv(o, i), "a": da(o)}, [o], [i], lambda e: g.vector.tensor_copy(A(o), A(i)) if e == "v" else
                   g.scalar.activation(A(o), A(i), AF.Copy))

    def tsf(o, i, s1, op0, s2, op1):
        if op1 is None:
            return g.vector.tensor_scalar(o, i, val(s1), None, op0)
        return g.vector.tensor_scalar(o, i, val(s1), val(s2), op0, op1)

    def ts(o, i, s1, op0, s2=None, op1=None):
        return add("v", dv(o, i), [o], [i] + [s for s in (s1, s2) if isinstance(s, tuple)], lambda: tsf(A(o), A(i), s1, op0, s2, op1))

    def lin(o, i, k, c, e="va"):
        return add(e, {"v": dv(o, i), "a": da(o)}, [o], [i] + ([k] if isinstance(k, tuple) else []),
                   lambda e: g.vector.tensor_scalar(A(o), A(i), val(k), c, OP.mult, OP.add)
                   if e == "v" else g.scalar.activation(A(o), A(i), AF.Identity, bias=c, scale=val(k)))

    def tt(o, i, j, op):
        k = 1 if "ps" in (i[0][:2], j[0][:2]) else 2
        return add("v", cv(k * num(o)), [o], [i, j], lambda: g.vector.tensor_tensor(A(o), A(i), A(j), op))

    def act(o, i, func, bias=0.0, scale=1.0):
        return add("a", da(o), [o], [i] + ([bias] if isinstance(bias, tuple) else []),
                   lambda: g.scalar.activation(A(o), A(i), func, bias=val(bias), scale=scale))

    def mset(o, c):
        return add("v", dv(o), [o], [], lambda: g.vector.memset(A(o), c))

    def scans(lst, init, op0, op1):
        return add("v", sum(dv(*x) for x in lst), [x[0] for x in lst], [y for x in lst for y in x[1:]],
                   lambda: [g.vector.tensor_tensor_scan(A(o), A(i), A(j), init, op0, op1) for o, i, j in lst], inc=len(lst))

    def gather(e, o, win, off):
        f = lambda: A(win).indirect(A(off))
        return add(e, dg(o), [o], [win, off], lambda e: g.vector.tensor_copy(A(o), f()) if e == "v" else
                   g.scalar.activation(A(o), f(), AF.Copy))

    def glin(o, win, off, k, c):
        f = lambda: A(win).indirect(A(off))
        return add("va", dg(o), [o], [win, off], lambda e: g.vector.tensor_scalar(A(o), f(), k, c, OP.mult, OP.add)
                   if e == "v" else g.scalar.activation(A(o), f(), AF.Identity, bias=c, scale=k))

    def gtt(o, win, off, j):
        return add("v", dg(o)["v"], [o], [win, off, j],
                   lambda: g.vector.tensor_tensor(A(o), A(win).indirect(A(off)), A(j), OP.subtract))

    def mms(lst):
        w, r, d = [], [], 0.03
        for x in lst:
            if x[0] not in w:
                w.append(x[0])
            for y in x[1:3]:
                if y not in r:
                    r.append(y)
            d = d + max(64, num(x[2])) * PE * (4 if not two(x[2]) else 1)

        def fn():
            z = None
            for x in lst:
                k = x[5] if len(x) > 5 else None
                z = g.tensor.matmul(A(x[0]), A(x[1], k), A(x[2], k), x[3], x[4])
            return z
        return add("p", d, w, r, fn)

    def acc(o, pairs, first=True, last=True):
        n = len(pairs)
        return mms([(x[2] if len(x) > 2 else o, x[0], x[1], first and i == 0, last and i == n - 1) for i, x in enumerate(pairs)])

    phys, nbank = {}, [0]

    def bank(n):
        nbank[0] += 1
        return ("ps@%d" % nbank[0], 0, n, 1)

    ndma = [0]

    def dma(e, w, r, out, in_, dur=2.0, behind=()):
        s = "d%d" % ndma[0]; ndma[0] += 1
        i = add(e, 0.1, [], r, lambda: eng[e].dma_start(out, in_).then_inc(T.sem[s], 16), sem="loc", inc=0, after=behind)
        add(None, 0.0, w, r, None, sem=s, inc=16, after=[i], lat=dur)
        return i

    def iota(o, pattern, base, cm, ints=False):
        return add("g", 0.13 + num(o) * 2 * CY, [o], [], (lambda: g.iota(A(o), pattern, base, cm)) if ints else
                   (lambda: g.iota(A(o), pattern, base, cm, allow_small_or_imprecise_dtypes=True)))

    dma("s", [R("XT", 0, W)], [], T.XT[:, 0:W], T.xv[:, :], XLOAD)
    x = dma("a", [R("wni")], [], T.wni[0:8, :], T.wn[:, :])
    x = dma("a", [R("wli")], [], T.wli[:, :], T.wl[:, :], 2.5, [x])
    x = dma("a", [R("thi")], [], T.thi[0:8, :], T.th[:, :], 2.0, [x])
    dma("a", [R("wti")], [], T.wti[:, :], T.wt[:, :], 2.0, [x])
    col = lambda i: R("cols", i, i + 1)
    ci = lambda i: R("ci", i, i + 1)
    LA, LB, THR, TH, TN, WC, L32, LV, GP = [col(i) for i in range(9)]

    def select(o, i, pattern, op, fill, base, cm=1):
        return add("g", 0.17 + num(o) * 2 * CY, [o], [i], lambda: g.affine_select(A(o), A(i), pattern, op, float(fill), base, cm))

    def pick(o, pattern, base, k=1.0, zero="ZB"):
        return select(o, R(zero, 0, num(o)), pattern, OP.not_equal, k, base)

    mset(R("ZF32"), 0.0); mset(R("ZB", 0, 144), 0.0)
    iota(ci(0), [[0, 1]], 0, 1, True); ts(ci(1), ci(0), 15, OP.bitwise_and); copy(LA, ci(1)); ts(LB, LA, 16.0, OP.add)
    ts(ci(2), ci(0), 4, OP.arith_shift_right); copy(GP, ci(2))
    pick(R("E8"), [[-1, 8], [0, 16]], 0, zero="ZF32")
    add("v", cv(128), [R("wnf", 0, NW)], [R("wni")], lambda: g.vector.tensor_copy(A(R("wnf", 0, NW), 8), A(R("wni"), 8)))
    add("v", cv(1), [R("wnf", NW, NW + 1)], [R("thi")], lambda: g.vector.tensor_copy(A(R("wnf", NW, NW + 1), 8), A(R("thi"), 8)))
    bn = bank(NW + 1)
    add("p", 0.3, [bn], [R("E8"), R("wnf")], lambda: g.tensor.matmul(A(bn), A(R("E8"), 8), A(R("wnf"), 8), True, True))
    for x in range(4):
        pick(R("PM%d" % x), [[-32, 4], [1000, 2], [-2, 16]], -(x % 2) - 1000 * (x // 2))
    for b, nx in enumerate(NXS):
        cur["plus"] = NBK - 1 - b
        w0, w1 = W0[b], W0[b] + nx
        x, y = P * w0, P * w1
        ts(R("IM", x, y), R("wli", x, y), float(-HALF), OP.add)
        add("v", 2 * cv(16 * nx), [R("NLi", x, y)], [bn, LA, LB], lambda x=x, y=y: [g.vector.tensor_scalar(
            A(R("NLi", x + h, y, 2)), A(R(bn[0], x // 2, y // 2)), A(k), float(DEAD), OP.is_le, OP.mult) for h, k in ((0, LA), (1, LB))], inc=2)
        tt(R("IN", x, y), R("NLi", x, y), R("IM", x, y), OP.add)
        add("v", nx * cv(1), [R3("OT", w0, w1, 0, P)], [R("IN", x, y)], lambda w0=w0, w1=w1: [
            g.vector.transpose(A(R3("OT", w, None, 0, P)), A(R("IN", P * w, P * w + P))) for w in range(w0, w1)], inc=nx)
        mms([(R3("psz", w0, w1, 16 * i, 16 * i + 16), R("PM%d" % (2 * j + i)), R3("OT", w0, w1, 16 * j, 16 * j + 16),
              j == 0, j == 1) for i in (0, 1) for j in (0, 1)])
        z = R3("psz", w0, w1, 0, P)
        ts(R3("nm", 2 * b, 2 * b + 2, 0, 64), z, float(HALF), OP.add, float(DEAD), OP.min)
        lin(R3("NF", 2 * b, 2 * b + 2, 0, 64), z, 1.0, float(HALF))
    cur["plus"] = 0.0
    ts(THR, R(bn[0], NW, NW + 1), 0.5, OP.mult)
    ts(TH, THR, 0.25, OP.add, 400.0, OP.mult); ts(TN, TH, -1.0, OP.mult)
    mset(R("XT", W, W + 16), 255.0)
    pick(R("ID"), [[-1, 128]], 0)
    lin(R("N97"), R("ID"), -9776.0, 0.0, "v")
    for n, k in (("NEG", -1), ("N8", -8192), ("IDF", 1)):
        lin(R(n), R("ID"), float(k), 0.0)
    U = [R("NEG") if k == -1 else R("U", 128 * i, 128 * i + 128) for i, k in enumerate(UK)]
    for i, k in enumerate(UK):
        if i in UG:
            pick(U[i], [[-1, 128]], 0, k)
        elif k != -1:
            lin(U[i], R("ID"), float(k), 0.0, CQ)
    pick(R("SH", 0, 128), [[-1, 128]], 0, -0.5); select(R("SH", 0, 128), R("SH", 0, 128), [[-1, 128]], OP.not_equal, -0.5, 1)
    pick(R("SH", 128), [[-P, 4]], 1 - P, -0.5)
    copy(WC, R("wti")); mset(R("EW"), 0.0); mset(R("WW"), 0.0); mset(R("ONE"), 1.0)
    select(R("E9"), R("ONE", 0, 9), [[-16, 9]], OP.is_ge, 0, 0); select(R("EW", 15, 144, 16), R("E9"), [[16, 9]], OP.is_ge, 0, 15, -1)
    ts(R("WW", 15, 144, 16), R("EW", 15, 144, 16), WC, OP.mult)
    if any(map(any, RV)):
        lin(R("EN"), R("EW"), -1.0, 0.0)
    for n, k in (("K0", 0.0), ("PAT", 1.0), ("TWO", 2.0), ("MQ", -0.25), ("CK", 167.0 / 32), ("HF", 0.5)):
        mset(R(n), k)
    mset(R("K0", 0, LM, P), 16384.0); mset(R("K0", LM), 8 * 255.0); mset(R("PAT", 0, LM, P), 0.0); mset(R("LUT", FULL), 0.0)
    for b, nx in enumerate(NXS):
        mset(R("V%d" % b, 0, 16), 0.0)
    for n in sorted(set(STAGE)):
        mset(R3(n, 0, 8, 48, CELLS), float(DEAD - HALF))
    iota(R("YI"), [[1, 16]], 0, 0); iota(R("CG"), [[1, 8], [0, 16]], 0, 0)
    ts(R("MK"), R("YI", 0, 16), LA, OP.is_equal); ts(R("BLK"), R("CG"), GP, OP.is_equal)
    mset(R("ZB", 144), 0.0)
    for x in range(0, 16, 4):
        if x // 4 in SG:
            pick(R("SEL", 128 * x, 128 * x + 512), [[-1, 4], [-16, 8], [0, 16]], -x)
        else:
            for y in range(x, x + 4):
                lin(R("SEL", 128 * y, 128 * y + 128), R("BLK"), R("MK", y, y + 1), 0.0)
    iota(R("RA"), [[16, LM]], 0, 0); ts(R("RAMP"), R("RA"), LA, OP.add)
    for x in sorted(set(NXS)):
        iota(R("BW%d" % x), [[0, 8], [CELLS * x, 2], [CELLS, x]], 0, 0); lin(R("BE%d" % x), R("BW%d" % x), 1.0, 48.0)
    iota(R("W5"), [[512, 8]], 0, 0); iota(R("BH"), [[0, 16], [CELLS, 4]], 0, 0)
    pick(R("SHF"), [[-1, 128]], 16); select(R("SHF"), R("SHF"), [[-1, 128]], OP.not_equal, 1, -112)
    tt(R("MK8"), R("MK", 0, 8), R("MK", 8, 16), OP.add)
    for e, j in sorted({(e, j) for x in NJ for y in x for z in y for e, j0, j1 in z for j in range(j0, j1)}):
        lin(R("DE" if e == "v" else "DF", 128 * j, 128 * j + 128), R("SHF"), R("MK8", j, j + 1), 0.0, CQ)
    for x in range(4):
        pick(R("XB", 128 * x, 128 * x + 128), [[-16, 8], [-1, 8], [1000, 2]], -8 * (x // 2) - 1000 * (x % 2), zero="ZF32")
    ts(L32, LA, 32.0, OP.mult); ts(R("W32"), R("W5"), L32, OP.add)
    for x in range(0, 16, 4):
        pick(R("DR", 144 * x, 144 * x + 576), [[-1, 4], [-16, 9], [1000, 16]], 16 - x - 15000)
    select(R("DR", 15, None, 144), R("DR", 15, None, 144), [[-1, 16]], OP.not_equal, 1, -112)
    for x in range(4):
        pick(R("XM%d" % x), [[-16, 8], [1000, 2], [-2, 8]], -(x % 2) - 1000 * (x // 2))
    copy(LV, ci(0))
    scans([(R("R2"), R("HF"), R("ZB", 0, 8))], 2.0, OP.mult, OP.add)
    ts(R("bi"), R("R2"), LV, OP.mult, -0.49, OP.add); ts(R("bj"), R("bi"), 1, OP.bitwise_and); copy(R("bf"), R("bj"))
    scans([(R("pre"), R("ONE", 0, 8), R("bf"))], 0.0, OP.mult, OP.add)
    ts(R("pb"), R("pre"), -200.0, OP.mult, 100.0, OP.add)
    add("a", 1.3 + 7 * (FA + 16 * CY), [R("VY")], [R("YI"), R("pb")], lambda: [g.scalar.activation(
        A(R("VY", 16 * p, 16 * p + 16)), A(R("YI")), AF.Sigmoid, bias=A(R("pb", p, p + 1)), scale=200.0) for p in range(7)], inc=7)
    f = bank(128)
    add("p", 0.03 + 1024 * PE, [f], [R("VY"), R("ONE"), R("ID")], lambda f=f: [g.tensor.matmul(
        A(f, 16), A(R("VY", 16 * p, 16 * p + 16) if p < 7 else R("ONE", 0, 16)), A(R("ID")), p == 0, p == 7) for p in range(8)][-1])
    add("va", {"v": dv(f), "a": da(f)}, [R("TD")], [f], lambda e, f=f: g.vector.tensor_copy(A(R("TD"), 16), A(f, 16))
        if e == "v" else g.scalar.activation(A(R("TD"), 16), A(f, 16), AF.Copy))
    pick(R("WD"), [[0, 9], [-1, 16]], 0)
    for y in range(0, 16, 4):
        f = bank(512)
        mms([(R(f[0], 128 * (c - y), 128 * (c - y + 1)), R("WD", 16 - c, 144 - c), R("TD"), True, True, 16 - c) for c in range(y, y + 4)])
        copy(R("LUT", 128 * y, 128 * y + 512), f, CQ)
    nloc = [0]
    win = lambda name, r: R(name, 15 - r, 143 - r)
    sends, used = {}, set()

    def transmit(k, t, b):
        before = []
        for parts in [ws for j, ws in calls(t, b) if j == k]:
            ws = [x + leg(topo, core, T.cores[target(rank, nr, t, x[0])], t, b, k) for x in parts]
            nloc[0] += sum(len(x[6]) for x in ws)
            i = add("g", CALL + (0.0 if sends else ONCE), [], [R3(x[1] + "S", x[2], x[2] + x[4], 0, SCRATCH[x[1] + "S"][1][2]) for x in ws],
                    lambda ws=ws: g.remote_dma_fused(
                        [transfer(T, topo, core, to, T[u + "S"][:, s:s + m, :], T[u + "R"][:, r:r + m, :], e, "m%d%d%d%d" % (k, t, b, h))
                         for h, u, s, r, m, to, e in ws], local_sem=T.sem["loc"]), sem="loc", inc=0, after=before)
            sends[i] = (t, b, k, parts)
            before = [i]
            for h, u, _, r, m, out, _ in ws:
                src = T.cores[[q for q in range(nr) if target(q, nr, t, h) == rank][0]]
                to = leg(topo, src, core, t, b, k)[0]
                last, size = [i], BYTE * (2 * m * SCRATCH[u + "S"][1][2] - 128)
                if to != core:
                    last = [add(None, 0.0, [], [], None, sem="loc", inc=0, after=last,
                                lat=HOP0 + (HALFE + size if len(ws) > 1 else size / 2))]
                    last = [add(str(out % 2), CALL + (0.0 if out in used else ONCE), [], [], None, sem="loc", inc=0, after=last)]
                    used.add(out)
                add(None, 0.0, [R3(u + "R", r, r + m, 0, SCRATCH[u + "R"][1][2])], [], None, sem="m%d%d%d%d" % (k, t, b, h), after=last,
                    lat=HOP1 + size, inc=len(topo.engines(src if to == core else to, core)))

    def rows(h, t, b, first, m, lo=0, hi=P):
        x = MROWS * (t * NBK + b)
        n, x = ("MS", x + first) if h is None else ("MR", 2 * x + MROWS * h + first)
        return R3(n, x, None if m is None else x + m, lo, hi)

    def put_half(t, b, h, x):
        n, nx = R3("n1%d" % b, 2 * h, 2 * h + 2, 0, P), NXS[b]
        ts(n, x, W - 1, OP.bitwise_and)
        ts(rows(None, t, b, NR[1] + 2 * h, 2), n, float(-HALF), OP.add)
        transmit(2 + h, t, b)

    def put_names(e, t, b, x, lo=0, hi=P, shift=0):
        n, nx = "n%d%d" % (e, b), NXS[b]
        u = UROWS * b + 2 + nx * e
        if shift:
            ts(R3(n, 0, nx, lo, hi), x, shift, OP.arith_shift_right, W - 1, OP.bitwise_and)
        else:
            ts(R3(n, 0, nx, lo, hi), x, W - 1, OP.bitwise_and)
        if t == RO - 1 and hi == P:
            ts(R3("US", u, u + nx, 0, 16), R3(n, 0, nx, 16, P), float(-HALF), OP.add)
            transmit(1 + e, t, b)
        ts(rows(None, t, b, NR[e], nx, lo, hi), R3(n, 0, nx, lo, hi), float(-HALF), OP.add)
        if t < RO - 1:
            transmit(1 + e, t, b)

    def chunks(t, b):
        s, nx, own = str(b), NXS[b], 0 if t < RO - 1 else None
        num16 = lambda h, y, hi=16: (rows(h, t, b, S_C, None, 16 * y, 16 * y + hi) if t < RO - 1 else
                                     R3("US" if h is None else "UR", UROWS * b + y, None, 0, hi))
        copy(R3("IX" + s, 0, nx, 4, 8), num16(own, 1))
        f = bank(4 * nx)
        acc(f, [(R("ID"), num16(1, 0)), (R("ID"), num16(own, 0, 14), R(f[0], 2, 4 * nx))])
        ts(R3("IX" + s, 0, nx, 0, 4), f, float(FULL), OP.min)

    def join_halves(t, b):
        s, nx = str(b), NXS[b]
        chunks(t, b)
        for w in range(nx):
            gather(GG, R3("GH" + s, w // 2, None, w % 2, 192, 2), R("LUT"), R3("IX" + s, w, None, 2, 8))
        f = bank(64)
        acc(f, [(R("ID"), R3("GH" + s, 0, 2, 32 * c, 32 * c + 32)) for c in range(6)] + [(R("ID"), R("BH"))])
        copy(R("of" + s), f)
        for h in HO:
            st = STAGE[h]
            u = UROWS * NBK + nx * (t * NBK + b) + 2 * h
            for lo, hi, part in ((P, 48, 1), (0, P, 0)):
                mms([(R3(st, 4 * h + 2 * y, 4 * h + 2 * y + 2, lo, hi), R("XM%d" % (2 * e + y)),
                      R3("UR", u, u + 2, 0, 16) if PACK and part and e else rows(part, t, b, NR[e] + 2 * h, 2, 16 * part, P), e == 0, e == 1)
                     for y in (0, 1) for e in (0, 1)])
            wn = R("WN" + s, 4 * CELLS * h, 4 * CELLS * (h + 1))
            copy(wn, R3(st, 4 * h, 4 * h + 4, 0, CELLS), "va")
            f = bank(64)
            for i, (e, j0, j1) in enumerate(NJ[t][b][h]):
                x, n, d = 512 * h + 64 * j0, "N" if e == "v" else "NA", "DE" if e == "v" else "DF"
                gather(e, R(n + s, x, x + 64 * (j1 - j0)), wn, R("of" + s, x // 16, x // 16 + 4 * (j1 - j0)))
                acc(f, ([(R("N8"), R("MQ", 0, 64))] if i == 0 else []) +
                    [(R(d, 128 * j, 128 * j + 128), R(n + s, 512 * h + 64 * j, 512 * h + 64 * j + 64)) for j in range(j0, j1)],
                    i == 0, i == len(NJ[t][b][h]) - 1)
            copy(R3("nm", 2 * b, 2 * b + 2, 32 * h, 32 * h + 32), f)
            copy(R3("NF", 2 * b, 2 * b + 2, 32 * h, 32 * h + 32), f, "va")

    def join(t, b):
        s, nx = str(b), NXS[b]
        nb, l, own = 16 * nx, P * nx, 0 if t < RO - 1 else None
        chunks(t, b)
        for w in range(nx):
            gather(GG, R("G" + s, w, None, nx), R("LUT"), R3("IX" + s, w, None, 2, 8))
        f = bank(nb)
        acc(f, [(R("ID"), R("G" + s, nb * c, nb * c + nb)) for c in range(6)] + [(R("ID"), R("BW%d" % nx))])
        copy(R("of" + s), f)
        st = STAGE[b]
        if t == RO - 1:
            tt(R("lv" + s), f, R("BE%d" % nx), OP.is_lt)
            if st not in STAGE[:b]:
                mset(R3(st, 0, 8, 48, CELLS), float(-HALF))
        up = lambda e: R3("UR", UROWS * b + 2 + nx * e, UROWS * b + 2 + nx * e + nx, 0, 16)
        parts = [(P, 48, up), (0, P, lambda e: rows(own, t, b, NR[e], nx))]
        for lo, hi, x in (parts if t < RO - 1 else parts[::-1]):
            mms([(R3(st, nx * y, nx * y + nx, lo, hi), R("XM%d" % (2 * e + y)), x(e), e == 0, e == 1) for y in (0, 1) for e in (0, 1)])
        copy(R("WN" + s), R3(st, 0, 2 * nx, 0, CELLS), "va")

    def joined(t, b):
        s, nx = str(b), NXS[b]
        nb, l = 16 * nx, P * nx
        f = bank(l)
        for y in range(0, 16, 4):
            gather("v", R("N" + s, nb * y, nb * y + 4 * nb), R("WN" + s), R("of" + s, nx * y, nx * y + 4 * nx))
            acc(f, ([(R("N8"), R("MQ", 0, l))] if y == 0 else []) +
                [(R("DR", 144 * (8 * e + x // 2) + 15 - x, 144 * (8 * e + x // 2) + 143 - x), R("N" + s, nb * x, nb * x + nb), R(f[0], e, l, 2))
                 for x in range(y, y + 4) for e in (0, 1)], y == 0, y == 12)
        return f

    def step(o, i, more):
        return add("va", {"v": dv(o, i), "a": da(o)}, [o], [i, TH, TN, THR, R("VY")],
                   lambda e: g.vector.tensor_scalar(A(o), A(i), A(THR), None, OP.is_gt if more else OP.is_le) if e == "v" else
                   g.scalar.activation(A(o), A(i), AF.Sigmoid, bias=A(TN if more else TH), scale=400.0 if more else -400.0))

    for t in range(RO):
        for b, NX in enumerate(NXS):
            s = str(b)
            L, LO, WO = P * NX, P * W0[b], 16 * W0[b]
            ROWS = 16 * L
            r = lambda n, lo=0, hi=None, step=1: R(n + s, lo, hi, step)
            cur["plus"] = NBK - 1 - b
            if t:
                join_halves(t - 1, b)
            for w in range(NX):
                gather(VG, r("V", 16 + CH * w, 16 + CH * w + CH), R("XT", 0, W + 16), R3("nm", 2 * b + w // 2, None, P * (w % 2), P * (w % 2) + P))
            if t:
                vs = lambda x, back=0: r("V", 16 + 8 * L * (x % 2) + x // 2 - 8 * back, 16 + 8 * L * (x % 2 + 1) - 8 * back, 8)
                lanes = list(range(0, 16, 2)) + list(range(1, 16, 2))
            else:
                vs = lambda x, back=0: r("V", 16 + x - 16 * back, 16 + ROWS - 16 * back, 16)
                lanes = list(range(16))
            D = bank(L + 4)
            DL = R(D[0], 0, L)
            f = bank(128)
            for y in (0, 8):
                mms([(R(f[0], x, 128, 16), vs(x), R("EW", 15, 143, 16), True, True) for x in lanes[y:y + 8]])
            add("va", {"v": dv(f), "a": da(f)}, [r("S")], [f], lambda e, f=f, s=s, L=L: g.vector.tensor_copy(A(R("S" + s), L), A(f, L))
                if e == "v" else g.scalar.activation(A(R("S" + s), L), A(f, L), AF.Copy))
            for y in range(0, 16, 4):
                scans([(r("M", L * x, L * x + L), vs(x, 1), vs(x)) for x in lanes[y:y + 4]], 256.0, OP.min, OP.max)
                acc(DL, ([(R("ID"), R("K0"), D)] if y == 0 else []) + [(win("EW", x), r("M", L * x, L * x + L)) for x in lanes[y:y + 4]], y == 0, False)
            mms([(D, r("S"), R("SH"), False, True)])
            step(r("C"), DL, False)
            lin(r("E", 0, L - 1), r("C", 1, L), -1.0, 1.0)
            step(r("E", P - 1, L, P), R(D[0], L, L + 4), True)
            per = 4 if NX > 2 else 8
            fu = bank(L)
            for y in range(0, 16, per):
                f = bank(per * L)
                mms([(R(f[0], L * (x - y), L * (x - y + 1)), R("SEL", 128 * x, 128 * x + 128), r("C"), True, True) for x in range(y, y + per)])
                n, o = f[0], 0
                if y // per in ZC[b]:
                    n, o = "CR" + s, L * y
                    copy(R(n, o, o + per * L), f, "a")
                scans([(r("Z", x, ROWS, 16), R(n, o + L * (x - y), o + L * (x - y + 1)), vs(x)) for x in range(y, y + per)],
                      0.0, OP.mult, OP.max)
                acc(fu, [(win("WW", x), r("Z", x, ROWS, 16)) for x in range(y, y + per)], y == 0, y + per == 16)
            scans([(r("cs", L), R("PAT", 0, L), r("E"))], 0.0, OP.mult, OP.add)
            x, y = r("cs", 0, L), r("cs", L)
            add("va", {"v": dv(x, y), "a": da(x)}, [x], [y], lambda e, x=x, y=y: g.vector.tensor_scalar(A(x), A(y), -16.0, 0.0, OP.add, OP.max)
                if e == "v" else g.scalar.activation(A(x), A(y), AF.Relu, bias=-16.0))
            f = bank(8 * NX)
            acc(f, [(U[i], r("cs", i, None, 8)) for i in range(8)] +
                [(U[8], r("cs", L + P - 1, None, P), R(f[0], c, 4 * NX, 4)) for c in (0, 1)])
            ts(rows(None, t, b, S_C, None) if t < RO - 1 else R3("US", UROWS * b, UROWS * b + 2, 0, 16), f, float(FULL), OP.min)
            transmit(0, t, b)
            scans([(r("cm"), r("C"), R("TWO", 0, L))], 0.0, OP.mult, OP.add)
            c2, hm = R3("c2" + s, 0, NX, 0, P), R3("hm" + s, 0, NX, 0, P)
            lin(c2, r("cm"), 1.0, 1.0)
            f = bank(L)
            if t:
                acc(f, [(R("N8"), r("C"))] + [(R("XB", 128 * (2 * e + y), 128 * (2 * e + y + 1)), R3("NF", 2 * b + y, None, 0, 64), R(f[0], e, L, 2))
                                              for y in (0, 1) for e in (0, 1)])
            else:
                acc(f, [(R("IDF"), R3("NF", 2 * b, 2 * b + 2, 0, 64)), (R("N8"), r("C"))])
            scans([(R(f[0], L, 2 * L), r("C"), f)], 0.0, OP.mult, OP.max)
            if t == 0:
                tt(r("ni"), R(f[0], L, 2 * L), c2, OP.mult)
                put_names(0, t, b, r("ni"), shift=2)
            else:
                tt(r("na"), R(f[0], L, 2 * L), c2, OP.mult)
                ts(r("ni"), r("na"), 0.25, OP.mult, R("AC", t, t + 1), OP.add)
                put_names(0, t, b, r("ni"))
            f = bank(L)
            acc(f, [(R("ID"), R("RAMP", 0, L)), (R("N8"), r("E"))])
            scans([(R("y", LO, LO + L), R("K0", 0, L), f)], 0.0, OP.add, OP.min)
            ts(r("zo"), R("y", LO + P - 1, LO + L, P), 8192.0, OP.add, float(ROWS - 1), OP.min)
            glin(R("ZF", WO, WO + 16 * NX), r("Z"), r("zo"), 1.0, -192.0)
            f = bank(L)
            acc(f, [(R("N97"), r("cm")), (R("N8"), R("CK", 0, L))])
            for w0, w1 in HH[t][b]:
                x, y = P * w0, P * w1
                lin(r("r", x, y), R(fu[0], x, y), -1.0, HALF - 0.5 - MAGIC)
                tt(r("v", x, y), R(fu[0], x, y), r("r", x, y), OP.add)
                act(r("sq", x, y), r("v", x, y), AF.Square, 592.0 + MAGIC)
                tt(r("si", x, y), r("sq", x, y), R(f[0], x, y), OP.subtract)
                ts(R3("hm" + s, w0, w1, 0, P), r("si", x, y), 5, OP.arith_shift_right, W - 1, OP.bitwise_and)
                copy(r("hu", x, y), R3("hm" + s, w0, w1, 0, P))
            xa = min(XA[t][b], NX)

            def distance(w, lo, hi):
                o, z = r("D2", CH * w + lo, CH * w + hi), r("Z", CH * w + lo, CH * w + hi)
                off = r("hu", P * w + lo // 16, P * w + hi // 16)
                if w < xa:
                    gather("a", o, R("XT", 0, W), off)
                    f = bank(hi - lo)
                    acc(f, [(R("NEG"), z), (R("ID"), o)])
                    act(R3("AD" + s, w, None, lo, hi), f, AF.Abs)
                else:
                    gtt(o, R("XT", 0, W), off, z)
                    if w in RV[t][b]:
                        ts(R3("AD" + s, w, None, lo, hi), o, 0.0, OP.max, 2.0, OP.mult)
                    else:
                        act(R3("AD" + s, w, None, lo, hi), o, AF.Abs)

            if t < RO - 1:
                for h in HO:
                    fd = bank(64)
                    for w in (2 * h, 2 * h + 1):
                        distance(w, 0, CH)
                    less = 2 * h in RV[t][b]
                    if less:
                        acc(fd, [(win("EN", x), r("D2", 2 * CH * h + x, 2 * CH * (h + 1), 16)) for x in range(16)], True, False)
                    acc(fd, [(win("EW", x), R3("AD" + s, 2 * h, 2 * h + 2, x, CH, 16)) for x in range(16)], not less)
                    tt(fd, fd, R3("c2" + s, 2 * h, 2 * h + 2, 0, P), OP.mult)
                    tt(r("nj", 64 * h, 64 * h + 64), fd, R3("hm" + s, 2 * h, 2 * h + 2, 0, P), OP.add)
                    put_half(t, b, h, r("nj", 64 * h, 64 * h + 64))
                if PACK:
                    u = UROWS * NBK + NX * (t * NBK + b)
                    ts(R3("US", u, u + NX, 0, 16), R3("n1" + s, 0, NX, 16, P), float(-HALF), OP.add)
                transmit(4, t, b)
            else:
                y = L // 2
                for h in (1, 0):
                    fd = bank(y)
                    for w in range(NX):
                        distance(w, CH // 2 * h, CH // 2 * (h + 1))
                    acc(fd, [(win("EW", x), R3("AD" + s, 0, NX, CH // 2 * h + x, CH // 2 * (h + 1), 16)) for x in range(16)])
                    tt(fd, fd, R3("c2" + s, 0, NX, 16 * h, 16 * h + 16), OP.mult)
                    tt(r("nj", y * h, y * h + y), fd, R3("hm" + s, 0, NX, 16 * h, 16 * h + 16), OP.add)
                    put_names(1, t, b, r("nj", y * h, y * h + y), 16 * h, 16 * h + 16)
            x, y, z = WO, WO + 16 * xa, xa - xa % 2
            if xa < NX:
                glin(R("e2", x + 16 * z, x + 16 * NX), r("D2"), r("zo", z), 0.5, 191.75)
            if xa:
                gtt(R("e1", x, y), r("D2"), r("zo", 0, xa), R("ZF", x, y))
                lin(R("e2", x, y), R("e1", x, y), 0.5, 95.75)
        cur["plus"] = 0.0
        if t < RO - 1:
            f = bank(1)
            acc(f, [(R("ONE"), R("cs%d" % b, x, x + 1)) for b in range(NBK) for x in range(P * NXS[b] + P - 1, 2 * P * NXS[b], P)])
            copy(R("ATi"), f)
            ts(R("ATj"), R("ATi"), 255, OP.bitwise_and); ts(R("AC", t + 1, t + 2), R("ATj"), -0.375, OP.add)
        f = bank(8)
        acc(f, [(win("WW", x), R("ZF", x, NW, 16)) for x in range(16)])
        copy(R("wa"), f); ts(R("wb"), R("wa"), 31, OP.bitwise_and)
        ts(R("iv"), R("y", P - 1, 2 * NW, P), 0.0, OP.is_ge, float(W + 16), OP.mult)
        tt(R("bs"), R("iv"), R("W32"), OP.add); tt(R("wf"), R("wb"), R("bs"), OP.add); copy(R("WL"), R("wf"))
        add("v", 0.05 + NW * CY * 3.5, [R("XT")], [R("ZF"), R("e2"), R("WL")],
            lambda: g.vector.tensor_tensor(A(R("XT")).indirect(A(R("WL"))), A(R("ZF")), A(R("e2")), OP.add))
    for q in range(4):
        if q in YV:
            tt(R("YX", 512 * q, 512 * q + 512), R("XT", 1024 * q, 1024 * q + 1024, 2), R("XT", 1024 * q + 1, 1024 * q + 1024, 2), OP.add)
        else:
            f = bank(512)
            acc(f, [(R("ID"), R("XT", 1024 * q + e, 1024 * q + 1024, 2)) for e in (0, 1)])
            copy(R("YX", 512 * q, 512 * q + 512), f, "va")
        if q % 2:
            dma("s", [("yx", q, q + 1, 1)], [R("YX", 512 * q - 512, 512 * q + 512)], T.yx[:, 512 * q - 512:512 * q + 512],
                T.YX[:, 512 * q - 512:512 * q + 512], 3.0)
    for x in range(4):
        pat, base = [[-32, 4], [-1, 16], [1000, 2]], -16 * (x // 2) - 16 - 1000 * (x % 2)
        pick(R("QM%d" % x), pat, base)
        if x // 2:
            select(R("QM%d" % x), R("QM%d" % x), pat, OP.not_equal, 1, base + 128)
    t = RO - 1
    for b in range(NBK):
        cur["plus"] = NBK - 1 - b
        join(t, b)
    for b, nx in enumerate(NXS):
        s, nb, w0, wo = str(b), 16 * nx, W0[b], 16 * W0[b]
        cur["plus"] = NBK - 1 - b
        f = joined(t, b)
        z = bank(nb)
        add("p", 0.15, [z], [R("EW"), R("lv" + s)], lambda z=z, s=s, nx=nx: [g.tensor.matmul(
            A(R(z[0], 16 * w, 16 * w + 16), 8), A(R("EW", 15, 143, 16)), A(R("lv" + s, w, 16 * nx, nx)), True, True) for w in range(nx)][-1])
        add("v", cv(1), [R("yno", wo, wo + nb)], [z], lambda z=z, wo=wo, nb=nb: g.vector.tensor_scalar(A(R("yno", wo, wo + nb), 8), A(z, 8), 2.0, None, OP.mult))
        ts(R3("NB" + s, 0, nx, 0, P), f, float(-HALF), OP.add)
        l = []
        for x in (0, 1):
            o = R3("psz", w0, w0 + nx, 16 * x, 16 * x + 16)
            l += [(o, R("QM%d" % (2 * x), 0, 128), R3("NB" + s, 0, nx, 0, 16), True, False), (o, R("N8"), R("MQ", 0, nb), False, False),
                  (o, R("QM%d" % (2 * x + 1), 0, 128), R3("NB" + s, 0, nx, 16, P), False, True)]
        mms(l)
        add("v", nx * cv(1), [R("yl" + s)], [R("psz")], lambda w0=w0, s=s, nx=nx: [
            g.vector.transpose(A(R("yl" + s, P * w, P * w + P)), A(R3("psz", w0 + w, None, 0, P))) for w in range(nx)], inc=nx)
        dma("s" if b % 2 else "a", [("yl", b, b + 1, 1)], [R("yl" + s)], T.yl[:, P * w0:P * w0 + P * nx], T["yl" + s][:, :])
    cur["plus"] = 0.0
    dma("s", [("yn", 0, 1, 1)], [R("yno")], T.yn[:, :], T.yno[0:8, :])

    n = len(nodes)
    users = [[] for _ in range(n)]
    for i, x in enumerate(nodes):
        for j in x["deps"]:
            users[j].append(i)
    prio = [0.0] * n
    for i in range(n - 1, -1, -1):
        x = nodes[i]
        prio[i] = (min(x["d"].values()) if x["e"] == "va" else x["d"][x["e"]] if x["e"] else 0.0) + x["lat"] + LINK[0] + max([prio[k] for k in users[i]] + [0.0])
    free = {k: 0.0 for k in "vapgs01"}
    gaps = lambda a, b: LINK if a != b else 0.0 if a == "p" else SAME
    gap = lambda a, b, g0=(float(LINK[0]), float(SAME[0])): g0[0] if a != b else 0.0 if a == "p" else g0[1]

    def sweep(urgency, back, on, urge, vpen):
        before, after = (users, [x["deps"] for x in nodes]) if back else ([x["deps"] for x in nodes], users)
        left = [len(x) for x in before]
        ready_at, at, fin, took, more = [0.0] * n, [0.0] * n, [0.0] * n, [None] * n, [[] for _ in range(n)]
        busy = dict(free)
        ready = {k: [] for k in free}
        order, banks, bleft = [], {}, {}
        bfree = [0.0] * NPS
        blast = [[] for _ in range(NPS)]
        for x in nodes:
            for k in x["banks"]:
                bleft[k] = bleft.get(k, 0) + 1

        def done(i):
            for k in after[i]:
                ready_at[k] = max(ready_at[k], fin[i] + gap(took[i], on[k]) + nodes[k if back else i]["lat"])
                left[k] -= 1
                if left[k] == 0:
                    release(k)

        def release(k):
            if on[k] is None:
                at[k] = fin[k] = ready_at[k]
                done(k)
            else:
                for e in on[k]:
                    ready[e].append(k)

        for i in [i for i in range(n) if not before[i]]:
            ready_at[i] = nodes[i]["lat"] if back else 0.0
            release(i)
        while any(ready.values()):
            best = None
            fr = [z for z in bfree if z is not None]
            for e in free:
                for k in ready[e]:
                    st = max(busy[e], ready_at[k])
                    if not back and [y for y in nodes[k]["banks"] if y not in banks]:
                        if not fr:
                            continue
                        st = max(st, min(fr))
                    key = (st + (vpen if len(on[k]) > 1 and e == "v" else 0.0) - urge * urgency[k], -urgency[k])
                    if best is None or key < best[0]:
                        best = (key, e, k, st)
            _, e, k, st = best
            for y in on[k]:
                ready[y].remove(k)
            took[k], at[k], fin[k] = e, st, st + nodes[k]["d"][e]
            for y in ([] if back else nodes[k]["banks"]):
                if y not in banks:
                    z = min([z for z in range(NPS) if bfree[z] is not None], key=lambda z: bfree[z])
                    banks[y] = z
                    bfree[z] = None
                    more[k] += blast[z]
                    blast[z] = []
                bleft[y] -= 1
                blast[banks[y]].append(k)
                if bleft[y] == 0:
                    bfree[banks[y]] = fin[k] + LINK[0]
            busy[e] = fin[k]
            order.append(k)
            done(k)
        return max(fin[i] + nodes[i]["lat"] for i in range(n)), order, took, at, fin, banks, more

    def again(res):
        fin, busy = [None] * n, {k: 0.0 * one for k in free}
        for i in sorted(range(n), key=lambda i: (res[3][i], i)):
            e = res[2][i]
            st = busy[e] if e else 0.0 * one
            for j in nodes[i]["deps"] + res[6][i]:
                st = np.maximum(st, fin[j] + gaps(e, res[2][j]))
            if e:
                busy[e] = st + nodes[i]["dd"][e]
            fin[i] = busy[e] if e else st + nodes[i]["ll"]
        return np.max(fin, axis=0)

    if not KEPT:
        pool, rng = [], np.random.default_rng(SEED)

        def passes(late, urge, vpen, k):
            for _ in range(k):
                res = sweep(late, False, [x["e"] for x in nodes], urge, vpen)
                ends = again(res)
                KEPT.setdefault("scale", ends)
                both = float(np.sum(WEIGHT * ends / KEPT["scale"]))
                late = sweep(res[4], True, res[2], urge, vpen)[4]
                if all(abs(both - z[0]) > 1e-4 for z in pool):
                    pool.append((both, res, late, urge, vpen))

        for first, urge, vpen in RULES:
            passes([prio[i] + first * nodes[i]["plus"] for i in range(n)], urge, vpen, PASSES)
        for _ in range(AGAIN):
            pool.sort(key=lambda z: z[0])
            del pool[POOL:]
            _, _, late, urge, vpen = pool[int(rng.integers(len(pool)))]
            k = NOISE * rng.random()
            passes([z + y for z, y in zip(late, k * rng.standard_normal(n))], urge, vpen, 2)
        pool.sort(key=lambda z: z[0])
        KEPT["first"] = [z[0] for z in pool]
        polish(nodes, sends, [z[1] for z in pool[:POOL]])
    if g is None:
        return
    end, order, took, at, fin, banks, more = KEPT["res"]
    phys.update(banks)
    for i, x in enumerate(nodes):
        x["e"], x["t"], x["deps"] = took[i], at[i], sorted(set(x["deps"] + more[i]))
    if "want_est" in T.tables:
        T.tables["want_est"].append((end, {e: sum(x["d"][e] for x in nodes if x["e"] == e) for e in free}, n, nodes))
    cnt = {"v": 0, "a": 0, "p": 0, "g": 0}
    for k in order:
        x = nodes[k]
        if x["sem"] is None:
            cnt[x["e"]] += x["inc"]
            x["at"] = (esem[x["e"]], cnt[x["e"]])
        else:
            x["at"] = (x["sem"], x["inc"])
    for x in nodes:
        if x["e"] is None:
            x["at"] = (x["sem"], x["inc"])
    known = {k: {} for k in free}
    for k in order:
        x = nodes[k]
        if x["e"] not in eng:
            continue
        q = eng[x["e"]]
        need = {}
        for j in x["deps"]:
            sm, v = nodes[j]["at"]
            if sm != "loc" and not (j in x["soft"] and nodes[j]["e"] == x["e"]):
                need[sm] = max(need.get(sm, 0), v)
        for sm in sorted(need):
            if known[x["e"]].get(sm, 0) < need[sm]:
                q.wait_ge(T.sem[sm], need[sm])
                known[x["e"]][sm] = need[sm]
        z = x["fn"](x["e"])
        if x["sem"] is None:
            for y in (z if isinstance(z, list) else [z]):
                y.then_inc(T.sem[esem[x["e"]]], 1)
        elif x["sem"] != "loc":
            z.then_inc(T.sem[x["sem"]], x["inc"])
    for e in ("v", "a", "p", "g"):
        g.wait_ge(T.sem[esem[e]], cnt[e])
    for i in range(ndma[0]):
        g.wait_ge(T.sem["d%d" % i], 16)
    g.wait_ge(T.sem["loc"], nloc[0])
